import numpy as np, ml_dtypes
CORES = [10,34,74,98]
N = 4
BF = ml_dtypes.bfloat16
V, D, L, RO, HOP = 3072, 12, 256, 4, 2
def meet(rng, n, rest):
    p = np.argsort(rng.random((N, 8, n, V)), axis=-1); h = np.zeros_like(p)
    np.put_along_axis(h, p[..., 0::2], p[..., 1::2], 3); np.put_along_axis(h, p[..., 1::2], p[..., 0::2], 3)
    o = np.concatenate([h, rest], axis=2)
    return np.ascontiguousarray(np.take_along_axis(o, np.argsort(rng.random(o.shape), axis=2), 2))
def court(rng, lo, hi):
    c = rng.integers(0, V, (N, 8, V))
    for r in range(N):
        for g in range(8):
            h = int(rng.integers(3, 10)); chief = rng.permutation(V)[:h]; w = np.add.accumulate(np.exp2(-(0.1 + rng.random()) * np.arange(h)))
            j = np.minimum(np.searchsorted(w, rng.random(V) * w[-1], side="right"), h - 1)
            c[r, g] = np.where(rng.random(V) < lo + (hi - lo) * rng.random(), chief[j], c[r, g])
    return c
def hubs(rng, og, n):
    z = rng.permutation(V)[:RO * n]; vv = np.concatenate([D * rng.permutation(L)[:16 * n] + t for t in range(RO)]).reshape(RO * n, 16)
    og[rng.integers(0, 16, vv.shape), vv] = z[:, None]; og[:, z] = vv.T
    return z
def pack(o, x, c):
    return {"hol": np.ascontiguousarray(o.reshape(N, 128, V)).astype(np.int32), "sha": np.ascontiguousarray(x.reshape(N, 128, V)).astype(np.float32).astype(BF), "ctl": c.astype(np.int32)}
def setup_inputs(rng):
    o = meet(rng, 8, rng.integers(0, V, (N, 8, 8, V))); c = court(rng, 0.85, 0.95); x = rng.integers(0, 16, (N, 8, 16, V))
    for r in range(N):
        for g in range(8): hubs(rng, o[r, g], 2)
    return pack(o, x, c)
def setup_inputs_spread(rng):
    e = rng.integers(1, 7, (N, 8, 1, 1)); o = meet(rng, 8, np.minimum((V * rng.random((N, 8, 8, V)) ** e).astype(np.int64), V - 1))
    c = court(rng, 0.5, 1.0); q = np.minimum((V * rng.random((N, 8, V)) ** rng.integers(1, 9, (N, 8, 1))).astype(np.int64), V - 1)
    c = np.where(rng.random((N, 8, V)) < 0.15, q, c)
    x = np.minimum((rng.random((N, 8, 16, V)) * rng.choice(np.array([1, 2, 3, 6, 11, 16]), (N, 8, 1, V))).astype(np.int64), 15)
    return pack(o, x, c)
def setup_inputs_ends(rng):
    top = V - 1; p = rng.choice(np.array([0.15, 0.5, 0.85]), (N, 8, 1, V)); odd = np.arange(16) % 2
    o = meet(rng, 6, np.where(rng.random((N, 8, 10, V)) < p, top, 0)); c = top * rng.integers(0, 2, (N, 8, V)); kind = rng.random((N, 8, 1, V))
    x = 15 * np.where(kind < 0.45, 1, np.where(kind < 0.55, 0, rng.integers(0, 2, (N, 8, 16, V))))
    for r in range(N):
        for g in range(8):
            og, xg, cg = o[r, g], x[r, g], c[r, g]
            if g % 4 == 1: cg[0] = top; cg[top] = 0
            elif g % 4 != 3 or g == 7:
                cg[0] = 0; cg[top] = top; xg[:, 0] = 15; xg[:, top] = 15; og[:, 0] = top * odd
                for t in range(RO):
                    v = D * (L - 1) + t; og[:, v] = top; xg[:, v] = 15
                    v = D * (L - 2) + t; og[:, v] = top * odd; xg[:, v] = 15
                    v = D + t; og[:, v] = top * (1 - odd); xg[:, v] = 15
                    xg[:, 2 * D + t] = 0
                    v = D * (L - 3) + t; z = D * (L - 1 - 2 * t) + D - 2; og[:, v] = top; xg[:, v] = 15
                    for k, a in ((14, z), (15, z - D)): og[k, v] = a; og[15, a] = v; xg[:, a] = 0; cg[a] = 0
    return pack(o, x, c)
def setup_inputs_corners(rng):
    o = meet(rng, 8, rng.integers(0, V, (N, 8, 8, V))); c = court(rng, 0.8, 1.0); x = rng.integers(0, 16, (N, 8, 16, V)); own = np.arange(V)
    kind = rng.integers(0, 8, (N, 8, 1, V)); x = np.where(kind == 0, 0, np.where(kind == 1, 15, x))
    for r in range(N):
        mo, ho = rng.permutation(8), rng.permutation(8)
        for g in range(8):
            og = o[r, g]; m, h = int(mo[g]), int(ho[g])
            if m == 0: c[r, g] = own
            elif m == 1: c[r, g] = 0
            elif m == 2: c[r, g] = V - 1
            elif m == 3: c[r, g] = (own + 1) % V
            elif m == 4: c[r, g] = V - 1 - own
            elif m == 5: c[r, g] = np.choose(rng.integers(0, 3, V), [np.zeros_like(own), own, np.full_like(own, V - 1)])
            if h in (0, 4): og[rng.integers(0, 16, V), own] = own
            elif h == 1: one = rng.random(V) < 0.3; og[:, one] = og[:1, one]
            elif h == 2: og[:] = np.choose(rng.integers(0, 3, (16, V)), [np.zeros((16, V), np.int64), np.broadcast_to(own, (16, V)), np.full((16, V), V - 1)])
            elif h == 3: og[3] = (own + 1) % V; og[12] = (own - 1) % V
    return pack(o, x, c)
def setup_inputs_ties(rng):
    o = meet(rng, 8, rng.integers(0, V, (N, 8, 8, V))); x = rng.integers(14, 16, (N, 8, 16, V)); c = np.zeros((N, 8, V), np.int64); idle = np.flatnonzero(np.arange(V) % D >= RO)
    for g in range(8):
        f = rng.permutation(idle)[:3]; f = f[:2 + g % 2]
        for r in range(N):
            c[r, g] = f[rng.integers(0, 2, V)]
            if g % 2: c[r, g] = np.where(rng.random(V) < 0.1, f[2], c[r, g])
            c[r, g, f] = f
            if g % 4 == 1: x[r, g] = 15
            elif g % 4 == 2:
                n = 9 if g == 2 else int(rng.integers(8, 11)); x[r, g] = (rng.permutation(16) < n).astype(np.int64)[:, None] * rng.integers(1, 16, (16, 1))
            elif g % 4 == 3: x[r, g] -= 7
    return pack(o, x, c)
def setup_inputs_rush(rng):
    o = meet(rng, 8, rng.integers(0, V, (N, 8, 8, V))); x = rng.integers(6, 16, (N, 8, 16, V)); low = rng.integers(0, 4, (N, 8, 16, V)); c = np.zeros((N, 8, V), np.int64)
    act, idle = np.flatnonzero(np.arange(V) % D < RO), np.flatnonzero(np.arange(V) % D >= RO)
    for g in range(8):
        f = rng.permutation(idle)[:2]; tp = {5: 0, 7: RO - 1}.get(g, -1)
        if tp >= 0: f[0] = D * int(rng.integers(0, L)) + tp
        for r in range(N):
            og = o[r, g]; k = rng.integers(0, 16, V); c[r, g] = np.where(rng.random(V) < 0.8, f[0], f[1]); z = act
            if g % 4 == 0: z = hubs(rng, og, L // 16)
            elif g % 4 == 1:
                for t in range(RO):
                    q = D * rng.permutation(L) + t; a, b = q[0::2], q[1::2]; og[k[a], a] = b; og[k[b], b] = a
            elif g % 4 == 2:
                og[k[act], act] = act; h = act[rng.random(len(act)) < 0.5]; og[(k[h] + 5) % 16, h] = h
            else:
                n = min(len(act), len(idle)); a, z = rng.permutation(act)[:n], rng.permutation(idle)[:n]
                for j in range(5): og[(k[a] + j) % 16, a] = z; og[(k[z] + j) % 16, z] = a
            c[r, g, z] = f[1]; x[r, g][:, z] = low[r, g][:, z]
            c[r, g, f] = f; x[r, g][:, f[0]] = 15
            if tp >= 0:
                h, y = [int(e) for e in rng.permutation(idle[idle != f[1]])[:2]]; i1, i2 = [int(e) for e in rng.permutation(16)[:2]]
                v = D * ((int(f[0]) // D + 1 + int(rng.integers(0, L - 1))) % L) + tp
                og[:, v] = h; og[i1, v] = f[0]; og[i2, v] = y; og[int(rng.integers(0, 16)), y] = v
                og[:, f[0]] = h; og[int(rng.integers(0, 16)), f[0]] = v
                c[r, g, h] = f[0]; c[r, g, v] = f[1]; c[r, g, y] = f[1]; x[r, g][:, h] = 15; x[r, g][:, v] = rng.integers(1, 4, 16)
    return pack(o, x, c)
def check_inputs(d):
    bad = []
    for k, hi in (("hol", V - 1), ("sha", 15), ("ctl", V - 1)):
        v = np.asarray(d[k]).astype(np.float64)
        if not (np.min(v) >= 0 and np.max(v) <= hi): bad.append("range of " + k)
        elif np.any(v != np.floor(v)): bad.append("whole numbers of " + k)
    return bad
def reference(hol, sha, ctl):
    o = hol.astype(np.int64).reshape(N, 8, 16, V); x = sha.astype(np.float32).astype(np.int64).reshape(N, 8, 16, V); c = ctl.astype(np.int64)
    last = np.zeros(N, np.int64)
    for t in range(RO):
        d = 1 + t % (N - 1); vs = D * np.arange(L) + t
        no, nc, wins = [], [], []
        for r in range(N):
            a = o[r][:, :, vs]; af = a.reshape(8, 16 * L); cf = af
            for h in range(HOP): cf = np.take_along_axis(c[(r + h * d) % N], cf, 1)
            ck = cf.reshape(8, 16, L)
            xk = np.take_along_axis(x[r], af[:, None, :], 2).reshape(8, 16, 16, L); xv = x[r][:, :, vs]
            m = np.add.reduce(np.minimum(xk, xv[:, :, None, :]), axis=1)
            pool = np.add.reduce(np.where(ck[:, :, None, :] == ck[:, None, :, :], m[:, None, :, :], 0), axis=2)
            kb = np.argmax(pool, axis=1)
            b = np.take_along_axis(ck, kb[:, None, :], 1)[:, 0]
            mine = ck == b[:, None, :]
            part = np.add.reduce(np.where(mine[:, None, :, :], xk, 0), axis=2); full = np.add.reduce(xk, axis=2)
            win = np.add.reduce((2 * part > full).astype(np.int64), axis=1) >= 9 + (last[r] & 1)
            ok = np.take_along_axis(o[r], af[:, None, :], 2).reshape(8, 16, 16, L)
            stake = np.any(ok == vs, axis=1)
            xb = np.take_along_axis(x[r], b[:, None, :], 2)
            far = np.where(stake & ~mine, np.add.reduce(np.abs(xk - xb[:, :, None, :]), axis=1), -1)
            ks = np.argmax(far, axis=1); sells = win & (np.max(far, axis=1) >= 0)
            goal = np.take_along_axis(a, ks[:, None, :], 1)[:, 0]; cs = np.take_along_axis(ck, ks[:, None, :], 1)[:, 0]
            on = o[r] + 0; cn = c[r] + 0
            for g in range(8):
                ln = np.flatnonzero(sells[g]); tg, first = np.unique(goal[g, ln], return_index=True); w = ln[first]
                col = o[r, g][:, tg]; on[g][:, tg] = np.where(col == vs[w], cs[g, w], col)
                on[g, ks[g, ln], vs[ln]] = b[g, ln]
            cn[:, vs] = np.where(win, b, vs)
            no.append(on); nc.append(cn); wins.append(np.add.reduce(win.astype(np.int64).reshape(-1)))
        o = np.stack(no); c = np.stack(nc); last = np.array(wins, np.int64)
    return {"yo": o.reshape(N, 128, V).astype(np.float32), "yc": c.astype(np.float32)}

@@ -1,0 +1,616 @@
+from concourse.bass import DstId, RemoteDMATransfer
+from concourse.mybir import dt, AluOpType, AxisListType, ActivationFunctionType
+
+V_, RO, NR = 3072, 4, 4
+PAD = 256
+OP = AluOpType
+COPY = ActivationFunctionType.Copy
+IDENT = ActivationFunctionType.Identity
+
+
+def _decl():
+    s = {}
+
+    def sb(name, shape, dtype):
+        s[name] = ("sbuf", shape, dtype)
+    f, b, i, u = "float32", "bfloat16", "int32", "uint16"
+    sb("O", [128, V_ + PAD], f); sb("OI", [128, V_], i); sb("XX", [128, 2 * V_], b); sb("CC", [128, V_], b)
+    for d in (1, 2, 3): sb("WC%d" % d, [128, V_], b)
+    sb("CI", [128, 192], i); sb("CF", [128, 192], f); sb("HL0", [128, 384], b)
+    sb("TI", [128, 192], i); sb("TF", [128, 192], f); sb("CLf", [128, 192], f); sb("CLk", [128, 192], f); sb("CLu", [128, 192], u)
+    for r in range(NR): sb("L0_%d" % r, [128, 384], b)
+    sb("LU", [128, 12, 2, 8, 2], b); sb("SND", [128, 3, 2, 8, 2], b)
+    for t in range(2): sb("VT%d" % t, [128, 4096], f)
+    sb("VR", [128, 4, 256], f); sb("PM", [128, 4, 128], f); sb("KP", [128, 4, 96], f)
+    sb("VC", [128, 16], f)
+    for n in ("XK", "CG", "ST", "MN", "XM"): sb(n, [128, 2, 2048], b)
+    sb("MX", [128, 2, 4, 8, 64], b); sb("E", [128, 2, 8, 8, 16], b); sb("PR", [128, 2, 15, 8, 16], b)
+    for n in ("cS", "RM", "BR", "oh", "w", "brep", "BD", "cKv", "q2", "pz", "pc", "nC0", "nC", "BDc", "OC", "OE"): sb(n, [128, 2, 128], f)
+    for n in ("nm", "XB", "SX", "wp", "win", "el", "oh2_"): sb(n, [128, 2, 128], b)
+    sb("mS", [128, 2, 8, 24], b); sb("LM", [128, 256], u); sb("BZ", [128, 2, 128], f); sb("kS", [128, 2, 128], f); sb("HLz", [128, 2, 8, 16], b)
+    sb("LA", [128, 256], u); sb("LB", [128, 16], u); sb("ZL", [128, 16], u); sb("FZ", [128, 16], u); sb("ZU", [128, 256], u)
+    for n in ("aD", "ZQ", "ZS", "NC", "nlq", "fz", "FS", "XO", "QM"): sb(n, [128, 256], f)
+    sb("fl", [128, 16], f); sb("DL", [128, 16], f); sb("DE", [128, 4096], b)
+    for n in ("Ib", "Im", "Im16", "I256", "I16", "I3072", "BOb", "BN", "L4", "LW", "ONE", "K1", "K2"): sb(n, [128, 128], b)
+    for n in ("If", "BOf", "NF"): sb(n, [128, 128], f)
+    for n in ("DC", "C128", "oK"): sb(n, [128, 256], b)
+    for n in ("VH", "VL"): sb(n, [128, 4, 256], b)
+    for n in ("S1", "S16", "S32", "Sm16", "SHL"): sb(n, [128, 8], b)
+    sb("U8", [128, 8], f); sb("U4", [128, 96], f)
+    sb("ci", [128, 256], f); sb("cg", [128, 256], f); sb("cq", [128, 256], f)
+    sb("pi", [128, 1], i); sb("ti", [128, 16], i); sb("tf", [128, 16], f); sb("wq", [128, 16], f)
+    sb("zr", [128, 4], f); sb("zi", [128, 4], i); sb("Zc", [128, 1], f)
+    for n in ("pA0", "pA1", "pB0", "pB1", "pC0", "pC1", "pD"): s[n] = ("psum", [128, 8, 64], f)
+    s["pE"] = ("psum", [128, 512], f)
+    return s
+
+
+SCRATCH = _decl()
+SEMAPHORES = ["cV", "cS", "cP", "cG", "loc"] + ["d%d" % k for k in range(52)] + ["ar%d_%d" % (t, r) for t in range(4) for r in range(NR)]
+PS = ("pA0", "pA1", "pB0", "pB1", "pC0", "pC1", "pD", "pE")
+D_OF = [1 + t % 3 for t in range(RO)]
+CYC = 0.83e-3
+WAKE = 0.09
+GCY = 1.5
+ASG = {"XK1": "S", "CG0": "S", "CG1": "S", "XM0": "S", "XM1": "S", "compose0": "S", "compose1": "S", "compose2": "S", "compose3": "S"}
+NPC, NPM, NPS = 2, 2, 8
+WT = {'ST': -10, 'SX': -5, 'zr': -10, 'key': 10, 'XB1': 10, 'RW': 20, 'BDc': -10, 'LM': -10, 'LA': 2, 'compose1': 10, 'RM': 2, 'pc': -10, 'pz': -5, 'ld sha': 10, 'el': -20, 'q2': 20, 'cL': 20, 'ZQ': -20, 'ext': -5, 'win': -2, 'oh2T': 10, 'CLu': -10, 'mS': 10, 'HLz': 2, 'oh2': 10, 'VT': -10, 'XM0': -2, 'csv': -2, 'flat': -2, 'CLk': 5, 'nk': 2, 'ZU': 10, 'Zc': -2, 'LMa': 20, 'CLf': -20, 'OC': 10, 'ld ctl': 5, 'nlq': 20, 'ld list': 20, 'send': 20, 'nC0': 10, 'hb': 2, 'bmv': 2, 'lo': 2, 'ld hol': 10, 'a1': 10, 'CF': -5, 'sendb': 5, 'zm': 20, 'fl': -2, 'OE': 20, 'DUP1': -5, 'FZ': -5, 'nC': 2, 'RM2': -20, 'sp': 10, 'scatter': 5, 'SXc': -10, 'WCu': -10, 'wp': 10, 'cKv': -2, 'XO': -2, 'compose3': 10, 'st yo': 5, 'hi': 5, 'O': 5}
+MXS = ()
+PRS = ()
+
+
+def new_graph():
+    return {"ops": [], "wr": {}, "rd": {}, "bw": {}, "br": {}}
+
+
+def add(G, opts, fn, r=(), w=(), pr=(), pw=(), key=None, cnt=1, name=""):
+    n = len(G["ops"])
+    deps = {}
+
+    def dep(j, raw):
+        if j != n: deps[j] = deps.get(j, False) or raw
+    for (bn, lo, hi) in r:
+        for (a, b, j) in G["wr"].get(bn, []):
+            if a < hi and lo < b: dep(j, True)
+        G["rd"].setdefault(bn, []).append((lo, hi, n))
+    for (bn, lo, hi) in w:
+        for (a, b, j) in G["wr"].get(bn, []):
+            if a < hi and lo < b: dep(j, False)
+        for (a, b, j) in G["rd"].get(bn, []):
+            if a < hi and lo < b: dep(j, False)
+        G["wr"][bn] = [x for x in G["wr"].get(bn, []) if not (lo <= x[0] and x[1] <= hi)] + [(lo, hi, n)]
+        G["rd"][bn] = [x for x in G["rd"].get(bn, []) if not (lo <= x[0] and x[1] <= hi)]
+    engs = tuple(sorted(opts))
+    for bn in pr:
+        if bn in G["bw"]: dep(G["bw"][bn], True)
+        for j in G["br"].get(bn, []):
+            if G["ops"][j]["engs"] != engs or len(engs) > 1: dep(j, False)
+        G["br"].setdefault(bn, []).append(n)
+    for bn in pw:
+        if bn in G["bw"]: dep(G["bw"][bn], False)
+        for j in G["br"].get(bn, []): dep(j, False)
+        G["bw"][bn] = n; G["br"][bn] = []
+    G["ops"].append({"opts": opts, "engs": engs, "fn": fn, "deps": deps, "key": key, "cnt": cnt, "name": name})
+    return n
+
+
+def schedule(G, wake=WAKE, quant=0.08):
+    ops = G["ops"]; n = len(ops)
+    succ = [[] for _ in range(n)]; ind = [len(o["deps"]) for o in ops]
+    for i, o in enumerate(ops):
+        for j in o["deps"]: succ[j].append(i)
+    prio = [0.0] * n
+    for i in range(n - 1, -1, -1):
+        d = min(x[1] for x in ops[i]["opts"].values())
+        prio[i] = d + max([prio[s] + 0.5 * wake for s in succ[i]] or [0.0])
+    prio = [p + WT.get(o["name"], 0.0) for p, o in zip(prio, ops)]
+    free = {}; fin = [0.0] * n; eng = [None] * n; rdy = {}
+    order = []; t_ready = [0.0] * n
+    for i in range(n):
+        if ind[i] == 0: rdy[i] = True
+    while rdy:
+        best = None
+        for i in rdy:
+            for e, c in ops[i]["opts"].items():
+                st = free.get(e, 0.0)
+                for j, raw in ops[i]["deps"].items():
+                    x = fin[j] + (wake if eng[j] != e else (0.06 if raw else -1.0))
+                    if x > st: st = x
+                k = (int(st / quant), -prio[i], st)
+                if best is None or k < best[0]: best = (k, i, e, st)
+        _, i, e, st = best
+        del rdy[i]
+        c = ops[i]["opts"][e]
+        free[e] = st + c[0]; fin[i] = st + c[1]; eng[i] = e; t_ready[i] = st
+        order.append(i)
+        for s in succ[i]:
+            ind[s] -= 1
+            if ind[s] == 0: rdy[s] = True
+    return order, eng, fin, t_ready
+
+
+def vc(n, two=1.0): return max(64.0, n * two) * CYC * 1.2 + 0.01
+def sc(n): return max(64.0, n) * CYC * 1.2 + 0.03
+def pc_(n, f32=False): return max(64.0, n) * CYC * 1.1 * (4.0 if f32 else 1.0) + 0.01
+
+
+def build(core, T, topo, rank):
+    G = new_graph()
+    W = lambda n: (n, 0, 1 << 20)
+    nd = [0]
+
+    def vop(fn, n, r=(), w=(), pr=(), pw=(), two=1.0, name=""):
+        c = vc(n, two)
+        return add(G, {"V": (c, c)}, lambda Q, e: fn(Q["V"]), r, w, pr, pw, name=name)
+
+    def tt(o, a, b, op, n, r=(), w=(), pr=(), name="", pw=(), two=None):
+        vop(lambda v: v.tensor_tensor(o, a, b, op), n, r, w, pr, pw, two=two or (1.0 if pr else 2.0), name=name)
+
+    def ts(o, a, s1, op0, n, r=(), w=(), pr=(), s2=None, op1=None, two=1.0, name=""):
+        if op1 is None: vop(lambda v: v.tensor_scalar(o, a, s1, None, op0), n, r, w, pr, two=two, name=name)
+        else: vop(lambda v: v.tensor_scalar(o, a, s1, s2, op0, op1), n, r, w, pr, two=two, name=name)
+
+    def cpv(o, a, n, r=(), w=(), pr=(), name=""):
+        vop(lambda v: v.tensor_copy(o, a), n, r, w, pr, name=name)
+
+    def flex(o, a, n, r=(), w=(), pr=(), name="", cyc=1.0, only=None):
+        opts = {"V": (vc(n, cyc), vc(n, cyc)), "S": (sc(n * cyc), sc(n * cyc))}
+        only = only or ASG.get(name)
+        if only: opts = {only: opts[only]}
+        return add(G, opts, lambda Q, e: Q["V"].tensor_copy(o, a) if e == "V" else Q["S"].activation(o, a, COPY), r, w, pr, name=name)
+
+    def act(o, a, n, func=COPY, bias=0.0, scale=1.0, r=(), w=(), pr=(), name="", pw=()):
+        return add(G, {"S": (sc(n), sc(n))}, lambda Q, e: Q["S"].activation(o, a, func, bias=bias, scale=scale), r, w, pr, pw, name=name)
+
+    def mm(o, l, rh, start, stop, bank, n, r=(), f32=False, name=""):
+        c = pc_(n, f32)
+        return add(G, {"P": (c, c)}, lambda Q, e: Q["P"].matmul(o, l, rh, start, stop), r, (), (), (bank,), name=name)
+
+    def gop(fn, n, r=(), w=(), name=""):
+        c = 0.14 + 2 * n * CYC * 1.2
+        return add(G, {"G": (c, c)}, lambda Q, e: fn(Q["G"]), r, w, name=name)
+
+    def dma(o, a, kb, r=(), w=(), q="Y", name=""):
+        k = nd[0]; nd[0] += 1
+        return add(G, {q: (0.1, 2.0 + kb / 200.0)}, lambda Q, e: (Q["Y"] if e == "Y" else Q["S"]).dma_start(o, a).then_inc(T.sem["d%d" % k], 16), r, w, key="d%d" % k, cnt=16, name=name)
+
+    def send(dsts, src_ap, land, sem, r, kb, name):
+        m = 255
+        ne = len(topo.engines(core, dsts[0]))
+        for x in dsts: assert topo.may_write(core, x) and topo.mask(core, x) == topo.mask(core, dsts[0])
+
+        def fn(Q, e):
+            if len(dsts) == 1:
+                rid, pid = topo.addr(dsts[0])[:2]
+                Q["G"].remote_dma(out_ap=land, in_ap=src_ap, remote_sem=T.sem[sem], local_sem=T.sem.loc, pid=pid, routing_id=rid, dma_engine_mask=topo.mask(core, dsts[0]))
+            else:
+                ids = [DstId(rid=topo.addr(x)[0], pnc=topo.addr(x)[1]) for x in dsts]
+                Q["G"].remote_dma_fused([RemoteDMATransfer(dst_ids=ids, dma_engine_mask=topo.mask(core, dsts[0]), remote_sem=T.sem[sem], srcs=[src_ap], dsts=[land for x in dsts])], local_sem=T.sem.loc)
+        return add(G, {"G": (1.0, 1.0)}, fn, r, (), key="loc", cnt=ne, name=name)
+
+    def arrive(src_rank, t, after, kb):
+        nm = "L%d_%d" % (t, src_rank)
+        i = add(G, {"N%d_%d" % (t, src_rank): (0.0, 2.5 + kb / 40.0)}, None, (), (W(nm),), key="ar%d_%d" % (t, src_rank), cnt=len(topo.engines(T.cores[src_rank], core)), name="arrive")
+        G["ops"][i]["deps"][after] = True
+
+    H = (0, 1)
+
+    def ext(X, bank):
+        opts = {"V": (vc(64), vc(64)), "S": (sc(64), sc(64))}
+        if "ext" in ASG: opts = {ASG["ext"]: opts[ASG["ext"]]}
+        add(G, opts, lambda Q, e: Q["V"].tensor_copy(X[:, :, 16:24], X[:, :, 0:8]) if e == "V" else Q["S"].activation(X[:, :, 16:24], X[:, :, 0:8], COPY), (), (), (bank,), (bank,), name="ext")
+
+    def P(n, h): return T["p" + n + str(h)]
+    def B(n, h): return T[n][:, h]
+    def LU(t, r): return T.LU[:, 4 * (t - 1) + r]
+
+    dma(T.CI[:], T.ctl[:], 98, w=[W("CI")], name="ld ctl")
+    for c in range(4):
+        dma(T.OI[:, 768 * c:768 * c + 768], T.hol[:, 768 * c:768 * c + 768], 393, w=[("OI", 768 * c, 768 * c + 768)], q="Y", name="ld hol")
+    for e in range(2):
+        for b in range(6):
+            dma(T.TI[:, 32 * b + 16 * e:32 * b + 16 * e + 16], T.ctl[e::2, 512 * b:512 * b + 512], 8, w=[("TI", 32 * b + 16 * e, 32 * b + 16 * e + 16)], q="S", name="ld list")
+    for c in range(2):
+        dma(T.XX[:, 1536 * c:1536 * c + 1536], T.sha[:, 1536 * c:1536 * c + 1536], 393, w=[("XX", 1536 * c, 1536 * c + 1536)], q="S", name="ld sha")
+    cpv(T.CF[:], T.CI[:], 192, r=[W("CI")], w=[W("CF")], name="CF")
+    cpv(T.HL0[:, 0:192], T.CF[:], 192, r=[W("CF")], w=[("HL0", 0, 192)])
+    tt(T.HL0[:, 192:384], T.CF[:], T.HL0[:, 0:192], OP.subtract, 192, r=[W("CF"), ("HL0", 0, 192)], w=[("HL0", 192, 384)])
+    me = T.cores[rank]
+    first = T.cores[(rank - D_OF[0]) % NR]
+    rest = [T.cores[(rank - d) % NR] for d in (1, 2, 3) if (rank - d) % NR != (rank - D_OF[0]) % NR]
+    lands = "L0_%d" % rank
+    s1 = send([first], T.HL0[:], T[lands][:], "ar0_%d" % rank, [W("HL0")], 98, "send0")
+    s2 = send(rest, T.HL0[:], T[lands][:], "ar0_%d" % rank, [W("HL0")], 196, "send0b")
+    gop(lambda g: g.iota(T.pi[:], [[1, 1]], 0, 1), 1, w=[W("pi")])
+    gop(lambda g: g.iota(T.ci[:], [[1, 256]], 0, 0, allow_small_or_imprecise_dtypes=True), 256, w=[W("ci")])
+    gop(lambda g: g.iota(T.cg[:], [[1, 16], [0, 16]], 0, 0, allow_small_or_imprecise_dtypes=True), 256, w=[W("cg")])
+    gop(lambda g: g.iota(T.cq[:], [[0, 16], [1, 16]], 0, 0, allow_small_or_imprecise_dtypes=True), 256, w=[W("cq")])
+    gop(lambda g: g.iota(T.DL[:], [[16, 16]], V_, 0, allow_small_or_imprecise_dtypes=True), 16, w=[W("DL")])
+    for t in range(RO):
+        gop(lambda g, t=t: g.iota(T.VR[:, t], [[12, 256]], t, 0, allow_small_or_imprecise_dtypes=True), 256, w=[W("VR%d" % t)])
+
+    def vt(t):
+        for c in range(4):
+            i = gop(lambda g, c=c: g.iota(T["VT%d" % (t % 2)][:, 1024 * c:1024 * c + 1024], [[12, 64], [0, 16]], t + 768 * c, 0, allow_small_or_imprecise_dtypes=True), 1024, w=[("VT%d" % (t % 2), 1024 * c, 1024 * c + 1024)], name="VT")
+            G["ops"][i]["deps"][s2] = False
+    vt(0)
+    vt(1)
+    for t in range(RO):
+        gop(lambda g, t=t: g.iota(T.VH[:, t], [[48, 64], [0, 4]], 0, 0, allow_small_or_imprecise_dtypes=True), 256, w=[W("VH%d" % t)])
+        gop(lambda g, t=t: g.iota(T.VL[:, t], [[0, 64], [12, 4]], t, 0, allow_small_or_imprecise_dtypes=True), 256, w=[W("VL%d" % t)])
+    vop(lambda v: v.memset(T.WC1[:], 0.0), V_, w=[W("WC1")], two=0.5)
+    for d in (2, 3):
+        i = gop(lambda g, d=d: g.iota(T["WC%d" % d][:], [[0, V_]], 0, 0, allow_small_or_imprecise_dtypes=True), V_, w=[W("WC%d" % d)])
+        G["ops"][i]["deps"][s2] = False
+    for d in (1, 2, 3):
+        s = (rank + d) % NR
+        arrive(s, 0, s1 if d == D_OF[0] else s2, 98 if d == D_OF[0] else 196)
+        for x in (0, 1):
+            dma(T["WC%d" % d][x:128:16, :], T["L0_%d" % s][:, 192 * x:192 * x + 192], 49, r=[W("L0_%d" % s)], w=[W("WC%d" % d)] if x == 0 else [("WC%d" % d, 0, 1 << 19)], name="flat")
+            if x == 0: G["wr"]["WC%d" % d] = [y for y in G["wr"]["WC%d" % d]]
+    def sh(o, k): ts(T.ti[:, o:o + 1], T.pi[:], k, OP.arith_shift_right, 1, r=[W("pi")], w=[("ti", o, o + 1)])
+    def an(o, src, k, rr): ts(T.ti[:, o:o + 1], src, k, OP.bitwise_and, 1, r=rr, w=[("ti", o, o + 1)])
+    sh(1, 4); an(2, T.pi[:], 15, [W("pi")])
+    cpv(T.ti[:, 0:1], T.pi[:], 1, r=[W("pi")], w=[("ti", 0, 1)])
+    an(8, T.pi[:], 3, [W("pi")])
+    ts(T.ti[:, 9:10], T.ti[:, 8:9], 12, OP.mult, 1, r=[("ti", 8, 9)], w=[("ti", 9, 10)])
+    for t in range(RO):
+        ts(T.ti[:, 10 + t:11 + t], T.ti[:, 9:10], t, OP.add, 1, r=[("ti", 9, 10)], w=[("ti", 10 + t, 11 + t)])
+        an(3 + t, T.ti[:, 10 + t:11 + t], 15, [("ti", 10 + t, 11 + t)])
+    ts(T.ti[:, 14:15], T.pi[:], 12, OP.mult, 1, r=[W("pi")], w=[("ti", 14, 15)])
+    ts(T.ti[:, 7:8], T.ti[:, 14:15], 4, OP.arith_shift_right, 1, r=[("ti", 14, 15)], w=[("ti", 7, 8)])
+    ts(T.ti[:, 15:16], T.ti[:, 1:2], 8, OP.add, 1, r=[("ti", 1, 2)], w=[("ti", 15, 16)])
+    cpv(T.tf[:], T.ti[:], 16, r=[W("ti")], w=[W("tf")])
+    F = lambda k: T.tf[:, k:k + 1]
+    tfr = [W("tf")]
+    for h in H:
+        for t in range(RO):
+            k = 2 * t + h
+            ts(T.VC[:, k:k + 1], F(0), 12.0, OP.mult, 1, r=tfr, w=[("VC", k, k + 1)], s2=float(12 * 128 * h + t), op1=OP.add)
+            ts(T.VC[:, 8 + k:9 + k], F(0), -12.0, OP.mult, 1, r=tfr, w=[("VC", 8 + k, 9 + k)], s2=float(-12 * 128 * h - t), op1=OP.add)
+    ts(T.DL[:], T.DL[:], F(2), OP.add, 16, r=tfr + [W("DL")], w=[W("DL")])
+    ci = T.ci[:, 0:128]; rc = tfr + [W("ci")]; rq = tfr + [W("cq")]; rg = tfr + [W("cg")]
+    ts(T.If[:], ci, F(0), OP.is_equal, 128, r=rc, w=[W("If")])
+    ts(T.BOf[:], T.cg[:, 0:128], F(1), OP.is_equal, 128, r=rg, w=[W("BOf")])
+    for src, nmx, s in (("If", "Ib", 1.0), ("If", "Im", -1.0), ("If", "Im16", -16.0), ("If", "I16", 16.0), ("If", "I3072", 3072.0), ("BOf", "BOb", 1.0), ("BOf", "L4", 4.0), ("BOf", "BN", -128.0)):
+        act(T[nmx][:], T[src][:], 128, COPY, scale=s, r=[W(src)], w=[W(nmx)])
+    ts(T.QM[:], T.cq[:], F(2), OP.is_equal, 256, r=rq, w=[W("QM")])
+    ts(T.NF[:], T.cq[:, 0:128], 0.0, OP.not_equal, 128, r=[W("cq")], w=[W("NF")])
+    for nmx, s in (("S1", 1.0), ("S16", 16.0), ("S32", 32.0)):
+        ts(T[nmx][:], T.ci[:, 0:8], F(1), OP.is_equal, 8, r=rc, w=[W(nmx)], s2=s, op1=OP.mult)
+    ts(T.wq[:, 0:1], F(2), 1.0, OP.is_le, 1, r=tfr, w=[("wq", 0, 1)])
+    ts(T.SHL[:], T.ci[:, 0:8], F(1), OP.is_equal, 8, r=rc + [("wq", 0, 1)], w=[W("SHL")], s2=T.wq[:, 0:1], op1=OP.mult)
+    ts(T.U8[:], T.ci[:, 0:8], F(1), OP.is_equal, 8, r=rc, w=[W("U8")])
+    ts(T.U4[:], T.ci[:, 0:96], F(7), OP.is_equal, 96, r=rc, w=[W("U4")])
+    for t in range(RO): ts(T.PM[:, t], T.cq[:, 0:128], F(3 + t), OP.is_equal, 128, r=rq, w=[W("PM%d" % t)])
+    ts(T.K1[:], T.cq[:, 0:128], -1.0, OP.mult, 128, r=[W("cq")], w=[W("K1")], s2=15.0, op1=OP.add)
+    ts(T.K2[:], T.cq[:, 0:128], -1.0, OP.mult, 128, r=[W("cq")], w=[W("K2")], s2=31.0, op1=OP.add)
+    vop(lambda v: v.memset(T.ONE[:], 1.0), 128, w=[W("ONE")])
+    for q in range(16): vop(lambda v, q=q: v.memset(T.fz[:, q::16], 2.0 ** -q), 16, w=[W("fz")])
+    tt(T.FS[:], T.fz[:], T.QM[:], OP.mult, 256, r=[W("fz"), W("QM")], w=[W("FS")])
+    vop(lambda v: v.tensor_reduce(T.wq[:, 1:2], T.FS[:, 0:16], AxisListType.X, OP.add), 16, r=[W("FS")], w=[("wq", 1, 2)])
+    ts(T.LW[:], T.BOf[:], T.wq[:, 1:2], OP.mult, 128, r=[W("BOf"), ("wq", 1, 2)], w=[W("LW")])
+    ts(T.nlq[:], T.QM[:], 1024.0, OP.mult, 256, r=[W("QM")], w=[W("nlq")], s2=-1024.0, op1=OP.add)
+    act(T.C128[:], T.QM[:], 256, COPY, scale=128.0, r=[W("QM")], w=[W("C128")])
+    ts(T.DL[:], T.DL[:], 1.0, OP.add, 16, r=[W("DL")], w=[W("DL")])
+    ts(T.ZQ[:], T.FS[:], -2.0, OP.mult, 256, r=[W("FS")], w=[W("ZQ")])
+    tt(T.DC[:], T.nlq[:], T.ZQ[:], OP.add, 256, r=[W("nlq"), W("ZQ")], w=[W("DC")])
+    vop(lambda v: v.memset(T.O[:, V_:V_ + PAD], 0.0), PAD, w=[("O", V_, V_ + PAD)])
+    for h in H:
+        vop(lambda v, h=h: v.memset(B("BZ", h)[:], 0.0), 128, w=[W("BZ%d" % h)])
+        vop(lambda v, h=h: v.memset(B("HLz", h)[:], 0.0), 128, w=[W("HLz%d" % h)])
+    vop(lambda v: v.memset(T.Zc[:], 9.0), 1, w=[W("Zc")])
+    for t in range(RO):
+        mm(T.pE[:, 0:96], T.PM[:, t], T.U4[:], True, True, "pE", 96, r=[W("PM%d" % t), W("U4")], f32=True)
+        ts(T.KP[:, t], T.pE[:, 0:96], -1.0, OP.mult, 96, w=[W("KP%d" % t)], pr=["pE"], s2=1.0, op1=OP.add)
+    cpv(T.TF[:], T.TI[:], 192, r=[W("TI")], w=[W("TF")])
+    vop(lambda v: v.transpose(T.CLf[:], T.TF[:]), 192, r=[W("TF")], w=[W("CLf")])
+    cpv(T.CLu[:], T.CLf[:], 192, r=[W("CLf")], w=[W("CLu")])
+    for c in range(4):
+        cpv(T.O[:, 768 * c:768 * c + 768], T.OI[:, 768 * c:768 * c + 768], 768, r=[("OI", 768 * c, 768 * c + 768)], w=[("O", 768 * c, 768 * c + 768)], name="O f32")
+    for c in range(2):
+        a, z = 1536 * c, 1536 * c + 1536
+        add(G, {"V": (vc(1536, 0.5), vc(1536, 0.5)), "S": (sc(1536), sc(1536))},
+            lambda Q, e, a=a, z=z: Q["V"].tensor_scalar(T.XX[:, V_ + a:V_ + z], T.XX[:, a:z], -1.0, None, OP.mult) if e == "V" else Q["S"].activation(T.XX[:, V_ + a:V_ + z], T.XX[:, a:z], COPY, scale=-1.0),
+            [("XX", a, z)], [("XX", V_ + a, V_ + z)], name="-X")
+
+    for t in range(RO):
+        d = D_OF[t]; last = t == RO - 1
+        wc = "WC%d" % d
+        VT, VR = T["VT%d" % (t % 2)], T.VR[:, t]
+        XR = [("XX", 0, V_)]
+        hs = lambda h: slice(1536 * h + t, 1536 * h + 1536, 12)
+        oreg = lambda h: ("O", 1536 * h, 1536 * h + 1536)
+        S = lambda h: slice(128 * h, 128 * h + 128)
+        for h in H:
+            src = T.OI if t == 0 else T.O
+            cpv(T.LA[:, S(h)], src[:, hs(h)], 128, r=[("OI" if t == 0 else "O", 1536 * h, 1536 * h + 1536)], w=[("LA", 128 * h, 128 * h + 128)], name="LA")
+        for c in range(4):
+            flex(T.CC[:, 768 * c:768 * c + 768], T[wc][:].indirect(T.CLu[:, 48 * c:48 * c + 48]), 768, r=[W(wc), W("CLu")], w=[("CC", 768 * c, 768 * c + 768)], cyc=GCY, name="compose%d" % c)
+        la = lambda h: ("LA", 128 * h, 128 * h + 128)
+        pieces = lambda n: [(2048 // n * p, 2048 // n * (p + 1), 128 // n * p, 128 // n * (p + 1)) for p in range(n)]
+        for h in H:
+            for a, z, c, e in pieces(NPC): flex(B("XK", h)[:, a:z], T.XX[:, 0:V_].indirect(T.LA[:, 128 * h + c:128 * h + e]), z - a, r=XR + [la(h)], w=[("XK%d" % h, a, z)], cyc=GCY, name="XK%d" % h)
+        for h in H:
+            for a, z, c, e in pieces(NPC): flex(B("CG", h)[:, a:z], T.CC[:].indirect(T.LA[:, 128 * h + c:128 * h + e]), z - a, r=[W("CC"), la(h)], w=[("CG%d" % h, a, z)], cyc=GCY, name="CG%d" % h)
+        for h in H:
+            for a, z, c, e in pieces(NPS):
+                vop(lambda v, h=h, VT=VT, a=a, z=z, c=c, e=e: v.tensor_tensor(B("ST", h)[:, a:z], T.O[:, 0:V_].indirect(T.LA[:, 128 * h + c:128 * h + e]), VT[:, 2048 * h + a:2048 * h + z], OP.is_equal), z - a,
+                    r=[("O", 0, V_), la(h), ("VT%d" % (t % 2), 2048 * h + a, 2048 * h + z)], w=[("ST%d" % h, a, z)], two=GCY, name="ST")
+        if t + 2 < RO: vt(t + 2)
+        for h in H:
+            mm(P("C", h)[:, :, 0:16], T.Ib[:], T.XX[:, hs(h)], True, True, "pC%d" % h, 128, r=XR + [W("Ib")])
+        for h in H:
+            A = P("A", h); bk = "pA%d" % h
+            for k in range(16):
+                mm(A[:, :, k], B("CG", h)[:, k::16], T.SHL[:], True, True, bk, 8, r=[W("CG%d" % h), W("SHL")], name="cL")
+            ext(A, bk)
+            flex(B("cS", h)[:], A[:, :, 0:16], 128, w=[W("cS%d" % h)], pr=[bk], name="cS")
+            for s in range(1, 9):
+                tt(B("E", h)[:, s - 1], B("cS", h)[:], A[:, :, s:s + 16], OP.not_equal if h in PRS else OP.is_equal, 128, r=[W("cS%d" % h)], w=[("E%d" % h, s - 1, s)], pr=[bk], name="E")
+        for h in H:
+            if h in MXS: continue
+            for k in range(16):
+                mm(T.pE[:, 128 * h + k:128 * h + 128:16], B("XK", h)[:, k::16], T.S1[:], True, True, "pE", 8, r=[W("XK%d" % h), W("S1")], name="SX")
+            act(B("SX", h)[:], T.pE[:, S(h)], 128, w=[W("SX%d" % h)], pr=["pE"], name="SXc")
+        for h in H:
+            Bk = P("B", h); bk = "pB%d" % h
+            for k in range(16):
+                tt(B("MN", h)[:, S(k)], B("XK", h)[:, k::16], P("C", h)[:, :, 0:16], OP.min, 128, r=[W("XK%d" % h)], w=[("MN%d" % h, 128 * k, 128 * k + 128)], pr=["pC%d" % h], name="MN")
+            for k in range(16):
+                mm(Bk[:, :, k], B("MN", h)[:, S(k)], T.S1[:], True, True, bk, 8, r=[("MN%d" % h, 128 * k, 128 * k + 128), W("S1")], name="mL")
+            ext(Bk, bk)
+            mS = B("mS", h)
+            nx = 24 if h in PRS else 16
+            flex(mS[:, :, 0:nx], Bk[:, :, 0:nx], 8 * nx, w=[W("mS%d" % h)], pr=[bk], name="mS")
+            PRh, Eh = B("PR", h), B("E", h)
+            for c in range(4 if h in PRS else 0):
+                bn = "pE" if c % 2 else bk
+                n = min(4, 15 - 4 * c)
+                for jj in range(n):
+                    j = 4 * c + jj
+                    s = j + 1 if j < 8 else j - 7
+                    o = T.pE[:, S(jj)] if c % 2 else Bk[:, 2 * jj:2 * jj + 2, :]
+                    mm(o, T.Ib[:], mS[:, :, s:s + 16] if j < 8 else mS[:, :, 0:16], True, False, bn, 128, r=[W("mS%d" % h), W("Ib")], name="PRm")
+                    mm(o, T.I256[:], Eh[:, s - 1], False, True, bn, 128, r=[("E%d" % h, s - 1, s), W("I256")], name="PRm")
+                act(PRh[:, 4 * c:4 * c + n], T.pE[:, 0:128 * n] if c % 2 else Bk[:, 0:2 * n, :], 128 * n, ActivationFunctionType.Relu, w=[("PR%d" % h, 4 * c, 4 * c + n)], pr=[bn], name="PRa")
+            for s in range(1, 9 if h not in PRS else 0):
+                tt(PRh[:, s - 1], Eh[:, s - 1], Bk[:, :, s:s + 16], OP.mult, 128, r=[("E%d" % h, s - 1, s)], w=[("PR%d" % h, s - 1, s)], pr=[bk], name="PR")
+            for s in range(1, 8 if h not in PRS else 0):
+                tt(PRh[:, 7 + s], Eh[:, s - 1], Bk[:, :, 0:16], OP.mult, 128, r=[("E%d" % h, s - 1, s)], w=[("PR%d" % h, 7 + s, 8 + s)], pr=[bk], name="PR")
+            C = P("C", h); ck = "pC%d" % h
+            mm(C[:, :, 16:32], T.Ib[:], T.K1[:], True, False, ck, 128, r=[W("Ib"), W("K1")], name="key")
+            mm(C[:, :, 16:32], T.I16[:], mS[:, :, 0:16], False, False, ck, 128, r=[W("I16"), W("mS%d" % h)], name="key")
+            for s in range(1, 9):
+                mm(C[:, :, 16:32], T.I16[:], PRh[:, s - 1], False, False, ck, 128, r=[("PR%d" % h, s - 1, s)], name="key")
+            for s in range(1, 8):
+                mm(C[:, :, 16 + s:32], T.I16[:], PRh[:, 7 + s, :, 0:16 - s], False, False, ck, 128 - 8 * s, r=[("PR%d" % h, 7 + s, 8 + s)], name="key")
+                mm(C[:, :, 16:16 + s], T.I16[:], PRh[:, 7 + s, :, 16 - s:16], False, s == 7, ck, 8 * s, r=[("PR%d" % h, 7 + s, 8 + s)], name="key")
+
+        def spread(h, src, sreg, fin, freg, floor=None, bank=None):
+            bz = B("BZ", h); zr = [W("BZ%d" % h)]
+            if floor is None: cpv(bz[:, 0::16], src[:, 15::16], 8, r=[sreg], w=zr, name="sp")
+            else: ts(bz[:, 0::16], src[:, 15::16], floor, OP.max, 8, r=[sreg], w=zr, name="sp")
+            vop(lambda v: v.tensor_tensor_scan(fin, T.NF[:], bz[:], 0.0, OP.mult, OP.add), 128, r=zr + [W("NF")], w=[freg] if freg else [], pw=[bank] if bank else [], name="sp")
+
+        for h in H:
+            A, C = P("A", h), P("C", h); ak, ck = "pA%d" % h, "pC%d" % h
+            x = lambda n: W(n + str(h))
+            flex(B("kS", h)[:], C[:, :, 16:32], 128, w=[x("kS")], pr=[ck], name="kS")
+            vop(lambda v, h=h: v.tensor_tensor_scan(B("RM", h)[:], T.NF[:], B("kS", h)[:], 0.0, OP.mult, OP.max), 128, r=[W("NF"), x("kS")], w=[x("RM")], name="RM")
+            spread(h, B("RM", h), x("RM"), B("BR", h), x("BR"))
+            tt(B("oh", h)[:], B("BR", h)[:], C[:, :, 16:32], OP.is_equal, 128, r=[x("BR")], w=[x("oh")], pr=[ck], name="oh")
+            tt(B("w", h)[:], B("oh", h)[:], A[:, :, 0:16], OP.mult, 128, r=[x("oh")], w=[x("w")], pr=[ak], name="w")
+            vop(lambda v, h=h: v.tensor_tensor_scan(B("RM", h)[:], T.NF[:], B("w", h)[:], 0.0, OP.mult, OP.add), 128, r=[W("NF"), x("w")], w=[x("RM")], name="RW")
+            spread(h, B("RM", h), x("RM"), B("brep", h), x("brep"))
+            tt(B("nm", h)[:], B("brep", h)[:], A[:, :, 0:16], OP.not_equal, 128, r=[x("brep")], w=[x("nm")], pr=[ak], name="nm")
+            mm(C[:, :, 48:64], T.If[:], T.O[:, hs(h)], True, False, ck, 128, r=[oreg(h), W("If")], f32=True, name="LMa")
+            mm(C[:, :, 48:64], B("nm", h)[:], T.I3072[:], False, True, ck, 128, r=[x("nm"), W("I3072")], name="LMn")
+            cpv(T.LM[:, S(h)], C[:, :, 48:64], 128, w=[x("LM")], pr=[ck], name="LM")
+            for a, z, c, e in pieces(NPM): flex(B("XM", h)[:, a:z], T.XX[:].indirect(T.LM[:, 128 * h + c:128 * h + e]), z - a, r=[W("XX"), x("LM")], w=[("XM%d" % h, a, z)], cyc=GCY, name="XM%d" % h)
+            tt(B("BD", h)[:], B("brep", h)[:], T.QM[:, 0:128], OP.mult, 128, r=[x("brep"), W("QM")], w=[x("BD")], name="BD")
+            mm(A[:, :, 56], B("BD", h)[:], T.U8[:], True, True, ak, 8, r=[x("BD"), W("U8")], f32=True, name="LBp")
+            cpv(T.LB[:, 8 * h:8 * h + 8], A[:, :, 56], 8, w=[("LB", 8 * h, 8 * h + 8)], pr=[ak], name="LB")
+            flex(B("XB", h)[:], T.XX[:, 0:V_].indirect(T.LB[:, 8 * h:8 * h + 8]), 128, r=XR + [("LB", 8 * h, 8 * h + 8)], w=[x("XB")], cyc=GCY, name="XB%d" % h)
+            if h not in MXS: mm(C[:, :, 32:48], T.Ib[:], B("XB", h)[:], True, True, ck, 128, r=[x("XB")], name="XBp")
+        for h in H:
+            A, C, Bk = P("A", h), P("C", h), P("B", h); ak, ck, bk = "pA%d" % h, "pC%d" % h, "pB%d" % h
+            x = lambda n: W(n + str(h))
+            mm(A[:, :, 40:56], B("cS", h)[:], T.If[:], True, False, ak, 128, r=[x("cS"), W("If")], f32=True, name="cK")
+            mm(A[:, :, 40:56], T.Im[:], T.VH[:, t, S(h)], False, False, ak, 128, r=[W("Im"), W("VH%d" % t)], name="cK")
+            mm(A[:, :, 40:56], T.Im[:], T.VL[:, t, S(h)], False, True, ak, 128, r=[W("Im"), W("VL%d" % t)], name="cK")
+            act(B("cKv", h)[:], A[:, :, 40:56], 128, w=[x("cKv")], pr=[ak], name="cKv")
+            MX = B("MX", h)
+            if h in MXS:
+                for c in range(4):
+                    bn = ck if c % 2 else "pE"
+                    for kk in range(4):
+                        o = C[:, :, 16 * kk:16 * kk + 16] if c % 2 else T.pE[:, S(kk)]
+                        mm(o, T.Ib[:], B("XK", h)[:, 4 * c + kk::16], True, False, bn, 128, r=[x("XK")], name="DF")
+                        mm(o, T.Im[:], B("XB", h)[:], False, True, bn, 128, r=[x("XB")], name="DF")
+                    act(MX[:, c], C[:] if c % 2 else T.pE[:], 512, ActivationFunctionType.Abs, w=[("MX%d" % h, 4 * c, 4 * c + 4)], pr=[bn], name="MXa")
+            else:
+                for k in range(16):
+                    tt(MX[:, k // 4, 2 * (k % 4):2 * (k % 4) + 2], B("XK", h)[:, k::16], C[:, :, 32:48], OP.max, 128, r=[x("XK")], w=[("MX%d" % h, k, k + 1)], pr=[ck], name="MX")
+            mm(A[:, :, 24:40], T.Ib[:], T.K2[:], True, False, ak, 128, r=[W("Ib"), W("K2")], name="FL")
+            if h not in MXS: mm(A[:, :, 24:40], T.Im16[:], B("SX", h)[:], False, False, ak, 128, r=[W("Im16"), x("SX")], name="FL")
+            for k in range(16):
+                c, kk = divmod(k, 4)
+                mr = [("MX%d" % h, k, k + 1)]
+                if h in MXS:
+                    l = MX[:, c, :, 16 * kk:16 * kk + 16] if c % 2 else MX[:, c, 2 * kk:2 * kk + 2]
+                    mm(A[:, :, 24 + k], l, T.S16[:], False, k == 15, ak, 8, r=mr + [W("S16")], name="FL")
+                else:
+                    mm(A[:, :, 24 + k], MX[:, c, 2 * kk:2 * kk + 2], T.S32[:], False, k == 15, ak, 8, r=mr + [W("S32")], name="FL")
+            for k in range(16):
+                mm(Bk[:, :, 24 + k], B("ST", h)[:, k::16], T.S1[:], True, True, bk, 8, r=[x("ST"), W("S1")], name="SL")
+            tt(B("el", h)[:], B("nm", h)[:], Bk[:, :, 24:40], OP.min, 128, r=[x("nm")], w=[x("el")], pr=[bk], name="el")
+            tt(Bk[:, :, 0:16], B("el", h)[:], A[:, :, 24:40], OP.mult, 128, r=[x("el")], pr=[ak], pw=[bk], name="q1")
+            mm(C[:, :, 0:16], B("brep", h)[:], T.If[:], True, True, ck, 128, r=[x("brep"), W("If")], f32=True, name="bR")
+            act(T.aD[:, S(h)], T.O[:, hs(h)], 128, COPY, bias=1.0, r=[oreg(h)], w=[("aD", 128 * h, 128 * h + 128)], name="a1")
+            act(C[:, :, 16:32], B("brep", h)[:], 128, IDENT, bias=T.VC[:, 8 + 2 * t + h:9 + 2 * t + h], r=[x("brep"), W("VC")], pw=[ck], name="bmv")
+        for h in H:
+            Bk = P("B", h); bk = "pB%d" % h
+            x = lambda n: W(n + str(h))
+            ws = T.pD[:, :, 16 * h:16 * h + 16]
+            for p in range(NPM):
+                ln = 8 // NPM
+                for k in range(16):
+                    mm(T.pD[:, ln * p:ln * p + ln, 16 * h:16 * h + 16], T.Ib[:], B("XM", h)[:, 2048 // NPM * p + k:2048 // NPM * (p + 1):16], k == 0, k == 15, "pD", 128 // NPM, r=[("XM%d" % h, 2048 // NPM * p, 2048 // NPM * (p + 1))], name="WS")
+            ts(B("wp", h)[:], ws, 0.0, OP.is_gt, 128, w=[x("wp")], pr=["pD"], name="wp")
+            wn = T.pD[:, :, 32 + 16 * h:48 + 16 * h]
+            mm(wn, B("wp", h)[:], T.BOb[:], True, True, "pD", 128, r=[x("wp"), W("BOb")], name="WN")
+            ts(B("win", h)[:], wn, T.Zc[:, 0:1], OP.is_ge, 128, r=[W("Zc")], w=[x("win")], pr=["pD"], name="win")
+            tt(B("nC0", h)[:], B("win", h)[:], P("C", h)[:, :, 16:32], OP.mult, 128, r=[x("win")], w=[x("nC0")], pr=["pC%d" % h], name="nC0")
+            ts(B("nC", h)[:], B("nC0", h)[:], T.VC[:, 2 * t + h:2 * t + h + 1], OP.add, 128, r=[x("nC0"), W("VC")], w=[x("nC")], name="nC")
+            if not last:
+                SN = T.SND[:, t]; sr = lambda o: ("SND%d" % t, 2 * h + o, 2 * h + o + 1)
+                cpv(SN[:, h, :, 0], B("nC", h)[:, 0::16], 8, r=[x("nC")], w=[sr(0)], name="hi")
+                tt(SN[:, h, :, 1], B("nC", h)[:, 0::16], SN[:, h, :, 0], OP.subtract, 8, r=[x("nC"), sr(0)], w=[sr(1)], name="lo")
+        if not last:
+            ds = [D_OF[u] for u in range(t + 1, RO)]
+            land = LU(t + 1, rank); sem = "ar%d_%d" % (t + 1, rank)
+            sa = send([T.cores[(rank - ds[0]) % NR]], T.SND[:, t], land, sem, [W("SND%d" % t)], 8, "send")
+            sb_ = send([T.cores[(rank - q) % NR] for q in ds[1:]], T.SND[:, t], land, sem, [W("SND%d" % t)], 8, "sendb") if len(ds) > 1 else None
+        for h in H:
+            A, Bk, C = P("A", h), P("B", h), P("C", h); ak, bk, ck = "pA%d" % h, "pB%d" % h, "pC%d" % h
+            x = lambda n: W(n + str(h))
+            tt(B("q2", h)[:], B("win", h)[:], Bk[:, :, 0:16], OP.mult, 128, r=[x("win")], w=[x("q2")], pr=[bk], name="q2")
+            vop(lambda v, h=h: v.tensor_tensor_scan(B("RM", h)[:], T.NF[:], B("q2", h)[:], 0.0, OP.mult, OP.max), 128, r=[W("NF"), x("q2")], w=[x("RM")], name="RM2")
+            best = T.pE[:, 256 + 128 * h:384 + 128 * h]
+            spread(h, B("RM", h), x("RM"), best, None, floor=0.5, bank="pE")
+            tt(B("oh2_", h)[:], B("q2", h)[:], best, OP.is_equal, 128, r=[x("q2")], w=[x("oh2_")], pr=["pE"], name="oh2")
+            mm(Bk[:, :, 0:16], B("oh2_", h)[:], T.Ib[:], True, True, bk, 128, r=[x("oh2_")], name="oh2T")
+            tt(B("pz", h)[:], T.aD[:, S(h)], Bk[:, :, 0:16], OP.mult, 128, r=[("aD", 128 * h, 128 * h + 128)], w=[x("pz")], pr=[bk], name="pz")
+            tt(B("pc", h)[:], B("cKv", h)[:], Bk[:, :, 0:16], OP.mult, 128, r=[x("cKv")], w=[x("pc")], pr=[bk], name="pc")
+            hr = lambda n: (n, 128 * h, 128 * h + 128)
+            act(T.oK[:, S(h)], Bk[:, :, 0:16], 128, w=[hr("oK")], pr=[bk], name="oK")
+            act(C[:, :, 32:48], Bk[:, :, 0:16], 128, COPY, bias=1.0, scale=-1.0, pr=[bk], pw=[ck], name="nk")
+            zm = T.pD[:, :, 32 + 16 * h:48 + 16 * h]
+            mm(zm, T.BOf[:], B("pz", h)[:], True, True, "pD", 128, r=[W("BOf"), x("pz")], f32=True, name="zm")
+            tt(T.ZQ[:, S(h)], T.QM[:, S(h)], zm, OP.mult, 128, r=[W("QM")], w=[hr("ZQ")], pr=["pD"], name="ZQ")
+            cpv(T.ZU[:, S(h)], zm, 128, w=[hr("ZU")], pr=["pD"], name="ZU")
+            vop(lambda v, h=h: v.tensor_tensor_scan(T.ZS[:, S(h)], T.NF[:], T.ZQ[:, S(h)], 0.0, OP.mult, OP.add), 128, r=[W("NF"), hr("ZQ")], w=[hr("ZS")], name="ZS")
+            zl = ("ZL", 8 * h, 8 * h + 8)
+            ts(T.ZL[:, 8 * h:8 * h + 8], T.ZS[:, 128 * h + 15:128 * h + 128:16], -1.0, OP.add, 8, r=[hr("ZS")], w=[zl], s2=0.0, op1=OP.max, name="ZL")
+            mm(T.pD[:, :, 16 * h:16 * h + 16], T.BOf[:], B("pc", h)[:], True, True, "pD", 128, r=[x("pc")], f32=True, name="csv")
+            flex(B("OC", h)[:], T.O[:].indirect(T.ZL[:, 8 * h:8 * h + 8]), 128, r=[W("O"), zl], w=[x("OC")], cyc=GCY, name="OC", only="S")
+            vop(lambda v, h=h, VR=VR: v.tensor_tensor(B("OE", h)[:], T.O[:].indirect(T.ZL[:, 8 * h:8 * h + 8]), VR[:, S(h)], OP.is_equal), 128, r=[W("O"), zl, W("VR%d" % t)], w=[x("OE")], two=GCY, name="OE")
+            tt(C[:, :, 48:64], T.oK[:, S(h)], C[:, :, 0:16], OP.mult, 128, r=[hr("oK")], pr=[ck], pw=[ck], name="hb")
+        for h in H:
+            x = lambda n: W(n + str(h)); hr = lambda n: (n, 128 * h, 128 * h + 128)
+            n1 = T.pD[:, :, 16 * h:16 * h + 16]
+            tt(n1, B("OE", h)[:], n1, OP.mult, 128, r=[x("OE")], pr=["pD"], pw=["pD"], name="n1")
+            tt(T.NC[:, S(h)], B("OC", h)[:], n1, OP.add, 128, r=[x("OC")], w=[hr("NC")], pr=["pD"], name="NC")
+        def de(u, a, z):
+            ts(T.DE[:, 256 * u + a:256 * u + z], T.ZU[:, a:z], T.ZS[:, 16 * u + 15:16 * u + 16], OP.is_equal, z - a,
+               r=[("ZU", a, z), ("ZS", 16 * u, 16 * u + 16)], w=[("DE", 256 * u + a, 256 * u + z)], two=0.5, name="DE")
+
+        def dup(h, u, a, z, wt, stop=False):
+            mm(T.pE[:, a:z], T[wt][:], T.DE[:, 256 * u + a:256 * u + z], False, stop, "pE", z - a, r=[("DE", 256 * u + a, 256 * u + z), W(wt)], name="DUP%d" % h)
+        for h in H:
+            hr = ("oK", 128 * h, 128 * h + 128)
+            mm(T.pE[:, S(h)], T.Ib[:], T.DC[:, S(h)], True, False, "pE", 128, r=[W("Ib"), W("DC")], name="DUP%d" % h)
+            mm(T.pE[:, S(h)], T.Ib[:], T.C128[:, S(h)], False, False, "pE", 128, r=[W("C128")], name="DUP%d" % h)
+            mm(T.pE[:, S(h)], T.BN[:], T.oK[:, S(h)], False, False, "pE", 128, r=[W("BN"), hr], name="DUP%d" % h)
+            for u in range(8 * h + 8):
+                if u < 8 * h:
+                    de(u, 128, 256)
+                    dup(h, u, 128, 256, "L4")
+                    continue
+                de(u, 16 * u, 128 * h + 128)
+                if u < 8 * h + 7: dup(h, u, 16 * u + 16, 128 * h + 128, "L4")
+                dup(h, u, 16 * u, 16 * u + 16, "LW", u == 8 * h + 7)
+        vop(lambda v: v.tensor_scalar(T.pE[:, 0:256], T.pE[:, 0:256], 0.0, 8192.0, OP.is_ge, OP.mult), 256, pr=["pE"], pw=["pE"], name="nlq")
+        tt(T.fz[:], T.ZQ[:], T.pE[:, 0:256], OP.max, 256, r=[W("ZQ")], w=[W("fz")], pr=["pE"], name="fz")
+        for h in H:
+            vop(lambda v, h=h: v.tensor_tensor_scan(T.FS[:, S(h)], T.NF[:], T.fz[:, S(h)], 0.0, OP.mult, OP.add), 128, r=[W("NF"), ("fz", 128 * h, 128 * h + 128)], w=[("FS", 128 * h, 128 * h + 128)], name="FS")
+        tt(T.fl[:], T.FS[:, 15::16], T.DL[:], OP.min, 16, r=[W("FS"), W("DL")], w=[W("fl")], name="fl")
+        ts(T.FZ[:], T.fl[:], -1.0, OP.add, 16, r=[W("fl")], w=[W("FZ")], name="FZ")
+        vop(lambda v: v.tensor_copy(T.O[:].indirect(T.FZ[:]), T.NC[:]), 256, r=[W("NC"), W("FZ")], w=[W("O")], two=3.0, name="scatter")
+        G["wr"]["O"] = [y for y in G["wr"]["O"]]
+        for h in H:
+            hr = lambda n: (n, 128 * h, 128 * h + 128)
+            ck = "pC%d" % h
+            tt(T.XO[:, S(h)], T.O[:, hs(h)], P("C", h)[:, :, 32:48], OP.mult, 128, r=[oreg(h)], w=[hr("XO")], pr=[ck], name="XO")
+            tt(T.O[:, hs(h)], T.XO[:, S(h)], P("C", h)[:, :, 48:64], OP.add, 128, r=[hr("XO")], w=[("O", 1536 * h, 1536 * h + 1536)], pr=[ck], name="O")
+        for h in H:
+            x = lambda n: W(n + str(h)); ck = "pA%d" % h; C = P("A", h)
+            cr = lambda n: (n, 96 * h, 96 * h + 96)
+            tt(T.CLk[:, 96 * h:96 * h + 96], T.CLf[:, 96 * h:96 * h + 96], T.KP[:, t], OP.mult, 96, r=[cr("CLf"), W("KP%d" % t)], w=[cr("CLk")], name="CLk")
+            tt(B("BDc", h)[:], B("nC", h)[:], T.PM[:, t], OP.mult, 128, r=[x("nC"), W("PM%d" % t)], w=[x("BDc")], name="BDc")
+            mm(C[:, :, 0:12], T.If[:], T.CLk[:, 96 * h:96 * h + 96], True, False, ck, 96, r=[cr("CLk"), W("If")], f32=True, name="CLp")
+            mm(C[:, :, 0:12], B("BDc", h)[:], T.U4[:], False, True, ck, 96, r=[x("BDc"), W("U4")], f32=True, name="CLp")
+            if not last: cpv(T.CLu[:, 96 * h:96 * h + 96], C[:, :, 0:12], 96, w=[cr("CLu")], pr=[ck], name="CLu")
+            act(T.CLf[:, 96 * h:96 * h + 96], C[:, :, 0:12], 96, w=[cr("CLf")], pr=[ck], name="CLf")
+        if last: break
+        for h in H:
+            mm(T.pA1[:, :, 58], T.ONE[:], B("win", h)[:, 0::16], h == 0, h == 1, "pA1", 8, r=[W("win%d" % h), W("ONE")], name="ZC")
+        vop(lambda v: v.tensor_reduce(T.zr[:, 0:1], T.pA1[:, :, 58], AxisListType.X, OP.add), 8, w=[("zr", 0, 1)], pr=["pA1"], name="zr")
+        cpv(T.zi[:, 0:1], T.zr[:, 0:1], 1, r=[("zr", 0, 1)], w=[("zi", 0, 1)])
+        ts(T.zi[:, 1:2], T.zi[:, 0:1], 1, OP.bitwise_and, 1, r=[("zi", 0, 1)], w=[("zi", 1, 2)])
+        ts(T.Zc[:], T.zi[:, 1:2], 9.0, OP.add, 1, r=[("zi", 1, 2)], w=[W("Zc")], name="Zc")
+        for qi, q in enumerate(ds):
+            s = (rank + q) % NR; ln = "L%d_%d" % (t + 1, s)
+            arrive(s, t + 1, sa if qi == 0 else sb_, 8)
+            for h in H:
+                A = P("A", h); ak = "pA%d" % h
+                flex(B("HLz", h)[:, :, 0:2], LU(t + 1, s)[:, h], 16, r=[W(ln)], w=[W("HLz%d" % h)], name="HLz")
+                mm(A[:, :, 40:56], B("HLz", h)[:], T.Ib[:], True, True, ak, 128, r=[W("HLz%d" % h)], name="HLr")
+                flex(T["WC%d" % q][:, hs(h)], A[:, :, 40:56], 128, w=[("WC%d" % q, 1536 * h, 1536 * h + 1536)], pr=[ak], name="WCu")
+    vop(lambda v: v.transpose(T.TF[:], T.CLf[:]), 192, r=[W("CLf")], w=[W("TF")], name="yc")
+    for e in range(2):
+        for b in range(6):
+            dma(T.yc[e::2, 512 * b:512 * b + 512], T.TF[:, 32 * b + 16 * e:32 * b + 16 * e + 16], 8, r=[W("TF")], name="st yc")
+    dma(T.yo[:, 0:1536], T.O[:, 0:1536], 786, r=[("O", 0, 1536)], name="st yo")
+    dma(T.yo[:, 1536:3072], T.O[:, 1536:3072], 786, r=[("O", 1536, 3072)], q="S", name="st yo")
+    return G
+
+
+ORDER = {}
+
+
+def rank_program(g, core, T, topo):
+    rank = T.rank_of(core)
+    if rank is None:
+        return
+    G = build(core, T, topo, rank)
+    if "o" not in ORDER: ORDER["o"] = schedule(G)
+    order, eng, fin, st = ORDER["o"]
+    Q = {"V": g.vector, "S": g.scalar, "P": g.tensor, "G": g, "Y": g.sync}
+    ops = G["ops"]
+    count = {}; known = {"V": {}, "S": {}, "P": {}, "G": {}, "Y": {}}; done = [None] * len(ops); clock = [None] * len(ops)
+    for i in order:
+        o = ops[i]; e = eng[i]
+        if e not in Q:
+            done[i] = (o["key"], o["cnt"]); clock[i] = {}
+            continue
+        kn = known[e]
+        need = {}
+        for j, raw in o["deps"].items():
+            if eng[j] == e and not raw: continue
+            k, c = done[j]
+            if kn.get(k, 0) < c: need[k] = max(need.get(k, 0), c)
+        cand = sorted(need.items())
+        for j in o["deps"]:
+            if eng[j] == e and not o["deps"][j]: continue
+        for k, c in cand:
+            if kn.get(k, 0) >= c: continue
+            Q[e].wait_ge(T.sem[k], c)
+            kn[k] = max(kn.get(k, 0), c)
+            for j in o["deps"]:
+                if done[j] == (k, c):
+                    for kk, vv in clock[j].items(): kn[kk] = max(kn.get(kk, 0), vv)
+        ins = o["fn"](Q, e)
+        if o["key"] is None:
+            k = "c" + e
+            count[k] = count.get(k, 0) + 1
+            ins.then_inc(T.sem[k], 1)
+            done[i] = (k, count[k])
+        else:
+            k = o["key"]
+            count[k] = count.get(k, 0) + o["cnt"]
+            done[i] = (k, count[k])
+        c = dict(kn); c[done[i][0]] = max(c.get(done[i][0], 0), done[i][1])
+        clock[i] = c
+    for k in sorted(count): g.wait_ge(T.sem[k], count[k])

@@ -2,10 +2,19 @@ from concourse.bass import DstId, RemoteDMATransfer
 from concourse.mybir import dt, AluOpType, AxisListType, ActivationFunctionType
 
 V_, RO, NR = 3072, 4, 4
+HV = V_ // 2
 PAD = 256
+WW = V_ + HV
+MID = 1536
+BIG = 8192.0
+CEN = 1664.0
 OP = AluOpType
-COPY = ActivationFunctionType.Copy
-IDENT = ActivationFunctionType.Identity
+AF = ActivationFunctionType
+COPY, IDENT, RELU, SIGN = AF.Copy, AF.Identity, AF.Relu, AF.Sign
+GS, CO, NVT, SXT = True, True, 1, True
+STV = []
+XR = 2 if GS else 1
+MR = 4
 
 
 def _decl():
@@ -13,50 +22,66 @@ def _decl():
 
     def sb(name, shape, dtype):
         s[name] = ("sbuf", shape, dtype)
-    f, b, i, u = "float32", "bfloat16", "int32", "uint16"
-    sb("O", [128, V_ + PAD], f); sb("OI", [128, V_], i); sb("XX", [128, 2 * V_], b); sb("CC", [128, V_], b)
-    for d in (1, 2, 3): sb("WC%d" % d, [128, V_], b)
+    f, b, i, u, hf = "float32", "bfloat16", "int32", "uint16", "float16"
+    for h in range(2):
+        sb("O%d" % h, [128, WW + PAD], f); sb("XX%d" % h, [128, 2 * WW], b); sb("WC%d" % h, [128, V_], b)
     sb("CI", [128, 192], i); sb("CF", [128, 192], f); sb("HL0", [128, 384], b)
-    sb("TI", [128, 192], i); sb("TF", [128, 192], f); sb("CLf", [128, 192], f); sb("CLk", [128, 192], f); sb("CLu", [128, 192], u)
     for r in range(NR): sb("L0_%d" % r, [128, 384], b)
-    sb("LU", [128, 12, 2, 8, 2], b); sb("SND", [128, 3, 2, 8, 2], b)
-    for t in range(2): sb("VT%d" % t, [128, 4096], f)
-    sb("VR", [128, 4, 256], f); sb("PM", [128, 4, 128], f); sb("KP", [128, 4, 96], f)
-    sb("VC", [128, 16], f)
-    for n in ("XK", "CG", "ST", "MN", "XM"): sb(n, [128, 2, 2048], b)
-    sb("MX", [128, 2, 4, 8, 64], b); sb("E", [128, 2, 8, 8, 16], b); sb("PR", [128, 2, 15, 8, 16], b)
-    for n in ("cS", "RM", "BR", "oh", "w", "brep", "BD", "cKv", "q2", "pz", "pc", "nC0", "nC", "BDc", "OC", "OE"): sb(n, [128, 2, 128], f)
-    for n in ("nm", "XB", "SX", "wp", "win", "el", "oh2_"): sb(n, [128, 2, 128], b)
-    sb("mS", [128, 2, 8, 24], b); sb("LM", [128, 256], u); sb("BZ", [128, 2, 128], f); sb("kS", [128, 2, 128], f); sb("HLz", [128, 2, 8, 16], b)
-    sb("LA", [128, 256], u); sb("LB", [128, 16], u); sb("ZL", [128, 16], u); sb("FZ", [128, 16], u); sb("ZU", [128, 256], u)
-    for n in ("aD", "ZQ", "ZS", "NC", "nlq", "fz", "FS", "XO", "QM"): sb(n, [128, 256], f)
-    sb("fl", [128, 16], f); sb("DL", [128, 16], f); sb("DE", [128, 4096], b)
-    for n in ("Ib", "Im", "Im16", "I256", "I16", "I3072", "BOb", "BN", "L4", "LW", "ONE", "K1", "K2"): sb(n, [128, 128], b)
-    for n in ("If", "BOf", "NF"): sb(n, [128, 128], f)
-    for n in ("DC", "C128", "oK"): sb(n, [128, 256], b)
-    for n in ("VH", "VL"): sb(n, [128, 4, 256], b)
-    for n in ("S1", "S16", "S32", "Sm16", "SHL"): sb(n, [128, 8], b)
-    sb("U8", [128, 8], f); sb("U4", [128, 96], f)
-    sb("ci", [128, 256], f); sb("cg", [128, 256], f); sb("cq", [128, 256], f)
-    sb("pi", [128, 1], i); sb("ti", [128, 16], i); sb("tf", [128, 16], f); sb("wq", [128, 16], f)
-    sb("zr", [128, 4], f); sb("zi", [128, 4], i); sb("Zc", [128, 1], f)
-    for n in ("pA0", "pA1", "pB0", "pB1", "pC0", "pC1", "pD"): s[n] = ("psum", [128, 8, 64], f)
-    s["pE"] = ("psum", [128, 512], f)
+    sb("LU", [128, 24, 2, 4, 2], b); sb("SND", [128, 8, 2, 4, 2], b)
+    sb("VR", [128, 4, 128], f); sb("VC", [128, 16], f); sb("VB", [128, 32], f); sb("VL", [128, 4, 128], b)
+    sb("OI", [128, HV], i)
+    for n in ("XK", "MN", "CG"): sb(n, [128, 2, 2048], b)
+    sb("OB", [128, 2, 8, 256], b)
+    sb("E", [128, 2, 8, 8, 16], b); sb("PR", [128, 2, 8, 8, 16], b); sb("PQ", [128, 8, 7, 40], b)
+    for n in ("cK", "F", "TT", "BD", "ZUf", "OE"): sb(n, [128, 2, 128], f)
+    for n in ("cS", "wN", "pc", "pz", "ZQ"): sb(n, [128, 2, 128], hf)
+    for n in ("oh", "wp", "w", "nst", "oh2", "sg", "DS"): sb(n, [128, 2, 128], b)
+    sb("aN", [128, 2, 4, 2, 16], hf); sb("mine", [128, 2, 4, 2, 16], b); sb("LMf", [128, 2, 16, 4, 2], f)
+    if CO:
+        sb("CC0", [128, WW], b); sb("CC1", [128, WW], b); sb("KD", [128, 12, 128], f); sb("NE", [128, 16], f); sb("NB", [128, 2, 128], b)
+        sb("TI", [128, 2, 3, 2, 16], i); sb("TF", [128, 2, 3, 2, 16], f); sb("CLf", [128, 2, 96], f); sb("CLu", [128, 2, 96], u)
+    else: sb("YC", [128, HV], f)
+    if STV: sb("VT", [128, NVT, 2048], f)
+    pass; sb("mS", [128, 2, 128], b); sb("XB", [128, 2, 128 * XR], b); sb("HLz", [128, 8, 2, 4, 16], b)
+    for n in ("LA", "LM") if CO else ("LA", "LM", "L0", "LC"): sb(n, [128, 2, 128], u)
+    sb("ZU", [128, 2, 256], u); sb("LB", [128, 2, 8 * XR], u); sb("ZL", [128, 2, 8], u); sb("FZ", [128, 2, 16], u)
+    for n in ("OC", "NN"): sb(n, [128, 2, 256], f)
+    sb("fl", [128, 2, 16], f); sb("SPL", [128, 16], f)
+    for n in ("BM", "BP", "t8", "n8", "ZLf"): sb(n, [128, 2, 8], f)
+    sb("DE", [128, 2, 8, 256], b); sb("SHL2", [128, 4, 8, 3], b)
+    if SXT: sb("SX", [128, 2, 128], b); sb("SXB", [128, 2, HV], b)
+    sb("CB", [128, len(CBN), 128], b); sb("CH", [128, len(CHN), 128], hf); sb("CX", [128, len(CXN), 128], f)
+    sb("SEL", [128, 16, 128], b)
+    for n in ("S1", "S32", "Sm16", "U8b", "HH"): sb(n, [128, 8], b)
+    sb("SY", [128, 12], b)
+    sb("S12", [128, 8, 4], b); sb("S1h", [128, 8], hf); sb("U8", [128, XR, 8], f)
+    sb("ci", [128, 128], b); sb("cg", [128, 128], b); sb("cq", [128, 128], b); sb("c2", [128, 16], b); sb("c3", [128, 128], b)
+    sb("pi", [128, 1], i); sb("ti", [128, 8], i); sb("tf", [128, 8], f); sb("wq", [128, 44], f)
+    sb("zr", [128, 24], f); sb("zi", [128, 4], i); sb("Zb", [128, 1], f)
+    for n in ("pA0", "pA1", "pB0", "pB1"): s[n] = ("psum", [128, 8, 64], f)
+    for n in ("pC0", "pC1", "pD0", "pD1"): s[n] = ("psum", [128, 4, 128], f)
     return s
 
 
+CBN = ["Ib", "Im", "I16", "I256", "ImW", "IB", "ImB", "Ib2", "Imb2", "Imax", "BOb", "BOy", "TRI", "ONE", "K1", "K2", "KM", "KH", "KL",
+       "QB", "QmB", "QC", "VH", "LR", "LRx", "KW0", "KW1", "KW2", "KW3", "Im16", "BO6", "Im256", "BOm512", "PM0", "PM1", "PM2", "PM3"]
+CHN = ["Ih", "Imh", "BOh", "PA0", "PA1", "PA2", "PA3", "BOm", "BOx"]
+CXN = ["If", "BOf", "SW", "NF", "QM"]
 SCRATCH = _decl()
-SEMAPHORES = ["cV", "cS", "cP", "cG", "loc"] + ["d%d" % k for k in range(52)] + ["ar%d_%d" % (t, r) for t in range(4) for r in range(NR)]
-PS = ("pA0", "pA1", "pB0", "pB1", "pC0", "pC1", "pD", "pE")
+SEMAPHORES = ["cV", "cS", "cP", "cG", "loc"] + ["d%d" % k for k in range(60)] + ["ar%d_%d_%d" % (t, h, r) for t in range(4) for h in range(2) for r in range(NR)]
 D_OF = [1 + t % 3 for t in range(RO)]
 CYC = 0.83e-3
-WAKE = 0.09
-GCY = 1.5
-ASG = {"XK1": "S", "CG0": "S", "CG1": "S", "XM0": "S", "XM1": "S", "compose0": "S", "compose1": "S", "compose2": "S", "compose3": "S"}
-NPC, NPM, NPS = 2, 2, 8
-WT = {'ST': -10, 'SX': -5, 'zr': -10, 'key': 10, 'XB1': 10, 'RW': 20, 'BDc': -10, 'LM': -10, 'LA': 2, 'compose1': 10, 'RM': 2, 'pc': -10, 'pz': -5, 'ld sha': 10, 'el': -20, 'q2': 20, 'cL': 20, 'ZQ': -20, 'ext': -5, 'win': -2, 'oh2T': 10, 'CLu': -10, 'mS': 10, 'HLz': 2, 'oh2': 10, 'VT': -10, 'XM0': -2, 'csv': -2, 'flat': -2, 'CLk': 5, 'nk': 2, 'ZU': 10, 'Zc': -2, 'LMa': 20, 'CLf': -20, 'OC': 10, 'ld ctl': 5, 'nlq': 20, 'ld list': 20, 'send': 20, 'nC0': 10, 'hb': 2, 'bmv': 2, 'lo': 2, 'ld hol': 10, 'a1': 10, 'CF': -5, 'sendb': 5, 'zm': 20, 'fl': -2, 'OE': 20, 'DUP1': -5, 'FZ': -5, 'nC': 2, 'RM2': -20, 'sp': 10, 'scatter': 5, 'SXc': -10, 'WCu': -10, 'wp': 10, 'cKv': -2, 'XO': -2, 'compose3': 10, 'st yo': 5, 'hi': 5, 'O': 5}
-MXS = ()
-PRS = ()
+WAKE = 0.12
+GCY = 1.56
+PF, PO = 0.6, 0.02
+ASG = {"CG": "S", "cS": "S", "aN": "S", "ZLf": "V", "C1": "S", "SXb": "S", "compose": "S", "XM": "S", "yc": "S", "XK0": "S", "XK1": "S", "XB": "S", "mS": "S", "WCu": "S", "CLf": "S", "HLz": "S"}
+RATE, LAT, FAR = 200.0, 2.2, 3.5
+SAME, PER, STRETCH, SWEEPS = 0.06, 33.0, 1.25, 2
+NPC, NPM, NCP = 2, 2, 2
+WT = {'yct': 6, 'OC': -2, 'UG': 2, 'MN': -1, 'Ox': 4, 'bm': 1, 'E': 1, 'LA': 2, 'st yc': 2, 'pzp': 2, 'US': 4, 'sendb': 2, 'XV': 6, 'LMp': 4, 'ZL': 2, 'pz': -2, 'LMt': 4, 'FZ': 1, 'G': -1, 'CCx': 4, 'flat': 1, 'SL': 1, 'SXp': -1, 'b8': -2, 'st yo': 6, 'DE': 6, 'WCu': 2, 'ZUp': -1, 'nst': 1, 'ld list': 1, 'fl': -1, 'csv': -1, 'bR': 6, 't8': -2, 'Osw': 4, 'send0b': 6, 'SXc': -1, 'ld hol0': 6, 'hi': -4, 'OB': -2, 'OE': 4, 'mS': 2, 'wp': -2, 'LM': -4, 'send': -4, 'Oc': 4}
+FIRST = ["ld ctl", "send0", "ld hol0", "ld sha0"]
+SHORT = {}
+PRS = []
 
 
 def new_graph():
@@ -77,7 +102,7 @@ def add(G, opts, fn, r=(), w=(), pr=(), pw=(), key=None, cnt=1, name=""):
         for (a, b, j) in G["wr"].get(bn, []):
             if a < hi and lo < b: dep(j, False)
         for (a, b, j) in G["rd"].get(bn, []):
-            if a < hi and lo < b: dep(j, False)
+            if a < hi and lo < b: dep(j, True)
         G["wr"][bn] = [x for x in G["wr"].get(bn, []) if not (lo <= x[0] and x[1] <= hi)] + [(lo, hi, n)]
         G["rd"][bn] = [x for x in G["rd"].get(bn, []) if not (lo <= x[0] and x[1] <= hi)]
     engs = tuple(sorted(opts))
@@ -90,61 +115,101 @@ def add(G, opts, fn, r=(), w=(), pr=(), pw=(), key=None, cnt=1, name=""):
         if bn in G["bw"]: dep(G["bw"][bn], False)
         for j in G["br"].get(bn, []): dep(j, False)
         G["bw"][bn] = n; G["br"][bn] = []
-    G["ops"].append({"opts": opts, "engs": engs, "fn": fn, "deps": deps, "key": key, "cnt": cnt, "name": name})
+    G["ops"].append({"opts": opts, "engs": engs, "fn": fn, "deps": deps, "key": key, "cnt": cnt, "name": name, "h": G.get("h"), "t": G.get("t")})
     return n
 
 
-def schedule(G, wake=WAKE, quant=0.08):
+def place(busy, t, d):
+    lo, hi = 0, len(busy)
+    while lo < hi:
+        m = (lo + hi) // 2
+        if busy[m][1] <= t: lo = m + 1
+        else: hi = m
+    while lo < len(busy) and busy[lo][0] < t + d - 1e-9:
+        t = max(t, busy[lo][1]); lo += 1
+    return t, lo
+
+
+def schedule(G):
     ops = G["ops"]; n = len(ops)
-    succ = [[] for _ in range(n)]; ind = [len(o["deps"]) for o in ops]
+    succ = [[] for _ in range(n)]
     for i, o in enumerate(ops):
         for j in o["deps"]: succ[j].append(i)
+    pred = [list(o["deps"]) for o in ops]
+
+    def lag(j, ej, i, ei):
+        c = ops[j]["opts"][ej]
+        if ej != ei: return c[1] + WAKE
+        return c[1] + SAME if ops[i]["deps"][j] or ops[j]["key"] else c[0]
+
+    def sweep(key, before, eng, only=None):
+        at = [0.0] * n; on = [None] * n; busy = {}
+        idx = [i for i in range(n) if only is None or only[i]]
+        for j in (idx if eng is None else idx[::-1]):
+            for i in before[j]:
+                if only is None or only[i]: key[j] = max(key[j], key[i] + 1e-6)
+        for i in sorted(idx, key=lambda i: key[i]):
+            best = None
+            bf = before[i] if only is None else [j for j in before[i] if only[j]]
+            for e in (ops[i]["opts"] if eng is None else [eng[i]]):
+                c = ops[i]["opts"][e]
+                if eng is None: t = max([0.0] + [at[j] + lag(j, on[j], i, e) for j in bf])
+                else: t = max([c[1] - c[0]] + [at[j] + ops[j]["opts"][eng[j]][0] + lag(i, e, j, eng[j]) - c[0] for j in bf])
+                t, k = place(busy.setdefault(e, []), t, c[0])
+                if best is None or t + c[0] < best[0]: best = (t + c[0], t, k, e)
+            end, at[i], k, on[i] = best
+            busy[on[i]].insert(k, (at[i], end))
+        return at, on
+
+    def both(prio, sweeps, only=None):
+        best = None
+        idx = [i for i in range(n) if only is None or only[i]]
+        for it in range(sweeps):
+            at, eng = sweep(prio, pred, None, only)
+            fin = [at[i] + ops[i]["opts"][eng[i]][1] if eng[i] else 0.0 for i in range(n)]
+            if best is None or max(fin) < max(best[2]): best = (sorted(idx, key=lambda i: (at[i], i)), eng, fin, at)
+            back, _ = sweep([-(at[i] + ops[i]["opts"][eng[i]][0]) if eng[i] else 0.0 for i in range(n)], succ, eng, only)
+            prio = [-(back[i] + ops[i]["opts"][eng[i]][0]) if eng[i] else 0.0 for i in range(n)]
+            for i in idx:
+                if ops[i]["name"] in FIRST: prio[i] = FIRST.index(ops[i]["name"]) - 1e4
+        return best, prio
     prio = [0.0] * n
     for i in range(n - 1, -1, -1):
-        d = min(x[1] for x in ops[i]["opts"].values())
-        prio[i] = d + max([prio[s] + 0.5 * wake for s in succ[i]] or [0.0])
-    prio = [p + WT.get(o["name"], 0.0) for p, o in zip(prio, ops)]
-    free = {}; fin = [0.0] * n; eng = [None] * n; rdy = {}
-    order = []; t_ready = [0.0] * n
-    for i in range(n):
-        if ind[i] == 0: rdy[i] = True
-    while rdy:
-        best = None
-        for i in rdy:
-            for e, c in ops[i]["opts"].items():
-                st = free.get(e, 0.0)
-                for j, raw in ops[i]["deps"].items():
-                    x = fin[j] + (wake if eng[j] != e else (0.06 if raw else -1.0))
-                    if x > st: st = x
-                k = (int(st / quant), -prio[i], st)
-                if best is None or k < best[0]: best = (k, i, e, st)
-        _, i, e, st = best
-        del rdy[i]
-        c = ops[i]["opts"][e]
-        free[e] = st + c[0]; fin[i] = st + c[1]; eng[i] = e; t_ready[i] = st
-        order.append(i)
-        for s in succ[i]:
-            ind[s] -= 1
-            if ind[s] == 0: rdy[s] = True
-    return order, eng, fin, t_ready
+        prio[i] = min(x[1] for x in ops[i]["opts"].values()) + max([prio[s] + 0.5 * WAKE for s in succ[i]] or [0.0])
+    _, late = both([-p for p in prio], 3, [o["h"] == 0 and o["t"] is not None for o in ops])
+    blocks = {}
+    for i, o in enumerate(ops):
+        if o["t"] is not None: blocks.setdefault((o["t"], o["h"]), []).append(i)
+    key = [None] * n
+    for (t, h), b in blocks.items():
+        ref = blocks[t, 0]; byname = {}; seen = {}
+        for i in ref: byname.setdefault(ops[i]["name"], []).append(late[i] - late[ref[0]])
+        for i in b:
+            nm = ops[i]["name"]; k = seen.get(nm, 0); seen[nm] = k + 1
+            if k < len(byname.get(nm, [])): key[i] = (2 * t + h) * PER / 2 + STRETCH * byname[nm][k] - WT.get(nm, 0.0) - sum(SHORT.get(e, 0.0) for e, c in ops[i]["opts"].items() if c[0] < 0.3)
+    for i in range(n - 1, -1, -1):
+        if key[i] is None: key[i] = min([key[s] for s in succ[i]] or [1e3]) - min(x[1] for x in ops[i]["opts"].values()) - WT.get(ops[i]["name"], 0.0)
+    key = [FIRST.index(o["name"]) - 1e4 if o["name"] in FIRST else k for k, o in zip(key, ops)]
+    return both(key, SWEEPS)[0]
 
 
-def vc(n, two=1.0): return max(64.0, n * two) * CYC * 1.2 + 0.01
-def sc(n): return max(64.0, n) * CYC * 1.2 + 0.03
-def pc_(n, f32=False): return max(64.0, n) * CYC * 1.1 * (4.0 if f32 else 1.0) + 0.01
+def vc(n, two=1.0): return n * two * CYC + 0.05
+def sc(n): return n * CYC + 0.065
+def gc_(n, e): return n * GCY * CYC + (0.05 if e == "V" else 0.065)
+def pc_(n, f32=False): return max(64.0, n) * CYC * PF * (4.0 if f32 else 1.0) + PO
 
 
 def build(core, T, topo, rank):
     G = new_graph()
     W = lambda n: (n, 0, 1 << 20)
-    nd = [0]
+    keys = {}
 
-    def vop(fn, n, r=(), w=(), pr=(), pw=(), two=1.0, name=""):
-        c = vc(n, two)
+    def vop(fn, n, r=(), w=(), pr=(), pw=(), two=1.0, name="", c=None):
+        c = c or vc(n, two)
         return add(G, {"V": (c, c)}, lambda Q, e: fn(Q["V"]), r, w, pr, pw, name=name)
 
-    def tt(o, a, b, op, n, r=(), w=(), pr=(), name="", pw=(), two=None):
-        vop(lambda v: v.tensor_tensor(o, a, b, op), n, r, w, pr, pw, two=two or (1.0 if pr else 2.0), name=name)
+    def tt(o, a, b, op, n, r=(), w=(), pr=(), name="", pw=(), c=None):
+        vop(lambda v: v.tensor_tensor(o, a, b, op), n, r, w, pr, pw, two=1.0 if pr else 2.0, name=name, c=c)
 
     def ts(o, a, s1, op0, n, r=(), w=(), pr=(), s2=None, op1=None, two=1.0, name=""):
         if op1 is None: vop(lambda v: v.tensor_scalar(o, a, s1, None, op0), n, r, w, pr, two=two, name=name)
@@ -153,29 +218,45 @@ def build(core, T, topo, rank):
     def cpv(o, a, n, r=(), w=(), pr=(), name=""):
         vop(lambda v: v.tensor_copy(o, a), n, r, w, pr, name=name)
 
-    def flex(o, a, n, r=(), w=(), pr=(), name="", cyc=1.0, only=None):
-        opts = {"V": (vc(n, cyc), vc(n, cyc)), "S": (sc(n * cyc), sc(n * cyc))}
-        only = only or ASG.get(name)
-        if only: opts = {only: opts[only]}
-        return add(G, opts, lambda Q, e: Q["V"].tensor_copy(o, a) if e == "V" else Q["S"].activation(o, a, COPY), r, w, pr, name=name)
+    def scan(o, a, n, r=(), w=(), pr=(), name=""):
+        vop(lambda v: v.tensor_tensor_scan(o, X("NF"), a, 0.0, OP.mult, OP.max), n, list(r) + [W("NF")], w, pr, name=name)
 
-    def act(o, a, n, func=COPY, bias=0.0, scale=1.0, r=(), w=(), pr=(), name="", pw=()):
-        return add(G, {"S": (sc(n), sc(n))}, lambda Q, e: Q["S"].activation(o, a, func, bias=bias, scale=scale), r, w, pr, pw, name=name)
+    def flex(o, a, n, r=(), w=(), pr=(), name="", gather=False, only=None, two=1.0, bias=None, scale=1.0):
+        opts = {"V": (gc_(n, "V") if gather else vc(n, two),) * 2, "S": (gc_(n, "S") if gather else sc(n),) * 2}
+        only = only or (None if G.get("free") and gather else ASG.get(name))
+        if only: opts = {only: opts[only]}
+
+        def fn(Q, e):
+            if bias is None: return Q["V"].tensor_copy(o, a) if e == "V" else Q["S"].activation(o, a, COPY)
+            return Q["V"].tensor_scalar(o, a, scale, bias, OP.mult, OP.add) if e == "V" else Q["S"].activation(o, a, COPY, bias=bias, scale=scale)
+        return add(G, opts, fn, r, w, pr, name=name)
+
+    def act(o, a, n, func=COPY, bias=0.0, scale=1.0, r=(), w=(), pr=(), name="", c=None):
+        c = c or sc(n)
+        return add(G, {"S": (c, c)}, lambda Q, e: Q["S"].activation(o, a, func, bias=bias, scale=scale), r, w, pr, name=name)
 
     def mm(o, l, rh, start, stop, bank, n, r=(), f32=False, name=""):
         c = pc_(n, f32)
         return add(G, {"P": (c, c)}, lambda Q, e: Q["P"].matmul(o, l, rh, start, stop), r, (), (), (bank,), name=name)
 
+    def grp(o, bank, terms, name, n=128, start=True, stop=True):
+        for j, x in enumerate(terms):
+            mm(o, x[0], x[1], start and j == 0, stop and j == len(terms) - 1, bank, n, r=x[2], f32=len(x) > 3, name=name)
+
     def gop(fn, n, r=(), w=(), name=""):
-        c = 0.14 + 2 * n * CYC * 1.2
+        c = 0.14 + 2 * n * CYC
         return add(G, {"G": (c, c)}, lambda Q, e: fn(Q["G"]), r, w, name=name)
 
-    def dma(o, a, kb, r=(), w=(), q="Y", name=""):
-        k = nd[0]; nd[0] += 1
-        return add(G, {q: (0.1, 2.0 + kb / 200.0)}, lambda Q, e: (Q["Y"] if e == "Y" else Q["S"]).dma_start(o, a).then_inc(T.sem["d%d" % k], 16), r, w, key="d%d" % k, cnt=16, name=name)
+    def iota(o, pat, base, n, w, cm=0):
+        return gop(lambda g: g.iota(o, pat, base, cm, allow_small_or_imprecise_dtypes=True), n, w=w, name="up" if G.get("up") else "")
 
-    def send(dsts, src_ap, land, sem, r, kb, name):
-        m = 255
+    def fill(o, v, n, w): vop(lambda q: q.memset(o, float(v)), n, w=w, two=0.5, name="fill")
+
+    def dma(o, a, kb, key, r=(), w=(), q="Y", name=""):
+        k = "d%d" % keys.setdefault(key, len(keys))
+        return add(G, {q: (max(0.15, kb / RATE) if q == "Y" else 0.15, LAT + kb / RATE)}, lambda Q, e: (Q["Y"] if e == "Y" else Q["S"]).dma_start(o, a).then_inc(T.sem[k], 16), r, w, key=k, cnt=16, name=name)
+
+    def send(dsts, src_ap, land, sem, r, name):
         ne = len(topo.engines(core, dsts[0]))
         for x in dsts: assert topo.may_write(core, x) and topo.mask(core, x) == topo.mask(core, dsts[0])
 
@@ -188,382 +269,399 @@ def build(core, T, topo, rank):
                 Q["G"].remote_dma_fused([RemoteDMATransfer(dst_ids=ids, dma_engine_mask=topo.mask(core, dsts[0]), remote_sem=T.sem[sem], srcs=[src_ap], dsts=[land for x in dsts])], local_sem=T.sem.loc)
         return add(G, {"G": (1.0, 1.0)}, fn, r, (), key="loc", cnt=ne, name=name)
 
-    def arrive(src_rank, t, after, kb):
-        nm = "L%d_%d" % (t, src_rank)
-        i = add(G, {"N%d_%d" % (t, src_rank): (0.0, 2.5 + kb / 40.0)}, None, (), (W(nm),), key="ar%d_%d" % (t, src_rank), cnt=len(topo.engines(T.cores[src_rank], core)), name="arrive")
+    def arrive(src_rank, t, h, after, kb):
+        nm = "%d_%d_%d" % (t, h, src_rank)
+        i = add(G, {"N" + nm: (0.0, FAR + kb / 30.0)}, None, (), (W("L" + nm),), key="ar" + nm, cnt=len(topo.engines(T.cores[src_rank], core)), name="arrive")
         G["ops"][i]["deps"][after] = True
 
     H = (0, 1)
+    LO, UP = slice(0, 64), slice(64, 128)
 
-    def ext(X, bank):
-        opts = {"V": (vc(64), vc(64)), "S": (sc(64), sc(64))}
-        if "ext" in ASG: opts = {ASG["ext"]: opts[ASG["ext"]]}
-        add(G, opts, lambda Q, e: Q["V"].tensor_copy(X[:, :, 16:24], X[:, :, 0:8]) if e == "V" else Q["S"].activation(X[:, :, 16:24], X[:, :, 0:8], COPY), (), (), (bank,), (bank,), name="ext")
+    def sets():
+        for h in H:
+            G["h"] = h
+            yield h
+        G["h"] = None
 
+    def X(n): return T.CB[:, CBN.index(n)] if n in CBN else T.CH[:, CHN.index(n)] if n in CHN else T.CX[:, CXN.index(n)]
     def P(n, h): return T["p" + n + str(h)]
     def B(n, h): return T[n][:, h]
-    def LU(t, r): return T.LU[:, 4 * (t - 1) + r]
+    def LU(t, h, r): return T.LU[:, 8 * (t - 1) + 4 * h + r]
+    def S(j): return slice(128 * j, 128 * j + 128)
 
-    dma(T.CI[:], T.ctl[:], 98, w=[W("CI")], name="ld ctl")
-    for c in range(4):
-        dma(T.OI[:, 768 * c:768 * c + 768], T.hol[:, 768 * c:768 * c + 768], 393, w=[("OI", 768 * c, 768 * c + 768)], q="Y", name="ld hol")
-    for e in range(2):
-        for b in range(6):
-            dma(T.TI[:, 32 * b + 16 * e:32 * b + 16 * e + 16], T.ctl[e::2, 512 * b:512 * b + 512], 8, w=[("TI", 32 * b + 16 * e, 32 * b + 16 * e + 16)], q="S", name="ld list")
-    for c in range(2):
-        dma(T.XX[:, 1536 * c:1536 * c + 1536], T.sha[:, 1536 * c:1536 * c + 1536], 393, w=[("XX", 1536 * c, 1536 * c + 1536)], q="S", name="ld sha")
-    cpv(T.CF[:], T.CI[:], 192, r=[W("CI")], w=[W("CF")], name="CF")
-    cpv(T.HL0[:, 0:192], T.CF[:], 192, r=[W("CF")], w=[("HL0", 0, 192)])
-    tt(T.HL0[:, 192:384], T.CF[:], T.HL0[:, 0:192], OP.subtract, 192, r=[W("CF"), ("HL0", 0, 192)], w=[("HL0", 192, 384)])
-    me = T.cores[rank]
+    def swap(buf, rows, a, n, kb, key, r, w, name):
+        dma(buf[rows(1), a - HV:a], buf[rows(0), a:a + HV], kb, key, r=r, w=[w[0]], name=name)
+        dma(buf[rows(0), a + HV:a + V_], buf[rows(1), a:a + HV], kb, key, r=r, w=[w[1]], name=name, q=n)
+
+    dma(T.CI[:], T.ctl[:], 98, "ctl", w=[W("CI")], name="ld ctl")
+    for h in sets():
+        g4 = slice(64 * h, 64 * h + 64)
+        for hh, pp in enumerate((LO, UP)):
+            if h == 0: dma(T.OI[pp, :], T.hol[g4, HV * hh:HV * hh + HV], 393, "hol0", w=[("OI", hh, hh + 1)], name="ld hol0")
+            dma(T["XX%d" % h][pp, HV * (1 - hh):HV * (1 - hh) + V_], T.sha[g4, :], 393, "sha%d" % h, w=[("X%d" % h, hh, hh + 1)], name="ld sha%d" % h)
+            for e in range(2 if CO else 0):
+                dma(T.TI[pp, h, :, e], T.ctl[4 * h + e:4 * h + 4:2, HV * hh:HV * hh + HV], 12, "list%d" % h, w=[("TI%d" % h, 2 * hh + e, 2 * hh + e + 1)], q="S", name="ld list")
+    cpv(T.CF[:], T.CI[:], 192, r=[W("CI")], w=[W("CF")], name="send0")
+    cpv(T.HL0[:, 0:192], T.CF[:], 192, r=[W("CF")], w=[("HL0", 0, 192)], name="send0")
+    tt(T.HL0[:, 192:384], T.CF[:], T.HL0[:, 0:192], OP.subtract, 192, r=[W("CF"), ("HL0", 0, 192)], w=[("HL0", 192, 384)], name="send0")
     first = T.cores[(rank - D_OF[0]) % NR]
     rest = [T.cores[(rank - d) % NR] for d in (1, 2, 3) if (rank - d) % NR != (rank - D_OF[0]) % NR]
     lands = "L0_%d" % rank
-    s1 = send([first], T.HL0[:], T[lands][:], "ar0_%d" % rank, [W("HL0")], 98, "send0")
-    s2 = send(rest, T.HL0[:], T[lands][:], "ar0_%d" % rank, [W("HL0")], 196, "send0b")
+    s1 = send([first], T.HL0[:], T[lands][:], "ar0_0_%d" % rank, [W("HL0")], "send0")
+    s2 = send(rest, T.HL0[:], T[lands][:], "ar0_0_%d" % rank, [W("HL0")], "send0b")
     gop(lambda g: g.iota(T.pi[:], [[1, 1]], 0, 1), 1, w=[W("pi")])
-    gop(lambda g: g.iota(T.ci[:], [[1, 256]], 0, 0, allow_small_or_imprecise_dtypes=True), 256, w=[W("ci")])
-    gop(lambda g: g.iota(T.cg[:], [[1, 16], [0, 16]], 0, 0, allow_small_or_imprecise_dtypes=True), 256, w=[W("cg")])
-    gop(lambda g: g.iota(T.cq[:], [[0, 16], [1, 16]], 0, 0, allow_small_or_imprecise_dtypes=True), 256, w=[W("cq")])
-    gop(lambda g: g.iota(T.DL[:], [[16, 16]], V_, 0, allow_small_or_imprecise_dtypes=True), 16, w=[W("DL")])
-    for t in range(RO):
-        gop(lambda g, t=t: g.iota(T.VR[:, t], [[12, 256]], t, 0, allow_small_or_imprecise_dtypes=True), 256, w=[W("VR%d" % t)])
+    iota(T.ci[:], [[1, 128]], 0, 128, [W("ci")])
+    iota(T.cg[:], [[1, 8], [0, 16]], 0, 128, [W("cg")])
+    iota(T.cq[:], [[0, 8], [1, 16]], 0, 128, [W("cq")])
+    iota(T.c2[:], [[1, 8], [0, 2]], 0, 16, [W("c2")])
+    Wq = lambda k: T.wq[:, k:k + 1]
+    wq = lambda k: ("wq", k, k + 1)
+    OFF, OFF1, OFFZ, P64 = range(40, 44)
+    late = [iota(T.HH[:], [[HV, 2], [0, 4]], 0, 8, [W("HH")]), iota(T.c3[:], [[-128, 2], [0, 64]], 0, 128, [W("c3")]), iota(T.VL[:], [[1, 4], [0, 32], [12, 4]], 0, 512, [W("VL")]),
+            iota(T.VC[:, 0:4], [[-1, 4]], MID, 4, [("VC", 0, 4)], -12), iota(T.VC[:, 4:8], [[1, 4]], MID, 4, [("VC", 4, 8)], 12), iota(T.VC[:, 8:9], [[1, 1]], V_ + 1 - int(BIG) - 17 * int(CEN), 1, [("VC", 8, 9)], 1)]
+    for hh, pp in enumerate((LO, UP)):
+        hw = lambda n: [(n, hh, hh + 1)]
+        G["up"] = hh
+        iota(T.wq[pp, OFF:OFF + 2], [[-1, 2]], HV * (1 - hh), 2, [("wq", OFF, OFF + 2)])
+        late += [iota(T.wq[pp, OFFZ:OFFZ + 1], [[0, 1]], HV * (1 - hh) + 65535 + 16 * int(CEN), 1, [wq(OFFZ)]), iota(T.wq[pp, P64:P64 + 1], [[0, 1]], 64 * (1 - hh), 1, [wq(P64)], 1),
+                 iota(T.SPL[pp, :], [[128 - 256 * hh, 2], [16, 8]], V_ + 1 - 65536 - 16 * int(CEN) + 128 * hh, 16, hw("SPL")), iota(X("VH")[pp], [[48, 32], [0, 4]], HV * (hh - 1), 128, hw("VH")),
+                 iota(T.VB[pp, :], [[-1, 4], [-192, 8]], -HV * hh, 32, hw("VB")), iota(T.VR[pp], [[1, 4], [12, 128]], HV * hh, 512, hw("VR")), iota(X("LR")[pp], [[1, 128]], 128 * hh, 128, hw("LR")),
+                 iota(X("LRx")[pp], [[1 - hh, 128]], (128, -4096)[hh], 128, hw("LRx")), iota(X("KM")[pp], [[0, 128]], (0 if GS else WW) + MID + HV * (1 - hh), 128, hw("KM"))]
+    G["up"] = 0
+    for nmx, v in (("ONE", 1), ("KH", MID + 12288), ("KL", MID - 12288)): late.append(iota(X(nmx), [[0, 128]], v, 128, [W(nmx)]))
+    late.append(iota(X("K1"), [[0, 8], [-1, 16]], 15, 128, [W("K1")]))
+    late.append(iota(X("K2"), [[0, 8], [-1, 16]], 31, 128, [W("K2")]))
+    for h in sets():
+        O = T["O%d" % h]
+        fill(T["WC%d" % h][:], -MID, V_, [W("WC%d" % h)])
+        for j, (pp, a) in enumerate(((UP, 0), (LO, V_)) if CO else ()): fill(T["CC%d" % h][pp, a:a + HV], -MID, HV, [("CC%d" % h, 10 + j, 11 + j)])
+        for j, (pp, a) in enumerate(((LO, WW), (UP, V_))):
+            G["up"] = j
+            late.append(iota(O[pp, a:a + PAD], [[0, PAD]], 0, PAD, [("O%d" % h, 3 + j, 4 + j)]))
+        G["up"] = 0
+        for s in range(0 if h else 7): late.append(iota(T.PQ[:, :, s], [[0, 320]], 0, 320, [("PQ", s, s + 1)]))
+        late.append(iota(T.HLz[:, 4 * h:4 * h + 4], [[0, 512]], 0, 512, [("HLz", 4 * h, 4 * h + 4)]))
+        late.append(iota(B("OC", h)[:, 128:256], [[0, 128]], 0, 128, [("OC%d" % h, 1, 2)]))
+        for u in range(0, 8, 4): late.append(iota(B("DE", h)[:, u:u + 4], [[0, 1024]], 0, 1024, [("DE%d" % h, u, u + 4)]))
+    for i in late: G["ops"][i]["deps"][s2] = False
 
-    def vt(t):
-        for c in range(4):
-            i = gop(lambda g, c=c: g.iota(T["VT%d" % (t % 2)][:, 1024 * c:1024 * c + 1024], [[12, 64], [0, 16]], t + 768 * c, 0, allow_small_or_imprecise_dtypes=True), 1024, w=[("VT%d" % (t % 2), 1024 * c, 1024 * c + 1024)], name="VT")
-            G["ops"][i]["deps"][s2] = False
-    vt(0)
-    vt(1)
-    for t in range(RO):
-        gop(lambda g, t=t: g.iota(T.VH[:, t], [[48, 64], [0, 4]], 0, 0, allow_small_or_imprecise_dtypes=True), 256, w=[W("VH%d" % t)])
-        gop(lambda g, t=t: g.iota(T.VL[:, t], [[0, 64], [12, 4]], t, 0, allow_small_or_imprecise_dtypes=True), 256, w=[W("VL%d" % t)])
-    vop(lambda v: v.memset(T.WC1[:], 0.0), V_, w=[W("WC1")], two=0.5)
-    for d in (2, 3):
-        i = gop(lambda g, d=d: g.iota(T["WC%d" % d][:], [[0, V_]], 0, 0, allow_small_or_imprecise_dtypes=True), V_, w=[W("WC%d" % d)])
-        G["ops"][i]["deps"][s2] = False
-    for d in (1, 2, 3):
+    for d in (1, 2, 3): arrive((rank + d) % NR, 0, 0, s1 if d == D_OF[0] else s2, 98 if d == D_OF[0] else 196)
+
+    def flat(d, h):
         s = (rank + d) % NR
-        arrive(s, 0, s1 if d == D_OF[0] else s2, 98 if d == D_OF[0] else 196)
-        for x in (0, 1):
-            dma(T["WC%d" % d][x:128:16, :], T["L0_%d" % s][:, 192 * x:192 * x + 192], 49, r=[W("L0_%d" % s)], w=[W("WC%d" % d)] if x == 0 else [("WC%d" % d, 0, 1 << 19)], name="flat")
-            if x == 0: G["wr"]["WC%d" % d] = [y for y in G["wr"]["WC%d" % d]]
-    def sh(o, k): ts(T.ti[:, o:o + 1], T.pi[:], k, OP.arith_shift_right, 1, r=[W("pi")], w=[("ti", o, o + 1)])
-    def an(o, src, k, rr): ts(T.ti[:, o:o + 1], src, k, OP.bitwise_and, 1, r=rr, w=[("ti", o, o + 1)])
-    sh(1, 4); an(2, T.pi[:], 15, [W("pi")])
+        src, sr = (T["L0_%d" % s], W("L0_0_%d" % s)) if d else (T.HL0, W("HL0"))
+        for hh in H:
+            for x in H:
+                k = 4 * d + 2 * hh + x
+                dma(T["WC%d" % h][64 * hh + d + 8 * x:64 * hh + 64:16, :], src[64 * h:64 * h + 64, 192 * x:192 * x + 192], 25, "flat%d%d" % (min(d, 2), h), r=[sr], w=[("WC%d" % h, k, k + 1)], name="flat")
+    for h in sets(): flat(D_OF[0] if CO else 0, h)
+    def an(o, src, k, op, rr): ts(T.ti[:, o:o + 1], src, k, op, 1, r=rr, w=[("ti", o, o + 1)])
     cpv(T.ti[:, 0:1], T.pi[:], 1, r=[W("pi")], w=[("ti", 0, 1)])
-    an(8, T.pi[:], 3, [W("pi")])
-    ts(T.ti[:, 9:10], T.ti[:, 8:9], 12, OP.mult, 1, r=[("ti", 8, 9)], w=[("ti", 9, 10)])
-    for t in range(RO):
-        ts(T.ti[:, 10 + t:11 + t], T.ti[:, 9:10], t, OP.add, 1, r=[("ti", 9, 10)], w=[("ti", 10 + t, 11 + t)])
-        an(3 + t, T.ti[:, 10 + t:11 + t], 15, [("ti", 10 + t, 11 + t)])
-    ts(T.ti[:, 14:15], T.pi[:], 12, OP.mult, 1, r=[W("pi")], w=[("ti", 14, 15)])
-    ts(T.ti[:, 7:8], T.ti[:, 14:15], 4, OP.arith_shift_right, 1, r=[("ti", 14, 15)], w=[("ti", 7, 8)])
-    ts(T.ti[:, 15:16], T.ti[:, 1:2], 8, OP.add, 1, r=[("ti", 1, 2)], w=[("ti", 15, 16)])
-    cpv(T.tf[:], T.ti[:], 16, r=[W("ti")], w=[W("tf")])
+    for o, k, op in ((1, 4, OP.arith_shift_right), (2, 15, OP.bitwise_and), (3, 5, OP.arith_shift_right), (5, 6, OP.arith_shift_right), (6, 7, OP.bitwise_and)): an(o, T.pi[:], k, op, [W("pi")])
+    an(4, T.ti[:, 1:2], 1, OP.bitwise_and, [("ti", 1, 2)])
+    cpv(T.tf[:, 0:7], T.ti[:, 0:7], 7, r=[W("ti")], w=[W("tf")])
     F = lambda k: T.tf[:, k:k + 1]
-    tfr = [W("tf")]
-    for h in H:
-        for t in range(RO):
-            k = 2 * t + h
-            ts(T.VC[:, k:k + 1], F(0), 12.0, OP.mult, 1, r=tfr, w=[("VC", k, k + 1)], s2=float(12 * 128 * h + t), op1=OP.add)
-            ts(T.VC[:, 8 + k:9 + k], F(0), -12.0, OP.mult, 1, r=tfr, w=[("VC", 8 + k, 9 + k)], s2=float(-12 * 128 * h - t), op1=OP.add)
-    ts(T.DL[:], T.DL[:], F(2), OP.add, 16, r=tfr + [W("DL")], w=[W("DL")])
-    ci = T.ci[:, 0:128]; rc = tfr + [W("ci")]; rq = tfr + [W("cq")]; rg = tfr + [W("cg")]
-    ts(T.If[:], ci, F(0), OP.is_equal, 128, r=rc, w=[W("If")])
-    ts(T.BOf[:], T.cg[:, 0:128], F(1), OP.is_equal, 128, r=rg, w=[W("BOf")])
-    for src, nmx, s in (("If", "Ib", 1.0), ("If", "Im", -1.0), ("If", "Im16", -16.0), ("If", "I16", 16.0), ("If", "I3072", 3072.0), ("BOf", "BOb", 1.0), ("BOf", "L4", 4.0), ("BOf", "BN", -128.0)):
-        act(T[nmx][:], T[src][:], 128, COPY, scale=s, r=[W(src)], w=[W(nmx)])
-    ts(T.QM[:], T.cq[:], F(2), OP.is_equal, 256, r=rq, w=[W("QM")])
-    ts(T.NF[:], T.cq[:, 0:128], 0.0, OP.not_equal, 128, r=[W("cq")], w=[W("NF")])
-    for nmx, s in (("S1", 1.0), ("S16", 16.0), ("S32", 32.0)):
+    tfr = [W("tf")]; rc = tfr + [W("ci")]; rq = tfr + [W("cq")]; rg = tfr + [W("cg")]
+
+    def col(k, src, a, op0, b=None, op1=None, r=()): ts(Wq(k), src, a, op0, 1, r=tfr + list(r), w=[wq(k)], s2=b, op1=op1)
+    GM4 = 24
+    col(GM4, F(1), -4.0, OP.add)
+    ts(T.VC[:, 0:8], T.VC[:, 0:8], 0.5, OP.mult, 8, r=[("VC", 0, 8)], w=[("VC", 0, 8)])
+    ts(T.SPL[:], T.SPL[:], F(2), OP.add, 16, r=tfr + [W("SPL")], w=[W("SPL")])
+    ts(X("If"), T.ci[:], F(0), OP.is_equal, 128, r=rc, w=[W("If")])
+    ts(X("SW"), T.ci[:], Wq(P64), OP.is_equal, 128, r=[W("ci"), wq(P64)], w=[W("SW")])
+    ts(X("BOf"), T.cg[:], F(1), OP.is_equal, 128, r=rg, w=[W("BOf")])
+    ts(X("BOx"), T.cg[:], Wq(GM4), OP.is_equal, 128, r=[W("cg"), wq(GM4)], w=[W("BOx")], s2=-1.0, op1=OP.mult)
+    ts(X("BOy"), T.cg[:], -4.0, OP.add, 128, r=rg, w=[W("BOy")], s2=F(1), op1=OP.is_equal, two=0.5)
+    ts(X("QM"), T.cq[:], F(2), OP.is_equal, 128, r=rq, w=[W("QM")])
+    ts(X("NF"), T.cq[:], 0.0, OP.not_equal, 128, r=[W("cq")], w=[W("NF")])
+    for src, nmx, s, o in (("If", "Ib", 1, 0), ("If", "Im", -1, 0), ("If", "I16", 16, 0), ("If", "I256", 256, 0), ("If", "ImW", -WW, 0), ("If", "Im16", -16, 0), ("If", "Im256", -256, 0), ("BOf", "BOm512", -512, 0), ("If", "IB", BIG, 0), ("If", "ImB", -BIG, 0), ("If", "Ib2", BIG / 2, 0),
+                           ("If", "Imb2", -BIG / 2, 0), ("If", "Imax", -2.0 ** 23, 0), ("BOf", "BOb", 1, 0),
+                           ("BOf", "BOm", -1, 0), ("QM", "QB", BIG, 0), ("QM", "QC", BIG, -BIG)):
+        flex(X(nmx), X(src), 128, r=[W(src)], w=[W(nmx)], bias=float(o), scale=float(s), only="S")
+    tt(X("QmB"), T.c3[:], X("QB"), OP.subtract, 128, r=[W("c3"), W("QB")], w=[W("QmB")])
+    for src, nmx, s in (("If", "Ih", 1.0), ("If", "Imh", -1.0), ("BOf", "BOh", 1.0)): ts(X(nmx), X(src), s, OP.mult, 128, r=[W(src)], w=[W(nmx)])
+    for nmx, s in (("S1", 1.0), ("S32", 32.0), ("Sm16", -16.0), ("U8b", BIG / 2), ("S1h", 1.0)):
         ts(T[nmx][:], T.ci[:, 0:8], F(1), OP.is_equal, 8, r=rc, w=[W(nmx)], s2=s, op1=OP.mult)
-    ts(T.wq[:, 0:1], F(2), 1.0, OP.is_le, 1, r=tfr, w=[("wq", 0, 1)])
-    ts(T.SHL[:], T.ci[:, 0:8], F(1), OP.is_equal, 8, r=rc + [("wq", 0, 1)], w=[W("SHL")], s2=T.wq[:, 0:1], op1=OP.mult)
-    ts(T.U8[:], T.ci[:, 0:8], F(1), OP.is_equal, 8, r=rc, w=[W("U8")])
-    ts(T.U4[:], T.ci[:, 0:96], F(7), OP.is_equal, 96, r=rc, w=[W("U4")])
-    for t in range(RO): ts(T.PM[:, t], T.cq[:, 0:128], F(3 + t), OP.is_equal, 128, r=rq, w=[W("PM%d" % t)])
-    ts(T.K1[:], T.cq[:, 0:128], -1.0, OP.mult, 128, r=[W("cq")], w=[W("K1")], s2=15.0, op1=OP.add)
-    ts(T.K2[:], T.cq[:, 0:128], -1.0, OP.mult, 128, r=[W("cq")], w=[W("K2")], s2=31.0, op1=OP.add)
-    vop(lambda v: v.memset(T.ONE[:], 1.0), 128, w=[W("ONE")])
-    for q in range(16): vop(lambda v, q=q: v.memset(T.fz[:, q::16], 2.0 ** -q), 16, w=[W("fz")])
-    tt(T.FS[:], T.fz[:], T.QM[:], OP.mult, 256, r=[W("fz"), W("QM")], w=[W("FS")])
-    vop(lambda v: v.tensor_reduce(T.wq[:, 1:2], T.FS[:, 0:16], AxisListType.X, OP.add), 16, r=[W("FS")], w=[("wq", 1, 2)])
-    ts(T.LW[:], T.BOf[:], T.wq[:, 1:2], OP.mult, 128, r=[W("BOf"), ("wq", 1, 2)], w=[W("LW")])
-    ts(T.nlq[:], T.QM[:], 1024.0, OP.mult, 256, r=[W("QM")], w=[W("nlq")], s2=-1024.0, op1=OP.add)
-    act(T.C128[:], T.QM[:], 256, COPY, scale=128.0, r=[W("QM")], w=[W("C128")])
-    ts(T.DL[:], T.DL[:], 1.0, OP.add, 16, r=[W("DL")], w=[W("DL")])
-    ts(T.ZQ[:], T.FS[:], -2.0, OP.mult, 256, r=[W("FS")], w=[W("ZQ")])
-    tt(T.DC[:], T.nlq[:], T.ZQ[:], OP.add, 256, r=[W("nlq"), W("ZQ")], w=[W("DC")])
-    vop(lambda v: v.memset(T.O[:, V_:V_ + PAD], 0.0), PAD, w=[("O", V_, V_ + PAD)])
-    for h in H:
-        vop(lambda v, h=h: v.memset(B("BZ", h)[:], 0.0), 128, w=[W("BZ%d" % h)])
-        vop(lambda v, h=h: v.memset(B("HLz", h)[:], 0.0), 128, w=[W("HLz%d" % h)])
-    vop(lambda v: v.memset(T.Zc[:], 9.0), 1, w=[W("Zc")])
-    for t in range(RO):
-        mm(T.pE[:, 0:96], T.PM[:, t], T.U4[:], True, True, "pE", 96, r=[W("PM%d" % t), W("U4")], f32=True)
-        ts(T.KP[:, t], T.pE[:, 0:96], -1.0, OP.mult, 96, w=[W("KP%d" % t)], pr=["pE"], s2=1.0, op1=OP.add)
-    cpv(T.TF[:], T.TI[:], 192, r=[W("TI")], w=[W("TF")])
-    vop(lambda v: v.transpose(T.CLf[:], T.TF[:]), 192, r=[W("TF")], w=[W("CLf")])
-    cpv(T.CLu[:], T.CLf[:], 192, r=[W("CLf")], w=[W("CLu")])
-    for c in range(4):
-        cpv(T.O[:, 768 * c:768 * c + 768], T.OI[:, 768 * c:768 * c + 768], 768, r=[("OI", 768 * c, 768 * c + 768)], w=[("O", 768 * c, 768 * c + 768)], name="O f32")
-    for c in range(2):
-        a, z = 1536 * c, 1536 * c + 1536
-        add(G, {"V": (vc(1536, 0.5), vc(1536, 0.5)), "S": (sc(1536), sc(1536))},
-            lambda Q, e, a=a, z=z: Q["V"].tensor_scalar(T.XX[:, V_ + a:V_ + z], T.XX[:, a:z], -1.0, None, OP.mult) if e == "V" else Q["S"].activation(T.XX[:, V_ + a:V_ + z], T.XX[:, a:z], COPY, scale=-1.0),
-            [("XX", a, z)], [("XX", V_ + a, V_ + z)], name="-X")
+    for j in range(XR): ts(T.U8[:, j], T.ci[:, 0:8], F(1), OP.is_equal, 8, r=rc, w=[("U8", j, j + 1)])
+    col(0, F(2), 7.0, OP.is_equal)
+    ts(T.wq[:, 26:30], T.ci[:, 0:4], F(6), OP.is_equal, 4, r=rc + [wq(0)], w=[("wq", 26, 30)], s2=Wq(0), op1=OP.add)
+    ts(T.wq[:, 32:36], T.ci[:, 0:4], F(6), OP.not_equal, 4, r=rc, w=[("wq", 32, 36)])
+    col(1, F(6), 0.0, OP.is_equal); col(2, F(2), 6.0, OP.is_equal); col(11, F(1), 16.0, OP.mult, 6.0, OP.add)
+    ts(X("BO6"), T.ci[:], Wq(11), OP.is_equal, 128, r=[W("ci"), wq(11)], w=[W("BO6")], two=0.5)
+    for a, c in ((0, 0), (4, 8), (8, 4)): ts(T.SY[:, a:a + 4], T.ci[:, c:c + 4], F(1), OP.is_equal, 4, r=rc + [wq(1)], w=[("SY", a, a + 4)], s2=Wq(1), op1=OP.mult)
+    for k in range(4):
+        if k:
+            ts(T.SHL2[:, k, :, 0:2], T.c2[:], F(1), OP.is_equal, 16, r=tfr + [W("c2"), wq(26 + k)], w=[("SHL2", 2 * k, 2 * k + 1)], s2=Wq(26 + k), op1=OP.mult)
+            ts(T.SHL2[:, k, :, 2], T.ci[:, 0:8], F(1), OP.is_equal, 8, r=rc + [wq(2)], w=[("SHL2", 2 * k + 1, 2 * k + 2)], s2=Wq(2), op1=OP.mult)
+        act(X("KW%d" % k), X("If"), 128, IDENT, scale=Wq(32 + k), r=[W("If"), wq(32 + k)], w=[W("KW%d" % k)])
+    for j in (0, 2): ts(T.S12[:, :, j:j + 2], T.c2[:], F(1), OP.is_equal, 16, r=tfr + [W("c2")], w=[("S12", j, j + 2)])
+    ts(X("TRI"), T.cq[:], F(2), OP.is_le, 128, r=rq, w=[W("TRI")], s2=BIG, op1=OP.mult)
+    col(3, F(3), 32.0, OP.mult); col(4, F(2), 2.0, OP.mult, Wq(3), OP.add, r=[wq(3)])
+    for e2 in range(2 if GS else 0):
+        col(5 + e2, F(4), float(e2), OP.not_equal, 1000.0, OP.mult)
+        col(7 + e2, Wq(5 + e2), Wq(4), OP.add, r=[("wq", 4, 7)])
+        for e in range(2):
+            ts(X("PA%d" % (2 * e2 + e)), T.ci[:], float(e), OP.subtract, 128, r=[W("ci"), wq(7 + e2)], w=[W("PA%d" % (2 * e2 + e))], s2=Wq(7 + e2), op1=OP.is_equal, two=0.5)
+            ts(X("PM%d" % (2 * e2 + e)), X("PA%d" % (2 * e2 + e)), float(WW), OP.mult, 128, r=[W("PA%d" % (2 * e2 + e))], w=[W("PM%d" % (2 * e2 + e))], two=0.5)
+    if CO:
+        ts(T.NE[:], T.ci[:, 0:16], F(2), OP.not_equal, 16, r=rc, w=[W("NE")])
+        tt(T.NE[:, 0:4], T.NE[:, 0:4], T.NE[:, 12:16], OP.mult, 4, r=[W("NE")], w=[W("NE")])
+        for t in range(RO):
+            for o in range(3):
+                k = (0, 8, 4)[o] + t
+                act(T.KD[:, 3 * t + o], X("If"), 128, IDENT, scale=T.NE[:, k:k + 1], r=[W("If"), W("NE")], w=[("KD", 3 * t + o, 3 * t + o + 1)])
+    col(9, F(6), 0.0, OP.not_equal, 1000.0, OP.mult); col(10, F(1), 16.0, OP.mult, Wq(9), OP.add, r=[wq(9)])
+    for k in range(16): ts(T.SEL[:, k], T.ci[:], float(k), OP.subtract, 128, r=[W("ci"), wq(10)], w=[("SEL", k, k + 1)], s2=Wq(10), op1=OP.is_equal, two=0.5)
+    vop(lambda v: v.memset(T.Zb[:], -1.0), 1, w=[W("Zb")])
 
-    for t in range(RO):
-        d = D_OF[t]; last = t == RO - 1
-        wc = "WC%d" % d
-        VT, VR = T["VT%d" % (t % 2)], T.VR[:, t]
-        XR = [("XX", 0, V_)]
-        hs = lambda h: slice(1536 * h + t, 1536 * h + 1536, 12)
-        oreg = lambda h: ("O", 1536 * h, 1536 * h + 1536)
-        S = lambda h: slice(128 * h, 128 * h + 128)
-        for h in H:
-            src = T.OI if t == 0 else T.O
-            cpv(T.LA[:, S(h)], src[:, hs(h)], 128, r=[("OI" if t == 0 else "O", 1536 * h, 1536 * h + 1536)], w=[("LA", 128 * h, 128 * h + 128)], name="LA")
-        for c in range(4):
-            flex(T.CC[:, 768 * c:768 * c + 768], T[wc][:].indirect(T.CLu[:, 48 * c:48 * c + 48]), 768, r=[W(wc), W("CLu")], w=[("CC", 768 * c, 768 * c + 768)], cyc=GCY, name="compose%d" % c)
-        la = lambda h: ("LA", 128 * h, 128 * h + 128)
-        pieces = lambda n: [(2048 // n * p, 2048 // n * (p + 1), 128 // n * p, 128 // n * (p + 1)) for p in range(n)]
-        for h in H:
-            for a, z, c, e in pieces(NPC): flex(B("XK", h)[:, a:z], T.XX[:, 0:V_].indirect(T.LA[:, 128 * h + c:128 * h + e]), z - a, r=XR + [la(h)], w=[("XK%d" % h, a, z)], cyc=GCY, name="XK%d" % h)
-        for h in H:
-            for a, z, c, e in pieces(NPC): flex(B("CG", h)[:, a:z], T.CC[:].indirect(T.LA[:, 128 * h + c:128 * h + e]), z - a, r=[W("CC"), la(h)], w=[("CG%d" % h, a, z)], cyc=GCY, name="CG%d" % h)
-        for h in H:
-            for a, z, c, e in pieces(NPS):
-                vop(lambda v, h=h, VT=VT, a=a, z=z, c=c, e=e: v.tensor_tensor(B("ST", h)[:, a:z], T.O[:, 0:V_].indirect(T.LA[:, 128 * h + c:128 * h + e]), VT[:, 2048 * h + a:2048 * h + z], OP.is_equal), z - a,
-                    r=[("O", 0, V_), la(h), ("VT%d" % (t % 2), 2048 * h + a, 2048 * h + z)], w=[("ST%d" % h, a, z)], two=GCY, name="ST")
-        if t + 2 < RO: vt(t + 2)
-        for h in H:
-            mm(P("C", h)[:, :, 0:16], T.Ib[:], T.XX[:, hs(h)], True, True, "pC%d" % h, 128, r=XR + [W("Ib")])
-        for h in H:
-            A = P("A", h); bk = "pA%d" % h
-            for k in range(16):
-                mm(A[:, :, k], B("CG", h)[:, k::16], T.SHL[:], True, True, bk, 8, r=[W("CG%d" % h), W("SHL")], name="cL")
-            ext(A, bk)
-            flex(B("cS", h)[:], A[:, :, 0:16], 128, w=[W("cS%d" % h)], pr=[bk], name="cS")
-            for s in range(1, 9):
-                tt(B("E", h)[:, s - 1], B("cS", h)[:], A[:, :, s:s + 16], OP.not_equal if h in PRS else OP.is_equal, 128, r=[W("cS%d" % h)], w=[("E%d" % h, s - 1, s)], pr=[bk], name="E")
-        for h in H:
-            if h in MXS: continue
-            for k in range(16):
-                mm(T.pE[:, 128 * h + k:128 * h + 128:16], B("XK", h)[:, k::16], T.S1[:], True, True, "pE", 8, r=[W("XK%d" % h), W("S1")], name="SX")
-            act(B("SX", h)[:], T.pE[:, S(h)], 128, w=[W("SX%d" % h)], pr=["pE"], name="SXc")
-        for h in H:
-            Bk = P("B", h); bk = "pB%d" % h
-            for k in range(16):
-                tt(B("MN", h)[:, S(k)], B("XK", h)[:, k::16], P("C", h)[:, :, 0:16], OP.min, 128, r=[W("XK%d" % h)], w=[("MN%d" % h, 128 * k, 128 * k + 128)], pr=["pC%d" % h], name="MN")
-            for k in range(16):
-                mm(Bk[:, :, k], B("MN", h)[:, S(k)], T.S1[:], True, True, bk, 8, r=[("MN%d" % h, 128 * k, 128 * k + 128), W("S1")], name="mL")
-            ext(Bk, bk)
-            mS = B("mS", h)
-            nx = 24 if h in PRS else 16
-            flex(mS[:, :, 0:nx], Bk[:, :, 0:nx], 8 * nx, w=[W("mS%d" % h)], pr=[bk], name="mS")
-            PRh, Eh = B("PR", h), B("E", h)
-            for c in range(4 if h in PRS else 0):
-                bn = "pE" if c % 2 else bk
-                n = min(4, 15 - 4 * c)
-                for jj in range(n):
-                    j = 4 * c + jj
-                    s = j + 1 if j < 8 else j - 7
-                    o = T.pE[:, S(jj)] if c % 2 else Bk[:, 2 * jj:2 * jj + 2, :]
-                    mm(o, T.Ib[:], mS[:, :, s:s + 16] if j < 8 else mS[:, :, 0:16], True, False, bn, 128, r=[W("mS%d" % h), W("Ib")], name="PRm")
-                    mm(o, T.I256[:], Eh[:, s - 1], False, True, bn, 128, r=[("E%d" % h, s - 1, s), W("I256")], name="PRm")
-                act(PRh[:, 4 * c:4 * c + n], T.pE[:, 0:128 * n] if c % 2 else Bk[:, 0:2 * n, :], 128 * n, ActivationFunctionType.Relu, w=[("PR%d" % h, 4 * c, 4 * c + n)], pr=[bn], name="PRa")
-            for s in range(1, 9 if h not in PRS else 0):
-                tt(PRh[:, s - 1], Eh[:, s - 1], Bk[:, :, s:s + 16], OP.mult, 128, r=[("E%d" % h, s - 1, s)], w=[("PR%d" % h, s - 1, s)], pr=[bk], name="PR")
-            for s in range(1, 8 if h not in PRS else 0):
-                tt(PRh[:, 7 + s], Eh[:, s - 1], Bk[:, :, 0:16], OP.mult, 128, r=[("E%d" % h, s - 1, s)], w=[("PR%d" % h, 7 + s, 8 + s)], pr=[bk], name="PR")
-            C = P("C", h); ck = "pC%d" % h
-            mm(C[:, :, 16:32], T.Ib[:], T.K1[:], True, False, ck, 128, r=[W("Ib"), W("K1")], name="key")
-            mm(C[:, :, 16:32], T.I16[:], mS[:, :, 0:16], False, False, ck, 128, r=[W("I16"), W("mS%d" % h)], name="key")
-            for s in range(1, 9):
-                mm(C[:, :, 16:32], T.I16[:], PRh[:, s - 1], False, False, ck, 128, r=[("PR%d" % h, s - 1, s)], name="key")
-            for s in range(1, 8):
-                mm(C[:, :, 16 + s:32], T.I16[:], PRh[:, 7 + s, :, 0:16 - s], False, False, ck, 128 - 8 * s, r=[("PR%d" % h, 7 + s, 8 + s)], name="key")
-                mm(C[:, :, 16:16 + s], T.I16[:], PRh[:, 7 + s, :, 16 - s:16], False, s == 7, ck, 8 * s, r=[("PR%d" % h, 7 + s, 8 + s)], name="key")
+    for h in sets():
+        O, XX = T["O%d" % h], T["XX%d" % h]
+        for hh, pp in enumerate((LO, UP) if h else ()): dma(T.OI[pp, :], T.hol[64:128, HV * hh:HV * hh + HV], 393, "hol1", w=[("OI", hh, hh + 1)], name="ld hol1")
+        cpv(O[:, HV:V_], T.OI[:], HV, r=[W("OI")], w=[("O%d" % h, 0, 1)], name="O f32")
+        swap(O, lambda hh: (LO, UP)[hh], HV, "Y", 393, "ox%d" % h, [("O%d" % h, 0, 1)], [("O%d" % h, 1, 2), ("O%d" % h, 2, 3)], "Ox")
+        flex(XX[:, WW + HV:WW + V_], XX[:, HV:V_], HV, r=[("X%d" % h, 0, 2)], w=[("X%d" % h, 6, 7)], two=0.5, bias=512.0 if GS else 0.0, scale=512.0 if GS else -1.0, name="X2")
+        if CO:
+            cpv(B("TF", h), B("TI", h), 96, r=[W("TI%d" % h)], w=[W("TF%d" % h)])
+            for b in range(3): vop(lambda v, h=h, b=b: v.transpose(B("CLf", h)[:, b::3], B("TF", h)[:, b]), 32, r=[W("TF%d" % h)], w=[("CLf%d" % h, b, b + 1)])
+            cpv(B("CLu", h), B("CLf", h), 96, r=[W("CLf%d" % h)], w=[W("CLu%d" % h)])
+        swap(XX, lambda hh: (LO, UP)[hh], WW + HV, "Y", 196, "xx%d" % h, [("X%d" % h, 6, 7)], [("X%d" % h, 5, 6), ("X%d" % h, 7, 8)], "Xx")
 
-        def spread(h, src, sreg, fin, freg, floor=None, bank=None):
-            bz = B("BZ", h); zr = [W("BZ%d" % h)]
-            if floor is None: cpv(bz[:, 0::16], src[:, 15::16], 8, r=[sreg], w=zr, name="sp")
-            else: ts(bz[:, 0::16], src[:, 15::16], floor, OP.max, 8, r=[sreg], w=zr, name="sp")
-            vop(lambda v: v.tensor_tensor_scan(fin, T.NF[:], bz[:], 0.0, OP.mult, OP.add), 128, r=zr + [W("NF")], w=[freg] if freg else [], pw=[bank] if bank else [], name="sp")
+    def renew(t, h, d):
+        WC, D, dk, k = T["WC%d" % h], P("D", h), "pD%d" % h, 4 * h + d
+        s = (rank + d) % NR
+        src, sr = (LU(t + 1, h, s), W("L%d_%d_%d" % (t + 1, h, s))) if d else (T.SND[:, 2 * t + h], W("SND%d" % (2 * t + h)))
+        flex(T.HLz[:, k, :, :, d::8], src, 16, r=[sr], w=[("HLz", k, k + 1)], name="HLz")
+        for j in H:
+            mm(D[:, 2 + j], X("KW%d" % d), WC[:, HV * j + t:HV * j + HV:12], True, False, dk, 128, r=[W("WC%d" % h), W("KW%d" % d)], name="HLr")
+            for pp in (LO, UP): mm(D[pp, 2 + j], T.HLz[:, k, j], X("Ib"), False, True, dk, 128, r=[("HLz", k, k + 1)], name="HLr")
+        flex(WC[:, t:V_:12], D[:, 2:4], 256, w=[W("WC%d" % h)], pr=[dk], name="WCu")
 
-        for h in H:
-            A, C = P("A", h), P("C", h); ak, ck = "pA%d" % h, "pC%d" % h
-            x = lambda n: W(n + str(h))
-            flex(B("kS", h)[:], C[:, :, 16:32], 128, w=[x("kS")], pr=[ck], name="kS")
-            vop(lambda v, h=h: v.tensor_tensor_scan(B("RM", h)[:], T.NF[:], B("kS", h)[:], 0.0, OP.mult, OP.max), 128, r=[W("NF"), x("kS")], w=[x("RM")], name="RM")
-            spread(h, B("RM", h), x("RM"), B("BR", h), x("BR"))
-            tt(B("oh", h)[:], B("BR", h)[:], C[:, :, 16:32], OP.is_equal, 128, r=[x("BR")], w=[x("oh")], pr=[ck], name="oh")
-            tt(B("w", h)[:], B("oh", h)[:], A[:, :, 0:16], OP.mult, 128, r=[x("oh")], w=[x("w")], pr=[ak], name="w")
-            vop(lambda v, h=h: v.tensor_tensor_scan(B("RM", h)[:], T.NF[:], B("w", h)[:], 0.0, OP.mult, OP.add), 128, r=[W("NF"), x("w")], w=[x("RM")], name="RW")
-            spread(h, B("RM", h), x("RM"), B("brep", h), x("brep"))
-            tt(B("nm", h)[:], B("brep", h)[:], A[:, :, 0:16], OP.not_equal, 128, r=[x("brep")], w=[x("nm")], pr=[ak], name="nm")
-            mm(C[:, :, 48:64], T.If[:], T.O[:, hs(h)], True, False, ck, 128, r=[oreg(h), W("If")], f32=True, name="LMa")
-            mm(C[:, :, 48:64], B("nm", h)[:], T.I3072[:], False, True, ck, 128, r=[x("nm"), W("I3072")], name="LMn")
-            cpv(T.LM[:, S(h)], C[:, :, 48:64], 128, w=[x("LM")], pr=[ck], name="LM")
-            for a, z, c, e in pieces(NPM): flex(B("XM", h)[:, a:z], T.XX[:].indirect(T.LM[:, 128 * h + c:128 * h + e]), z - a, r=[W("XX"), x("LM")], w=[("XM%d" % h, a, z)], cyc=GCY, name="XM%d" % h)
-            tt(B("BD", h)[:], B("brep", h)[:], T.QM[:, 0:128], OP.mult, 128, r=[x("brep"), W("QM")], w=[x("BD")], name="BD")
-            mm(A[:, :, 56], B("BD", h)[:], T.U8[:], True, True, ak, 8, r=[x("BD"), W("U8")], f32=True, name="LBp")
-            cpv(T.LB[:, 8 * h:8 * h + 8], A[:, :, 56], 8, w=[("LB", 8 * h, 8 * h + 8)], pr=[ak], name="LB")
-            flex(B("XB", h)[:], T.XX[:, 0:V_].indirect(T.LB[:, 8 * h:8 * h + 8]), 128, r=XR + [("LB", 8 * h, 8 * h + 8)], w=[x("XB")], cyc=GCY, name="XB%d" % h)
-            if h not in MXS: mm(C[:, :, 32:48], T.Ib[:], B("XB", h)[:], True, True, ck, 128, r=[x("XB")], name="XBp")
-        for h in H:
-            A, C, Bk = P("A", h), P("C", h), P("B", h); ak, ck, bk = "pA%d" % h, "pC%d" % h, "pB%d" % h
-            x = lambda n: W(n + str(h))
-            mm(A[:, :, 40:56], B("cS", h)[:], T.If[:], True, False, ak, 128, r=[x("cS"), W("If")], f32=True, name="cK")
-            mm(A[:, :, 40:56], T.Im[:], T.VH[:, t, S(h)], False, False, ak, 128, r=[W("Im"), W("VH%d" % t)], name="cK")
-            mm(A[:, :, 40:56], T.Im[:], T.VL[:, t, S(h)], False, True, ak, 128, r=[W("Im"), W("VL%d" % t)], name="cK")
-            act(B("cKv", h)[:], A[:, :, 40:56], 128, w=[x("cKv")], pr=[ak], name="cKv")
-            MX = B("MX", h)
-            if h in MXS:
-                for c in range(4):
-                    bn = ck if c % 2 else "pE"
-                    for kk in range(4):
-                        o = C[:, :, 16 * kk:16 * kk + 16] if c % 2 else T.pE[:, S(kk)]
-                        mm(o, T.Ib[:], B("XK", h)[:, 4 * c + kk::16], True, False, bn, 128, r=[x("XK")], name="DF")
-                        mm(o, T.Im[:], B("XB", h)[:], False, True, bn, 128, r=[x("XB")], name="DF")
-                    act(MX[:, c], C[:] if c % 2 else T.pE[:], 512, ActivationFunctionType.Abs, w=[("MX%d" % h, 4 * c, 4 * c + 4)], pr=[bn], name="MXa")
-            else:
-                for k in range(16):
-                    tt(MX[:, k // 4, 2 * (k % 4):2 * (k % 4) + 2], B("XK", h)[:, k::16], C[:, :, 32:48], OP.max, 128, r=[x("XK")], w=[("MX%d" % h, k, k + 1)], pr=[ck], name="MX")
-            mm(A[:, :, 24:40], T.Ib[:], T.K2[:], True, False, ak, 128, r=[W("Ib"), W("K2")], name="FL")
-            if h not in MXS: mm(A[:, :, 24:40], T.Im16[:], B("SX", h)[:], False, False, ak, 128, r=[W("Im16"), x("SX")], name="FL")
-            for k in range(16):
-                c, kk = divmod(k, 4)
-                mr = [("MX%d" % h, k, k + 1)]
-                if h in MXS:
-                    l = MX[:, c, :, 16 * kk:16 * kk + 16] if c % 2 else MX[:, c, 2 * kk:2 * kk + 2]
-                    mm(A[:, :, 24 + k], l, T.S16[:], False, k == 15, ak, 8, r=mr + [W("S16")], name="FL")
-                else:
-                    mm(A[:, :, 24 + k], MX[:, c, 2 * kk:2 * kk + 2], T.S32[:], False, k == 15, ak, 8, r=mr + [W("S32")], name="FL")
-            for k in range(16):
-                mm(Bk[:, :, 24 + k], B("ST", h)[:, k::16], T.S1[:], True, True, bk, 8, r=[x("ST"), W("S1")], name="SL")
-            tt(B("el", h)[:], B("nm", h)[:], Bk[:, :, 24:40], OP.min, 128, r=[x("nm")], w=[x("el")], pr=[bk], name="el")
-            tt(Bk[:, :, 0:16], B("el", h)[:], A[:, :, 24:40], OP.mult, 128, r=[x("el")], pr=[ak], pw=[bk], name="q1")
-            mm(C[:, :, 0:16], B("brep", h)[:], T.If[:], True, True, ck, 128, r=[x("brep"), W("If")], f32=True, name="bR")
-            act(T.aD[:, S(h)], T.O[:, hs(h)], 128, COPY, bias=1.0, r=[oreg(h)], w=[("aD", 128 * h, 128 * h + 128)], name="a1")
-            act(C[:, :, 16:32], B("brep", h)[:], 128, IDENT, bias=T.VC[:, 8 + 2 * t + h:9 + 2 * t + h], r=[x("brep"), W("VC")], pw=[ck], name="bmv")
-        for h in H:
-            Bk = P("B", h); bk = "pB%d" % h
-            x = lambda n: W(n + str(h))
-            ws = T.pD[:, :, 16 * h:16 * h + 16]
-            for p in range(NPM):
-                ln = 8 // NPM
-                for k in range(16):
-                    mm(T.pD[:, ln * p:ln * p + ln, 16 * h:16 * h + 16], T.Ib[:], B("XM", h)[:, 2048 // NPM * p + k:2048 // NPM * (p + 1):16], k == 0, k == 15, "pD", 128 // NPM, r=[("XM%d" % h, 2048 // NPM * p, 2048 // NPM * (p + 1))], name="WS")
-            ts(B("wp", h)[:], ws, 0.0, OP.is_gt, 128, w=[x("wp")], pr=["pD"], name="wp")
-            wn = T.pD[:, :, 32 + 16 * h:48 + 16 * h]
-            mm(wn, B("wp", h)[:], T.BOb[:], True, True, "pD", 128, r=[x("wp"), W("BOb")], name="WN")
-            ts(B("win", h)[:], wn, T.Zc[:, 0:1], OP.is_ge, 128, r=[W("Zc")], w=[x("win")], pr=["pD"], name="win")
-            tt(B("nC0", h)[:], B("win", h)[:], P("C", h)[:, :, 16:32], OP.mult, 128, r=[x("win")], w=[x("nC0")], pr=["pC%d" % h], name="nC0")
-            ts(B("nC", h)[:], B("nC0", h)[:], T.VC[:, 2 * t + h:2 * t + h + 1], OP.add, 128, r=[x("nC0"), W("VC")], w=[x("nC")], name="nC")
-            if not last:
-                SN = T.SND[:, t]; sr = lambda o: ("SND%d" % t, 2 * h + o, 2 * h + o + 1)
-                cpv(SN[:, h, :, 0], B("nC", h)[:, 0::16], 8, r=[x("nC")], w=[sr(0)], name="hi")
-                tt(SN[:, h, :, 1], B("nC", h)[:, 0::16], SN[:, h, :, 0], OP.subtract, 8, r=[x("nC"), sr(0)], w=[sr(1)], name="lo")
+    def compose(t, h):
+        CC = T["CC%d" % h]; n = HV // NCP
+        for c in range(NCP):
+            flex(CC[:, HV + n * c:HV + n * c + n], T["WC%d" % h][:].indirect(B("CLu", h)[:, n // 16 * c:n // 16 * (c + 1)]), n, r=[W("WC%d" % h), W("CLu%d" % h)], w=[("CC%d" % h, c, c + 1)], gather=True, name="compose")
+        swap(CC, lambda hh: slice(64 * hh + D_OF[t], 64 * hh + 64, 8), HV, "Y", 25, "cc%d" % h, [("CC%d" % h, 0, NCP)], [("CC%d" % h, 10, 11), ("CC%d" % h, 11, 12)], "CCx")
+        if SXT: dma(CC[6::16, HV:V_], T.SXB[6::16, h], 25, "cc%d" % h, r=[W("SXB%d" % h), ("CC%d" % h, 0, NCP)], w=[("CC%d" % h, 12, 13)], name="CCx")
+    for h in sets():
+        G["free"] = True
+        if CO:
+            for c in range(3 if SXT else 0):
+                mm(P("D", h)[:], X("BO6"), T["XX%d" % h][:, HV + 512 * c:HV + 512 * c + 512], True, True, "pD%d" % h, 512, r=[("X%d" % h, 0, 2), W("BO6")], name="SXp")
+                flex(T.SXB[:, h, 512 * c:512 * c + 512], P("D", h)[:], 512, w=[("SXB%d" % h, c, c + 1)], pr=["pD%d" % h], name="SXb")
+            for hh in H if SXT else ():
+                a = V_ * hh
+                dma(T["CC%d" % h][64 * (1 - hh) + 6:64 * (2 - hh):16, a:a + HV], T.SXB[64 * hh + 6:64 * hh + 64:16, h], 12, "sx%d" % h, r=[W("SXB%d" % h), ("CC%d" % h, 10 + hh, 11 + hh)], w=[("CC%d" % h, 13 + hh, 14 + hh)], name="SXx")
+            compose(0, h)
+            for q in D_OF[1:3]: flat(q, h)
+
+    def round_(t, h):
+        last = t == RO - 1
+        x = lambda n: W(n + str(h))
+        O, XX, WC = T["O%d" % h], T["XX%d" % h], T["WC%d" % h]
+        G["free"] = (t, h) == (0, 0)
+        A, Bk, C, D = P("A", h), P("B", h), P("C", h), P("D", h); ak, bk, ck, dk = "pA%d" % h, "pB%d" % h, "pC%d" % h, "pD%d" % h
+        XRD = [("X%d" % h, 0, 4)]
+        OW = [x("O"), x("Oown")]
+        hs = slice(HV + t, V_, 12)
+        LA, GM = B("LA", h), B("MN", h)
+        ts(LA, O[:, hs], Wq(OFF), OP.add, 128, r=[("O%d" % h, 0, 1), wq(OFF)], w=[x("LA")], name="LA")
+        ln = 128 // NPC
+        if not CO:
+            cpv(B("L0", h), O[:, hs], 128, r=[("O%d" % h, 0, 1)], w=[x("L0")], name="L0")
+            for c in range(0, 128, ln): flex(B("CG", h)[:, 16 * c:16 * (c + ln)], WC[:].indirect(B("L0", h)[:, c:c + ln]), 16 * ln, r=[x("WC"), x("L0")], w=[("CG%d" % h, c, c + ln)], gather=True, name="C1")
+            grp(A[:, :, 24:40], ak, [(T.SEL[:, k], B("CG", h)[:, k::16], [x("CG"), ("SEL", k, k + 1)]) for k in range(16)], "LCp")
+            cpv(B("LC", h), A[:, :, 24:40], 128, w=[x("LC")], pr=[ak], name="LC")
+            if t: renew(t - 1, h, D_OF[t])
+            else: flat(D_OF[0], h)
+        tab, lst, rd = (T["CC%d" % h], LA, [x("CC"), x("LA")]) if CO else (WC, B("LC", h), [x("WC"), x("LC")])
+        for j, c in enumerate(range(0, 128, ln)): flex(B("XK", h)[:, 16 * c:16 * (c + ln)], XX[:, 0:WW].indirect(LA[:, c:c + ln]), 16 * ln, r=XRD + [x("LA")], w=[("XK%d" % h, c, c + ln)], gather=True, name="XK%d" % j)
+        for c in range(0, 128, ln): flex(B("CG", h)[:, 16 * c:16 * (c + ln)], tab[:].indirect(lst[:, c:c + ln]), 16 * ln, r=rd, w=[("CG%d" % h, c, c + ln)], gather=True, name="CG")
+        for q in D_OF[t + 1:]:
+            if t: renew(t - 1, h, q)
+            elif q != D_OF[0] and not CO: flat(q, h)
+        fused = (t, h) in STV
+        if fused and (h == 0 or (t, 0) not in STV):
+            for hh, pp in enumerate((LO, UP)):
+                G["up"] = hh
+                for c in range(2): iota(T.VT[pp, t % NVT, 1024 * c:1024 * c + 1024], [[12, 64], [0, 16]], t + 768 * c + HV * hh, 1024, [("VT%d" % (t % NVT), 2 * c + hh, 2 * c + hh + 1)])
+            G["up"] = 0
+        for u in range(0, 8 if fused else 0):
+            tt(B("OB", h)[:, u], O[:, 0:WW].indirect(LA[:, 16 * u:16 * u + 16]), T.VT[:, t % NVT, 256 * u:256 * u + 256], OP.is_equal, 256, r=OW + [x("LA"), ("VT%d" % (t % NVT), u // 4 * 2, u // 4 * 2 + 2)], w=[("OB%d" % h, u, u + 1)], name="STf", c=gc_(256, "V"))
+        for u in range(0 if fused else 8):
+            act(B("OB", h)[:, u], O[:, 0:WW].indirect(LA[:, 16 * u:16 * u + 16]), 256, IDENT, bias=T.VB[:, 8 * t + u:8 * t + u + 1], r=OW + [x("LA"), W("VB")], w=[("OB%d" % h, u, u + 1)], name="OB", c=gc_(256, "S"))
+        G["free"] = False
+        for q in range(0 if fused else 16):
+            a = B("OB", h)[:, :, 16 * q:16 * q + 16]
+            ts(a, a, 12.0 * q, OP.is_equal, 128, r=[x("OB")], w=[("ST%d" % h, q, q + 1)], two=0.5, name="ST")
+        for j in range(MR): mm(C[:, 0:MR, j::MR], X("Ib"), XX[:, hs], True, True, ck, 128, r=[("X%d" % h, 0, 2), W("Ib")], name="XV")
+        flex(B("aN", h), O[:, hs], 128, r=[("O%d" % h, 0, 1)], w=[x("aN")], bias=-float(MID), name="aN")
+        for k in range(16):
+            shl = T.SHL2[:, D_OF[t]]
+            if k < 8: mm(A[:, :, k:k + 33:16], B("CG", h)[:, k::16], shl, True, True, ak, 24, r=[x("CG"), W("SHL2")], name="cL")
+            else: mm(A[:, :, k:k + 33:32], B("CG", h)[:, k::16], shl[:, :, 1:3], True, True, ak, 16, r=[x("CG"), W("SHL2")], name="cL")
+        flex(B("cS", h), A[:, :, 0:16], 128, w=[x("cS")], pr=[ak], name="cS")
+        if SXT: act(B("SX", h), A[:, :, 32:48], 128, w=[x("SX")], pr=[ak], name="SXc")
+        for s in range(1, 9):
+            tt(B("E", h)[:, :, s - 1], B("cS", h), A[:, :, s:s + 16], OP.is_equal, 128, r=[x("cS")], w=[("E%d" % h, s - 1, s)], pr=[ak], name="E")
+        mm(A[:, :, 48:64], B("cS", h), X("Ih"), True, True, ak, 128, r=[x("cS"), W("Ih")], name="cK")
+        act(B("cK", h), A[:, :, 48:64], 128, w=[x("cK")], pr=[ak], name="cKc")
+        mr = 16 // MR
+        for k in range(mr):
+            tt(B("MN", h)[:, k::mr], B("XK", h)[:, k::mr], C[:, 0:MR], OP.min, 128 * MR, r=[x("XK")], w=[("MN%d" % h, k, k + 1), x("GM")], pr=[ck], name="MN")
+        for k in sorted(range(16), key=lambda k: k % mr):
+            rr = [("MN%d" % h, k % mr, k % mr + 1), W("S12")]
+            mm(Bk[:, :, k::16], B("MN", h)[:, k::16], T.S12[:], True, True, bk, 32, r=rr, name="mL")
+        mS, PRh, Eh = B("mS", h), B("PR", h), B("E", h)
+        flex(mS, Bk[:, :, 0:16], 128, w=[x("mS")], pr=[bk], name="mS")
+        for a, z in ((0, 4), (4, 7)): tt(T.PQ[:, :, a:z, 8:24], Eh[:, :, a:z], Bk[:, :, 0:16 * (z - a)], OP.mult, 128 * (z - a), r=[("E%d" % h, a, z)], w=[("PQ", a, z)], pr=[bk], name="PQ")
+        for s in range(1, 9): tt(PRh[:, s - 1], Eh[:, :, s - 1], Bk[:, :, s:s + 16], OP.mult, 128, r=[("E%d" % h, s - 1, s)], w=[("PR%d" % h, s - 1, s)], pr=[bk], name="PR")
+        key = C[:, 0]
+        grp(key, ck, [(X("Ib"), X("K1"), [W("Ib"), W("K1")]), (X("I16"), mS, [W("I16"), x("mS")])]
+            + [(X("I16"), T.PQ[:, :, s - 1, o - s:o + 16 - s], [("PQ", s - 1, s)]) for s in range(1, 8) for o in (8, 24)]
+            + [(X("I16"), PRh[:, s - 1], [("PR%d" % h, s - 1, s)]) for s in range(1, 9)], "key")
+        for k in range(16):
+            mm(D[:, 2, k::16], B("OB", h)[:, :, k::16], T.S1[:], True, True, dk, 8, r=[x("ST"), x("OB"), W("S1")], name="SL")
+        act(B("nst", h), D[:, 2], 128, RELU, bias=1.0, scale=-1.0, w=[x("nst")], pr=[dk], name="nst")
+        scan(B("F", h), key, 128, w=[x("F")], pr=[ck], name="F")
+        scan(B("TT", h)[:, ::-1], B("F", h)[:, ::-1], 128, r=[x("F")], w=[x("TT")], name="T")
+        tt(B("oh", h), B("TT", h), key, OP.is_equal, 128, r=[x("TT")], w=[x("oh")], pr=[ck], name="oh")
+        mm(A[:, :, 24:40], B("oh", h), X("Ib"), True, True, ak, 128, r=[x("oh")], name="ohT")
+        tt(B("wN", h), B("cK", h), A[:, :, 24:40], OP.mult, 128, r=[x("cK")], w=[x("wN")], pr=[ak], name="wN")
+        mm(A[:, :, 40:56], X("BOh"), B("wN", h), True, True, ak, 128, r=[x("wN"), W("BOh")], name="bR")
+        grp(Bk[:, :, 24:40], bk, [(X("Ib"), X("QB"), [W("QB")]), (B("wN", h), X("BOh"), [x("wN")])], "bL")
+        tt(B("mine", h), B("cK", h), A[:, :, 40:56], OP.is_equal, 128, r=[x("cK")], w=[x("mine")], pr=[ak], name="mine")
+        act(B("BD", h), Bk[:, :, 24:40], 128, RELU, bias=MID + 1 - BIG, w=[x("BD")], pr=[bk], name="BD")
+        mm(Bk[:, 0:XR, 40:48], B("BD", h), T.U8[:], True, True, bk, 8 * XR, r=[x("BD"), W("U8")], f32=True, name="LBp")
+        ts(B("LB", h), Bk[:, 0:XR, 40:48], Wq(OFF1), OP.add, 8 * XR, r=[wq(OFF1)], w=[x("LB")], pr=[bk], name="LB")
+        flex(B("XB", h), XX[:, 0:WW].indirect(B("LB", h)), 128 * XR, r=XRD + [x("LB")], w=[x("XB")], gather=True, name="XB")
+        XM = B("CG", h); lm = 128 // NPM
+        if not GS:
+            grp(C[:, 1], ck, [(X("Ib"), X("KM"), [W("KM")]), (X("Ih"), B("aN", h), [x("aN")]), (X("ImW"), B("mine", h), [x("mine"), W("ImW")])], "LMp")
+            cpv(B("LM", h), C[:, 1], 128, w=[x("LM")], pr=[ck], name="LM")
+            for c in range(0, 128, lm): flex(XM[:, 16 * c:16 * (c + lm)], XX[:].indirect(B("LM", h)[:, c:c + lm]), 16 * lm, r=[x("X"), x("LM")], w=[("CG%d" % h, c, c + lm)], gather=True, name="XM")
+            for j in range(MR): mm(D[:, 0:MR, j::MR], X("Ib"), B("XB", h), True, True, dk, 128, r=[x("XB")], name="XBp")
+            for k in range(mr): tt(GM[:, k::mr], B("XK", h)[:, k::mr], D[:, 0:MR], OP.max, 128 * MR, r=[x("XK")], w=[("GM%d" % h, k, k + 1), ("MN%d" % h, k, k + 1)], pr=[dk], name="MX")
+        else:
+            mm(C[:, 0:4, 0:32], X("Ib"), X("KM"), True, False, ck, 128, r=[W("KM")], name="LMp")
+            for src, cn in (("aN", "PA"), ("mine", "PM")):
+                for e2 in range(2):
+                    for e in range(2):
+                        mm(C[:, 0:4, 16 * e2:16 * e2 + 16], X(cn + str(2 * e2 + e)), B(src, h)[:, :, e], False, src == "mine" and e2 + e == 2, ck, 64, r=[x(src), W(cn + str(2 * e2 + e))], name="LMp")
+            for j in range(4): vop(lambda v, j=j: v.transpose(B("LMf", h)[:, :, j], C[:, j, 0:32]), 32, w=[("LMf%d" % h, j, j + 1)], pr=[ck], name="LMt")
+            cpv(B("LM", h), B("LMf", h), 128, r=[x("LMf")], w=[x("LM")], name="LM")
+            for k in range(0, 16, XR):
+                tt(GM[:, 128 * k:128 * (k + XR)], XX[:].indirect(B("LM", h)[:, 8 * k:8 * (k + XR)]), B("XB", h), OP.max, 128 * XR, r=[x("X"), x("LM"), x("XB")], w=[("GM%d" % h, k, k + XR), ("MN%d" % h, 0, 16)], name="G", c=gc_(128 * XR, "V"))
+        for nmx, o, sg in (("BM", 0, "Im"), ("BP", 4, "Ib")):
+            grp(Bk[:, :, 56 + o], bk, [(X(sg), T.HH[:], [W("HH"), W(sg)]), (B("wN", h), T.S1h[:], [x("wN"), W("S1h")])], "b8", n=8)
+        for nmx, o in (("BM", 0), ("BP", 4)):
+            act(B(nmx, h), Bk[:, :, 56 + o], 8, IDENT, bias=T.VC[:, o + t:o + t + 1], scale=0.5, r=[W("VC")], w=[x(nmx)], pr=[bk], name="bm")
+        U = A[:, :, 0:16]
+        if GS: grp(U, ak, [(X("Im256"), B("XK", h)[:, k::16], [x("XK"), W("Im256")]) for k in range(16)] + [(X("BOm512"), B("mine", h), [x("mine"), W("BOm512")])], "US", stop=False)
+        else: grp(U, ak, [(X("Ib"), XM[:, k::16], [x("CG")]) for k in range(16)], "WS")
+        mm(key, X("Ib"), X("K2"), True, False, ck, 128, r=[W("K2")], name="K2")
+        for k in range(0 if SXT else 16): mm(C[:, 0, k::16], B("XK", h)[:, k::16], T.Sm16[:], False, False, ck, 8, r=[x("XK"), W("Sm16")], name="SX")
+        grp(key, ck, ([(X("Im16"), B("SX", h), [x("SX"), W("Im16")])] if SXT else []) + [(B("mine", h), X("Imax"), [x("mine"), W("Imax")]), (X("Imax"), B("nst", h), [x("nst")])], "K2", start=False, stop=False)
+        for k in range(16 if GS else 0):
+            gr = [("GM%d" % h, k, k + 1)]
+            mm(U, X("Ib"), GM[:, S(k)], False, k == 15, ak, 128, r=gr, name="UG")
+            mm(C[:, 0, k::16], GM[:, S(k)], T.S32[:], False, k == 15, ck, 8, r=gr + [W("S32")], name="FL")
+        for j, k in enumerate(sorted(range(0 if GS else 16), key=lambda k: k % mr)):
+            mm(C[:, 0, k::16], GM[:, k::16], T.S32[:], False, j == 15, ck, 8, r=[("GM%d" % h, k % mr, k % mr + 1), W("S32")], name="FL")
+        act(B("wp", h), U, 128, SIGN, bias=-248.0 if GS else -0.5, w=[x("wp")], pr=[ak], name="wp")
+        mm(Bk[:, :, 0:16], B("wp", h), X("BOb"), True, True, bk, 128, r=[x("wp"), W("BOb")], name="WN")
+        act(B("w", h), Bk[:, :, 0:16], 128, SIGN, bias=T.Zb[:, 0:1], r=[W("Zb")], w=[x("w")], pr=[bk], name="w")
+        SN = T.SND[:, 2 * t + h]; sn = "SND%d" % (2 * t + h)
+        tt(B("t8", h), B("w", h)[:, 0::16], B("BM", h), OP.mult, 8, r=[x("w"), x("BM")], w=[x("t8")], name="t8")
+        tt(B("n8", h), B("t8", h), B("BP", h), OP.add, 8, r=[x("t8"), x("BP")], w=[x("n8")], name="n8")
+        cpv(SN[:, :, :, 0], B("n8", h), 8, r=[x("n8")], w=[(sn, 0, 1)], name="hi")
+        tt(SN[:, :, :, 1], B("n8", h), SN[:, :, :, 0], OP.subtract, 8, r=[x("n8"), (sn, 0, 1)], w=[(sn, 1, 2)], name="lo")
+        ds = [D_OF[u] for u in range(t + 1, RO)]
         if not last:
-            ds = [D_OF[u] for u in range(t + 1, RO)]
-            land = LU(t + 1, rank); sem = "ar%d_%d" % (t + 1, rank)
-            sa = send([T.cores[(rank - ds[0]) % NR]], T.SND[:, t], land, sem, [W("SND%d" % t)], 8, "send")
-            sb_ = send([T.cores[(rank - q) % NR] for q in ds[1:]], T.SND[:, t], land, sem, [W("SND%d" % t)], 8, "sendb") if len(ds) > 1 else None
-        for h in H:
-            A, Bk, C = P("A", h), P("B", h), P("C", h); ak, bk, ck = "pA%d" % h, "pB%d" % h, "pC%d" % h
-            x = lambda n: W(n + str(h))
-            tt(B("q2", h)[:], B("win", h)[:], Bk[:, :, 0:16], OP.mult, 128, r=[x("win")], w=[x("q2")], pr=[bk], name="q2")
-            vop(lambda v, h=h: v.tensor_tensor_scan(B("RM", h)[:], T.NF[:], B("q2", h)[:], 0.0, OP.mult, OP.max), 128, r=[W("NF"), x("q2")], w=[x("RM")], name="RM2")
-            best = T.pE[:, 256 + 128 * h:384 + 128 * h]
-            spread(h, B("RM", h), x("RM"), best, None, floor=0.5, bank="pE")
-            tt(B("oh2_", h)[:], B("q2", h)[:], best, OP.is_equal, 128, r=[x("q2")], w=[x("oh2_")], pr=["pE"], name="oh2")
-            mm(Bk[:, :, 0:16], B("oh2_", h)[:], T.Ib[:], True, True, bk, 128, r=[x("oh2_")], name="oh2T")
-            tt(B("pz", h)[:], T.aD[:, S(h)], Bk[:, :, 0:16], OP.mult, 128, r=[("aD", 128 * h, 128 * h + 128)], w=[x("pz")], pr=[bk], name="pz")
-            tt(B("pc", h)[:], B("cKv", h)[:], Bk[:, :, 0:16], OP.mult, 128, r=[x("cKv")], w=[x("pc")], pr=[bk], name="pc")
-            hr = lambda n: (n, 128 * h, 128 * h + 128)
-            act(T.oK[:, S(h)], Bk[:, :, 0:16], 128, w=[hr("oK")], pr=[bk], name="oK")
-            act(C[:, :, 32:48], Bk[:, :, 0:16], 128, COPY, bias=1.0, scale=-1.0, pr=[bk], pw=[ck], name="nk")
-            zm = T.pD[:, :, 32 + 16 * h:48 + 16 * h]
-            mm(zm, T.BOf[:], B("pz", h)[:], True, True, "pD", 128, r=[W("BOf"), x("pz")], f32=True, name="zm")
-            tt(T.ZQ[:, S(h)], T.QM[:, S(h)], zm, OP.mult, 128, r=[W("QM")], w=[hr("ZQ")], pr=["pD"], name="ZQ")
-            cpv(T.ZU[:, S(h)], zm, 128, w=[hr("ZU")], pr=["pD"], name="ZU")
-            vop(lambda v, h=h: v.tensor_tensor_scan(T.ZS[:, S(h)], T.NF[:], T.ZQ[:, S(h)], 0.0, OP.mult, OP.add), 128, r=[W("NF"), hr("ZQ")], w=[hr("ZS")], name="ZS")
-            zl = ("ZL", 8 * h, 8 * h + 8)
-            ts(T.ZL[:, 8 * h:8 * h + 8], T.ZS[:, 128 * h + 15:128 * h + 128:16], -1.0, OP.add, 8, r=[hr("ZS")], w=[zl], s2=0.0, op1=OP.max, name="ZL")
-            mm(T.pD[:, :, 16 * h:16 * h + 16], T.BOf[:], B("pc", h)[:], True, True, "pD", 128, r=[x("pc")], f32=True, name="csv")
-            flex(B("OC", h)[:], T.O[:].indirect(T.ZL[:, 8 * h:8 * h + 8]), 128, r=[W("O"), zl], w=[x("OC")], cyc=GCY, name="OC", only="S")
-            vop(lambda v, h=h, VR=VR: v.tensor_tensor(B("OE", h)[:], T.O[:].indirect(T.ZL[:, 8 * h:8 * h + 8]), VR[:, S(h)], OP.is_equal), 128, r=[W("O"), zl, W("VR%d" % t)], w=[x("OE")], two=GCY, name="OE")
-            tt(C[:, :, 48:64], T.oK[:, S(h)], C[:, :, 0:16], OP.mult, 128, r=[hr("oK")], pr=[ck], pw=[ck], name="hb")
-        for h in H:
-            x = lambda n: W(n + str(h)); hr = lambda n: (n, 128 * h, 128 * h + 128)
-            n1 = T.pD[:, :, 16 * h:16 * h + 16]
-            tt(n1, B("OE", h)[:], n1, OP.mult, 128, r=[x("OE")], pr=["pD"], pw=["pD"], name="n1")
-            tt(T.NC[:, S(h)], B("OC", h)[:], n1, OP.add, 128, r=[x("OC")], w=[hr("NC")], pr=["pD"], name="NC")
-        def de(u, a, z):
-            ts(T.DE[:, 256 * u + a:256 * u + z], T.ZU[:, a:z], T.ZS[:, 16 * u + 15:16 * u + 16], OP.is_equal, z - a,
-               r=[("ZU", a, z), ("ZS", 16 * u, 16 * u + 16)], w=[("DE", 256 * u + a, 256 * u + z)], two=0.5, name="DE")
+            land = LU(t + 1, h, rank); sem = "ar%d_%d_%d" % (t + 1, h, rank)
+            sa = send([T.cores[(rank - ds[0]) % NR]], SN, land, sem, [W(sn)], "send")
+            sb_ = send([T.cores[(rank - q) % NR] for q in ds[1:]], SN, land, sem, [W(sn)], "sendb") if len(ds) > 1 else None
+            for q in ds: arrive((rank + q) % NR, t + 1, h, sa if q == ds[0] else sb_, 4)
+            mm(D[:, 3, 0:8], X("ONE"), B("w", h)[:, 0::16], True, True, dk, 8, r=[x("w"), W("ONE")], name="ZC")
+            add(G, {"S": (sc(8) + 0.03,) * 2}, lambda Q, e: Q["S"].activation(T.zr[:, 8 * h:8 * h + 8], D[:, 3, 0:8], COPY, bias=256.0, accum_out=T.zr[:, 16 + h:17 + h]), (), [x("zr")], [dk], name="zr")
+            if h == 1:
+                ts(T.zi[:, 0:1], T.zr[:, 16:17], T.zr[:, 17:18], OP.add, 1, r=[W("zr0"), W("zr1")], w=[("zi", 0, 1)], s2=0.5, op1=OP.mult, name="Z")
+                ts(T.zi[:, 1:2], T.zi[:, 0:1], 1, OP.bitwise_and, 1, r=[("zi", 0, 1)], w=[("zi", 1, 2)], name="Z")
+                ts(T.Zb[:], T.zi[:, 1:2], -2.0, OP.mult, 1, r=[("zi", 1, 2)], w=[W("Zb")], s2=-1.0, op1=OP.add, name="Z")
+        if CO:
+            HLo = T.HLz[:, 4 * h]
+            flex(HLo[:, :, :, 0::8], SN, 16, r=[W(sn)], w=[("HLz", 4 * h, 4 * h + 1)], name="HLz")
+            mm(D[:, 2], HLo, X("Ib"), True, True, dk, 128, r=[("HLz", 4 * h, 4 * h + 1)], name="HLr")
+            flex(B("NB", h), D[:, 2], 128, w=[x("NB")], pr=[dk], name="WCu")
+            for o in range(3):
+                grp(D[:, 3, o:96:3], dk, [(T.KD[:, 3 * t + o], B("CLf", h)[:, o::3], [x("CLf"), ("KD", 3 * t + o, 3 * t + o + 1)], 1)]
+                    + [(T.SEL[:, (12 * r_ + t) % 16], B("NB", h)[:, r_::4], [x("NB"), W("SEL")]) for r_ in range(4) if (12 * r_ + t) // 16 == o], "CLp", n=32)
+            if not last: cpv(B("CLu", h), D[:, 3, 0:96], 96, w=[x("CLu")], pr=[dk], name="CLu")
+            flex(B("CLf", h), D[:, 3, 0:96], 96, w=[x("CLf")], pr=[dk], name="CLf")
+            if last:
+                for b in range(3): vop(lambda v, b=b: v.transpose(B("TF", h)[:, b], B("CLf", h)[:, b::3]), 32, r=[x("CLf")], w=[("TF%d" % h, b, b + 1)], name="yct")
+                for hh, pp in enumerate((LO, UP)):
+                    for e in range(2): dma(T.yc[4 * h + e:4 * h + 4:2, HV * hh:HV * hh + HV], T.TF[pp, h, :, e], 12, "yc%d" % h, r=[x("TF")], name="st yc")
+            else:
+                renew(t, h, ds[0])
+                compose(t + 1, h)
+        else: renew(t, h, 0)
+        if last and not CO:
+            for c in range(3):
+                for hh in H: mm(D[0:8], T.SY[:, 4 * hh:4 * hh + 8], WC[:, HV * hh + 512 * c:HV * hh + 512 * c + 512], hh == 0, hh == 1, dk, 512, r=[x("WC"), W("SY")], name="ycp")
+                flex(T.YC[0:8, 512 * c:512 * c + 512], D[0:8], 512, w=[("YC", c, c + 1)], pr=[dk], name="yc")
+            for hh in H: dma(T.yc[4 * h:4 * h + 4, HV * hh:HV * hh + HV], T.YC[4 * hh:4 * hh + 4, :], 25, "yc%d" % h, r=[W("YC")], name="st yc")
+        scan(B("F", h), key, 128, w=[x("F")], pr=[ck], name="F2")
+        scan(B("TT", h)[:, ::-1], B("F", h)[:, ::-1], 128, r=[x("F")], w=[x("TT")], name="T2")
+        tt(B("oh2", h), B("TT", h), key, OP.is_equal, 128, r=[x("TT")], w=[x("oh2")], pr=[ck], name="oh2")
+        grp(A[:, :, 16:32], ak, [(X("Imh"), B("aN", h), [x("aN"), W("Imh")]), (X("Ib"), X("LR"), [W("LR")]), (B("w", h), X("Ib2"), [x("w"), W("Ib2")]), (B("oh2", h), X("IB"), [x("oh2"), W("IB")])], "pzp")
+        ts(B("pz", h), A[:, :, 16:32], V_ - MID - 1.5 * BIG - CEN, OP.add, 128, w=[x("pz")], pr=[ak], s2=-CEN, op1=OP.max, name="pz")
+        grp(Bk[:, :, 0:16], bk, [(X("Im"), X("QmB"), [W("QmB")]), (B("pz", h), X("BOm"), [x("pz"), W("BOm")])], "ZQp")
+        grp(A[:, 0:4, 32:64], ak, [(X("Ib"), X("LR"), [W("LR")]), (X("BOm"), B("pz", h), [x("pz"), W("BOm")])], "ZUp")
+        grp(A[:, 4:8, 32:64], ak, [(X("Ib"), X("LRx"), [W("LRx")]), (X("BOx"), B("pz", h), [x("pz"), W("BOx")])], "ZUp")
+        ts(B("ZQ", h), Bk[:, :, 0:16], T.VC[:, 8:9], OP.add, 128, r=[W("VC")], w=[x("ZQ")], pr=[bk], s2=-CEN, op1=OP.max, name="ZQ")
+        ts(B("ZU", h), A[:, :, 32:64], V_ + 1.0 - 16 * CEN, OP.add, 256, w=[x("ZU")], pr=[ak], name="ZU")
+        act(B("ZUf", h), A[:, 0:4, 32:64], 128, COPY, bias=V_ + 1.0 - 32 * CEN, w=[x("ZUf")], pr=[ak], name="ZUf")
+        mm(Bk[:, :, 57], B("ZQ", h), T.S1h[:], True, True, bk, 8, r=[x("ZQ")], name="ZLp")
+        flex(B("ZLf", h), Bk[:, :, 57], 8, w=[x("ZLf")], pr=[bk], bias=16 * CEN, name="ZLf")
+        ts(B("ZL", h), Bk[:, :, 57], Wq(OFF1), OP.add, 8, r=[wq(OFF1)], w=[x("ZL")], pr=[bk], s2=16 * CEN, op1=OP.add, name="ZL")
+        mm(Bk[:, :, 24:40], B("oh2", h), X("Ib"), True, True, bk, 128, r=[x("oh2")], name="ohT2")
+        tt(B("pc", h), B("cK", h), Bk[:, :, 24:40], OP.mult, 128, r=[x("cK")], w=[x("pc")], pr=[bk], name="pc")
+        grp(Bk[:, :, 40:56], bk, [(X("Im"), X("VH"), [W("VH"), W("Im")]), (X("Im"), T.VL[:, t], [W("VL")]), (X("BOh"), B("pc", h), [x("pc")])], "csv")
+        OC, NN = B("OC", h), B("NN", h); oc, nn = ("OC%d" % h, 0, 1), ("NN%d" % h, 0, 1)
+        flex(OC[:, 0:128], O[:].indirect(B("ZL", h)), 128, r=OW + [x("ZL")], w=[oc], gather=True, name="OC", only="S")
+        tt(B("OE", h), O[:].indirect(B("ZL", h)), T.VR[:, t], OP.is_equal, 128, r=OW + [x("ZL"), W("VR")], w=[x("OE")], name="OE", c=gc_(128, "V"))
+        tt(NN[:, 0:128], B("OE", h), Bk[:, :, 40:56], OP.mult, 128, r=[x("OE")], w=[nn], pr=[bk], name="NN")
+        grp(Bk[:, :, 0:16], bk, [(X("SW"), OC[:, 0:128], [oc, W("SW")], 1), (X("SW"), NN[:, 0:128], [nn], 1)], "NCx")
+        act(NN[:, 128:256], Bk[:, :, 0:16], 128, w=[("NN%d" % h, 1, 2)], pr=[bk], name="NCc")
+        for o, kn, a, b_ in ((0, "KH", "ImB", "Imb2"), (1, "KL", "IB", "Ib2")):
+            grp(D[:, o], dk, [(X("Ib"), X(kn), [W(kn)]), (X("BOh"), B("wN", h), [x("wN")]), (B("w", h), X(b_), [x("w"), W(b_)]), (B("oh2", h), X(a), [x("oh2"), W(a)])], "HL")
+        grp(C[:, 1], ck, [(X("Ib"), X("TRI"), [W("TRI")]), (B("ZQ", h), X("BOh"), [x("ZQ")])], "DSp")
+        tt(B("DS", h), B("ZUf", h), C[:, 1], OP.is_equal, 128, r=[x("ZUf")], w=[x("DS")], pr=[ck], name="DS")
+        DE = B("DE", h); de = lambda u: [("DE%d" % h, u, u + 1)]
+        for u in range(8):
+            a = 16 * u + 16
+            ts(DE[:, u, a:256], B("ZU", h)[:, a:256], B("ZLf", h)[:, u:u + 1], OP.is_equal, 256 - a, r=[x("ZU"), x("ZLf")], w=de(u), two=0.5, name="DE")
+        grp(key, ck, [(X("Ib"), X("QC"), [W("QC")]), (B("DS", h), X("BOb"), [x("DS")])]
+            + [(DE[:, u, S(j)], X(("BOb", "BOy")[j]), de(u) + [W("BOy")]) for u in range(8) for j in H if u < 7 or j], "DUP")
+        act(B("sg", h), key, 128, SIGN, bias=-0.5, w=[x("sg")], pr=[ck], name="sg")
+        for pp, qq, o in ((slice(0, 128), slice(0, 128), 32), (LO, UP, 40), (UP, LO, 40)):
+            grp(A[pp, 7, o:o + 8], ak, [(B("ZQ", h)[:, qq], T.S1h[:], [x("ZQ")]), (B("sg", h)[:, qq], T.U8b[:], [x("sg"), W("U8b")])], "FZp", n=8)
+        tt(B("fl", h), T.SPL[:], A[:, 7, 32:48], OP.min, 16, r=[W("SPL")], w=[x("fl")], pr=[ak], name="fl")
+        ts(B("FZ", h), B("fl", h), Wq(OFFZ), OP.add, 16, r=[x("fl"), wq(OFFZ)], w=[x("FZ")], name="FZ")
+        tt(O[:].indirect(B("FZ", h)), OC, NN, OP.add, 256, r=[x("OC"), x("NN"), x("FZ")], w=OW, name="scatter", c=vc(256, 3.5))
+        tt(B("OE", h), O[:, hs], D[:, 0], OP.min, 128, r=[x("O")], w=[x("OE")], pr=[dk], name="XO")
+        tt(O[:, hs], B("OE", h), D[:, 1], OP.max, 128, r=[x("OE"), x("O")], w=[("Oown%d" % h, 0, 1)], pr=[dk], name="O")
+        if last:
+            for hh, pp in enumerate((LO, UP)): dma(T.yo[64 * h:64 * h + 64, HV * hh:HV * hh + HV], O[pp, HV:V_], 393, "yo%d%d" % (h, hh), r=OW, q="YS"[hh], name="st yo")
+            return
+        mm(D[:, 2], X("SW"), O[:, hs], True, True, dk, 128, r=[("Oown%d" % h, 0, 1)], f32=True, name="Osw")
+        act(O[LO, V_ + t:WW:12], D[LO, 2], 128, r=[x("O")], w=[("Oown%d" % h, 1, 2)], pr=[dk], name="Oc")
+        act(O[UP, t:HV:12], D[UP, 2], 128, r=[x("O")], w=[("Oown%d" % h, 2, 3)], pr=[dk], name="Oc")
 
-        def dup(h, u, a, z, wt, stop=False):
-            mm(T.pE[:, a:z], T[wt][:], T.DE[:, 256 * u + a:256 * u + z], False, stop, "pE", z - a, r=[("DE", 256 * u + a, 256 * u + z), W(wt)], name="DUP%d" % h)
-        for h in H:
-            hr = ("oK", 128 * h, 128 * h + 128)
-            mm(T.pE[:, S(h)], T.Ib[:], T.DC[:, S(h)], True, False, "pE", 128, r=[W("Ib"), W("DC")], name="DUP%d" % h)
-            mm(T.pE[:, S(h)], T.Ib[:], T.C128[:, S(h)], False, False, "pE", 128, r=[W("C128")], name="DUP%d" % h)
-            mm(T.pE[:, S(h)], T.BN[:], T.oK[:, S(h)], False, False, "pE", 128, r=[W("BN"), hr], name="DUP%d" % h)
-            for u in range(8 * h + 8):
-                if u < 8 * h:
-                    de(u, 128, 256)
-                    dup(h, u, 128, 256, "L4")
-                    continue
-                de(u, 16 * u, 128 * h + 128)
-                if u < 8 * h + 7: dup(h, u, 16 * u + 16, 128 * h + 128, "L4")
-                dup(h, u, 16 * u, 16 * u + 16, "LW", u == 8 * h + 7)
-        vop(lambda v: v.tensor_scalar(T.pE[:, 0:256], T.pE[:, 0:256], 0.0, 8192.0, OP.is_ge, OP.mult), 256, pr=["pE"], pw=["pE"], name="nlq")
-        tt(T.fz[:], T.ZQ[:], T.pE[:, 0:256], OP.max, 256, r=[W("ZQ")], w=[W("fz")], pr=["pE"], name="fz")
-        for h in H:
-            vop(lambda v, h=h: v.tensor_tensor_scan(T.FS[:, S(h)], T.NF[:], T.fz[:, S(h)], 0.0, OP.mult, OP.add), 128, r=[W("NF"), ("fz", 128 * h, 128 * h + 128)], w=[("FS", 128 * h, 128 * h + 128)], name="FS")
-        tt(T.fl[:], T.FS[:, 15::16], T.DL[:], OP.min, 16, r=[W("FS"), W("DL")], w=[W("fl")], name="fl")
-        ts(T.FZ[:], T.fl[:], -1.0, OP.add, 16, r=[W("fl")], w=[W("FZ")], name="FZ")
-        vop(lambda v: v.tensor_copy(T.O[:].indirect(T.FZ[:]), T.NC[:]), 256, r=[W("NC"), W("FZ")], w=[W("O")], two=3.0, name="scatter")
-        G["wr"]["O"] = [y for y in G["wr"]["O"]]
-        for h in H:
-            hr = lambda n: (n, 128 * h, 128 * h + 128)
-            ck = "pC%d" % h
-            tt(T.XO[:, S(h)], T.O[:, hs(h)], P("C", h)[:, :, 32:48], OP.mult, 128, r=[oreg(h)], w=[hr("XO")], pr=[ck], name="XO")
-            tt(T.O[:, hs(h)], T.XO[:, S(h)], P("C", h)[:, :, 48:64], OP.add, 128, r=[hr("XO")], w=[("O", 1536 * h, 1536 * h + 1536)], pr=[ck], name="O")
-        for h in H:
-            x = lambda n: W(n + str(h)); ck = "pA%d" % h; C = P("A", h)
-            cr = lambda n: (n, 96 * h, 96 * h + 96)
-            tt(T.CLk[:, 96 * h:96 * h + 96], T.CLf[:, 96 * h:96 * h + 96], T.KP[:, t], OP.mult, 96, r=[cr("CLf"), W("KP%d" % t)], w=[cr("CLk")], name="CLk")
-            tt(B("BDc", h)[:], B("nC", h)[:], T.PM[:, t], OP.mult, 128, r=[x("nC"), W("PM%d" % t)], w=[x("BDc")], name="BDc")
-            mm(C[:, :, 0:12], T.If[:], T.CLk[:, 96 * h:96 * h + 96], True, False, ck, 96, r=[cr("CLk"), W("If")], f32=True, name="CLp")
-            mm(C[:, :, 0:12], B("BDc", h)[:], T.U4[:], False, True, ck, 96, r=[x("BDc"), W("U4")], f32=True, name="CLp")
-            if not last: cpv(T.CLu[:, 96 * h:96 * h + 96], C[:, :, 0:12], 96, w=[cr("CLu")], pr=[ck], name="CLu")
-            act(T.CLf[:, 96 * h:96 * h + 96], C[:, :, 0:12], 96, w=[cr("CLf")], pr=[ck], name="CLf")
-        if last: break
-        for h in H:
-            mm(T.pA1[:, :, 58], T.ONE[:], B("win", h)[:, 0::16], h == 0, h == 1, "pA1", 8, r=[W("win%d" % h), W("ONE")], name="ZC")
-        vop(lambda v: v.tensor_reduce(T.zr[:, 0:1], T.pA1[:, :, 58], AxisListType.X, OP.add), 8, w=[("zr", 0, 1)], pr=["pA1"], name="zr")
-        cpv(T.zi[:, 0:1], T.zr[:, 0:1], 1, r=[("zr", 0, 1)], w=[("zi", 0, 1)])
-        ts(T.zi[:, 1:2], T.zi[:, 0:1], 1, OP.bitwise_and, 1, r=[("zi", 0, 1)], w=[("zi", 1, 2)])
-        ts(T.Zc[:], T.zi[:, 1:2], 9.0, OP.add, 1, r=[("zi", 1, 2)], w=[W("Zc")], name="Zc")
-        for qi, q in enumerate(ds):
-            s = (rank + q) % NR; ln = "L%d_%d" % (t + 1, s)
-            arrive(s, t + 1, sa if qi == 0 else sb_, 8)
-            for h in H:
-                A = P("A", h); ak = "pA%d" % h
-                flex(B("HLz", h)[:, :, 0:2], LU(t + 1, s)[:, h], 16, r=[W(ln)], w=[W("HLz%d" % h)], name="HLz")
-                mm(A[:, :, 40:56], B("HLz", h)[:], T.Ib[:], True, True, ak, 128, r=[W("HLz%d" % h)], name="HLr")
-                flex(T["WC%d" % q][:, hs(h)], A[:, :, 40:56], 128, w=[("WC%d" % q, 1536 * h, 1536 * h + 1536)], pr=[ak], name="WCu")
-    vop(lambda v: v.transpose(T.TF[:], T.CLf[:]), 192, r=[W("CLf")], w=[W("TF")], name="yc")
-    for e in range(2):
-        for b in range(6):
-            dma(T.yc[e::2, 512 * b:512 * b + 512], T.TF[:, 32 * b + 16 * e:32 * b + 16 * e + 16], 8, r=[W("TF")], name="st yc")
-    dma(T.yo[:, 0:1536], T.O[:, 0:1536], 786, r=[("O", 0, 1536)], name="st yo")
-    dma(T.yo[:, 1536:3072], T.O[:, 1536:3072], 786, r=[("O", 1536, 3072)], q="S", name="st yo")
+    for t in range(RO):
+        G["t"] = t
+        for h in sets(): round_(t, h)
     return G
 
 
@@ -578,7 +676,7 @@ def rank_program(g, core, T, topo):
     if "o" not in ORDER: ORDER["o"] = schedule(G)
     order, eng, fin, st = ORDER["o"]
     Q = {"V": g.vector, "S": g.scalar, "P": g.tensor, "G": g, "Y": g.sync}
-    ops = G["ops"]
+    ops = G["ops"]; apart = [False]
     count = {}; known = {"V": {}, "S": {}, "P": {}, "G": {}, "Y": {}}; done = [None] * len(ops); clock = [None] * len(ops)
     for i in order:
         o = ops[i]; e = eng[i]
@@ -588,19 +686,20 @@ def rank_program(g, core, T, topo):
         kn = known[e]
         need = {}
         for j, raw in o["deps"].items():
-            if eng[j] == e and not raw: continue
+            if eng[j] == e and not raw and ops[j]["key"] is None: continue
             k, c = done[j]
-            if kn.get(k, 0) < c: need[k] = max(need.get(k, 0), c)
-        cand = sorted(need.items())
-        for j in o["deps"]:
-            if eng[j] == e and not o["deps"][j]: continue
-        for k, c in cand:
+            if kn.get(k, 0) < c: need[k] = count[k] if k[0] == "d" else max(need.get(k, 0), c)
+        for k, c in sorted(need.items()):
             if kn.get(k, 0) >= c: continue
             Q[e].wait_ge(T.sem[k], c)
             kn[k] = max(kn.get(k, 0), c)
             for j in o["deps"]:
-                if done[j] == (k, c):
+                if done[j][0] == k and done[j][1] <= c:
                     for kk, vv in clock[j].items(): kn[kk] = max(kn.get(kk, 0), vv)
+        if e == "G" and o["key"] is None:
+            if (o["name"] == "up" or apart[0]) and kn.get("cG", 0) < count.get("cG", 0):
+                g.wait_ge(T.sem.cG, count["cG"]); kn["cG"] = count["cG"]
+            apart[0] = o["name"] == "up"
         ins = o["fn"](Q, e)
         if o["key"] is None:
             k = "c" + e

@@ -1,121 +1,137 @@
+import numpy as np
 from concourse.bass import DstId, RemoteDMATransfer
 from concourse.mybir import dt, AluOpType, AxisListType, ActivationFunctionType
 
 V_, RO, NR = 3072, 4, 4
-HV = V_ // 2
-PAD = 256
-WW = V_ + HV
 MID = 1536
-BIG = 8192.0
-CEN = 1664.0
+BIG = 65536.0
 OP = AluOpType
 AF = ActivationFunctionType
 COPY, IDENT, RELU, SIGN = AF.Copy, AF.Identity, AF.Relu, AF.Sign
-GS, CO, NVT, SXT = True, True, 1, True
-STV = []
-XR = 2 if GS else 1
-MR = 4
+D_OF = [1 + t % 3 for t in range(RO)]
+ORD = (1, 0)
+LO, UP = slice(0, 64), slice(64, 128)
+CBN = ["Ib", "IB", "ImB", "Im3072", "Id128", "Imh2", "BOb", "QB", "TR0", "TR1", "K1", "ONE", "KH", "KL"]
+TMP = ["ci", "cg", "cq", "cd", "c64", "c32", "cw0", "cw1"]
+CHN = ["ME0", "ME1", "I128", "I8192", "Ih", "Imh", "Im128", "Im8192", "Ih128", "I32h", "Im16h", "BOh", "BOm", "A1"]
+CXN = ["NF", "NFa"]
+LAND = [(t, d) for t in range(RO - 1) for d in D_OF[t + 1:]]
 
 
 def _decl():
     s = {}
-
-    def sb(name, shape, dtype):
-        s[name] = ("sbuf", shape, dtype)
     f, b, i, u, hf = "float32", "bfloat16", "int32", "uint16", "float16"
-    for h in range(2):
-        sb("O%d" % h, [128, WW + PAD], f); sb("XX%d" % h, [128, 2 * WW], b); sb("WC%d" % h, [128, V_], b)
-    sb("CI", [128, 192], i); sb("CF", [128, 192], f); sb("HL0", [128, 384], b)
-    for r in range(NR): sb("L0_%d" % r, [128, 384], b)
-    sb("LU", [128, 24, 2, 4, 2], b); sb("SND", [128, 8, 2, 4, 2], b)
-    sb("VR", [128, 4, 128], f); sb("VC", [128, 16], f); sb("VB", [128, 32], f); sb("VL", [128, 4, 128], b)
-    sb("OI", [128, HV], i)
-    for n in ("XK", "MN", "CG"): sb(n, [128, 2, 2048], b)
-    sb("OB", [128, 2, 8, 256], b)
-    sb("E", [128, 2, 8, 8, 16], b); sb("PR", [128, 2, 8, 8, 16], b); sb("PQ", [128, 8, 7, 40], b)
-    for n in ("cK", "F", "TT", "BD", "ZUf", "OE"): sb(n, [128, 2, 128], f)
-    for n in ("cS", "wN", "pc", "pz", "ZQ"): sb(n, [128, 2, 128], hf)
-    for n in ("oh", "wp", "w", "nst", "oh2", "sg", "DS"): sb(n, [128, 2, 128], b)
-    sb("aN", [128, 2, 4, 2, 16], hf); sb("mine", [128, 2, 4, 2, 16], b); sb("LMf", [128, 2, 16, 4, 2], f)
-    if CO:
-        sb("CC0", [128, WW], b); sb("CC1", [128, WW], b); sb("KD", [128, 12, 128], f); sb("NE", [128, 16], f); sb("NB", [128, 2, 128], b)
-        sb("TI", [128, 2, 3, 2, 16], i); sb("TF", [128, 2, 3, 2, 16], f); sb("CLf", [128, 2, 96], f); sb("CLu", [128, 2, 96], u)
-    else: sb("YC", [128, HV], f)
-    if STV: sb("VT", [128, NVT, 2048], f)
-    pass; sb("mS", [128, 2, 128], b); sb("XB", [128, 2, 128 * XR], b); sb("HLz", [128, 8, 2, 4, 16], b)
-    for n in ("LA", "LM") if CO else ("LA", "LM", "L0", "LC"): sb(n, [128, 2, 128], u)
-    sb("ZU", [128, 2, 256], u); sb("LB", [128, 2, 8 * XR], u); sb("ZL", [128, 2, 8], u); sb("FZ", [128, 2, 16], u)
-    for n in ("OC", "NN"): sb(n, [128, 2, 256], f)
-    sb("fl", [128, 2, 16], f); sb("SPL", [128, 16], f)
-    for n in ("BM", "BP", "t8", "n8", "ZLf"): sb(n, [128, 2, 8], f)
-    sb("DE", [128, 2, 8, 256], b); sb("SHL2", [128, 4, 8, 3], b)
-    if SXT: sb("SX", [128, 2, 128], b); sb("SXB", [128, 2, HV], b)
+
+    def sb(names, shape, dtype):
+        for n in names.split(): s[n] = ("sbuf", shape, dtype)
+    sb("OI", [128, V_], i); sb("O", [128, V_ + 32], f); sb("P YC", [128, V_], f); sb("XX", [128, 2 * V_], b); sb("WC1 WC2 WC3", [128, V_], b)
+    sb("CI", [128, 384], i); sb("CA PR", [128, 384], f); sb("CHi HL0 L1 L2 L3 XR", [128, 384], b)
+    sb("LD", [128, len(LAND), 256], b); sb("PL", [128, RO - 1, 256], b)
+    sb("VT", [128, 2, 4096], f); sb("VR", [128, 4, 256], f); sb("VRh", [128, 4, 256], hf); sb("VC", [128, 8], f)
+    sb("XK MN", [128, 2, 2048], hf); sb("CG", [128, 2, 2048], b); sb("ST", [128, 2, 8, 256], b); sb("VB", [128, 64], f); sb("WL", [128, 2, 8, 2, 128], hf)
+    sb("LA LC LM", [128, 2, 128], u); sb("LB ZL FZ", [128, 2, 8], u); sb("N32", [128, 256], b); sb("S1p", [128, 8], hf); sb("c8p", [128, 8], b)
+    sb("aN uS wN pz ZQ SA", [128, 2, 128], hf); sb("R3 KS", [128, 2, 3, 128], hf); sb("S2", [128, 2, 2, 2, 64], hf)
+    sb("hi oh mine nst XB nw oh2", [128, 2, 128], b); sb("SB", [128, 2, 144], b)
+    sb("F TT OC OE", [128, 2, 128], f); sb("BV B8 t8 x8", [128, 2, 8], f)
     sb("CB", [128, len(CBN), 128], b); sb("CH", [128, len(CHN), 128], hf); sb("CX", [128, len(CXN), 128], f)
-    sb("SEL", [128, 16, 128], b)
-    for n in ("S1", "S32", "Sm16", "U8b", "HH"): sb(n, [128, 8], b)
-    sb("SY", [128, 12], b)
-    sb("S12", [128, 8, 4], b); sb("S1h", [128, 8], hf); sb("U8", [128, XR, 8], f)
-    sb("ci", [128, 128], b); sb("cg", [128, 128], b); sb("cq", [128, 128], b); sb("c2", [128, 16], b); sb("c3", [128, 128], b)
-    sb("pi", [128, 1], i); sb("ti", [128, 8], i); sb("tf", [128, 8], f); sb("wq", [128, 44], f)
-    sb("zr", [128, 24], f); sb("zi", [128, 4], i); sb("Zb", [128, 1], f)
-    for n in ("pA0", "pA1", "pB0", "pB1"): s[n] = ("psum", [128, 8, 64], f)
-    for n in ("pC0", "pC1", "pD0", "pD1"): s[n] = ("psum", [128, 4, 128], f)
+    sb("WD", [128, 8, 128], hf); sb("Rd", [128, 3, 8], hf); sb("S1h R16", [128, 8], hf); sb("S1b Rc c8", [128, 8], b); sb("U8 pk", [128, 8], f)
+    sb("pi", [128, 1], i); sb("ti", [128, 4], i); sb("tf", [128, 4], f); sb("wq", [128, 16], f); sb("zr", [128, 9], f); sb("zi", [128, 2], i); sb("Zt", [128, 1], f)
+    for n in "ABCD":
+        for h in range(2): s["p%s%d" % (n, h)] = ("psum", [128, 4, 128], f)
     return s
 
 
-CBN = ["Ib", "Im", "I16", "I256", "ImW", "IB", "ImB", "Ib2", "Imb2", "Imax", "BOb", "BOy", "TRI", "ONE", "K1", "K2", "KM", "KH", "KL",
-       "QB", "QmB", "QC", "VH", "LR", "LRx", "KW0", "KW1", "KW2", "KW3", "Im16", "BO6", "Im256", "BOm512", "PM0", "PM1", "PM2", "PM3"]
-CHN = ["Ih", "Imh", "BOh", "PA0", "PA1", "PA2", "PA3", "BOm", "BOx"]
-CXN = ["If", "BOf", "SW", "NF", "QM"]
 SCRATCH = _decl()
-SEMAPHORES = ["cV", "cS", "cP", "cG", "loc"] + ["d%d" % k for k in range(60)] + ["ar%d_%d_%d" % (t, h, r) for t in range(4) for h in range(2) for r in range(NR)]
-D_OF = [1 + t % 3 for t in range(RO)]
-CYC = 0.83e-3
-WAKE = 0.12
-GCY = 1.56
-PF, PO = 0.6, 0.02
-ASG = {"CG": "S", "cS": "S", "aN": "S", "ZLf": "V", "C1": "S", "SXb": "S", "compose": "S", "XM": "S", "yc": "S", "XK0": "S", "XK1": "S", "XB": "S", "mS": "S", "WCu": "S", "CLf": "S", "HLz": "S"}
-RATE, LAT, FAR = 200.0, 2.2, 3.5
-SAME, PER, STRETCH, SWEEPS = 0.06, 33.0, 1.25, 2
-NPC, NPM, NCP = 2, 2, 2
-WT = {'yct': 6, 'OC': -2, 'UG': 2, 'MN': -1, 'Ox': 4, 'bm': 1, 'E': 1, 'LA': 2, 'st yc': 2, 'pzp': 2, 'US': 4, 'sendb': 2, 'XV': 6, 'LMp': 4, 'ZL': 2, 'pz': -2, 'LMt': 4, 'FZ': 1, 'G': -1, 'CCx': 4, 'flat': 1, 'SL': 1, 'SXp': -1, 'b8': -2, 'st yo': 6, 'DE': 6, 'WCu': 2, 'ZUp': -1, 'nst': 1, 'ld list': 1, 'fl': -1, 'csv': -1, 'bR': 6, 't8': -2, 'Osw': 4, 'send0b': 6, 'SXc': -1, 'ld hol0': 6, 'hi': -4, 'OB': -2, 'OE': 4, 'mS': 2, 'wp': -2, 'LM': -4, 'send': -4, 'Oc': 4}
-FIRST = ["ld ctl", "send0", "ld hol0", "ld sha0"]
-SHORT = {}
-PRS = []
+SEMAPHORES = ["cV", "cS", "cP", "cG", "loc"] + ["d%d" % k for k in range(30)] + ["ar%d_%d" % (t, j) for t in range(RO) for j in range(3)]
+CYC, WAKE, SAME, GCY, SCY, PF, PO = 0.83e-3, 0.125, 0.07, 1.56, 3.5, 0.6, 0.02
+RATE, LAT, FAR, ROW = 230.0, 2.2, 4.5, 0.1
+NPG = 2
+ONV = [("XK", 1, 1), ("XK", 0, 1), ("CG", 1, 1), ("CG", 0, 1)]
+INDIRECT = "XK CG XM ST XB OC OE scatter".split()
+CASES = []
+SEED = [12345]
+APART = [-4.0, -3.0, -2.0]
+LINK = [25.0]
+DEAL = []
+LEAD = [0.0]
+NPW = 1
+LOADS = {"ld ctl": -9, "ld xr": -8, "ld sha": -7, "ld hol1": -6, "ld rows": -5, "ld hol0": -4, "ld flat": 12}
+START = 11.0
+SAME_AS = {"XO": "F", "BD": "F", "FR": "uS", "wp": "hi", "pc": "uS"}
+ASG = {n: "S" for n in "R3 Y2 aN mS cS KS hi XB bm FR PL Pu OC YC WCu Oc XK CG XM n8b H8".split() + [""]}
+WT = {}
+STS = [8, 8]
+PLAN = [(0, 0.3, "LA"), (0.3, 3.1, "XK"), (3.2, 4.1, "dec"), (4.2, 5.8, "Y2 R3 uT LC"), (5.8, 8.6, "CG"), (8.7, 9.6, "cL"), (9.7, 11, "cS TK KS"), (11, 13, "D"), (11.3, 13.5, "clip"),
+        (11.8, 13.8, "pool"), (13.8, 16.6, "hi hi- F T oh ohT wN bR mine LMp LM"), (15.5, 16.7, "bL BD LBp LB XB XBp"), (16.7, 19.4, "XM"), (17.2, 19.1, "MX"), (17.7, 19.9, "FL"),
+        (18.2, 20.3, "WS"), (19.9, 21.3, "FR K2 F2 T2 oh2"), (20.3, 21.1, "wp WN nw"), (21.4, 24.6, "pzp pz ZQp ZQ DSp DS DM x8 fl FZp FZ"), (22.0, 24.4, "ohT2 pc ZLp ZL csv OC OE NN"),
+        (24.6, 27, "scatter"), (21.2, 24, "t8 n8 H8 DG PL send"), (24, 27, "Pp Pu"), (6.5, 8.5, "MN"), (7.5, 9.2, "mL"), (9.3, 9.6, "mS"), (15, 17.5, "ST"), (11, 15, "OB"), (15.5, 17.5, "SQ"), (17.5, 19, "SL"), (19.2, 19.5, "nst"),
+        (27.5, 30, "XO O Osw Oc"), (24, 26, "HL"), (26, 28, "YCp YC ZC zr Z"), (3.2, 3.4, "aN"), (-1, 0, "XV"), (16, 17, "b8 bm"), (10.5, 11, "K1"), (36, 37, "sendb")]
+PER = [30.0, 1.1, 6.0]
+SWEEPS = 2
+TRIES = [1500, 5, 3.0, 0.3]
+_ = slice(None)
+SIZE = {"float32": 4, "int32": 4}
 
 
-def new_graph():
-    return {"ops": [], "wr": {}, "rd": {}, "bw": {}, "br": {}}
+def bits(ix):
+    m = np.zeros(int(ix.max()) + 1, np.uint8); m[ix.reshape(-1)] = 1
+    return int.from_bytes(np.packbits(m, bitorder="little").tobytes(), "little")
 
 
-def add(G, opts, fn, r=(), w=(), pr=(), pw=(), key=None, cnt=1, name=""):
-    n = len(G["ops"])
-    deps = {}
+MASKS = {}
+SOLO = []
+
+
+def ref(T, name, *ix):
+    ix = ix or (_,)
+    if name not in SCRATCH: return (None, T[name][ix], 0, 0, 0, 4, False, None)
+    key = (name, repr(ix))
+    where, shape, dtype = SCRATCH[name]
+    if key not in MASKS:
+        fr = np.arange(int(np.prod(shape[1:]))).reshape(shape[1:])[ix[1:]]
+        MASKS[key] = (bits(np.arange(128)[ix[0]]), bits(np.asarray(fr)), int(np.asarray(fr).size))
+    return (name, T[name][ix]) + MASKS[key] + (SIZE.get(dtype, 2), where == "psum", None)
+
+
+def ind(win, off): return (win[0], win[1].indirect(off[1]), win[2], win[3], 16 * off[4], win[5], False, off)
+def ap(x): return x[1] if isinstance(x, tuple) else x
+
+
+def add(G, opts, fn, r=(), w=(), key=None, cnt=1, name=""):
+    n = len(G["ops"]); deps = {}
+    r = [x for x in r if isinstance(x, tuple)]
+    r += [x[7] for x in list(r) + list(w) if x[7] is not None]
+    engs = tuple(sorted(opts))
 
     def dep(j, raw):
         if j != n: deps[j] = deps.get(j, False) or raw
-    for (bn, lo, hi) in r:
-        for (a, b, j) in G["wr"].get(bn, []):
-            if a < hi and lo < b: dep(j, True)
-        G["rd"].setdefault(bn, []).append((lo, hi, n))
-    for (bn, lo, hi) in w:
-        for (a, b, j) in G["wr"].get(bn, []):
-            if a < hi and lo < b: dep(j, False)
-        for (a, b, j) in G["rd"].get(bn, []):
-            if a < hi and lo < b: dep(j, True)
-        G["wr"][bn] = [x for x in G["wr"].get(bn, []) if not (lo <= x[0] and x[1] <= hi)] + [(lo, hi, n)]
-        G["rd"][bn] = [x for x in G["rd"].get(bn, []) if not (lo <= x[0] and x[1] <= hi)]
-    engs = tuple(sorted(opts))
-    for bn in pr:
-        if bn in G["bw"]: dep(G["bw"][bn], True)
-        for j in G["br"].get(bn, []):
-            if G["ops"][j]["engs"] != engs or len(engs) > 1: dep(j, False)
-        G["br"].setdefault(bn, []).append(n)
-    for bn in pw:
-        if bn in G["bw"]: dep(G["bw"][bn], False)
-        for j in G["br"].get(bn, []): dep(j, False)
-        G["bw"][bn] = n; G["br"][bn] = []
-    G["ops"].append({"opts": opts, "engs": engs, "fn": fn, "deps": deps, "key": key, "cnt": cnt, "name": name, "h": G.get("h"), "t": G.get("t")})
+    for x in r:
+        if x[0] is None: continue
+        if x[6]:
+            if x[0] in G["bw"]: dep(G["bw"][x[0]], True)
+            for j in G["br"].get(x[0], []):
+                if G["ops"][j]["engs"] != engs or len(engs) > 1: dep(j, False)
+            continue
+        for (a, b, j) in G["wr"].get(x[0], []):
+            if a & x[2] and b & x[3]: dep(j, True)
+    for x in w:
+        if x[0] is None: continue
+        if x[6]:
+            if x[0] in G["bw"]: dep(G["bw"][x[0]], False)
+            for j in G["br"].get(x[0], []): dep(j, False)
+            G["bw"][x[0]] = n; G["br"][x[0]] = []
+            continue
+        for (a, b, j) in G["wr"].get(x[0], []):
+            if a & x[2] and b & x[3]: dep(j, True)
+        for (a, b, j) in G["rd"].get(x[0], []):
+            if a & x[2] and b & x[3]: dep(j, True)
+        for k in ("wr", "rd"): G[k][x[0]] = [y for y in G[k].get(x[0], []) if y[0] & ~x[2] or y[1] & ~x[3]]
+        G["wr"][x[0]].append((x[2], x[3], n))
+    for x in r:
+        if x[0] is None: continue
+        if x[6]: G["br"].setdefault(x[0], []).append(n)
+        else: G["rd"].setdefault(x[0], []).append((x[2], x[3], n))
+    G["ops"].append({"opts": opts, "engs": engs, "fn": fn, "deps": deps, "key": key, "cnt": cnt, "name": name, "t": G.get("t"), "h": G.get("h")})
     return n
 
 
@@ -130,538 +146,455 @@ def place(busy, t, d):
     return t, lo
 
 
-def schedule(G):
+def schedule(G, solo=False):
     ops = G["ops"]; n = len(ops)
-    succ = [[] for _ in range(n)]
+    succ = [[] for i in range(n)]
     for i, o in enumerate(ops):
         for j in o["deps"]: succ[j].append(i)
     pred = [list(o["deps"]) for o in ops]
 
-    def lag(j, ej, i, ei):
-        c = ops[j]["opts"][ej]
-        if ej != ei: return c[1] + WAKE
-        return c[1] + SAME if ops[i]["deps"][j] or ops[j]["key"] else c[0]
+    eng = [o["engs"][0] for o in ops]
+    use = [o["opts"][e][0] for o, e in zip(ops, eng)]; end = [o["opts"][e][1] for o, e in zip(ops, eng)]
+    lag = lambda j, i: end[j] + WAKE if eng[j] != eng[i] else end[j] + SAME if ops[i]["deps"][j] or ops[j]["key"] else use[j]
+    fore = [[(j, lag(j, i)) for j in pred[i]] for i in range(n)]
+    aft = [[(j, use[j] + lag(i, j) - use[i]) for j in succ[i]] for i in range(n)]
+    first = [(i, LOADS[o["name"]]) for i, o in enumerate(ops) if o["name"] in LOADS]
 
-    def sweep(key, before, eng, only=None):
-        at = [0.0] * n; on = [None] * n; busy = {}
-        idx = [i for i in range(n) if only is None or only[i]]
-        for j in (idx if eng is None else idx[::-1]):
-            for i in before[j]:
-                if only is None or only[i]: key[j] = max(key[j], key[i] + 1e-6)
-        for i in sorted(idx, key=lambda i: key[i]):
-            best = None
-            bf = before[i] if only is None else [j for j in before[i] if only[j]]
-            for e in (ops[i]["opts"] if eng is None else [eng[i]]):
-                c = ops[i]["opts"][e]
-                if eng is None: t = max([0.0] + [at[j] + lag(j, on[j], i, e) for j in bf])
-                else: t = max([c[1] - c[0]] + [at[j] + ops[j]["opts"][eng[j]][0] + lag(i, e, j, eng[j]) - c[0] for j in bf])
-                t, k = place(busy.setdefault(e, []), t, c[0])
-                if best is None or t + c[0] < best[0]: best = (t + c[0], t, k, e)
-            end, at[i], k, on[i] = best
-            busy[on[i]].insert(k, (at[i], end))
-        return at, on
+    link = {i: o["link"] for i, o in enumerate(ops) if "link" in o}
 
-    def both(prio, sweeps, only=None):
+    def sweep(key, before, least):
+        at = [0.0] * n; busy = {e: [] for e in eng}; wire = []
+        for i in sorted(range(n), key=lambda i: key[i]):
+            t = least[i]
+            for j, d in before[i]:
+                if at[j] + d > t: t = at[j] + d
+            b = busy[eng[i]]
+            if i in link:
+                while True:
+                    t, k = place(wire, place(b, t, use[i])[0], link[i])
+                    if place(b, t, use[i])[0] == t: break
+                wire.insert(k, (t, t + link[i]))
+            if not b or b[-1][1] <= t: b.append((t, t + use[i]))
+            else:
+                t, k = place(b, t, use[i]); b.insert(k, (t, t + use[i]))
+            at[i] = t
+        return at
+    none = [0.0] * n; tail = [end[i] - use[i] for i in range(n)]
+
+    def both(prio, sweeps):
         best = None
-        idx = [i for i in range(n) if only is None or only[i]]
         for it in range(sweeps):
-            at, eng = sweep(prio, pred, None, only)
-            fin = [at[i] + ops[i]["opts"][eng[i]][1] if eng[i] else 0.0 for i in range(n)]
-            if best is None or max(fin) < max(best[2]): best = (sorted(idx, key=lambda i: (at[i], i)), eng, fin, at)
-            back, _ = sweep([-(at[i] + ops[i]["opts"][eng[i]][0]) if eng[i] else 0.0 for i in range(n)], succ, eng, only)
-            prio = [-(back[i] + ops[i]["opts"][eng[i]][0]) if eng[i] else 0.0 for i in range(n)]
-            for i in idx:
-                if ops[i]["name"] in FIRST: prio[i] = FIRST.index(ops[i]["name"]) - 1e4
+            for i, k in first: prio[i] = k
+            for i in range(n - 1, -1, -1):
+                k = prio[i] - 1e-4
+                for j in pred[i]:
+                    if prio[j] > k: prio[j] = k
+            at = sweep(prio, fore, none)
+            fin = [at[i] + end[i] for i in range(n)]
+            if best is None or max(fin) < max(best[2]): best = (None, eng, fin, at)
+            if it + 1 < sweeps:
+                key = [-(at[i] + use[i]) for i in range(n)]
+                for i in range(n):
+                    k = key[i] - 1e-4
+                    for j in succ[i]:
+                        if key[j] > k: key[j] = k
+                back = sweep(key, aft, tail)
+                prio = [max(fin) - (back[i] + use[i]) for i in range(n)]
         return best, prio
-    prio = [0.0] * n
-    for i in range(n - 1, -1, -1):
-        prio[i] = min(x[1] for x in ops[i]["opts"].values()) + max([prio[s] + 0.5 * WAKE for s in succ[i]] or [0.0])
-    _, late = both([-p for p in prio], 3, [o["h"] == 0 and o["t"] is not None for o in ops])
-    blocks = {}
+    when = {}
+    for a, z, names in PLAN:
+        for k, x in enumerate(names.split()): when[x] = (a + (z - a) * k / len(names.split()), (z - a) / len(names.split()))
+    seen, total, key = {}, {}, [None] * n
+    for o in ops: total[o["t"], o["name"], o["h"]] = total.get((o["t"], o["name"], o["h"]), 0) + 1
     for i, o in enumerate(ops):
-        if o["t"] is not None: blocks.setdefault((o["t"], o["h"]), []).append(i)
-    key = [None] * n
-    for (t, h), b in blocks.items():
-        ref = blocks[t, 0]; byname = {}; seen = {}
-        for i in ref: byname.setdefault(ops[i]["name"], []).append(late[i] - late[ref[0]])
-        for i in b:
-            nm = ops[i]["name"]; k = seen.get(nm, 0); seen[nm] = k + 1
-            if k < len(byname.get(nm, [])): key[i] = (2 * t + h) * PER / 2 + STRETCH * byname[nm][k] - WT.get(nm, 0.0) - sum(SHORT.get(e, 0.0) for e, c in ops[i]["opts"].items() if c[0] < 0.3)
+        c = (o["t"], o["name"], o["h"]); k = seen.get(c, 0); seen[c] = k + 1
+        if o["t"] is not None and o["h"] is not None and o["name"] in when:
+            key[i] = START + o["t"] * PER[0] + ORD.index(o["h"]) * PER[2] + PER[1] * (when[o["name"]][0] + when[o["name"]][1] * k / total[c]) - WT.get(o["name"], 0.0)
     for i in range(n - 1, -1, -1):
-        if key[i] is None: key[i] = min([key[s] for s in succ[i]] or [1e3]) - min(x[1] for x in ops[i]["opts"].values()) - WT.get(ops[i]["name"], 0.0)
-    key = [FIRST.index(o["name"]) - 1e4 if o["name"] in FIRST else k for k, o in zip(key, ops)]
-    return both(key, SWEEPS)[0]
+        if key[i] is None: key[i] = min([key[s] for s in succ[i]] or [1e3]) - min(x[1] for x in ops[i]["opts"].values())
 
+    def deal(shift):
+        at = [0.0] * n; free = {e: 0.0 for e in eng}; ready = {e: [] for e in eng}; left = [len(p) for p in pred]; est = [0.0] * n; due = [0.0] * n; base = {}
 
-def vc(n, two=1.0): return n * two * CYC + 0.05
-def sc(n): return n * CYC + 0.065
-def gc_(n, e): return n * GCY * CYC + (0.05 if e == "V" else 0.065)
-def pc_(n, f32=False): return max(64.0, n) * CYC * PF * (4.0 if f32 else 1.0) + PO
+        def push(i):
+            o = ops[i]; t = 0.0
+            for j, d in fore[i]:
+                if at[j] + d > t: t = at[j] + d
+            est[i] = t; c = (o["t"], o["h"])
+            if o["name"] == "XK" and c not in base: base[c] = t
+            due[i] = base.get(c, t) + rel[i] + shift.get((o["name"], o["h"]), 0.0) if rel[i] is not None else key[i] if o["name"] in LOADS else t + shift.get((o["name"], o["h"]), 0.0)
+            ready[eng[i]].append(i)
+        for i in range(n):
+            if not left[i]: push(i)
+        for it in range(n):
+            c = None
+            for e, r in ready.items():
+                for i in r:
+                    x = max(est[i], free[e]) + use[i]
+                    if c is None or x < c: c = x; q = e
+            i = min([i for i in ready[q] if est[i] <= c], key=lambda i: due[i])
+            ready[q].remove(i); at[i] = max(est[i], free[q]); free[q] = at[i] + use[i]
+            for j in succ[i]:
+                left[j] -= 1
+                if not left[j]: push(j)
+        return at
+    if DEAL:
+        rel = [None if o["t"] is None or o["h"] is None or o["name"] not in when else key[i] - o["t"] * PER[0] - o["h"] * PER[2] - (LEAD[0] if o["h"] == 0 else 0) for i, o in enumerate(ops)]
+        for i, k in first: key[i] = k
+        key = deal(DEAL[0])
+        if SWEEPS == 0: return (sorted(range(n), key=lambda i: (key[i], i)), eng, [key[i] + end[i] for i in range(n)], key)
+    kinds = {}
+    for i, o in enumerate(ops): kinds.setdefault((o["name"], o["h"]), []).append(i)
+    kinds = list(kinds.values()); x = [SEED[0]]
+
+    def rnd():
+        x[0] = (x[0] * 1103515245 + 12345) % 2 ** 31
+        return x[0] / 2 ** 31
+
+    cases = []
+    for gather, fix, pe, po, wake, same, far, lat in CASES:
+        u = [(x - 0.06) * gather + 0.06 if o["name"] in INDIRECT else x + fix if e in "VS" else (x - PO) * pe + po if e == "P" else x for x, e, o in zip(use, eng, ops)]
+        z = [a + y - x + (far if e[0] == "N" else lat if o["key"] and o["key"][0] == "d" else 0.0) for a, x, y, e, o in zip(u, use, end, eng, ops)]
+        cases.append((u, z, [[(j, z[j] + (wake if eng[j] != eng[i] else same)) for j in pred[i] if eng[j] != eng[i] or ops[i]["deps"][j] or ops[j]["key"]] for i in range(n)]))
+
+    def score(b):
+        order = sorted(range(n), key=lambda i: (b[3][i], i)); s = 0.0
+        for u, z, before in cases:
+            at = [0.0] * n; free = {e: 0.0 for e in eng}; last = 0.0
+            for i in order:
+                t = free[eng[i]]
+                for j, d in before[i]:
+                    if at[j] + d > t: t = at[j] + d
+                at[i] = t; free[eng[i]] = t + u[i]
+                if t + z[i] > last: last = t + z[i]
+            s += last
+        return (s + max(b[2])) / (len(cases) + 1)
+
+    def mend(best, tries):
+        cur = best; low = now = score(best)
+        for it in range(tries):
+            key = list(cur[3])
+            for k in range(1 + int(rnd() * TRIES[1])):
+                d = (rnd() - 0.5) * TRIES[2]
+                for i in kinds[int(rnd() * len(kinds))]: key[i] += d
+            new = both(key, 1 + (rnd() < 0.3))[0]
+            if max(new[2]) > max(cur[2]) + 3.0: continue
+            s = score(new)
+            if s <= now + TRIES[3] * (1 - it / tries) * rnd(): cur = new; now = s
+            if now < low: best = cur; low = now
+        SOLO.append(low)
+        return best, low
+    starts = [mend(both([k + (d if o["h"] == ORD[1] and o["t"] is not None else 0.0) for k, o in zip(key, ops)], SWEEPS)[0], TRIES[0] // (2 * len(APART))) for d in APART]
+    best = mend(min(starts, key=lambda b: b[1])[0], TRIES[0] // 2)[0]
+    return (sorted(range(n), key=lambda i: (best[3][i], i)),) + best[1:]
 
 
 def build(core, T, topo, rank):
-    G = new_graph()
-    W = lambda n: (n, 0, 1 << 20)
-    keys = {}
+    G = {"ops": [], "wr": {}, "rd": {}, "bw": {}, "br": {}}
+    nd = [0]
+    R = lambda n, *ix: ref(T, n, *ix)
 
-    def vop(fn, n, r=(), w=(), pr=(), pw=(), two=1.0, name="", c=None):
-        c = c or vc(n, two)
-        return add(G, {"V": (c, c)}, lambda Q, e: fn(Q["V"]), r, w, pr, pw, name=name)
+    def cost(e, o, ins, two=False):
+        fix = 0.05 if e == "V" else 0.065
+        ts_ = [x for x in [o] + ins if isinstance(x, tuple) and x[4] > 1]
+        n = max([1] + [x[4] for x in ts_])
+        if o[7] is not None: return fix + max(n, 56) * SCY * CYC
+        if any(x[7] is not None for x in ts_): return fix + n * GCY * CYC
+        if e == "S": return fix + n * CYC
+        if two: return fix + n * CYC * (1.0 if any(x[6] for x in ts_) else 2.0)
+        return fix + n * CYC * (0.5 if all(x[5] == 2 for x in ts_) else 1.0)
 
-    def tt(o, a, b, op, n, r=(), w=(), pr=(), name="", pw=(), c=None):
-        vop(lambda v: v.tensor_tensor(o, a, b, op), n, r, w, pr, pw, two=1.0 if pr else 2.0, name=name, c=c)
+    def vop(fn, o, ins, name, two=False):
+        c = cost("V", o, ins, two)
+        return add(G, {"V": (c, c)}, lambda Q, e: fn(Q["V"]), ins, [o], name=name)
 
-    def ts(o, a, s1, op0, n, r=(), w=(), pr=(), s2=None, op1=None, two=1.0, name=""):
-        if op1 is None: vop(lambda v: v.tensor_scalar(o, a, s1, None, op0), n, r, w, pr, two=two, name=name)
-        else: vop(lambda v: v.tensor_scalar(o, a, s1, s2, op0, op1), n, r, w, pr, two=two, name=name)
+    def tt(o, a, b, op, name=""): return vop(lambda v: v.tensor_tensor(o[1], a[1], b[1], op), o, [a, b], name, True)
 
-    def cpv(o, a, n, r=(), w=(), pr=(), name=""):
-        vop(lambda v: v.tensor_copy(o, a), n, r, w, pr, name=name)
+    def ts(o, a, s1, op0, s2=None, op1=None, name=""):
+        if op1 is None: return vop(lambda v: v.tensor_scalar(o[1], a[1], ap(s1), None, op0), o, [a, s1], name)
+        return vop(lambda v: v.tensor_scalar(o[1], a[1], ap(s1), ap(s2), op0, op1), o, [a, s1, s2], name)
 
-    def scan(o, a, n, r=(), w=(), pr=(), name=""):
-        vop(lambda v: v.tensor_tensor_scan(o, X("NF"), a, 0.0, OP.mult, OP.max), n, list(r) + [W("NF")], w, pr, name=name)
+    def cpv(o, a, name=""): return vop(lambda v: v.tensor_copy(o[1], a[1]), o, [a], name)
+    def scan(o, d0, a, op0, init, name): return vop(lambda v: v.tensor_tensor_scan(o[1], d0[1], a[1], init, op0, OP.max), o, [d0, a], name)
+    def fill(o, v, name="fill"): return vop(lambda q: q.memset(o[1], v), o, [], name)
 
-    def flex(o, a, n, r=(), w=(), pr=(), name="", gather=False, only=None, two=1.0, bias=None, scale=1.0):
-        opts = {"V": (gc_(n, "V") if gather else vc(n, two),) * 2, "S": (gc_(n, "S") if gather else sc(n),) * 2}
-        only = only or (None if G.get("free") and gather else ASG.get(name))
-        if only: opts = {only: opts[only]}
+    def flex(o, a, name="", bias=None, scale=1.0, only=None):
+        opts = {e: (cost(e, o, [a]),) * 2 for e in (only or ASG.get(name, "VS"))}
 
         def fn(Q, e):
-            if bias is None: return Q["V"].tensor_copy(o, a) if e == "V" else Q["S"].activation(o, a, COPY)
-            return Q["V"].tensor_scalar(o, a, scale, bias, OP.mult, OP.add) if e == "V" else Q["S"].activation(o, a, COPY, bias=bias, scale=scale)
-        return add(G, opts, fn, r, w, pr, name=name)
+            if bias is None: return Q["V"].tensor_copy(o[1], a[1]) if e == "V" else Q["S"].activation(o[1], a[1], COPY)
+            if e == "V": return Q["V"].tensor_scalar(o[1], a[1], scale, ap(bias), OP.mult, OP.add)
+            return Q["S"].activation(o[1], a[1], IDENT if isinstance(bias, tuple) else COPY, bias=ap(bias), scale=ap(scale))
+        return add(G, opts, fn, [a, bias, scale], [o], name=name)
 
-    def act(o, a, n, func=COPY, bias=0.0, scale=1.0, r=(), w=(), pr=(), name="", c=None):
-        c = c or sc(n)
-        return add(G, {"S": (c, c)}, lambda Q, e: Q["S"].activation(o, a, func, bias=bias, scale=scale), r, w, pr, name=name)
+    def act(o, a, func, bias=0.0, scale=1.0, name=""):
+        c = cost("S", o, [a])
+        return add(G, {"S": (c, c)}, lambda Q, e: Q["S"].activation(o[1], a[1], func, bias=ap(bias), scale=scale), [a, bias], [o], name=name)
 
-    def mm(o, l, rh, start, stop, bank, n, r=(), f32=False, name=""):
-        c = pc_(n, f32)
-        return add(G, {"P": (c, c)}, lambda Q, e: Q["P"].matmul(o, l, rh, start, stop), r, (), (), (bank,), name=name)
+    def mm(o, l, rh, start=True, stop=True, name=""):
+        c = max(min(64, l[4]), rh[4]) * CYC * PF * (4.0 if l[5] == 4 else 1.0) + PO
+        return add(G, {"P": (c, c)}, lambda Q, e: Q["P"].matmul(o[1], l[1], rh[1], start, stop), [l, rh], [o], name=name)
 
-    def grp(o, bank, terms, name, n=128, start=True, stop=True):
-        for j, x in enumerate(terms):
-            mm(o, x[0], x[1], start and j == 0, stop and j == len(terms) - 1, bank, n, r=x[2], f32=len(x) > 3, name=name)
+    def grp(o, terms, name, start=True, stop=True):
+        for j, x in enumerate(terms): mm(o, x[0], x[1], start and j == 0, stop and j == len(terms) - 1, name)
 
-    def gop(fn, n, r=(), w=(), name=""):
-        c = 0.14 + 2 * n * CYC
-        return add(G, {"G": (c, c)}, lambda Q, e: fn(Q["G"]), r, w, name=name)
+    def iota(o, pat, base, cm=0, name=""):
+        c = 0.14 + 2 * o[4] * CYC
+        flag = {} if o[0] == "pi" else {"allow_small_or_imprecise_dtypes": True}
+        return add(G, {"G": (c, c)}, lambda Q, e: Q["G"].iota(o[1], pat, base, cm, **flag), [], [o], name=name)
 
-    def iota(o, pat, base, n, w, cm=0):
-        return gop(lambda g: g.iota(o, pat, base, cm, allow_small_or_imprecise_dtypes=True), n, w=w, name="up" if G.get("up") else "")
+    def gcopy(o, a, name):
+        c = 0.17 + 2 * o[4] * CYC
+        return add(G, {"G": (c, c)}, lambda Q, e: Q["G"].affine_select(o[1], a[1], [[0, o[4]]], OP.is_ge, 0.0, 0, 0), [a], [o], name=name)
 
-    def fill(o, v, n, w): vop(lambda q: q.memset(o, float(v)), n, w=w, two=0.5, name="fill")
+    def dma(o, a, kb, name, q="Y", rows=64):
+        k = "d%d" % nd[0]; nd[0] += 1
+        c = kb / RATE + rows / 16 * ROW
+        return add(G, {q: (c if q == "Y" else 0.15, LAT + c)}, lambda Q, e: Q[e].dma_start(o[1], a[1]).then_inc(T.sem[k], 16), [a], [o], key=k, cnt=16, name=name)
 
-    def dma(o, a, kb, key, r=(), w=(), q="Y", name=""):
-        k = "d%d" % keys.setdefault(key, len(keys))
-        return add(G, {q: (max(0.15, kb / RATE) if q == "Y" else 0.15, LAT + kb / RATE)}, lambda Q, e: (Q["Y"] if e == "Y" else Q["S"]).dma_start(o, a).then_inc(T.sem[k], 16), r, w, key=k, cnt=16, name=name)
-
-    def send(dsts, src_ap, land, sem, r, name):
-        ne = len(topo.engines(core, dsts[0]))
+    def send(ds, src, land, sem, kb, name):
+        dsts = [T.cores[(rank - d) % NR] for d in ds]
         for x in dsts: assert topo.may_write(core, x) and topo.mask(core, x) == topo.mask(core, dsts[0])
 
         def fn(Q, e):
-            if len(dsts) == 1:
+            if len(ds) == 1:
                 rid, pid = topo.addr(dsts[0])[:2]
-                Q["G"].remote_dma(out_ap=land, in_ap=src_ap, remote_sem=T.sem[sem], local_sem=T.sem.loc, pid=pid, routing_id=rid, dma_engine_mask=topo.mask(core, dsts[0]))
+                Q["G"].remote_dma(out_ap=land(ds[0])[1], in_ap=src[1], remote_sem=T.sem[sem], local_sem=T.sem.loc, pid=pid, routing_id=rid, dma_engine_mask=topo.mask(core, dsts[0]))
             else:
                 ids = [DstId(rid=topo.addr(x)[0], pnc=topo.addr(x)[1]) for x in dsts]
-                Q["G"].remote_dma_fused([RemoteDMATransfer(dst_ids=ids, dma_engine_mask=topo.mask(core, dsts[0]), remote_sem=T.sem[sem], srcs=[src_ap], dsts=[land for x in dsts])], local_sem=T.sem.loc)
-        return add(G, {"G": (1.0, 1.0)}, fn, r, (), key="loc", cnt=ne, name=name)
+                Q["G"].remote_dma_fused([RemoteDMATransfer(dst_ids=ids, dma_engine_mask=topo.mask(core, dsts[0]), remote_sem=T.sem[sem], srcs=[src[1]], dsts=[land(d)[1] for d in ds])], local_sem=T.sem.loc)
+        s = add(G, {"G": (1.0, 1.0)}, fn, [src], [], key="loc", cnt=len(topo.engines(core, dsts[0])), name=name)
+        G["ops"][s]["link"] = kb * len(ds) / LINK[0]
+        i = add(G, {"N" + sem: (0.0, FAR + kb * len(ds) / LINK[0])}, None, [], [land(d) for d in ds], key=sem, cnt=sum(len(topo.engines(T.cores[(rank + d) % NR], core)) for d in ds), name="arrive")
+        G["ops"][i]["deps"][s] = True
+        return s
 
-    def arrive(src_rank, t, h, after, kb):
-        nm = "%d_%d_%d" % (t, h, src_rank)
-        i = add(G, {"N" + nm: (0.0, FAR + kb / 30.0)}, None, (), (W("L" + nm),), key="ar" + nm, cnt=len(topo.engines(T.cores[src_rank], core)), name="arrive")
-        G["ops"][i]["deps"][after] = True
+    def X(n): return R("CG", _, 0, slice(128 * TMP.index(n), 128 * TMP.index(n) + 128)) if n in TMP else R("CB", _, CBN.index(n)) if n in CBN else R("CH", _, CHN.index(n)) if n in CHN else R("CX", _, CXN.index(n))
+    def sl(a, b=None, c=None): return slice(a, b, c)
 
-    H = (0, 1)
-    LO, UP = slice(0, 64), slice(64, 128)
-
-    def sets():
-        for h in H:
-            G["h"] = h
-            yield h
-        G["h"] = None
-
-    def X(n): return T.CB[:, CBN.index(n)] if n in CBN else T.CH[:, CHN.index(n)] if n in CHN else T.CX[:, CXN.index(n)]
-    def P(n, h): return T["p" + n + str(h)]
-    def B(n, h): return T[n][:, h]
-    def LU(t, h, r): return T.LU[:, 8 * (t - 1) + 4 * h + r]
-    def S(j): return slice(128 * j, 128 * j + 128)
-
-    def swap(buf, rows, a, n, kb, key, r, w, name):
-        dma(buf[rows(1), a - HV:a], buf[rows(0), a:a + HV], kb, key, r=r, w=[w[0]], name=name)
-        dma(buf[rows(0), a + HV:a + V_], buf[rows(1), a:a + HV], kb, key, r=r, w=[w[1]], name=name, q=n)
-
-    dma(T.CI[:], T.ctl[:], 98, "ctl", w=[W("CI")], name="ld ctl")
-    for h in sets():
-        g4 = slice(64 * h, 64 * h + 64)
-        for hh, pp in enumerate((LO, UP)):
-            if h == 0: dma(T.OI[pp, :], T.hol[g4, HV * hh:HV * hh + HV], 393, "hol0", w=[("OI", hh, hh + 1)], name="ld hol0")
-            dma(T["XX%d" % h][pp, HV * (1 - hh):HV * (1 - hh) + V_], T.sha[g4, :], 393, "sha%d" % h, w=[("X%d" % h, hh, hh + 1)], name="ld sha%d" % h)
-            for e in range(2 if CO else 0):
-                dma(T.TI[pp, h, :, e], T.ctl[4 * h + e:4 * h + 4:2, HV * hh:HV * hh + HV], 12, "list%d" % h, w=[("TI%d" % h, 2 * hh + e, 2 * hh + e + 1)], q="S", name="ld list")
-    cpv(T.CF[:], T.CI[:], 192, r=[W("CI")], w=[W("CF")], name="send0")
-    cpv(T.HL0[:, 0:192], T.CF[:], 192, r=[W("CF")], w=[("HL0", 0, 192)], name="send0")
-    tt(T.HL0[:, 192:384], T.CF[:], T.HL0[:, 0:192], OP.subtract, 192, r=[W("CF"), ("HL0", 0, 192)], w=[("HL0", 192, 384)], name="send0")
-    first = T.cores[(rank - D_OF[0]) % NR]
-    rest = [T.cores[(rank - d) % NR] for d in (1, 2, 3) if (rank - d) % NR != (rank - D_OF[0]) % NR]
-    lands = "L0_%d" % rank
-    s1 = send([first], T.HL0[:], T[lands][:], "ar0_0_%d" % rank, [W("HL0")], "send0")
-    s2 = send(rest, T.HL0[:], T[lands][:], "ar0_0_%d" % rank, [W("HL0")], "send0b")
-    gop(lambda g: g.iota(T.pi[:], [[1, 1]], 0, 1), 1, w=[W("pi")])
-    iota(T.ci[:], [[1, 128]], 0, 128, [W("ci")])
-    iota(T.cg[:], [[1, 8], [0, 16]], 0, 128, [W("cg")])
-    iota(T.cq[:], [[0, 8], [1, 16]], 0, 128, [W("cq")])
-    iota(T.c2[:], [[1, 8], [0, 2]], 0, 16, [W("c2")])
-    Wq = lambda k: T.wq[:, k:k + 1]
-    wq = lambda k: ("wq", k, k + 1)
-    OFF, OFF1, OFFZ, P64 = range(40, 44)
-    late = [iota(T.HH[:], [[HV, 2], [0, 4]], 0, 8, [W("HH")]), iota(T.c3[:], [[-128, 2], [0, 64]], 0, 128, [W("c3")]), iota(T.VL[:], [[1, 4], [0, 32], [12, 4]], 0, 512, [W("VL")]),
-            iota(T.VC[:, 0:4], [[-1, 4]], MID, 4, [("VC", 0, 4)], -12), iota(T.VC[:, 4:8], [[1, 4]], MID, 4, [("VC", 4, 8)], 12), iota(T.VC[:, 8:9], [[1, 1]], V_ + 1 - int(BIG) - 17 * int(CEN), 1, [("VC", 8, 9)], 1)]
-    for hh, pp in enumerate((LO, UP)):
-        hw = lambda n: [(n, hh, hh + 1)]
-        G["up"] = hh
-        iota(T.wq[pp, OFF:OFF + 2], [[-1, 2]], HV * (1 - hh), 2, [("wq", OFF, OFF + 2)])
-        late += [iota(T.wq[pp, OFFZ:OFFZ + 1], [[0, 1]], HV * (1 - hh) + 65535 + 16 * int(CEN), 1, [wq(OFFZ)]), iota(T.wq[pp, P64:P64 + 1], [[0, 1]], 64 * (1 - hh), 1, [wq(P64)], 1),
-                 iota(T.SPL[pp, :], [[128 - 256 * hh, 2], [16, 8]], V_ + 1 - 65536 - 16 * int(CEN) + 128 * hh, 16, hw("SPL")), iota(X("VH")[pp], [[48, 32], [0, 4]], HV * (hh - 1), 128, hw("VH")),
-                 iota(T.VB[pp, :], [[-1, 4], [-192, 8]], -HV * hh, 32, hw("VB")), iota(T.VR[pp], [[1, 4], [12, 128]], HV * hh, 512, hw("VR")), iota(X("LR")[pp], [[1, 128]], 128 * hh, 128, hw("LR")),
-                 iota(X("LRx")[pp], [[1 - hh, 128]], (128, -4096)[hh], 128, hw("LRx")), iota(X("KM")[pp], [[0, 128]], (0 if GS else WW) + MID + HV * (1 - hh), 128, hw("KM"))]
-    G["up"] = 0
-    for nmx, v in (("ONE", 1), ("KH", MID + 12288), ("KL", MID - 12288)): late.append(iota(X(nmx), [[0, 128]], v, 128, [W(nmx)]))
-    late.append(iota(X("K1"), [[0, 8], [-1, 16]], 15, 128, [W("K1")]))
-    late.append(iota(X("K2"), [[0, 8], [-1, 16]], 31, 128, [W("K2")]))
-    for h in sets():
-        O = T["O%d" % h]
-        fill(T["WC%d" % h][:], -MID, V_, [W("WC%d" % h)])
-        for j, (pp, a) in enumerate(((UP, 0), (LO, V_)) if CO else ()): fill(T["CC%d" % h][pp, a:a + HV], -MID, HV, [("CC%d" % h, 10 + j, 11 + j)])
-        for j, (pp, a) in enumerate(((LO, WW), (UP, V_))):
-            G["up"] = j
-            late.append(iota(O[pp, a:a + PAD], [[0, PAD]], 0, PAD, [("O%d" % h, 3 + j, 4 + j)]))
-        G["up"] = 0
-        for s in range(0 if h else 7): late.append(iota(T.PQ[:, :, s], [[0, 320]], 0, 320, [("PQ", s, s + 1)]))
-        late.append(iota(T.HLz[:, 4 * h:4 * h + 4], [[0, 512]], 0, 512, [("HLz", 4 * h, 4 * h + 4)]))
-        late.append(iota(B("OC", h)[:, 128:256], [[0, 128]], 0, 128, [("OC%d" % h, 1, 2)]))
-        for u in range(0, 8, 4): late.append(iota(B("DE", h)[:, u:u + 4], [[0, 1024]], 0, 1024, [("DE%d" % h, u, u + 4)]))
+    half = list(enumerate((LO, UP)))
+    for x, pp in half: dma(R("CI", pp), R("ctl"), 98, "ld ctl", "YS"[x])
+    for x, pp in half: dma(R("XR", pp), R("sha", sl(x, 128, 16)), 49, "ld xr", "S")
+    iota(R("pi"), [[1, 1]], 0, 1)
+    cpv(R("ti", _, sl(0, 1)), R("pi"))
+    for o, k, op in ((1, 4, OP.arith_shift_right), (2, 15, OP.bitwise_and), (3, 63, OP.bitwise_and)): ts(R("ti", _, sl(o, o + 1)), R("pi"), k, op)
+    cpv(R("tf"), R("ti"))
+    F = lambda k: R("tf", _, sl(k, k + 1))
+    Wq = lambda k: R("wq", _, sl(k, k + 1))
+    ts(Wq(12), F(0), 64.0, OP.is_lt, 1 / 128, OP.mult)
+    ts(Wq(13), Wq(12), -65.0, OP.mult, 1 / 128, OP.add); ts(Wq(14), Wq(12), 85.5 * 128, OP.mult, -1.5, OP.add)
+    ts(R("CHi"), R("CI"), 1 / 64, OP.mult, 168.0, OP.add, "dig")
+    ts(R("CA"), R("CI"), Wq(12), OP.mult, name="dig")
+    flex(R("PR"), R("CHi"), "dig", bias=Wq(14), scale=Wq(13), only="S")
+    tt(R("HL0"), R("CA"), R("PR"), OP.add, "dig")
+    s2 = send(D_OF[:1], R("HL0"), lambda d: R("L%d" % d), "ar0_0", 98, "send0")
+    send(D_OF[1:3], R("HL0"), lambda d: R("L%d" % d), "ar0_1", 98, "send0b")
+    tt(R("PR"), R("XR"), R("HL0"), OP.add, "PR")
+    dma(R("XX", _, sl(0, V_)), R("sha"), 786, "ld sha", "Y", 128)
+    for c in range(2):
+        cs = sl(MID * c, MID * c + MID)
+        for e in range(2): flex(R("P", _, sl(MID * c + 768 * e, MID * c + 768 * e + 768)), R("XX", _, sl(MID * c + 768 * e, MID * c + 768 * e + 768)), "P0", only="SV"[e])
+        flex(R("XX", _, sl(V_ + MID * c, V_ + MID * c + MID)), R("XX", _, cs), "negX", bias=0.0, scale=-1.0, only="V")
+    for x, pp in half: dma(R("P", sl(x, 128, 16)), R("PR", pp), 98, "ld rows")
+    for h in ORD:
+        cs = sl(MID * h, MID * h + MID)
+        dma(R("OI", _, cs), R("hol", _, cs), 786, "ld hol%d" % h, "Y", 128)
+        cpv(R("LA", _, h), R("OI", _, sl(MID * h, MID * h + MID, 12)), "LA")
+        for c in range(2): cpv(R("O", _, sl(MID * h + 768 * c, MID * h + 768 * c + 768)), R("OI", _, sl(MID * h + 768 * c, MID * h + 768 * c + 768)), "O32")
+    fill(R("O", _, sl(V_, V_ + 32)), 0.0)
+    for d in (1, 2, 3):
+        if d == D_OF[0]: fill(R("WC%d" % d), 0.0)
+        else: G["ops"][iota(R("WC%d" % d), [[0, V_]], 0, name="zero")]["deps"][s2] = False
+        for x, pp in half: dma(R("WC%d" % d, sl(x, 128, 16)), R("L%d" % d, pp), 49, "ld flat" if d == D_OF[0] else "flat")
+    for n, pat, base in (("ci", [[1, 128]], 0), ("cg", [[1, 8], [0, 16]], 0), ("cq", [[0, 8], [1, 16]], 0), ("c64", [[0, 2], [1, 64]], 0), ("cd", [[8, 2], [16, 4], [0, 16]], 0)): iota(X(n), pat, base)
+    late = [iota(X(n), pat, base) for n, pat, base in (("K1", [[0, 8], [-1, 16]], 15), ("ONE", [[0, 128]], 1), ("KH", [[0, 128]], MID + int(BIG)), ("KL", [[0, 128]], MID - int(BIG)),
+                                                        ("c32", [[0, 4], [1, 32]], 0), ("cw0", [[2, 4], [0, 32]], 0), ("cw1", [[2, 4], [0, 32]], 1))]
+    late.append(iota(R("c8p"), [[1, 2], [2, 4]], 0))
+    late += [iota(R("pk"), [[-1, 8]], 0, 1), iota(R("c8"), [[1, 4], [4, 2]], 0), iota(R("VC"), [[1, 4], [MID, 2]], -MID, 12), iota(R("VR"), [[1, 4], [12, 256]], 0), iota(R("SB"), [[0, 288]], 0), iota(R("VB"), [[-1, 4], [-MID, 2], [-192, 8]], 0)]
     for i in late: G["ops"][i]["deps"][s2] = False
+    fill(R("SA"), 0.0); fill(R("Zt"), 0.0)
+    c8 = R("CG", _, 0, sl(0, 8))
+    ts(X("Ib"), X("ci"), F(0), OP.is_equal)
+    for n, s in (("I128", 128), ("I8192", 8192), ("IB", BIG), ("ImB", -BIG), ("Im3072", -V_), ("Id128", 1 / 128), ("Imh2", -0.5), ("Ih", 1), ("Imh", -1), ("Im128", -128), ("Im8192", -8192), ("Ih128", 1 / 128), ("I32h", 32), ("Im16h", -16)):
+        flex(X(n), X("Ib"), bias=0.0, scale=float(s))
+    ts(X("BOb"), X("cg"), F(1), OP.is_equal)
+    for n, s in (("BOh", 1.0), ("BOm", -1.0)): flex(X(n), X("BOb"), bias=0.0, scale=s)
+    ts(X("QB"), X("cq"), F(2), OP.is_equal, BIG, OP.mult)
+    ts(Wq(10), F(2), float(V_ + 16), OP.add); ts(Wq(11), F(2), 16.0, OP.add)
+    for e in range(2):
+        ts(X("TR%d" % e), X("c32"), (F(2), Wq(11))[e], OP.is_ge, BIG, OP.mult)
+        ts(X("ME%d" % e), X("cw%d" % e), F(1), OP.is_equal, -1.0, OP.mult)
+        ts(R("N32", _, sl(128 * e, 128 * e + 128)), X("c32"), 0.0, OP.not_equal)
+    ts(R("S1p"), R("c8p"), F(1), OP.is_equal)
+    ts(X("NF"), X("cq"), 0.0, OP.not_equal)
+    ts(X("NFa"), X("cq"), 0.0, OP.is_equal, -2.0 ** 30, OP.mult)
+    ts(Wq(0), F(2), 0.0, OP.is_equal); ts(Wq(1), F(2), 1.0, OP.is_equal)
+    ts(Wq(2), Wq(1), 64.0, OP.mult, Wq(0), OP.add); ts(Wq(2), Wq(2), 128.0, OP.mult)
+    ts(Wq(3), Wq(1), -1 / 64, OP.mult, Wq(0), OP.add); ts(Wq(3), Wq(3), 96.0, OP.mult)
+    ts(Wq(4), F(0), 64.0, OP.is_lt, 4095.0, OP.mult); ts(Wq(4), Wq(4), 1.0, OP.add)
+    ts(Wq(5), F(2), float(V_), OP.add)
+    for n in ("S1h", "S1b", "U8"): ts(R(n), c8, F(1), OP.is_equal)
+    ts(R("Rc"), c8, F(1), OP.is_equal, Wq(2), OP.mult)
+    for j, w in ((0, Wq(0)), (1, Wq(1)), (2, 1.0)): ts(R("Rd", _, j), c8, F(1), OP.is_equal, w, OP.mult)
+    ts(R("R16"), R("c8"), F(1), OP.is_equal, 16.0, OP.mult)
+    ts(X("A1"), X("c64"), F(3), OP.is_equal, Wq(4), OP.mult)
+    for k in range(8):
+        ts(R("WD", _, k), X("cd"), R("pk", _, sl(k, k + 1)), OP.is_equal, 4096.0, OP.mult)
+        tt(R("WD", _, k), X("A1"), R("WD", _, k), OP.subtract)
+    flex(R("VRh"), R("VR"), bias=-float(MID))
+    cpv(R("CA", LO), R("CI", LO))
+    dma(R("YC", sl(0, 8)), R("CA", LO), 98, "yc0")
 
-    for d in (1, 2, 3): arrive((rank + d) % NR, 0, 0, s1 if d == D_OF[0] else s2, 98 if d == D_OF[0] else 196)
+    def firms(t):
+        for c in range(7, -1, -1):
+            if 2 * (c % 4) >= STS[c // 4]: iota(R("VT", _, t % 2, sl(512 * c, 512 * c + 512)), [[12, 32], [0, 16]], t + 384 * c, name="VT")
 
-    def flat(d, h):
-        s = (rank + d) % NR
-        src, sr = (T["L0_%d" % s], W("L0_0_%d" % s)) if d else (T.HL0, W("HL0"))
-        for hh in H:
-            for x in H:
-                k = 4 * d + 2 * hh + x
-                dma(T["WC%d" % h][64 * hh + d + 8 * x:64 * hh + 64:16, :], src[64 * h:64 * h + 64, 192 * x:192 * x + 192], 25, "flat%d%d" % (min(d, 2), h), r=[sr], w=[("WC%d" % h, k, k + 1)], name="flat")
-    for h in sets(): flat(D_OF[0] if CO else 0, h)
-    def an(o, src, k, op, rr): ts(T.ti[:, o:o + 1], src, k, op, 1, r=rr, w=[("ti", o, o + 1)])
-    cpv(T.ti[:, 0:1], T.pi[:], 1, r=[W("pi")], w=[("ti", 0, 1)])
-    for o, k, op in ((1, 4, OP.arith_shift_right), (2, 15, OP.bitwise_and), (3, 5, OP.arith_shift_right), (5, 6, OP.arith_shift_right), (6, 7, OP.bitwise_and)): an(o, T.pi[:], k, op, [W("pi")])
-    an(4, T.ti[:, 1:2], 1, OP.bitwise_and, [("ti", 1, 2)])
-    cpv(T.tf[:, 0:7], T.ti[:, 0:7], 7, r=[W("ti")], w=[W("tf")])
-    F = lambda k: T.tf[:, k:k + 1]
-    tfr = [W("tf")]; rc = tfr + [W("ci")]; rq = tfr + [W("cq")]; rg = tfr + [W("cg")]
+    def front(t, h):
+        B = lambda n, *ix: R(SAME_AS.get(n, n), _, h, *ix)
+        bank = lambda n: (lambda *ix: R("p%s%d" % (n, h), _, *ix))
+        A, Bk, C, D = bank("A"), bank("B"), bank("C"), bank("D")
+        col = lambda b, s, k: b(s, sl(k, None, 16))
+        rows = lambda n, k, m=16: B(n, sl(k, None, m))
+        O, P, XX, WC = "O", "P", "XX", "WC%d" % D_OF[t]
+        hs = sl(MID * h + t, MID * h + MID, 12); ls = sl(128 * h, 128 * h + 128)
+        n = 128 // NPG
+        pcs = [(sl(16 * c, 16 * (c + n)), sl(c, c + n)) for c in range(0, 128, n)]
+        Xw, Ow = R(XX, _, sl(0, V_)), R(O)
+        if t: cpv(B("LA"), R(O, _, hs), "LA")
+        on = lambda x, j: "V" if (x, h, j) in ONV else "S"
+        for j, (a, b) in enumerate(pcs): flex(B("XK", a), ind(R(P), B("LA", b)), "XK", only=on("XK", j))
+        for k in range(16): mm(col(A, sl(0, 3), k), rows("XK", k), R("Rd"), name="dec")
+        flex(B("KS", sl(0, 2)), A(sl(0, 2)), "Y2")
+        flex(B("R3"), A(sl(0, 3)), "R3", bias=float(MID))
+        grp(C(0), [(B("KS", 0), X("I128")), (B("KS", 1), X("I8192")), (B("R3", 0), X("Im128")), (B("R3", 1), X("Im8192"))], "uT")
+        ts(B("LC"), C(0), MID * 8321.0, OP.add, name="LC")
+        for j, (a, b) in enumerate(pcs): flex(B("CG", a), ind(R(WC), B("LC", b)), "CG", only=on("CG", j))
+        flex(B("aN"), R(O, _, hs), "aN", bias=-float(MID))
+        for j in range(4): mm(Bk(_, sl(j, None, 4)), X("Ib"), R(XX, _, hs), name="XV")
+        for k in range(4): tt(rows("MN", k, 4), rows("XK", k, 4), Bk(), OP.min, "MN")
+        for k in sorted(range(16), key=lambda k: k % 4): mm(col(D, 1, k), rows("MN", k), R("S1h"), name="mL")
+        flex(B("S2", _, 1), D(1), "mS", bias=float(MID))
+        for k in range(16): mm(col(C, 1, k), rows("CG", k), R("Rc"), name="cL")
+        flex(B("S2", _, 0), C(1), "cS")
+        for a, pp in half: mm(R("pA%d" % h, pp, 0), B("S2", a, 0), X("Ih"), name="TK")
+        for a in range(2): mm(A(1 + a), B("S2", a), X("Ih"), name="TK")
+        flex(B("KS"), A(sl(0, 3)), "KS")
+        cK = B("KS", 0)
+        key = D(0)
+        mm(key, X("Ib"), X("K1"), True, False, "K1")
+        for i in range(4):
+            b = (Bk, C)[i % 2]
+            for e in range(2): mm(b(sl(2 * e, 2 * e + 2)), R("WD", _, 2 * i + e), B("KS", sl(1, 3)), name="D")
+            ts(B("WL", sl(2 * i, 2 * i + 2)), b(), float(MID), OP.max, MID + 4096.0, OP.min, "clip")
+            for e in range(2):
+                for a in range(2): mm(D(0, sl(64 * a + 2 * i + e, 64 * a + 64, 8)), B("WL", 2 * i + e, a), R("R16"), False, i + e + a == 5, "pool")
+        flex(B("hi"), key, "hi", bias=2.0 ** 23 - 32767)
+        tt(key, key, B("hi"), OP.subtract, "hi-")
+        scan(B("F"), X("NFa"), key, OP.add, 0.0, "F")
+        scan(B("TT", sl(None, None, -1)), X("NFa"), B("F", sl(None, None, -1)), OP.add, 0.0, "T")
+        tt(B("oh"), B("TT"), key, OP.is_equal, "oh")
+        mm(A(0), B("oh"), X("Ib"), name="ohT")
+        tt(B("wN"), cK, A(0), OP.mult, "wN")
+        mm(A(1), X("BOh"), B("wN"), name="bR")
+        grp(Bk(0), [(X("Ib"), X("QB")), (B("wN"), X("BOh"))], "bL")
+        tt(B("mine"), cK, A(1), OP.is_equal, "mine")
+        grp(A(2), [(X("Ih"), B("aN")), (X("Im3072"), B("mine"))], "LMp")
+        ts(B("LM"), A(2), float(MID + V_), OP.add, name="LM")
+        for j, (a, b) in enumerate(pcs): flex(B("CG", a), ind(R(XX), B("LM", b)), "XM", only=on("XM", j))
+        act(B("BD"), Bk(0), RELU, bias=MID + 1 - BIG, name="BD")
+        mm(Bk(1, sl(0, 8)), B("BD"), R("U8"), name="LBp")
+        ts(B("LB"), Bk(1, sl(0, 8)), -1.0, OP.add, name="LB")
+        flex(B("XB"), ind(Xw, B("LB")), "XB")
+        mm(C(0, sl(0, 8)), B("wN"), R("S1h"), name="b8")
+        flex(B("B8"), C(0, sl(0, 8)), "bm")
+        flex(B("BV"), C(0, sl(0, 8)), "bm", bias=R("VC", _, sl(2 * t + h, 2 * t + h + 1)), scale=-1.0)
+        for j in range(4): mm(Bk(_, sl(j, None, 4)), X("Ib"), B("XB"), name="XBp")
+        for k in range(4): tt(rows("MN", k, 4), rows("XK", k, 4), Bk(), OP.max, "MX")
+        ns = STS[h]
+        for u in range(ns): act(B("ST", u), ind(Ow, B("LA", sl(16 * u, 16 * u + 16))), IDENT, bias=R("VB", _, sl(16 * t + 8 * h + u, 16 * t + 8 * h + u + 1)), name="OB")
+        for q in range(16 if ns else 0): ts(B("ST", sl(0, ns), sl(16 * q, 16 * q + 16)), B("ST", sl(0, ns), sl(16 * q, 16 * q + 16)), 12.0 * q, OP.is_equal, name="SQ")
+        for u in range(ns, 8): tt(B("ST", u), ind(Ow, B("LA", sl(16 * u, 16 * u + 16))), R("VT", _, t % 2, sl(2048 * h + 256 * u, 2048 * h + 256 * u + 256)), OP.is_equal, "ST")
+        for k in range(16): mm(col(C, 1, k), B("ST", _, sl(k, None, 16)), R("S1b"), name="SL")
+        act(B("nst"), C(1), RELU, bias=1.0, scale=-1.0, name="nst")
+        for k in sorted(range(16), key=lambda k: k % 4): mm(col(C, 2, k), rows("MN", k), R("S1h"), name="FL")
+        flex(B("FR"), C(2), "FR", bias=float(MID))
+        grp(key, [(X("Ib"), X("K1")), (X("Im16h"), B("R3", 2)), (B("mine"), X("ImB")), (X("ImB"), B("nst")), (X("I32h"), B("FR"))], "K2")
+        for c in range(NPW):
+            for k in range(16): mm(A(3, sl(128 // NPW * c, 128 // NPW * (c + 1))), X("Ib"), B("CG", sl(2048 // NPW * c + k, 2048 // NPW * (c + 1), 16)), k == 0, k == 15, "WS")
+        act(B("wp"), A(3), SIGN, bias=-0.5, name="wp")
+        mm(A(0), B("wp"), X("BOb"), name="WN")
+        ts(B("nw"), A(0), R("Zt"), OP.is_le, name="nw")
+        tt(B("t8"), rows("nw", 0), B("BV"), OP.mult, "t8")
+        tt(rows("SA", 0), B("t8"), B("B8"), OP.add, "n8")
+        if t < RO - 1:
+            flex(B("SB", sl(1, 129, 16)), rows("SA", 0), "H8", bias=192.0, scale=1 / 64)
+            grp(C(0), [(B("SA"), X("Ih128")), (B("SB", sl(0, 128)), X("Id128")), (B("SB", sl(1, 129)), X("Imh2"))], "DG")
+            PL = R("PL", _, t, ls)
+            flex(PL, C(0), "PL", bias=Wq(3))
+            ds = D_OF[t + 1:]
+            send(ds[:1], PL, lambda d: R("LD", _, LAND.index((t, d)), ls), "ar%d_%d" % (t + 1, 2 * h), 32, "send")
+            if h == ORD[1]:
+                land = lambda d: R("LD", _, LAND.index((t, d)))
+                if ds[1:]: send(ds[1:], R("PL", _, t), land, "ar%d_1" % (t + 1), 64, "sendb")
+                later.extend((d, land(d)) for d in ds)
+            grp(C(1), [(X("Ib"), R(XX, _, hs)), (X("Ib"), PL)], "Pp")
+            later.append((None, lambda: flex(R(P, _, hs), C(1), "Pu")))
+        y = R("pC%d" % h, sl(0, 8), 2)
+        mm(y, rows("SA", 0), X("Ih"), name="YCp")
+        flex(R("YC", sl(0, 8), hs), y, "YC", bias=float(MID))
+        if t < RO - 1 and h == ORD[1]:
+            z = C(3, sl(0, 8))
+            grp(z, [(X("ONE"), R("nw", _, e, sl(0, None, 16))) for e in ORD], "ZC")
+            add(G, {"S": (0.1, 0.1)}, lambda Q, e: Q["S"].activation(T.zr[:, 0:8], z[1], COPY, accum_out=T.zr[:, 8:9]), [z], [R("zr")], name="zr")
+            cpv(R("zi", _, sl(0, 1)), R("zr", _, sl(8, 9)), "Z")
+            ts(R("zi", _, sl(1, 2)), R("zi", _, sl(0, 1)), 1, OP.bitwise_and, name="Z")
+            ts(R("Zt"), R("zi", _, sl(1, 2)), 2.0, OP.mult, name="Z")
+        scan(B("F"), X("NF"), key, OP.mult, 0.0, "F2")
+        scan(B("TT", sl(None, None, -1)), X("NF"), B("F", sl(None, None, -1)), OP.mult, 0.0, "T2")
+        tt(B("oh2"), B("TT"), key, OP.is_equal, "oh2")
+        grp(A(1), [(X("Imh"), B("aN")), (B("nw"), X("ImB")), (B("oh2"), X("IB"))], "pzp")
+        mm(Bk(0), B("oh2"), X("Ib"), name="ohT2")
+        ts(B("pz"), A(1), -BIG, OP.add, -float(MID), OP.max, "pz")
+        grp(A(2), [(X("Ib"), X("QB")), (B("pz"), X("BOm"))], "ZQp")
+        tt(B("pc"), cK, Bk(0), OP.mult, "pc")
+        ts(B("ZQ"), A(2), V_ - 17.0 * MID - BIG, OP.add, -float(MID), OP.max, "ZQ")
+        z8 = Bk(1, sl(16, 24))
+        mm(z8, B("ZQ"), R("S1p"), name="ZLp")
+        for e in range(2): grp(D(1 + e), [(X("Ib"), X("TR%d" % e)), (X("BOm"), B("pz")), (B("ZQ"), X("ME%d" % e))], "DSp")
+        mm(Bk(1, sl(0, 8)), B("ZQ"), R("S1h"), name="ZLp")
+        ts(B("ZL"), Bk(1, sl(0, 8)), 16.0 * MID, OP.add, name="ZL")
+        grp(A(3), [(X("Imh"), R("VRh", _, t, ls)), (X("BOh"), B("pc"))], "csv")
+        flex(B("OC"), ind(Ow, B("ZL")), "OC")
+        ts(B("MN", sl(0, 256)), D(sl(1, 3)), 32.0 * MID - V_, OP.is_equal, 8192.0, OP.mult, "DS")
+        scan(B("MN", sl(256, 512)), R("N32"), B("MN", sl(0, 256)), OP.mult, 0.0, "DM")
+        tt(B("x8"), B("MN", sl(256 + 31, 512, 32)), z8, OP.add, "x8")
+        for e in range(2): ts(B("FZ", sl(e, 8, 2)), B("x8", sl(4 * e, 4 * e + 4)), 16.0 * MID, OP.add, Wq((5, 10)[e]), OP.min, "FZ")
+        tt(B("OE"), ind(Ow, B("ZL")), R("VR", _, t, ls), OP.is_equal, "OE")
+        tt(B("OE"), B("OE"), A(3), OP.mult, "NN")
+        for o, kn, a, b in ((1, "KH", "ImB", "IB"), (2, "KL", "IB", "ImB")): grp(D(o), [(X("Ib"), X(kn)), (X("BOh"), B("wN")), (B("nw"), X(b)), (B("oh2"), X(a))], "HL")
 
-    def col(k, src, a, op0, b=None, op1=None, r=()): ts(Wq(k), src, a, op0, 1, r=tfr + list(r), w=[wq(k)], s2=b, op1=op1)
-    GM4 = 24
-    col(GM4, F(1), -4.0, OP.add)
-    ts(T.VC[:, 0:8], T.VC[:, 0:8], 0.5, OP.mult, 8, r=[("VC", 0, 8)], w=[("VC", 0, 8)])
-    ts(T.SPL[:], T.SPL[:], F(2), OP.add, 16, r=tfr + [W("SPL")], w=[W("SPL")])
-    ts(X("If"), T.ci[:], F(0), OP.is_equal, 128, r=rc, w=[W("If")])
-    ts(X("SW"), T.ci[:], Wq(P64), OP.is_equal, 128, r=[W("ci"), wq(P64)], w=[W("SW")])
-    ts(X("BOf"), T.cg[:], F(1), OP.is_equal, 128, r=rg, w=[W("BOf")])
-    ts(X("BOx"), T.cg[:], Wq(GM4), OP.is_equal, 128, r=[W("cg"), wq(GM4)], w=[W("BOx")], s2=-1.0, op1=OP.mult)
-    ts(X("BOy"), T.cg[:], -4.0, OP.add, 128, r=rg, w=[W("BOy")], s2=F(1), op1=OP.is_equal, two=0.5)
-    ts(X("QM"), T.cq[:], F(2), OP.is_equal, 128, r=rq, w=[W("QM")])
-    ts(X("NF"), T.cq[:], 0.0, OP.not_equal, 128, r=[W("cq")], w=[W("NF")])
-    for src, nmx, s, o in (("If", "Ib", 1, 0), ("If", "Im", -1, 0), ("If", "I16", 16, 0), ("If", "I256", 256, 0), ("If", "ImW", -WW, 0), ("If", "Im16", -16, 0), ("If", "Im256", -256, 0), ("BOf", "BOm512", -512, 0), ("If", "IB", BIG, 0), ("If", "ImB", -BIG, 0), ("If", "Ib2", BIG / 2, 0),
-                           ("If", "Imb2", -BIG / 2, 0), ("If", "Imax", -2.0 ** 23, 0), ("BOf", "BOb", 1, 0),
-                           ("BOf", "BOm", -1, 0), ("QM", "QB", BIG, 0), ("QM", "QC", BIG, -BIG)):
-        flex(X(nmx), X(src), 128, r=[W(src)], w=[W(nmx)], bias=float(o), scale=float(s), only="S")
-    tt(X("QmB"), T.c3[:], X("QB"), OP.subtract, 128, r=[W("c3"), W("QB")], w=[W("QmB")])
-    for src, nmx, s in (("If", "Ih", 1.0), ("If", "Imh", -1.0), ("BOf", "BOh", 1.0)): ts(X(nmx), X(src), s, OP.mult, 128, r=[W(src)], w=[W(nmx)])
-    for nmx, s in (("S1", 1.0), ("S32", 32.0), ("Sm16", -16.0), ("U8b", BIG / 2), ("S1h", 1.0)):
-        ts(T[nmx][:], T.ci[:, 0:8], F(1), OP.is_equal, 8, r=rc, w=[W(nmx)], s2=s, op1=OP.mult)
-    for j in range(XR): ts(T.U8[:, j], T.ci[:, 0:8], F(1), OP.is_equal, 8, r=rc, w=[("U8", j, j + 1)])
-    col(0, F(2), 7.0, OP.is_equal)
-    ts(T.wq[:, 26:30], T.ci[:, 0:4], F(6), OP.is_equal, 4, r=rc + [wq(0)], w=[("wq", 26, 30)], s2=Wq(0), op1=OP.add)
-    ts(T.wq[:, 32:36], T.ci[:, 0:4], F(6), OP.not_equal, 4, r=rc, w=[("wq", 32, 36)])
-    col(1, F(6), 0.0, OP.is_equal); col(2, F(2), 6.0, OP.is_equal); col(11, F(1), 16.0, OP.mult, 6.0, OP.add)
-    ts(X("BO6"), T.ci[:], Wq(11), OP.is_equal, 128, r=[W("ci"), wq(11)], w=[W("BO6")], two=0.5)
-    for a, c in ((0, 0), (4, 8), (8, 4)): ts(T.SY[:, a:a + 4], T.ci[:, c:c + 4], F(1), OP.is_equal, 4, r=rc + [wq(1)], w=[("SY", a, a + 4)], s2=Wq(1), op1=OP.mult)
-    for k in range(4):
-        if k:
-            ts(T.SHL2[:, k, :, 0:2], T.c2[:], F(1), OP.is_equal, 16, r=tfr + [W("c2"), wq(26 + k)], w=[("SHL2", 2 * k, 2 * k + 1)], s2=Wq(26 + k), op1=OP.mult)
-            ts(T.SHL2[:, k, :, 2], T.ci[:, 0:8], F(1), OP.is_equal, 8, r=rc + [wq(2)], w=[("SHL2", 2 * k + 1, 2 * k + 2)], s2=Wq(2), op1=OP.mult)
-        act(X("KW%d" % k), X("If"), 128, IDENT, scale=Wq(32 + k), r=[W("If"), wq(32 + k)], w=[W("KW%d" % k)])
-    for j in (0, 2): ts(T.S12[:, :, j:j + 2], T.c2[:], F(1), OP.is_equal, 16, r=tfr + [W("c2")], w=[("S12", j, j + 2)])
-    ts(X("TRI"), T.cq[:], F(2), OP.is_le, 128, r=rq, w=[W("TRI")], s2=BIG, op1=OP.mult)
-    col(3, F(3), 32.0, OP.mult); col(4, F(2), 2.0, OP.mult, Wq(3), OP.add, r=[wq(3)])
-    for e2 in range(2 if GS else 0):
-        col(5 + e2, F(4), float(e2), OP.not_equal, 1000.0, OP.mult)
-        col(7 + e2, Wq(5 + e2), Wq(4), OP.add, r=[("wq", 4, 7)])
-        for e in range(2):
-            ts(X("PA%d" % (2 * e2 + e)), T.ci[:], float(e), OP.subtract, 128, r=[W("ci"), wq(7 + e2)], w=[W("PA%d" % (2 * e2 + e))], s2=Wq(7 + e2), op1=OP.is_equal, two=0.5)
-            ts(X("PM%d" % (2 * e2 + e)), X("PA%d" % (2 * e2 + e)), float(WW), OP.mult, 128, r=[W("PA%d" % (2 * e2 + e))], w=[W("PM%d" % (2 * e2 + e))], two=0.5)
-    if CO:
-        ts(T.NE[:], T.ci[:, 0:16], F(2), OP.not_equal, 16, r=rc, w=[W("NE")])
-        tt(T.NE[:, 0:4], T.NE[:, 0:4], T.NE[:, 12:16], OP.mult, 4, r=[W("NE")], w=[W("NE")])
-        for t in range(RO):
-            for o in range(3):
-                k = (0, 8, 4)[o] + t
-                act(T.KD[:, 3 * t + o], X("If"), 128, IDENT, scale=T.NE[:, k:k + 1], r=[W("If"), W("NE")], w=[("KD", 3 * t + o, 3 * t + o + 1)])
-    col(9, F(6), 0.0, OP.not_equal, 1000.0, OP.mult); col(10, F(1), 16.0, OP.mult, Wq(9), OP.add, r=[wq(9)])
-    for k in range(16): ts(T.SEL[:, k], T.ci[:], float(k), OP.subtract, 128, r=[W("ci"), wq(10)], w=[("SEL", k, k + 1)], s2=Wq(10), op1=OP.is_equal, two=0.5)
-    vop(lambda v: v.memset(T.Zb[:], -1.0), 1, w=[W("Zb")])
+    def sell(t, h):
+        B = lambda n, *ix: R(n, _, h, *ix)
+        for u in range(3, -1, -1): tt(ind(R("O"), B("FZ", sl(2 * u, 2 * u + 2))), B("OC", sl(32 * u, 32 * u + 32)), B("OE", sl(32 * u, 32 * u + 32)), OP.add, "scatter")
 
-    for h in sets():
-        O, XX = T["O%d" % h], T["XX%d" % h]
-        for hh, pp in enumerate((LO, UP) if h else ()): dma(T.OI[pp, :], T.hol[64:128, HV * hh:HV * hh + HV], 393, "hol1", w=[("OI", hh, hh + 1)], name="ld hol1")
-        cpv(O[:, HV:V_], T.OI[:], HV, r=[W("OI")], w=[("O%d" % h, 0, 1)], name="O f32")
-        swap(O, lambda hh: (LO, UP)[hh], HV, "Y", 393, "ox%d" % h, [("O%d" % h, 0, 1)], [("O%d" % h, 1, 2), ("O%d" % h, 2, 3)], "Ox")
-        flex(XX[:, WW + HV:WW + V_], XX[:, HV:V_], HV, r=[("X%d" % h, 0, 2)], w=[("X%d" % h, 6, 7)], two=0.5, bias=512.0 if GS else 0.0, scale=512.0 if GS else -1.0, name="X2")
-        if CO:
-            cpv(B("TF", h), B("TI", h), 96, r=[W("TI%d" % h)], w=[W("TF%d" % h)])
-            for b in range(3): vop(lambda v, h=h, b=b: v.transpose(B("CLf", h)[:, b::3], B("TF", h)[:, b]), 32, r=[W("TF%d" % h)], w=[("CLf%d" % h, b, b + 1)])
-            cpv(B("CLu", h), B("CLf", h), 96, r=[W("CLf%d" % h)], w=[W("CLu%d" % h)])
-        swap(XX, lambda hh: (LO, UP)[hh], WW + HV, "Y", 196, "xx%d" % h, [("X%d" % h, 6, 7)], [("X%d" % h, 5, 6), ("X%d" % h, 7, 8)], "Xx")
-
-    def renew(t, h, d):
-        WC, D, dk, k = T["WC%d" % h], P("D", h), "pD%d" % h, 4 * h + d
-        s = (rank + d) % NR
-        src, sr = (LU(t + 1, h, s), W("L%d_%d_%d" % (t + 1, h, s))) if d else (T.SND[:, 2 * t + h], W("SND%d" % (2 * t + h)))
-        flex(T.HLz[:, k, :, :, d::8], src, 16, r=[sr], w=[("HLz", k, k + 1)], name="HLz")
-        for j in H:
-            mm(D[:, 2 + j], X("KW%d" % d), WC[:, HV * j + t:HV * j + HV:12], True, False, dk, 128, r=[W("WC%d" % h), W("KW%d" % d)], name="HLr")
-            for pp in (LO, UP): mm(D[pp, 2 + j], T.HLz[:, k, j], X("Ib"), False, True, dk, 128, r=[("HLz", k, k + 1)], name="HLr")
-        flex(WC[:, t:V_:12], D[:, 2:4], 256, w=[W("WC%d" % h)], pr=[dk], name="WCu")
-
-    def compose(t, h):
-        CC = T["CC%d" % h]; n = HV // NCP
-        for c in range(NCP):
-            flex(CC[:, HV + n * c:HV + n * c + n], T["WC%d" % h][:].indirect(B("CLu", h)[:, n // 16 * c:n // 16 * (c + 1)]), n, r=[W("WC%d" % h), W("CLu%d" % h)], w=[("CC%d" % h, c, c + 1)], gather=True, name="compose")
-        swap(CC, lambda hh: slice(64 * hh + D_OF[t], 64 * hh + 64, 8), HV, "Y", 25, "cc%d" % h, [("CC%d" % h, 0, NCP)], [("CC%d" % h, 10, 11), ("CC%d" % h, 11, 12)], "CCx")
-        if SXT: dma(CC[6::16, HV:V_], T.SXB[6::16, h], 25, "cc%d" % h, r=[W("SXB%d" % h), ("CC%d" % h, 0, NCP)], w=[("CC%d" % h, 12, 13)], name="CCx")
-    for h in sets():
-        G["free"] = True
-        if CO:
-            for c in range(3 if SXT else 0):
-                mm(P("D", h)[:], X("BO6"), T["XX%d" % h][:, HV + 512 * c:HV + 512 * c + 512], True, True, "pD%d" % h, 512, r=[("X%d" % h, 0, 2), W("BO6")], name="SXp")
-                flex(T.SXB[:, h, 512 * c:512 * c + 512], P("D", h)[:], 512, w=[("SXB%d" % h, c, c + 1)], pr=["pD%d" % h], name="SXb")
-            for hh in H if SXT else ():
-                a = V_ * hh
-                dma(T["CC%d" % h][64 * (1 - hh) + 6:64 * (2 - hh):16, a:a + HV], T.SXB[64 * hh + 6:64 * hh + 64:16, h], 12, "sx%d" % h, r=[W("SXB%d" % h), ("CC%d" % h, 10 + hh, 11 + hh)], w=[("CC%d" % h, 13 + hh, 14 + hh)], name="SXx")
-            compose(0, h)
-            for q in D_OF[1:3]: flat(q, h)
-
-    def round_(t, h):
-        last = t == RO - 1
-        x = lambda n: W(n + str(h))
-        O, XX, WC = T["O%d" % h], T["XX%d" % h], T["WC%d" % h]
-        G["free"] = (t, h) == (0, 0)
-        A, Bk, C, D = P("A", h), P("B", h), P("C", h), P("D", h); ak, bk, ck, dk = "pA%d" % h, "pB%d" % h, "pC%d" % h, "pD%d" % h
-        XRD = [("X%d" % h, 0, 4)]
-        OW = [x("O"), x("Oown")]
-        hs = slice(HV + t, V_, 12)
-        LA, GM = B("LA", h), B("MN", h)
-        ts(LA, O[:, hs], Wq(OFF), OP.add, 128, r=[("O%d" % h, 0, 1), wq(OFF)], w=[x("LA")], name="LA")
-        ln = 128 // NPC
-        if not CO:
-            cpv(B("L0", h), O[:, hs], 128, r=[("O%d" % h, 0, 1)], w=[x("L0")], name="L0")
-            for c in range(0, 128, ln): flex(B("CG", h)[:, 16 * c:16 * (c + ln)], WC[:].indirect(B("L0", h)[:, c:c + ln]), 16 * ln, r=[x("WC"), x("L0")], w=[("CG%d" % h, c, c + ln)], gather=True, name="C1")
-            grp(A[:, :, 24:40], ak, [(T.SEL[:, k], B("CG", h)[:, k::16], [x("CG"), ("SEL", k, k + 1)]) for k in range(16)], "LCp")
-            cpv(B("LC", h), A[:, :, 24:40], 128, w=[x("LC")], pr=[ak], name="LC")
-            if t: renew(t - 1, h, D_OF[t])
-            else: flat(D_OF[0], h)
-        tab, lst, rd = (T["CC%d" % h], LA, [x("CC"), x("LA")]) if CO else (WC, B("LC", h), [x("WC"), x("LC")])
-        for j, c in enumerate(range(0, 128, ln)): flex(B("XK", h)[:, 16 * c:16 * (c + ln)], XX[:, 0:WW].indirect(LA[:, c:c + ln]), 16 * ln, r=XRD + [x("LA")], w=[("XK%d" % h, c, c + ln)], gather=True, name="XK%d" % j)
-        for c in range(0, 128, ln): flex(B("CG", h)[:, 16 * c:16 * (c + ln)], tab[:].indirect(lst[:, c:c + ln]), 16 * ln, r=rd, w=[("CG%d" % h, c, c + ln)], gather=True, name="CG")
-        for q in D_OF[t + 1:]:
-            if t: renew(t - 1, h, q)
-            elif q != D_OF[0] and not CO: flat(q, h)
-        fused = (t, h) in STV
-        if fused and (h == 0 or (t, 0) not in STV):
-            for hh, pp in enumerate((LO, UP)):
-                G["up"] = hh
-                for c in range(2): iota(T.VT[pp, t % NVT, 1024 * c:1024 * c + 1024], [[12, 64], [0, 16]], t + 768 * c + HV * hh, 1024, [("VT%d" % (t % NVT), 2 * c + hh, 2 * c + hh + 1)])
-            G["up"] = 0
-        for u in range(0, 8 if fused else 0):
-            tt(B("OB", h)[:, u], O[:, 0:WW].indirect(LA[:, 16 * u:16 * u + 16]), T.VT[:, t % NVT, 256 * u:256 * u + 256], OP.is_equal, 256, r=OW + [x("LA"), ("VT%d" % (t % NVT), u // 4 * 2, u // 4 * 2 + 2)], w=[("OB%d" % h, u, u + 1)], name="STf", c=gc_(256, "V"))
-        for u in range(0 if fused else 8):
-            act(B("OB", h)[:, u], O[:, 0:WW].indirect(LA[:, 16 * u:16 * u + 16]), 256, IDENT, bias=T.VB[:, 8 * t + u:8 * t + u + 1], r=OW + [x("LA"), W("VB")], w=[("OB%d" % h, u, u + 1)], name="OB", c=gc_(256, "S"))
-        G["free"] = False
-        for q in range(0 if fused else 16):
-            a = B("OB", h)[:, :, 16 * q:16 * q + 16]
-            ts(a, a, 12.0 * q, OP.is_equal, 128, r=[x("OB")], w=[("ST%d" % h, q, q + 1)], two=0.5, name="ST")
-        for j in range(MR): mm(C[:, 0:MR, j::MR], X("Ib"), XX[:, hs], True, True, ck, 128, r=[("X%d" % h, 0, 2), W("Ib")], name="XV")
-        flex(B("aN", h), O[:, hs], 128, r=[("O%d" % h, 0, 1)], w=[x("aN")], bias=-float(MID), name="aN")
-        for k in range(16):
-            shl = T.SHL2[:, D_OF[t]]
-            if k < 8: mm(A[:, :, k:k + 33:16], B("CG", h)[:, k::16], shl, True, True, ak, 24, r=[x("CG"), W("SHL2")], name="cL")
-            else: mm(A[:, :, k:k + 33:32], B("CG", h)[:, k::16], shl[:, :, 1:3], True, True, ak, 16, r=[x("CG"), W("SHL2")], name="cL")
-        flex(B("cS", h), A[:, :, 0:16], 128, w=[x("cS")], pr=[ak], name="cS")
-        if SXT: act(B("SX", h), A[:, :, 32:48], 128, w=[x("SX")], pr=[ak], name="SXc")
-        for s in range(1, 9):
-            tt(B("E", h)[:, :, s - 1], B("cS", h), A[:, :, s:s + 16], OP.is_equal, 128, r=[x("cS")], w=[("E%d" % h, s - 1, s)], pr=[ak], name="E")
-        mm(A[:, :, 48:64], B("cS", h), X("Ih"), True, True, ak, 128, r=[x("cS"), W("Ih")], name="cK")
-        act(B("cK", h), A[:, :, 48:64], 128, w=[x("cK")], pr=[ak], name="cKc")
-        mr = 16 // MR
-        for k in range(mr):
-            tt(B("MN", h)[:, k::mr], B("XK", h)[:, k::mr], C[:, 0:MR], OP.min, 128 * MR, r=[x("XK")], w=[("MN%d" % h, k, k + 1), x("GM")], pr=[ck], name="MN")
-        for k in sorted(range(16), key=lambda k: k % mr):
-            rr = [("MN%d" % h, k % mr, k % mr + 1), W("S12")]
-            mm(Bk[:, :, k::16], B("MN", h)[:, k::16], T.S12[:], True, True, bk, 32, r=rr, name="mL")
-        mS, PRh, Eh = B("mS", h), B("PR", h), B("E", h)
-        flex(mS, Bk[:, :, 0:16], 128, w=[x("mS")], pr=[bk], name="mS")
-        for a, z in ((0, 4), (4, 7)): tt(T.PQ[:, :, a:z, 8:24], Eh[:, :, a:z], Bk[:, :, 0:16 * (z - a)], OP.mult, 128 * (z - a), r=[("E%d" % h, a, z)], w=[("PQ", a, z)], pr=[bk], name="PQ")
-        for s in range(1, 9): tt(PRh[:, s - 1], Eh[:, :, s - 1], Bk[:, :, s:s + 16], OP.mult, 128, r=[("E%d" % h, s - 1, s)], w=[("PR%d" % h, s - 1, s)], pr=[bk], name="PR")
-        key = C[:, 0]
-        grp(key, ck, [(X("Ib"), X("K1"), [W("Ib"), W("K1")]), (X("I16"), mS, [W("I16"), x("mS")])]
-            + [(X("I16"), T.PQ[:, :, s - 1, o - s:o + 16 - s], [("PQ", s - 1, s)]) for s in range(1, 8) for o in (8, 24)]
-            + [(X("I16"), PRh[:, s - 1], [("PR%d" % h, s - 1, s)]) for s in range(1, 9)], "key")
-        for k in range(16):
-            mm(D[:, 2, k::16], B("OB", h)[:, :, k::16], T.S1[:], True, True, dk, 8, r=[x("ST"), x("OB"), W("S1")], name="SL")
-        act(B("nst", h), D[:, 2], 128, RELU, bias=1.0, scale=-1.0, w=[x("nst")], pr=[dk], name="nst")
-        scan(B("F", h), key, 128, w=[x("F")], pr=[ck], name="F")
-        scan(B("TT", h)[:, ::-1], B("F", h)[:, ::-1], 128, r=[x("F")], w=[x("TT")], name="T")
-        tt(B("oh", h), B("TT", h), key, OP.is_equal, 128, r=[x("TT")], w=[x("oh")], pr=[ck], name="oh")
-        mm(A[:, :, 24:40], B("oh", h), X("Ib"), True, True, ak, 128, r=[x("oh")], name="ohT")
-        tt(B("wN", h), B("cK", h), A[:, :, 24:40], OP.mult, 128, r=[x("cK")], w=[x("wN")], pr=[ak], name="wN")
-        mm(A[:, :, 40:56], X("BOh"), B("wN", h), True, True, ak, 128, r=[x("wN"), W("BOh")], name="bR")
-        grp(Bk[:, :, 24:40], bk, [(X("Ib"), X("QB"), [W("QB")]), (B("wN", h), X("BOh"), [x("wN")])], "bL")
-        tt(B("mine", h), B("cK", h), A[:, :, 40:56], OP.is_equal, 128, r=[x("cK")], w=[x("mine")], pr=[ak], name="mine")
-        act(B("BD", h), Bk[:, :, 24:40], 128, RELU, bias=MID + 1 - BIG, w=[x("BD")], pr=[bk], name="BD")
-        mm(Bk[:, 0:XR, 40:48], B("BD", h), T.U8[:], True, True, bk, 8 * XR, r=[x("BD"), W("U8")], f32=True, name="LBp")
-        ts(B("LB", h), Bk[:, 0:XR, 40:48], Wq(OFF1), OP.add, 8 * XR, r=[wq(OFF1)], w=[x("LB")], pr=[bk], name="LB")
-        flex(B("XB", h), XX[:, 0:WW].indirect(B("LB", h)), 128 * XR, r=XRD + [x("LB")], w=[x("XB")], gather=True, name="XB")
-        XM = B("CG", h); lm = 128 // NPM
-        if not GS:
-            grp(C[:, 1], ck, [(X("Ib"), X("KM"), [W("KM")]), (X("Ih"), B("aN", h), [x("aN")]), (X("ImW"), B("mine", h), [x("mine"), W("ImW")])], "LMp")
-            cpv(B("LM", h), C[:, 1], 128, w=[x("LM")], pr=[ck], name="LM")
-            for c in range(0, 128, lm): flex(XM[:, 16 * c:16 * (c + lm)], XX[:].indirect(B("LM", h)[:, c:c + lm]), 16 * lm, r=[x("X"), x("LM")], w=[("CG%d" % h, c, c + lm)], gather=True, name="XM")
-            for j in range(MR): mm(D[:, 0:MR, j::MR], X("Ib"), B("XB", h), True, True, dk, 128, r=[x("XB")], name="XBp")
-            for k in range(mr): tt(GM[:, k::mr], B("XK", h)[:, k::mr], D[:, 0:MR], OP.max, 128 * MR, r=[x("XK")], w=[("GM%d" % h, k, k + 1), ("MN%d" % h, k, k + 1)], pr=[dk], name="MX")
-        else:
-            mm(C[:, 0:4, 0:32], X("Ib"), X("KM"), True, False, ck, 128, r=[W("KM")], name="LMp")
-            for src, cn in (("aN", "PA"), ("mine", "PM")):
-                for e2 in range(2):
-                    for e in range(2):
-                        mm(C[:, 0:4, 16 * e2:16 * e2 + 16], X(cn + str(2 * e2 + e)), B(src, h)[:, :, e], False, src == "mine" and e2 + e == 2, ck, 64, r=[x(src), W(cn + str(2 * e2 + e))], name="LMp")
-            for j in range(4): vop(lambda v, j=j: v.transpose(B("LMf", h)[:, :, j], C[:, j, 0:32]), 32, w=[("LMf%d" % h, j, j + 1)], pr=[ck], name="LMt")
-            cpv(B("LM", h), B("LMf", h), 128, r=[x("LMf")], w=[x("LM")], name="LM")
-            for k in range(0, 16, XR):
-                tt(GM[:, 128 * k:128 * (k + XR)], XX[:].indirect(B("LM", h)[:, 8 * k:8 * (k + XR)]), B("XB", h), OP.max, 128 * XR, r=[x("X"), x("LM"), x("XB")], w=[("GM%d" % h, k, k + XR), ("MN%d" % h, 0, 16)], name="G", c=gc_(128 * XR, "V"))
-        for nmx, o, sg in (("BM", 0, "Im"), ("BP", 4, "Ib")):
-            grp(Bk[:, :, 56 + o], bk, [(X(sg), T.HH[:], [W("HH"), W(sg)]), (B("wN", h), T.S1h[:], [x("wN"), W("S1h")])], "b8", n=8)
-        for nmx, o in (("BM", 0), ("BP", 4)):
-            act(B(nmx, h), Bk[:, :, 56 + o], 8, IDENT, bias=T.VC[:, o + t:o + t + 1], scale=0.5, r=[W("VC")], w=[x(nmx)], pr=[bk], name="bm")
-        U = A[:, :, 0:16]
-        if GS: grp(U, ak, [(X("Im256"), B("XK", h)[:, k::16], [x("XK"), W("Im256")]) for k in range(16)] + [(X("BOm512"), B("mine", h), [x("mine"), W("BOm512")])], "US", stop=False)
-        else: grp(U, ak, [(X("Ib"), XM[:, k::16], [x("CG")]) for k in range(16)], "WS")
-        mm(key, X("Ib"), X("K2"), True, False, ck, 128, r=[W("K2")], name="K2")
-        for k in range(0 if SXT else 16): mm(C[:, 0, k::16], B("XK", h)[:, k::16], T.Sm16[:], False, False, ck, 8, r=[x("XK"), W("Sm16")], name="SX")
-        grp(key, ck, ([(X("Im16"), B("SX", h), [x("SX"), W("Im16")])] if SXT else []) + [(B("mine", h), X("Imax"), [x("mine"), W("Imax")]), (X("Imax"), B("nst", h), [x("nst")])], "K2", start=False, stop=False)
-        for k in range(16 if GS else 0):
-            gr = [("GM%d" % h, k, k + 1)]
-            mm(U, X("Ib"), GM[:, S(k)], False, k == 15, ak, 128, r=gr, name="UG")
-            mm(C[:, 0, k::16], GM[:, S(k)], T.S32[:], False, k == 15, ck, 8, r=gr + [W("S32")], name="FL")
-        for j, k in enumerate(sorted(range(0 if GS else 16), key=lambda k: k % mr)):
-            mm(C[:, 0, k::16], GM[:, k::16], T.S32[:], False, j == 15, ck, 8, r=[("GM%d" % h, k % mr, k % mr + 1), W("S32")], name="FL")
-        act(B("wp", h), U, 128, SIGN, bias=-248.0 if GS else -0.5, w=[x("wp")], pr=[ak], name="wp")
-        mm(Bk[:, :, 0:16], B("wp", h), X("BOb"), True, True, bk, 128, r=[x("wp"), W("BOb")], name="WN")
-        act(B("w", h), Bk[:, :, 0:16], 128, SIGN, bias=T.Zb[:, 0:1], r=[W("Zb")], w=[x("w")], pr=[bk], name="w")
-        SN = T.SND[:, 2 * t + h]; sn = "SND%d" % (2 * t + h)
-        tt(B("t8", h), B("w", h)[:, 0::16], B("BM", h), OP.mult, 8, r=[x("w"), x("BM")], w=[x("t8")], name="t8")
-        tt(B("n8", h), B("t8", h), B("BP", h), OP.add, 8, r=[x("t8"), x("BP")], w=[x("n8")], name="n8")
-        cpv(SN[:, :, :, 0], B("n8", h), 8, r=[x("n8")], w=[(sn, 0, 1)], name="hi")
-        tt(SN[:, :, :, 1], B("n8", h), SN[:, :, :, 0], OP.subtract, 8, r=[x("n8"), (sn, 0, 1)], w=[(sn, 1, 2)], name="lo")
-        ds = [D_OF[u] for u in range(t + 1, RO)]
-        if not last:
-            land = LU(t + 1, h, rank); sem = "ar%d_%d_%d" % (t + 1, h, rank)
-            sa = send([T.cores[(rank - ds[0]) % NR]], SN, land, sem, [W(sn)], "send")
-            sb_ = send([T.cores[(rank - q) % NR] for q in ds[1:]], SN, land, sem, [W(sn)], "sendb") if len(ds) > 1 else None
-            for q in ds: arrive((rank + q) % NR, t + 1, h, sa if q == ds[0] else sb_, 4)
-            mm(D[:, 3, 0:8], X("ONE"), B("w", h)[:, 0::16], True, True, dk, 8, r=[x("w"), W("ONE")], name="ZC")
-            add(G, {"S": (sc(8) + 0.03,) * 2}, lambda Q, e: Q["S"].activation(T.zr[:, 8 * h:8 * h + 8], D[:, 3, 0:8], COPY, bias=256.0, accum_out=T.zr[:, 16 + h:17 + h]), (), [x("zr")], [dk], name="zr")
-            if h == 1:
-                ts(T.zi[:, 0:1], T.zr[:, 16:17], T.zr[:, 17:18], OP.add, 1, r=[W("zr0"), W("zr1")], w=[("zi", 0, 1)], s2=0.5, op1=OP.mult, name="Z")
-                ts(T.zi[:, 1:2], T.zi[:, 0:1], 1, OP.bitwise_and, 1, r=[("zi", 0, 1)], w=[("zi", 1, 2)], name="Z")
-                ts(T.Zb[:], T.zi[:, 1:2], -2.0, OP.mult, 1, r=[("zi", 1, 2)], w=[W("Zb")], s2=-1.0, op1=OP.add, name="Z")
-        if CO:
-            HLo = T.HLz[:, 4 * h]
-            flex(HLo[:, :, :, 0::8], SN, 16, r=[W(sn)], w=[("HLz", 4 * h, 4 * h + 1)], name="HLz")
-            mm(D[:, 2], HLo, X("Ib"), True, True, dk, 128, r=[("HLz", 4 * h, 4 * h + 1)], name="HLr")
-            flex(B("NB", h), D[:, 2], 128, w=[x("NB")], pr=[dk], name="WCu")
-            for o in range(3):
-                grp(D[:, 3, o:96:3], dk, [(T.KD[:, 3 * t + o], B("CLf", h)[:, o::3], [x("CLf"), ("KD", 3 * t + o, 3 * t + o + 1)], 1)]
-                    + [(T.SEL[:, (12 * r_ + t) % 16], B("NB", h)[:, r_::4], [x("NB"), W("SEL")]) for r_ in range(4) if (12 * r_ + t) // 16 == o], "CLp", n=32)
-            if not last: cpv(B("CLu", h), D[:, 3, 0:96], 96, w=[x("CLu")], pr=[dk], name="CLu")
-            flex(B("CLf", h), D[:, 3, 0:96], 96, w=[x("CLf")], pr=[dk], name="CLf")
-            if last:
-                for b in range(3): vop(lambda v, b=b: v.transpose(B("TF", h)[:, b], B("CLf", h)[:, b::3]), 32, r=[x("CLf")], w=[("TF%d" % h, b, b + 1)], name="yct")
-                for hh, pp in enumerate((LO, UP)):
-                    for e in range(2): dma(T.yc[4 * h + e:4 * h + 4:2, HV * hh:HV * hh + HV], T.TF[pp, h, :, e], 12, "yc%d" % h, r=[x("TF")], name="st yc")
-            else:
-                renew(t, h, ds[0])
-                compose(t + 1, h)
-        else: renew(t, h, 0)
-        if last and not CO:
-            for c in range(3):
-                for hh in H: mm(D[0:8], T.SY[:, 4 * hh:4 * hh + 8], WC[:, HV * hh + 512 * c:HV * hh + 512 * c + 512], hh == 0, hh == 1, dk, 512, r=[x("WC"), W("SY")], name="ycp")
-                flex(T.YC[0:8, 512 * c:512 * c + 512], D[0:8], 512, w=[("YC", c, c + 1)], pr=[dk], name="yc")
-            for hh in H: dma(T.yc[4 * h:4 * h + 4, HV * hh:HV * hh + HV], T.YC[4 * hh:4 * hh + 4, :], 25, "yc%d" % h, r=[W("YC")], name="st yc")
-        scan(B("F", h), key, 128, w=[x("F")], pr=[ck], name="F2")
-        scan(B("TT", h)[:, ::-1], B("F", h)[:, ::-1], 128, r=[x("F")], w=[x("TT")], name="T2")
-        tt(B("oh2", h), B("TT", h), key, OP.is_equal, 128, r=[x("TT")], w=[x("oh2")], pr=[ck], name="oh2")
-        grp(A[:, :, 16:32], ak, [(X("Imh"), B("aN", h), [x("aN"), W("Imh")]), (X("Ib"), X("LR"), [W("LR")]), (B("w", h), X("Ib2"), [x("w"), W("Ib2")]), (B("oh2", h), X("IB"), [x("oh2"), W("IB")])], "pzp")
-        ts(B("pz", h), A[:, :, 16:32], V_ - MID - 1.5 * BIG - CEN, OP.add, 128, w=[x("pz")], pr=[ak], s2=-CEN, op1=OP.max, name="pz")
-        grp(Bk[:, :, 0:16], bk, [(X("Im"), X("QmB"), [W("QmB")]), (B("pz", h), X("BOm"), [x("pz"), W("BOm")])], "ZQp")
-        grp(A[:, 0:4, 32:64], ak, [(X("Ib"), X("LR"), [W("LR")]), (X("BOm"), B("pz", h), [x("pz"), W("BOm")])], "ZUp")
-        grp(A[:, 4:8, 32:64], ak, [(X("Ib"), X("LRx"), [W("LRx")]), (X("BOx"), B("pz", h), [x("pz"), W("BOx")])], "ZUp")
-        ts(B("ZQ", h), Bk[:, :, 0:16], T.VC[:, 8:9], OP.add, 128, r=[W("VC")], w=[x("ZQ")], pr=[bk], s2=-CEN, op1=OP.max, name="ZQ")
-        ts(B("ZU", h), A[:, :, 32:64], V_ + 1.0 - 16 * CEN, OP.add, 256, w=[x("ZU")], pr=[ak], name="ZU")
-        act(B("ZUf", h), A[:, 0:4, 32:64], 128, COPY, bias=V_ + 1.0 - 32 * CEN, w=[x("ZUf")], pr=[ak], name="ZUf")
-        mm(Bk[:, :, 57], B("ZQ", h), T.S1h[:], True, True, bk, 8, r=[x("ZQ")], name="ZLp")
-        flex(B("ZLf", h), Bk[:, :, 57], 8, w=[x("ZLf")], pr=[bk], bias=16 * CEN, name="ZLf")
-        ts(B("ZL", h), Bk[:, :, 57], Wq(OFF1), OP.add, 8, r=[wq(OFF1)], w=[x("ZL")], pr=[bk], s2=16 * CEN, op1=OP.add, name="ZL")
-        mm(Bk[:, :, 24:40], B("oh2", h), X("Ib"), True, True, bk, 128, r=[x("oh2")], name="ohT2")
-        tt(B("pc", h), B("cK", h), Bk[:, :, 24:40], OP.mult, 128, r=[x("cK")], w=[x("pc")], pr=[bk], name="pc")
-        grp(Bk[:, :, 40:56], bk, [(X("Im"), X("VH"), [W("VH"), W("Im")]), (X("Im"), T.VL[:, t], [W("VL")]), (X("BOh"), B("pc", h), [x("pc")])], "csv")
-        OC, NN = B("OC", h), B("NN", h); oc, nn = ("OC%d" % h, 0, 1), ("NN%d" % h, 0, 1)
-        flex(OC[:, 0:128], O[:].indirect(B("ZL", h)), 128, r=OW + [x("ZL")], w=[oc], gather=True, name="OC", only="S")
-        tt(B("OE", h), O[:].indirect(B("ZL", h)), T.VR[:, t], OP.is_equal, 128, r=OW + [x("ZL"), W("VR")], w=[x("OE")], name="OE", c=gc_(128, "V"))
-        tt(NN[:, 0:128], B("OE", h), Bk[:, :, 40:56], OP.mult, 128, r=[x("OE")], w=[nn], pr=[bk], name="NN")
-        grp(Bk[:, :, 0:16], bk, [(X("SW"), OC[:, 0:128], [oc, W("SW")], 1), (X("SW"), NN[:, 0:128], [nn], 1)], "NCx")
-        act(NN[:, 128:256], Bk[:, :, 0:16], 128, w=[("NN%d" % h, 1, 2)], pr=[bk], name="NCc")
-        for o, kn, a, b_ in ((0, "KH", "ImB", "Imb2"), (1, "KL", "IB", "Ib2")):
-            grp(D[:, o], dk, [(X("Ib"), X(kn), [W(kn)]), (X("BOh"), B("wN", h), [x("wN")]), (B("w", h), X(b_), [x("w"), W(b_)]), (B("oh2", h), X(a), [x("oh2"), W(a)])], "HL")
-        grp(C[:, 1], ck, [(X("Ib"), X("TRI"), [W("TRI")]), (B("ZQ", h), X("BOh"), [x("ZQ")])], "DSp")
-        tt(B("DS", h), B("ZUf", h), C[:, 1], OP.is_equal, 128, r=[x("ZUf")], w=[x("DS")], pr=[ck], name="DS")
-        DE = B("DE", h); de = lambda u: [("DE%d" % h, u, u + 1)]
-        for u in range(8):
-            a = 16 * u + 16
-            ts(DE[:, u, a:256], B("ZU", h)[:, a:256], B("ZLf", h)[:, u:u + 1], OP.is_equal, 256 - a, r=[x("ZU"), x("ZLf")], w=de(u), two=0.5, name="DE")
-        grp(key, ck, [(X("Ib"), X("QC"), [W("QC")]), (B("DS", h), X("BOb"), [x("DS")])]
-            + [(DE[:, u, S(j)], X(("BOb", "BOy")[j]), de(u) + [W("BOy")]) for u in range(8) for j in H if u < 7 or j], "DUP")
-        act(B("sg", h), key, 128, SIGN, bias=-0.5, w=[x("sg")], pr=[ck], name="sg")
-        for pp, qq, o in ((slice(0, 128), slice(0, 128), 32), (LO, UP, 40), (UP, LO, 40)):
-            grp(A[pp, 7, o:o + 8], ak, [(B("ZQ", h)[:, qq], T.S1h[:], [x("ZQ")]), (B("sg", h)[:, qq], T.U8b[:], [x("sg"), W("U8b")])], "FZp", n=8)
-        tt(B("fl", h), T.SPL[:], A[:, 7, 32:48], OP.min, 16, r=[W("SPL")], w=[x("fl")], pr=[ak], name="fl")
-        ts(B("FZ", h), B("fl", h), Wq(OFFZ), OP.add, 16, r=[x("fl"), wq(OFFZ)], w=[x("FZ")], name="FZ")
-        tt(O[:].indirect(B("FZ", h)), OC, NN, OP.add, 256, r=[x("OC"), x("NN"), x("FZ")], w=OW, name="scatter", c=vc(256, 3.5))
-        tt(B("OE", h), O[:, hs], D[:, 0], OP.min, 128, r=[x("O")], w=[x("OE")], pr=[dk], name="XO")
-        tt(O[:, hs], B("OE", h), D[:, 1], OP.max, 128, r=[x("OE"), x("O")], w=[("Oown%d" % h, 0, 1)], pr=[dk], name="O")
-        if last:
-            for hh, pp in enumerate((LO, UP)): dma(T.yo[64 * h:64 * h + 64, HV * hh:HV * hh + HV], O[pp, HV:V_], 393, "yo%d%d" % (h, hh), r=OW, q="YS"[hh], name="st yo")
-            return
-        mm(D[:, 2], X("SW"), O[:, hs], True, True, dk, 128, r=[("Oown%d" % h, 0, 1)], f32=True, name="Osw")
-        act(O[LO, V_ + t:WW:12], D[LO, 2], 128, r=[x("O")], w=[("Oown%d" % h, 1, 2)], pr=[dk], name="Oc")
-        act(O[UP, t:HV:12], D[UP, 2], 128, r=[x("O")], w=[("Oown%d" % h, 2, 3)], pr=[dk], name="Oc")
+    def own(t, h):
+        hs = sl(MID * h + t, MID * h + MID, 12)
+        tt(R("F", _, h), R("O", _, hs), R("pD%d" % h, _, 1), OP.min, "XO")
+        tt(R("O", _, hs), R("F", _, h), R("pD%d" % h, _, 2), OP.max, "O")
+        if t == RO - 1: dma(R("yo", _, sl(MID * h, MID * h + MID)), R("O", _, sl(MID * h, MID * h + MID)), 786, "st yo", "Y", 128)
 
     for t in range(RO):
-        G["t"] = t
-        for h in sets(): round_(t, h)
+        G["t"] = t; later = []
+        firms(t)
+        for step in (front, sell, own):
+            for h in ORD:
+                G["h"] = h; step(t, h)
+            for d, x in later:
+                if d is None: x()
+                else: (gcopy if "WCu" not in ASG or d != D_OF[t + 1] else flex)(R("WC%d" % d, _, sl(t, V_, 12)), x, "WCu")
+            later.clear()
+        G["h"] = None
+    dma(R("yc"), R("YC", sl(0, 8)), 98, "st yc", "S", 16)
     return G
 
 
@@ -677,18 +610,19 @@ def rank_program(g, core, T, topo):
     order, eng, fin, st = ORDER["o"]
     Q = {"V": g.vector, "S": g.scalar, "P": g.tensor, "G": g, "Y": g.sync}
     ops = G["ops"]; apart = [False]
-    count = {}; known = {"V": {}, "S": {}, "P": {}, "G": {}, "Y": {}}; done = [None] * len(ops); clock = [None] * len(ops)
+    count = {}; known = {e: {} for e in Q}; done = [None] * len(ops); clock = [None] * len(ops)
     for i in order:
         o = ops[i]; e = eng[i]
         if e not in Q:
-            done[i] = (o["key"], o["cnt"]); clock[i] = {}
+            done[i] = (o["key"], o["cnt"]); clock[i] = {}; count[o["key"]] = o["cnt"]
             continue
         kn = known[e]
         need = {}
         for j, raw in o["deps"].items():
             if eng[j] == e and not raw and ops[j]["key"] is None: continue
+            if ops[j]["key"] == "loc": continue
             k, c = done[j]
-            if kn.get(k, 0) < c: need[k] = count[k] if k[0] == "d" else max(need.get(k, 0), c)
+            if kn.get(k, 0) < c: need[k] = max(need.get(k, 0), c)
         for k, c in sorted(need.items()):
             if kn.get(k, 0) >= c: continue
             Q[e].wait_ge(T.sem[k], c)
@@ -701,15 +635,10 @@ def rank_program(g, core, T, topo):
                 g.wait_ge(T.sem.cG, count["cG"]); kn["cG"] = count["cG"]
             apart[0] = o["name"] == "up"
         ins = o["fn"](Q, e)
-        if o["key"] is None:
-            k = "c" + e
-            count[k] = count.get(k, 0) + 1
-            ins.then_inc(T.sem[k], 1)
-            done[i] = (k, count[k])
-        else:
-            k = o["key"]
-            count[k] = count.get(k, 0) + o["cnt"]
-            done[i] = (k, count[k])
-        c = dict(kn); c[done[i][0]] = max(c.get(done[i][0], 0), done[i][1])
+        k = o["key"] or "c" + e
+        count[k] = count.get(k, 0) + o["cnt"]
+        if o["key"] is None: ins.then_inc(T.sem[k], 1)
+        done[i] = (k, count[k])
+        c = dict(kn); c[k] = max(c.get(k, 0), count[k])
         clock[i] = c
     for k in sorted(count): g.wait_ge(T.sem[k], count[k])

@@ -5,15 +5,17 @@ from concourse.mybir import dt, AluOpType, AxisListType, ActivationFunctionType
 V_, RO, NR = 3072, 4, 4
 MID = 1536
 BIG = 65536.0
+TOP = V_ + 128.0
 OP = AluOpType
 AF = ActivationFunctionType
-COPY, IDENT, RELU, SIGN = AF.Copy, AF.Identity, AF.Relu, AF.Sign
+COPY, IDENT, RELU, SIGN, ABS = AF.Copy, AF.Identity, AF.Relu, AF.Sign, AF.Abs
 D_OF = [1 + t % 3 for t in range(RO)]
 ORD = (1, 0)
 LO, UP = slice(0, 64), slice(64, 128)
-CBN = ["Ib", "IB", "ImB", "Im3072", "Id128", "Imh2", "BOb", "QB", "TR0", "TR1", "K1", "ONE", "KH", "KL"]
-TMP = ["ci", "cg", "cq", "cd", "c64", "c32", "cw0", "cw1"]
-CHN = ["ME0", "ME1", "I128", "I8192", "Ih", "Imh", "Im128", "Im8192", "Ih128", "I32h", "Im16h", "BOh", "BOm", "A1"]
+CBN = ["Ib", "IB", "ImB", "IB2", "ImB2", "Imb", "Im3072", "Id128", "Imh2", "QB", "QN", "K1", "KK", "ONE", "KH", "KL"]
+CWN = ["BO2", "WA", "WQ"]
+TMP = ["ci", "cg", "cq", "cd", "c64", "cw0", "cw1", "cw2", "x0", "x1", "x2", "x3", "x4", "x5", "x6"]
+CHN = ["ME0", "ME1", "I128", "I8192", "Ih", "I01", "Imh", "Im128", "Im8192", "Ih128", "I32h", "Im16h", "I16h", "BOh", "BOm"]
 CXN = ["NF", "NFa"]
 LAND = [(t, d) for t in range(RO - 1) for d in D_OF[t + 1:]]
 
@@ -24,51 +26,61 @@ def _decl():
 
     def sb(names, shape, dtype):
         for n in names.split(): s[n] = ("sbuf", shape, dtype)
-    sb("OI", [128, V_], i); sb("O", [128, V_ + 32], f); sb("P YC", [128, V_], f); sb("XX", [128, 2 * V_], b); sb("WC1 WC2 WC3", [128, V_], b)
-    sb("CI", [128, 384], i); sb("CA PR", [128, 384], f); sb("CHi HL0 L1 L2 L3 XR", [128, 384], b)
-    sb("LD", [128, len(LAND), 256], b); sb("PL", [128, RO - 1, 256], b)
+    sb("OI", [128, V_], i); sb("O", [128, V_ + 48], f); sb("P WC0 WC1 WC2 WC3", [128, V_], f); sb("XX", [128, 2 * V_], b)
+    sb("CI", [128, 192], i); sb("CF F1 F2 F3 MT", [128, 192], f); sb("CA PR", [128, 192], f); sb("H16", [128, 384], hf); sb("CHi", [128, 192], b); sb("C16 L1 L2 L3", [128, 192], hf)
+    sb("LD", [128, len(LAND), 256], hf); sb("PL", [128, RO - 1, 256], hf)
     sb("VT", [128, 2, 4096], f); sb("VR", [128, 4, 256], f); sb("VRh", [128, 4, 256], hf); sb("VC", [128, 8], f)
-    sb("XK MN", [128, 2, 2048], hf); sb("CG", [128, 2, 2048], b); sb("ST", [128, 2, 8, 256], b); sb("VB", [128, 64], f); sb("WL", [128, 2, 8, 2, 128], hf)
-    sb("LA LC LM", [128, 2, 128], u); sb("LB ZL FZ", [128, 2, 8], u); sb("N32", [128, 256], b); sb("S1p", [128, 8], hf); sb("c8p", [128, 8], b)
-    sb("aN uS wN pz ZQ SA", [128, 2, 128], hf); sb("R3 KS", [128, 2, 3, 128], hf); sb("S2", [128, 2, 2, 2, 64], hf)
-    sb("hi oh mine nst XB nw oh2", [128, 2, 128], b); sb("SB", [128, 2, 144], b)
-    sb("F TT OC OE", [128, 2, 128], f); sb("BV B8 t8 x8", [128, 2, 8], f)
-    sb("CB", [128, len(CBN), 128], b); sb("CH", [128, len(CHN), 128], hf); sb("CX", [128, len(CXN), 128], f)
-    sb("WD", [128, 8, 128], hf); sb("Rd", [128, 3, 8], hf); sb("S1h R16", [128, 8], hf); sb("S1b Rc c8", [128, 8], b); sb("U8 pk", [128, 8], f)
+    sb("XK MN", [128, 2, 2048], hf); sb("CG", [128, 4096], hf); sb("ST", [128, 16, 256], b); sb("SV", [128, 2, 2048], b); sb("N16", [128, 1024], b); sb("VB", [128, 64], f); sb("WL", [128, 2, 4, 2, 128], hf)
+    sb("LA LC LM", [128, 2, 128], u); sb("LB ZL FZ", [128, 2, 8], u)
+    sb("aN uS wN pz ZQ", [128, 2, 128], hf); sb("SA", [128, RO, 272], hf); sb("R3 KS", [128, 2, 3, 128], hf); sb("S2", [128, 2, 2, 2, 64], hf)
+    sb("hi oh mine nst XB oh2", [128, 2, 128], b); sb("nw", [128, 2, 256], b); sb("SB", [128, 2, 144], b)
+    sb("F TT OC OE", [128, 2, 128], f); sb("BV B8 t8", [128, 2, 8], f); sb("E0 E2", [128, 2, 272], f); sb("E1", [128, 272], f); sb("TR", [128, 8, 34], b)
+    sb("CB", [128, len(CBN), 128], b); sb("CW", [128, len(CWN), 256], b); sb("CH", [128, len(CHN), 128], hf); sb("CX", [128, len(CXN), 128], f)
+    sb("WD", [128, 4, 128], hf); sb("R16", [128, 4, 64], hf); sb("Rd", [128, 3, 8], hf); sb("S1h S1n Rc", [128, 8], hf); sb("S1b", [128, 8], b); sb("U8 pk", [128, 8], f)
     sb("pi", [128, 1], i); sb("ti", [128, 4], i); sb("tf", [128, 4], f); sb("wq", [128, 16], f); sb("zr", [128, 9], f); sb("zi", [128, 2], i); sb("Zt", [128, 1], f)
-    for n in "ABCD":
-        for h in range(2): s["p%s%d" % (n, h)] = ("psum", [128, 4, 128], f)
+    for h in range(2):
+        for n in "ABC": s["p%s%d" % (n, h)] = ("psum", [128, 512], f)
+        s["pD%d" % h] = ("psum", [128, 8, 64], f)
     return s
 
 
 SCRATCH = _decl()
 SEMAPHORES = ["cV", "cS", "cP", "cG", "loc"] + ["d%d" % k for k in range(30)] + ["ar%d_%d" % (t, j) for t in range(RO) for j in range(3)]
 CYC, WAKE, SAME, GCY, SCY, PF, PO = 0.83e-3, 0.125, 0.07, 1.56, 3.5, 0.6, 0.02
-RATE, LAT, FAR, ROW = 230.0, 2.2, 4.5, 0.1
-NPG = 2
-ONV = [("XK", 1, 1), ("XK", 0, 1), ("CG", 1, 1), ("CG", 0, 1)]
-INDIRECT = "XK CG XM ST XB OC OE scatter".split()
-CASES = []
-SEED = [12345]
-APART = [-4.0, -3.0, -2.0]
-LINK = [25.0]
-DEAL = []
-LEAD = [0.0]
-NPW = 1
-LOADS = {"ld ctl": -9, "ld xr": -8, "ld sha": -7, "ld hol1": -6, "ld rows": -5, "ld hol0": -4, "ld flat": 12}
+RATE, LAT, FAR, ROW, LINK = 230.0, 2.2, 4.5, 0.1, 25.0
+CUT = {("XK", 1): [(64, "S"), (64, "V")], ("XK", 0): [(64, "S"), (64, "S")], ("CG", 1): [(48, "S"), (48, "S"), (32, "S")], ("CG", 0): [(48, "S"), (48, "S"), (32, "V")],
+       ("XM", 1): [(64, "S"), (64, "S")], ("XM", 0): [(48, "S"), (48, "S"), (32, "S")], ("ST", 1): [(64, "V"), (64, "V")], ("ST", 0): [(32, "V")] * 4}
+INDIRECT = "XK CG XM ST OB XB OC OE scatter".split()
+OPT = {"KS": 1, "R3": 0, "WV": [1, 0], "HIP": 0, "SL": "DD", "MG": 4}
+CASES = [(1.0, 1.0, 1.0, 0.125, 0.07, 0.0, 0.65), (1.6, 1.35, 1.35, 0.17, 0.09, 1.0, 0.25)]
+SEED = [7]
+APART = [0.0]
+LOADS = {"ld ctl": -9, "ld sha": -7, "ld hol1": -6, "ld hol0": -4, "ld flat": 12}
 START = 11.0
 SAME_AS = {"XO": "F", "BD": "F", "FR": "uS", "wp": "hi", "pc": "uS"}
-ASG = {n: "S" for n in "R3 Y2 aN mS cS KS hi XB bm FR PL Pu OC YC WCu Oc XK CG XM n8b H8".split() + [""]}
-WT = {}
-STS = [8, 8]
+ASG = {n: "S" for n in "R3 RS cK Y2 aN mS cS KS hi XB bm FR PL Pu OC YC WCu H8 slot dig BD nst DS".split() + [""]}
+FIXED = ["", "wide1"]
 PLAN = [(0, 0.3, "LA"), (0.3, 3.1, "XK"), (3.2, 4.1, "dec"), (4.2, 5.8, "Y2 R3 uT LC"), (5.8, 8.6, "CG"), (8.7, 9.6, "cL"), (9.7, 11, "cS TK KS"), (11, 13, "D"), (11.3, 13.5, "clip"),
         (11.8, 13.8, "pool"), (13.8, 16.6, "hi hi- F T oh ohT wN bR mine LMp LM"), (15.5, 16.7, "bL BD LBp LB XB XBp"), (16.7, 19.4, "XM"), (17.2, 19.1, "MX"), (17.7, 19.9, "FL"),
-        (18.2, 20.3, "WS"), (19.9, 21.3, "FR K2 F2 T2 oh2"), (20.3, 21.1, "wp WN nw"), (21.4, 24.6, "pzp pz ZQp ZQ DSp DS DM x8 fl FZp FZ"), (22.0, 24.4, "ohT2 pc ZLp ZL csv OC OE NN"),
-        (24.6, 27, "scatter"), (21.2, 24, "t8 n8 H8 DG PL send"), (24, 27, "Pp Pu"), (6.5, 8.5, "MN"), (7.5, 9.2, "mL"), (9.3, 9.6, "mS"), (15, 17.5, "ST"), (11, 15, "OB"), (15.5, 17.5, "SQ"), (17.5, 19, "SL"), (19.2, 19.5, "nst"),
-        (27.5, 30, "XO O Osw Oc"), (24, 26, "HL"), (26, 28, "YCp YC ZC zr Z"), (3.2, 3.4, "aN"), (-1, 0, "XV"), (16, 17, "b8 bm"), (10.5, 11, "K1"), (36, 37, "sendb")]
-PER = [30.0, 1.1, 6.0]
-SWEEPS = 2
-TRIES = [1500, 5, 3.0, 0.3]
+        (18.2, 20.3, "WS"), (19.9, 21.3, "FR K2 F2 T2 oh2"), (20.3, 21.1, "wp WN nw"), (21.4, 23.6, "pzp pz ZQp ZQ DSp DSq DSw DS DM FZ"), (22.0, 23.4, "ZLp ZL pc csv OC OE NN"),
+        (23.6, 26, "scatter"), (21.2, 24, "t8 n8 H8 DG PL send"), (24, 27, "Pp Pu"), (6.5, 8.5, "MN"), (7.5, 9.2, "mL"), (9.3, 9.6, "mS"), (3, 9, "ST"), (11, 15, "OB"), (15.5, 17.5, "SQ"), (17.5, 19, "SL"), (19.2, 19.5, "nst"),
+        (27.5, 30, "XO O"), (24, 26, "HL"), (26, 28, "YC ZC zr Z"), (3.2, 3.4, "aN"), (-1, 0, "XV"), (16, 17, "b8 bm"), (10.5, 11, "K1"), (36, 37, "sendb")]
+PER = [28.0, 3.0]
+STEPS = [("LA", .1, .2, .25, .4), ("XK", .3, .5, 1.7, 5.2), ("dec", 1.9, 2.8, 5.3, 6.2), ("Y2 R3", 3.1, 3.8, 6.2, 6.9), ("uT LC", 3.9, 4.6, 7.0, 7.7), ("WCp", 3, 5.0, 0, 0), ("WCu", 5.2, 5.5, 0, 0),
+         ("CG", 5.5, 8.3, 9.0, 12.5), ("cL", 8.9, 9.8, 12.5, 13.4), ("cS TK KS", 9.9, 11.2, 13.4, 14.7), ("K1 D", 11.0, 11.6, 14.6, 15.2), ("clip", 11.5, 12.5, 15.1, 16.1), ("pool", 12, 12.9, 15.6, 16.5),
+         ("hi hi- F T oh ohT wN", 12.9, 14.8, 16.5, 18.4), ("bL BD LBp LB XB XBp", 14.8, 16.8, 18.4, 20.4), ("bR mine LMp LM", 14.9, 16.2, 18.5, 19.8), ("XM", 16.7, 19.5, 20.3, 23.1),
+         ("MX", 16.9, 19.5, 20.4, 22.3), ("FL", 17.5, 19.8, 21, 22.6), ("WS", 19.8, 21.2, 23.2, 24.5), ("WV", 18.5, 21, 22, 24.5), ("FR", 19.8, 20, 22.6, 22.8), ("K2", 18, 22, 21, 24.5),
+         ("F2 T2 oh2 pzp pz ZQp ZQ", 20.5, 23, 23.2, 25.1), ("TRp", 20.1, 20.2, 22.9, 23), ("DSp DSq", 22.5, 23.5, 24.6, 25.6), ("wp WN nw", 21.3, 22.3, 24.5, 25.4),
+         ("DSw DS DM FZ", 23.5, 25, 25.5, 26.7), ("ZLp ZL pc csv OC OE NN", 23.1, 25, 25.2, 26.7), ("scatter", 25.2, 26.6, 26.8, 28), ("t8 n8 send", 22.4, 23, 25.4, 25.8),
+         ("H8 Pp", 24, 25, 26, 27), ("Pu", 0, 0, 27, 27.8), ("DG PL", 27, 28, 27.5, 28.5), ("MN", 2.5, 4.4, 7.5, 9.4), ("mL mS", 3.5, 8, 9, 12), ("ST", 4.6, 7.4, 9.4, 15),
+         ("SL nst", 13, 16, 16.5, 19), ("XO O", 29.8, 30.1, 30.1, 30.4), ("HL", 26.5, 27.5, 27.5, 28.2), ("ZC zr Z", 0, 0, 30, 36), ("aN", 8.5, 8.6, 12, 12.1), ("XV", 1, 1.3, 4, 4.3),
+         ("b8 bm", 17, 19, 21, 23), ("sendb", 0, 0, 29, 30), ("WCg", 0, 0, 40, 44), ("OB", 3, 9, 9, 15), ("SQ", 10, 12, 15, 17)]
+PERIOD = 28.3
+TRIES = [8500, 6000, 500, 2500, 5000]
+MOVES = [2.0, 0.4, 1.5, 0.7, 0.25, 0.06, 0.4]
+NOTE = []
+EARLY = {"P0d": -1.5, "pick": -4, "flat1": -1, "wide1": -1, "late": None, "next": 3, "c16": -3, "send0": -3, "dig": -2, "PR": -2, "rows": -2, "P0p": -1, "P0": -1, "LA": -1, "send0b": 20, "O32": 36, "negX": 2, "zero": None, "wide": None, "flat": None, "yc0": None, "fillW": -6}
+MARK = [0.4, "LC KS hi wN LM XB FR nw ZQ FZ PL".split()]
 _ = slice(None)
 SIZE = {"float32": 4, "int32": 4}
 
@@ -79,7 +91,6 @@ def bits(ix):
 
 
 MASKS = {}
-SOLO = []
 
 
 def ref(T, name, *ix):
@@ -97,11 +108,10 @@ def ind(win, off): return (win[0], win[1].indirect(off[1]), win[2], win[3], 16 *
 def ap(x): return x[1] if isinstance(x, tuple) else x
 
 
-def add(G, opts, fn, r=(), w=(), key=None, cnt=1, name=""):
+def add(G, e, use, end, fn, r=(), w=(), key=None, cnt=1, name="", alt=None):
     n = len(G["ops"]); deps = {}
     r = [x for x in r if isinstance(x, tuple)]
     r += [x[7] for x in list(r) + list(w) if x[7] is not None]
-    engs = tuple(sorted(opts))
 
     def dep(j, raw):
         if j != n: deps[j] = deps.get(j, False) or raw
@@ -110,7 +120,7 @@ def add(G, opts, fn, r=(), w=(), key=None, cnt=1, name=""):
         if x[6]:
             if x[0] in G["bw"]: dep(G["bw"][x[0]], True)
             for j in G["br"].get(x[0], []):
-                if G["ops"][j]["engs"] != engs or len(engs) > 1: dep(j, False)
+                if G["ops"][j]["eng"] != e or alt or G["ops"][j]["alt"]: dep(j, False)
             continue
         for (a, b, j) in G["wr"].get(x[0], []):
             if a & x[2] and b & x[3]: dep(j, True)
@@ -131,7 +141,7 @@ def add(G, opts, fn, r=(), w=(), key=None, cnt=1, name=""):
         if x[0] is None: continue
         if x[6]: G["br"].setdefault(x[0], []).append(n)
         else: G["rd"].setdefault(x[0], []).append((x[2], x[3], n))
-    G["ops"].append({"opts": opts, "engs": engs, "fn": fn, "deps": deps, "key": key, "cnt": cnt, "name": name, "t": G.get("t"), "h": G.get("h")})
+    G["ops"].append({"eng": e, "use": use, "end": end, "fn": fn, "deps": deps, "key": key, "cnt": cnt, "name": name, "t": G.get("t"), "h": G.get("h"), "alt": alt})
     return n
 
 
@@ -146,20 +156,17 @@ def place(busy, t, d):
     return t, lo
 
 
-def schedule(G, solo=False):
+def schedule(G):
     ops = G["ops"]; n = len(ops)
     succ = [[] for i in range(n)]
     for i, o in enumerate(ops):
         for j in o["deps"]: succ[j].append(i)
     pred = [list(o["deps"]) for o in ops]
-
-    eng = [o["engs"][0] for o in ops]
-    use = [o["opts"][e][0] for o, e in zip(ops, eng)]; end = [o["opts"][e][1] for o, e in zip(ops, eng)]
+    eng = [o["eng"] for o in ops]; use = [o["use"] for o in ops]; end = [o["end"] for o in ops]
     lag = lambda j, i: end[j] + WAKE if eng[j] != eng[i] else end[j] + SAME if ops[i]["deps"][j] or ops[j]["key"] else use[j]
     fore = [[(j, lag(j, i)) for j in pred[i]] for i in range(n)]
     aft = [[(j, use[j] + lag(i, j) - use[i]) for j in succ[i]] for i in range(n)]
     first = [(i, LOADS[o["name"]]) for i, o in enumerate(ops) if o["name"] in LOADS]
-
     link = {i: o["link"] for i, o in enumerate(ops) if "link" in o}
 
     def sweep(key, before, least):
@@ -190,8 +197,8 @@ def schedule(G, solo=False):
                 for j in pred[i]:
                     if prio[j] > k: prio[j] = k
             at = sweep(prio, fore, none)
-            fin = [at[i] + end[i] for i in range(n)]
-            if best is None or max(fin) < max(best[2]): best = (None, eng, fin, at)
+            fin = max([at[i] + end[i] for i in range(n)])
+            if best is None or fin < best[0]: best = (fin, at)
             if it + 1 < sweeps:
                 key = [-(at[i] + use[i]) for i in range(n)]
                 for i in range(n):
@@ -199,52 +206,22 @@ def schedule(G, solo=False):
                     for j in succ[i]:
                         if key[j] > k: key[j] = k
                 back = sweep(key, aft, tail)
-                prio = [max(fin) - (back[i] + use[i]) for i in range(n)]
-        return best, prio
+                prio = [fin - (back[i] + use[i]) for i in range(n)]
+        return best
     when = {}
     for a, z, names in PLAN:
         for k, x in enumerate(names.split()): when[x] = (a + (z - a) * k / len(names.split()), (z - a) / len(names.split()))
     seen, total, key = {}, {}, [None] * n
     for o in ops: total[o["t"], o["name"], o["h"]] = total.get((o["t"], o["name"], o["h"]), 0) + 1
+    kinds = {}
     for i, o in enumerate(ops):
         c = (o["t"], o["name"], o["h"]); k = seen.get(c, 0); seen[c] = k + 1
+        kinds.setdefault((o["name"], o["h"]), []).append(i)
+        if total[c] > 1 and o["t"] is not None: kinds.setdefault((o["name"], o["h"], k), []).append(i)
         if o["t"] is not None and o["h"] is not None and o["name"] in when:
-            key[i] = START + o["t"] * PER[0] + ORD.index(o["h"]) * PER[2] + PER[1] * (when[o["name"]][0] + when[o["name"]][1] * k / total[c]) - WT.get(o["name"], 0.0)
+            key[i] = START + o["t"] * PER[0] + ORD.index(o["h"]) * PER[2] + PER[1] * (when[o["name"]][0] + when[o["name"]][1] * k / total[c])
     for i in range(n - 1, -1, -1):
-        if key[i] is None: key[i] = min([key[s] for s in succ[i]] or [1e3]) - min(x[1] for x in ops[i]["opts"].values())
-
-    def deal(shift):
-        at = [0.0] * n; free = {e: 0.0 for e in eng}; ready = {e: [] for e in eng}; left = [len(p) for p in pred]; est = [0.0] * n; due = [0.0] * n; base = {}
-
-        def push(i):
-            o = ops[i]; t = 0.0
-            for j, d in fore[i]:
-                if at[j] + d > t: t = at[j] + d
-            est[i] = t; c = (o["t"], o["h"])
-            if o["name"] == "XK" and c not in base: base[c] = t
-            due[i] = base.get(c, t) + rel[i] + shift.get((o["name"], o["h"]), 0.0) if rel[i] is not None else key[i] if o["name"] in LOADS else t + shift.get((o["name"], o["h"]), 0.0)
-            ready[eng[i]].append(i)
-        for i in range(n):
-            if not left[i]: push(i)
-        for it in range(n):
-            c = None
-            for e, r in ready.items():
-                for i in r:
-                    x = max(est[i], free[e]) + use[i]
-                    if c is None or x < c: c = x; q = e
-            i = min([i for i in ready[q] if est[i] <= c], key=lambda i: due[i])
-            ready[q].remove(i); at[i] = max(est[i], free[q]); free[q] = at[i] + use[i]
-            for j in succ[i]:
-                left[j] -= 1
-                if not left[j]: push(j)
-        return at
-    if DEAL:
-        rel = [None if o["t"] is None or o["h"] is None or o["name"] not in when else key[i] - o["t"] * PER[0] - o["h"] * PER[2] - (LEAD[0] if o["h"] == 0 else 0) for i, o in enumerate(ops)]
-        for i, k in first: key[i] = k
-        key = deal(DEAL[0])
-        if SWEEPS == 0: return (sorted(range(n), key=lambda i: (key[i], i)), eng, [key[i] + end[i] for i in range(n)], key)
-    kinds = {}
-    for i, o in enumerate(ops): kinds.setdefault((o["name"], o["h"]), []).append(i)
+        if key[i] is None: key[i] = min([key[s] for s in succ[i]] or [1e3]) - end[i]
     kinds = list(kinds.values()); x = [SEED[0]]
 
     def rnd():
@@ -252,13 +229,13 @@ def schedule(G, solo=False):
         return x[0] / 2 ** 31
 
     cases = []
-    for gather, fix, pe, po, wake, same, far, lat in CASES:
-        u = [(x - 0.06) * gather + 0.06 if o["name"] in INDIRECT else x + fix if e in "VS" else (x - PO) * pe + po if e == "P" else x for x, e, o in zip(use, eng, ops)]
-        z = [a + y - x + (far if e[0] == "N" else lat if o["key"] and o["key"][0] == "d" else 0.0) for a, x, y, e, o in zip(u, use, end, eng, ops)]
+    for gather, rest, pe, wake, same, far in CASES:
+        u = [(x - 0.06) * gather + 0.06 if o["name"] in INDIRECT else x * rest if e in "VSG" else x * pe if e == "P" else x for x, e, o in zip(use, eng, ops)]
+        z = [a + y - x + (far if e[0] == "N" else 0.0) for a, x, y, e in zip(u, use, end, eng)]
         cases.append((u, z, [[(j, z[j] + (wake if eng[j] != eng[i] else same)) for j in pred[i] if eng[j] != eng[i] or ops[i]["deps"][j] or ops[j]["key"]] for i in range(n)]))
 
-    def score(b):
-        order = sorted(range(n), key=lambda i: (b[3][i], i)); s = 0.0
+    def times(b):
+        order = sorted(range(n), key=lambda i: (b[1][i], i)); out = [b[0]]
         for u, z, before in cases:
             at = [0.0] * n; free = {e: 0.0 for e in eng}; last = 0.0
             for i in order:
@@ -267,26 +244,319 @@ def schedule(G, solo=False):
                     if at[j] + d > t: t = at[j] + d
                 at[i] = t; free[eng[i]] = t + u[i]
                 if t + z[i] > last: last = t + z[i]
-            s += last
-        return (s + max(b[2])) / (len(cases) + 1)
+            out.append(last)
+        return out
+
+    def score(b):
+        s = times(b)
+        return s[0] * 0.5 + 0.5 * sum(a * 150.0 / w for a, w in zip(s[1:], (135.0, 200.0))) / len(cases) if cases else s[0]
 
     def mend(best, tries):
         cur = best; low = now = score(best)
         for it in range(tries):
-            key = list(cur[3])
+            key = list(cur[1])
             for k in range(1 + int(rnd() * TRIES[1])):
                 d = (rnd() - 0.5) * TRIES[2]
                 for i in kinds[int(rnd() * len(kinds))]: key[i] += d
-            new = both(key, 1 + (rnd() < 0.3))[0]
-            if max(new[2]) > max(cur[2]) + 3.0: continue
+            new = both(key, 1 + (rnd() < 0.3))
+            if new[0] > cur[0] + 2.0: continue
             s = score(new)
             if s <= now + TRIES[3] * (1 - it / tries) * rnd(): cur = new; now = s
             if now < low: best = cur; low = now
-        SOLO.append(low)
         return best, low
-    starts = [mend(both([k + (d if o["h"] == ORD[1] and o["t"] is not None else 0.0) for k, o in zip(key, ops)], SWEEPS)[0], TRIES[0] // (2 * len(APART))) for d in APART]
+    starts = [mend(both([k + (d if o["h"] == ORD[1] and o["t"] is not None else 0.0) for k, o in zip(key, ops)], 2), TRIES[0] // (2 * len(APART))) for d in APART]
     best = mend(min(starts, key=lambda b: b[1])[0], TRIES[0] // 2)[0]
-    return (sorted(range(n), key=lambda i: (best[3][i], i)),) + best[1:]
+    return sorted(range(n), key=lambda i: (best[1][i], i)), best[1], times(best)
+
+
+def schedule(G):
+    ops = G["ops"]; n = len(ops)
+    pred = [list(o["deps"]) for o in ops]
+    succ = [[] for i in range(n)]
+    for i in range(n):
+        for j in pred[i]: succ[j].append(i)
+    names = sorted({o["eng"] for o in ops}); eng = [names.index(o["eng"]) for o in ops]
+    link = [o.get("link", 0.0) for o in ops]
+    when = {}
+    for a, z, xs in PLAN:
+        for k, x in enumerate(xs.split()): when[x] = (a + (z - a) * k / len(xs.split()), (z - a) / len(xs.split()))
+    seen, total, key, kinds, kind = {}, {}, [None] * n, {}, [None] * n
+    for o in ops: total[o["t"], o["name"], o["h"]] = total.get((o["t"], o["name"], o["h"]), 0) + 1
+    for i, o in enumerate(ops):
+        c = (o["t"], o["name"], o["h"]); k = seen.get(c, 0); seen[c] = k + 1
+        kind[i] = kinds.setdefault((o["name"], o["h"], k) if o["t"] is not None else i, []); kind[i].append(i)
+        if o["name"] in LOADS: key[i] = LOADS[o["name"]]
+        elif o["t"] is not None and o["h"] is not None and o["name"] in when:
+            key[i] = START + o["t"] * PER[0] + ORD.index(o["h"]) * PER[2] + PER[1] * (when[o["name"]][0] + when[o["name"]][1] * k / total[c])
+    for i in range(n - 1, -1, -1):
+        if key[i] is None: key[i] = min([key[s] for s in succ[i]] or [1e3]) - ops[i]["end"]
+    x = [SEED[0]]
+
+    def rnd():
+        x[0] = (x[0] * 1103515245 + 12345) % 2 ** 31
+        return x[0] / 2 ** 31
+
+    cases = []
+    for gather, rest, pe, wake, same, far, weight in CASES:
+        u = [(o["use"] - 0.06) * gather + 0.06 if o["name"] in INDIRECT else o["use"] * (rest if o["eng"] in "VSG" else pe if o["eng"] == "P" else 1.0) for o in ops]
+        z = [a + o["end"] - o["use"] + (far if o["eng"][0] == "N" else 0.0) for a, o in zip(u, ops)]
+        cases.append((u, z, [[(j, z[j] + (wake if eng[j] != eng[i] else same)) for j in pred[i] if eng[j] != eng[i] or ops[i]["deps"][j] or ops[j]["key"]] for i in range(n)], weight))
+
+    def run(order, case):
+        u, z, before, weight = case
+        at = [0.0] * n; why = [-1] * n; free = [0.0] * len(names); who = [-1] * len(names); wire = 0.0; last = 0.0; end = 0
+        for i in order:
+            e = eng[i]; t = free[e]; w = -2 - who[e]
+            for j, d in before[i]:
+                d += at[j]
+                if d > t: t = d; w = j
+            if link[i]:
+                if wire > t: t = wire
+                wire = t + link[i]
+            at[i] = t; why[i] = w; free[e] = t + u[i]; who[e] = i
+            if t + z[i] > last: last = t + z[i]; end = i
+        return last, at, why, end
+
+    def settle(key, back):
+        if back:
+            for i in range(n - 1, -1, -1):
+                k = key[i] - 1e-5
+                for j in pred[i]:
+                    if key[j] > k: key[j] = k
+        else:
+            for i in range(n):
+                k = key[i] + 1e-5
+                for j in succ[i]:
+                    if key[j] < k: key[j] = k
+        order = sorted(range(n), key=lambda i: key[i])
+        rs = [run(order, c) for c in cases]
+        return sum(r[0] * c[3] for r, c in zip(rs, cases)), order, rs
+    cur = best = settle(key, True)
+    for it in range(TRIES[0]):
+        now, order, rs = cur
+        key = [0.0] * n
+        for p, i in enumerate(order): key[i] = rs[0][1][i] + p * 1e-7
+        last, at, why, i = rs[int(rnd() * len(rs))]
+        held = []
+        while i >= 0:
+            w = why[i]
+            if w < -1:
+                w = -2 - w; held.append((w, i))
+            i = w
+        r = rnd()
+        if held and r < 0.8:
+            j, i = held[int(rnd() * len(held))]
+            d = key[i] - key[j] + 1e-4 + (rnd() * TRIES[2] if rnd() < 0.3 else 0.0); back = rnd() < 0.5
+            m, d = (i, -d) if back else (j, d)
+        else:
+            m = int(rnd() * n); d = (rnd() - 0.5) * 2 * TRIES[2]; back = d < 0
+        for k in kind[m] if rnd() < TRIES[1] else [m]:
+            if ops[k]["name"] not in LOADS: key[k] += d
+        new = settle(key, back)
+        if new[0] <= now + TRIES[3] * (1 - it / TRIES[0]) * rnd(): cur = new
+        if cur[0] < best[0]: best = cur
+    return best[1], best[2][0][1], [r[0] for r in best[2]]
+
+
+def plan(ops):
+    when, total, key = {}, {}, [None] * len(ops)
+    for xs, *at in STEPS:
+        xs = xs.split()
+        for h, a, z in zip(ORD, at[0::2], at[1::2]):
+            for k, x in enumerate(xs): when[x, h] = (a + (z - a) * k / len(xs), (z - a) / len(xs))
+    for o in ops: total[o["t"], o["name"], o["h"]] = total.get((o["t"], o["name"], o["h"]), 0) + 1
+    for i, o in enumerate(ops):
+        c = when.get((o["name"], o["h"]))
+        if o["t"] is not None and c: key[i] = START + o["t"] * PERIOD + c[0] + c[1] * o["k"] / total[o["t"], o["name"], o["h"]]
+    return key
+
+
+def mend(ops, key, tries, alike, heat=1.0):
+    n = len(ops)
+    pred = [list(o["deps"]) for o in ops]; succ = [[] for o in ops]
+    for i in range(n):
+        for j in pred[i]: succ[j].append(i)
+    names = sorted({o["eng"] for o in ops} | {"V", "S"}); eng = [0] * n
+    link = [o.get("link", 0.0) for o in ops]
+    kinds = {}; kind = [kinds.setdefault((o["name"], o["h"], o["k"]) if o["t"] is not None else i, []) for i, o in enumerate(ops)]
+    for i, o in enumerate(ops):
+        kind[i].append(i)
+        if o["name"] in LOADS: key[i] = LOADS[o["name"]]
+    for i in range(n - 1, -1, -1):
+        if key[i] is None: key[i] = min([key[s] for s in succ[i]] or [1e3]) - ops[i]["end"]
+    x = [SEED[0]]
+
+    def rnd():
+        x[0] = (x[0] * 1103515245 + 12345) % 2 ** 31
+        return x[0] / 2 ** 31
+    cases = [([0.0] * n, [0.0] * n, [None] * n, c[6]) for c in CASES]
+    use, end = cases[0][:2]
+    fore = [None] * n; aft = [None] * n
+
+    def price(i):
+        o = ops[i]; eng[i] = names.index(o["eng"])
+        for (gather, rest, pe, wake, same, far, weight), c in zip(CASES, cases):
+            c[0][i] = (o["use"] - 0.06) * gather + 0.06 if o["name"] in INDIRECT else o["use"] * (rest if o["eng"] in "VSG" else pe if o["eng"] == "P" else 1.0)
+            c[1][i] = c[0][i] + o["end"] - o["use"] + (far if o["eng"][0] == "N" else 0.0)
+
+    def tie(i):
+        for (gather, rest, pe, wake, same, far, weight), c in zip(CASES, cases):
+            c[2][i] = [(j, c[1][j] + (wake if eng[j] != eng[i] else same)) for j in pred[i] if eng[j] != eng[i] or ops[i]["deps"][j] or ops[j]["key"]]
+        d = dict(cases[0][2][i]); fore[i] = [(j, d.get(j, use[j])) for j in pred[i]]
+
+    def untie(i): aft[i] = [(j, use[j] + dict(fore[j])[i] - use[i]) for j in succ[i]]
+
+    def flip(ks):
+        for i in ks:
+            o = ops[i]; a = o["alt"]; o["alt"] = (o["eng"], o["use"], o["fn"]); o["eng"], o["use"], o["fn"] = a; o["end"] = o["use"]; price(i)
+        for i in ks:
+            for j in [i] + succ[i]: tie(j)
+        for i in ks:
+            for j in [i] + pred[i]: untie(j)
+    for f in (price, tie, untie):
+        for i in range(n): f(i)
+    none = [o.get("least", 0.0) for o in ops]; tail = [end[i] - use[i] for i in range(n)]
+    loads = [i for i, o in enumerate(ops) if o["name"] in LOADS]
+
+    def sweep(key, before, least):
+        at = [0.0] * n; A = [[] for e in names]; Z = [[] for e in names]
+        for i in np.argsort(key, kind="stable").tolist():
+            t = least[i]
+            for j, d in before[i]:
+                d += at[j]
+                if d > t: t = d
+            a = A[eng[i]]; z = Z[eng[i]]; u = use[i]; k = m = len(z)
+            while k and z[k - 1] > t: k -= 1
+            while k < m and a[k] < t + u - 1e-9:
+                if z[k] > t: t = z[k]
+                k += 1
+            a.insert(k, t); z.insert(k, t + u); at[i] = t
+        return at
+
+    def run(order, case):
+        u, z, before, weight = case
+        at = [0.0] * n; why = [-1] * n; free = [0.0] * len(names); who = [-1] * len(names); wire = 0.0; last = 0.0; end = 0
+        for i in order:
+            e = eng[i]; t = free[e]; w = -2 - who[e]
+            if none[i] > t: t = none[i]; w = -1
+            for j, d in before[i]:
+                d += at[j]
+                if d > t: t = d; w = j
+            if link[i]:
+                if wire > t: t = wire
+                wire = t + link[i]
+            at[i] = t; why[i] = w; free[e] = t + u[i]; who[e] = i
+            if t + z[i] > last: last = t + z[i]; end = i
+        return last, at, why, end
+
+    def up(key):
+        for i in range(n - 1, -1, -1):
+            k = key[i] - 1e-5
+            for j in pred[i]:
+                if key[j] > k: key[j] = k
+
+    def shift(key, i, d):
+        key[i] += d; todo = [i]
+        while todo:
+            i = todo.pop()
+            for j in pred[i] if d < 0 else succ[i]:
+                if key[j] >= key[i] if d < 0 else key[j] <= key[i]: key[j] = key[i] + (-1e-5 if d < 0 else 1e-5); todo.append(j)
+
+    def settle(key, both=False):
+        at = sweep(key, fore, none)
+        if both:
+            key = [at[i] + use[i] for i in range(n)]
+            up(key); b = sweep([-k for k in key], aft, tail)
+            key = [-(b[i] + use[i]) for i in range(n)]
+            for i in loads: key[i] = at[i] - 1e3
+            up(key); at = sweep(key, fore, none)
+        order = np.argsort(at, kind="stable").tolist()
+        rs = [run(order, c) for c in cases]
+        return sum(r[0] * c[3] for r, c in zip(rs, cases)) + sum(rs[0][1][i] for i in marks) * MARK[0] / len(marks), order, rs
+    marks = [i for i, o in enumerate(ops) if o["name"] in MARK[1]]
+    up(key)
+    cur = best = min([settle(list(key), j) for j in (0, 1)], key=lambda b: b[0]); queues = [o["eng"] for o in ops]
+    far, slack, moves, aimed, both, swap = MOVES[:6]
+    for it in range(tries):
+        now, order, rs = cur
+        key = list(rs[0][1])
+        last, at, why, i = rs[int(rnd() * len(rs))]
+        held = []
+        while i >= 0:
+            w = why[i]
+            if w < -1: w = -2 - w; held.append((w, i))
+            i = w
+        early = rnd() < 0.5
+        for rep in range(1 + int(rnd() * moves)):
+            if held and rnd() < aimed:
+                j, i = held[int(rnd() * len(held))]
+                d = key[i] - key[j] + 1e-4 + (rnd() * far if rnd() < 0.5 else 0.0)
+                m, d = (i, -d) if early else (j, d)
+            else: m = int(rnd() * n); d = rnd() * far * (-1 if early else 1)
+            span = rnd() * 8.0 if rnd() < MOVES[6] else 0.0
+            for k in kind[m] if rnd() < alike else [m]:
+                todo = [k]; seen = {k}; last = key[k] + span
+                while todo:
+                    i = todo.pop()
+                    for j in succ[i]:
+                        if j not in seen and key[j] < last and ops[j]["h"] == ops[k]["h"]: seen.add(j); todo.append(j)
+                for i in sorted(seen, reverse=not early):
+                    if ops[i]["name"] not in LOADS: shift(key, i, d)
+        ks = []
+        if rnd() < swap:
+            c = [kind[y] for p in held for y in p if ops[y]["alt"]]
+            if c:
+                ks = c[int(rnd() * len(c))]; ks = [k for k in ks if ops[k]["alt"] and ops[k]["eng"] == ops[ks[-1]]["eng"]]
+                flip(ks)
+        new = settle(key, rnd() < both)
+        if new[0] <= now + heat * slack * (1 - it / tries) * rnd(): cur = new
+        else: flip(ks)
+        if cur[0] < best[0]: best = cur; queues = [o["eng"] for o in ops]
+    flip([i for i in range(n) if ops[i]["eng"] != queues[i]])
+    return best[1], best[2][0][1], [r[0] for r in best[2]]
+
+
+def middle(ops, ts):
+    need = {i for i, o in enumerate(ops) if ts[0] and o["t"] == ts[0] or o["t"] == ts[1] and o["name"] in ("scatter", "Pu", "send")}
+    for i in range(len(ops) - 1, -1, -1):
+        if i in need: need.update(j for j in ops[i]["deps"] if ops[j]["t"] in ts)
+    at = {i: k for k, i in enumerate(sorted(need))}
+    return [dict(ops[i], i=i, deps={at[j]: r for j, r in ops[i]["deps"].items() if j in at}) for i in sorted(need)]
+
+
+def schedule(G):
+    ops = G["ops"]; seen = {}
+    for o in ops:
+        c = (o["t"], o["name"], o["h"]); o["k"] = seen.get(c, 0); seen[c] = o["k"] + 1
+    mid = middle(ops, (1, 2))
+    order, at, times = mend(mid, plan(mid), TRIES[0], 1.0)
+    order, at, times = mend(mid, list(at), TRIES[3], 1.0, 0.4)
+    ends = [max(a + o["end"] for a, o in zip(at, mid) if o["t"] == t and o["name"] == "scatter") for t in (1, 2)]; per = ends[1] - ends[0]
+    like = {}
+    for a, o in zip(at, mid): like[o["name"], o["h"], o["k"]] = (a - ends[0] + (2 - o["t"]) * per, o["eng"])
+    key = plan(ops)
+    for i, o in enumerate(ops):
+        c = like.get((o["name"], o["h"], o["k"]))
+        if o["t"] is None: key[i] = EARLY.get(o["name"], i * 1e-3)
+        if c and o["t"] is not None:
+            key[i] = START + o["t"] * per + c[0]
+            if o["t"] == 0 and o["name"] == "XK": c = (c[0], "SV"[o["k"] % 2]); key[i] = START + (5.3 if o["h"] == ORD[1] else 1.3)
+            if c[1] != o["eng"] and o["alt"]: o["alt"], o["eng"], o["use"], o["fn"] = (o["eng"], o["use"], o["fn"]), *o["alt"]; o["end"] = o["use"]
+            if o["t"] == 0 and o["name"] == "XK": o["alt"] = None
+    NOTE.append((per, mid, at, ends, order))
+    head = middle(ops, (None, 0))
+    order, at, times = mend(head, [key[o["i"]] for o in head], TRIES[1], 0.0)
+    late = max(a + o["end"] for a, o in zip(at, head) if o["name"] == "scatter") - per - START
+    key = [k and k + late for k in key]
+    for a, o in zip(at, head):
+        key[o["i"]] = a
+        if o["t"] is not None or o["alt"]: ops[o["i"]].update({x: o[x] for x in ("alt", "eng", "use", "end", "fn")})
+    order, at, times = mend(ops, key, TRIES[2], 0.3)
+    keep = [i for i, o in enumerate(ops) if o["t"] == RO - 1 or at[i] > START + late + (RO - 1) * per - 3.0]; at_ = {i: k for k, i in enumerate(keep)}
+    tail = [dict(ops[i], i=i, deps={at_[j]: r for j, r in ops[i]["deps"].items() if j in at_}, least=max([at[j] + ops[j]["end"] + WAKE for j in ops[i]["deps"] if j not in at_] + [START + late + (RO - 1) * per - 3.0])) for i in keep]
+    for a, o in zip(mend(tail, [at[i] for i in keep], TRIES[4], 0.0, 0.5)[1], tail):
+        at[o["i"]] = a; ops[o["i"]].update({x: o[x] for x in ("alt", "eng", "use", "end", "fn")})
+    return mend(ops, list(at), 0, 0.0)
 
 
 def build(core, T, topo, rank):
@@ -306,7 +576,7 @@ def build(core, T, topo, rank):
 
     def vop(fn, o, ins, name, two=False):
         c = cost("V", o, ins, two)
-        return add(G, {"V": (c, c)}, lambda Q, e: fn(Q["V"]), ins, [o], name=name)
+        return add(G, "V", c, c, lambda Q: [fn(Q["V"])], ins, [o], name=name)
 
     def tt(o, a, b, op, name=""): return vop(lambda v: v.tensor_tensor(o[1], a[1], b[1], op), o, [a, b], name, True)
 
@@ -315,183 +585,270 @@ def build(core, T, topo, rank):
         return vop(lambda v: v.tensor_scalar(o[1], a[1], ap(s1), ap(s2), op0, op1), o, [a, s1, s2], name)
 
     def cpv(o, a, name=""): return vop(lambda v: v.tensor_copy(o[1], a[1]), o, [a], name)
-    def scan(o, d0, a, op0, init, name): return vop(lambda v: v.tensor_tensor_scan(o[1], d0[1], a[1], init, op0, OP.max), o, [d0, a], name)
+    def scan(o, d0, a, op0, name, op1=OP.max): return vop(lambda v: v.tensor_tensor_scan(o[1], d0[1], a[1], 0.0, op0, op1), o, [d0, a], name)
     def fill(o, v, name="fill"): return vop(lambda q: q.memset(o[1], v), o, [], name)
-
-    def flex(o, a, name="", bias=None, scale=1.0, only=None):
-        opts = {e: (cost(e, o, [a]),) * 2 for e in (only or ASG.get(name, "VS"))}
-
-        def fn(Q, e):
-            if bias is None: return Q["V"].tensor_copy(o[1], a[1]) if e == "V" else Q["S"].activation(o[1], a[1], COPY)
-            if e == "V": return Q["V"].tensor_scalar(o[1], a[1], scale, ap(bias), OP.mult, OP.add)
-            return Q["S"].activation(o[1], a[1], IDENT if isinstance(bias, tuple) else COPY, bias=ap(bias), scale=ap(scale))
-        return add(G, opts, fn, [a, bias, scale], [o], name=name)
 
     def act(o, a, func, bias=0.0, scale=1.0, name=""):
         c = cost("S", o, [a])
-        return add(G, {"S": (c, c)}, lambda Q, e: Q["S"].activation(o[1], a[1], func, bias=ap(bias), scale=scale), [a, bias], [o], name=name)
+        return add(G, "S", c, c, lambda Q: [Q["S"].activation(o[1], a[1], func, bias=ap(bias), scale=ap(scale))], [a, bias, scale], [o], name=name)
 
-    def mm(o, l, rh, start=True, stop=True, name=""):
-        c = max(min(64, l[4]), rh[4]) * CYC * PF * (4.0 if l[5] == 4 else 1.0) + PO
-        return add(G, {"P": (c, c)}, lambda Q, e: Q["P"].matmul(o[1], l[1], rh[1], start, stop), [l, rh], [o], name=name)
+    def flex(o, a, name="", bias=None, scale=1.0, only=None):
+        fs = lambda Q: Q["S"].activation(o[1], a[1], IDENT if isinstance(bias, tuple) else COPY, bias=ap(bias or 0.0), scale=scale)
+        fv = lambda Q: Q["V"].tensor_copy(o[1], a[1]) if bias is None else Q["V"].tensor_scalar(o[1], a[1], scale, ap(bias), OP.mult, OP.add)
+        return either(o, [a, bias], fv, fs, name, only)
 
-    def grp(o, terms, name, start=True, stop=True):
-        for j, x in enumerate(terms): mm(o, x[0], x[1], start and j == 0, stop and j == len(terms) - 1, name)
+    def either(o, ins, fv, fs, name, only=None):
+        ways = {e: (e, cost(e, o, ins), lambda Q, f=f: [f(Q)]) for e, f in (("V", fv), ("S", fs))}
+        e = only or ASG.get(name, "V")
+        return add(G, e, ways[e][1], ways[e][1], ways[e][2], ins, [o], name=name, alt=ways["VS".replace(e, "")] if name not in FIXED else None)
+
+    def relu(o, a, bias, scale, name):
+        fv = (lambda Q: Q["V"].tensor_scalar(o[1], a[1], bias, 0.0, OP.add, OP.max)) if scale == 1.0 else (lambda Q: Q["V"].tensor_scalar(o[1], a[1], 0.5, None, OP.is_lt))
+        return either(o, [a], fv, lambda Q: Q["S"].activation(o[1], a[1], RELU, bias=bias, scale=scale), name)
+
+    def mms(calls, name):
+        for k in range(0, len(calls), OPT["MG"]):
+            cs = calls[k:k + OPT["MG"]]
+            c = sum(max(min(64, l[4]), rh[4]) * CYC * PF * (4.0 if l[5] == 4 else 1.0) + PO for o, l, rh, a, z in cs)
+            add(G, "P", c, c, lambda Q, cs=cs: [Q["P"].matmul(o[1], l[1], rh[1], a, z) for o, l, rh, a, z in cs], [x for y in cs for x in y[1:3]], [y[0] for y in cs], cnt=len(cs), name=name)
+
+    def mm(o, l, rh, start=True, stop=True, name=""): mms([(o, l, rh, start, stop)], name)
+    def grp(o, terms, name, start=True, stop=True): mms([(o, x[0], x[1], start and j == 0, stop and j == len(terms) - 1) for j, x in enumerate(terms)], name)
 
     def iota(o, pat, base, cm=0, name=""):
         c = 0.14 + 2 * o[4] * CYC
         flag = {} if o[0] == "pi" else {"allow_small_or_imprecise_dtypes": True}
-        return add(G, {"G": (c, c)}, lambda Q, e: Q["G"].iota(o[1], pat, base, cm, **flag), [], [o], name=name)
+        return add(G, "G", c, c, lambda Q: [Q["G"].iota(o[1], pat, base, cm, **flag)], [], [o], name=name)
 
     def gcopy(o, a, name):
         c = 0.17 + 2 * o[4] * CYC
-        return add(G, {"G": (c, c)}, lambda Q, e: Q["G"].affine_select(o[1], a[1], [[0, o[4]]], OP.is_ge, 0.0, 0, 0), [a], [o], name=name)
+        return add(G, "G", c, c, lambda Q: [Q["G"].affine_select(o[1], a[1], [[0, o[4]]], OP.is_ge, 0.0, 0, 0)], [a], [o], name=name)
 
-    def dma(o, a, kb, name, q="Y", rows=64):
+    def select(o, a, pat, base):
+        c = 0.17 + 2 * o[4] * CYC
+        return add(G, "G", c, c, lambda Q: [Q["G"].affine_select(o[1], a[1], pat, OP.is_ge, 0.0, base, 0)], [a], [o])
+
+    def dma(o, a, kb, name, q="Y", rows=64, **kw):
         k = "d%d" % nd[0]; nd[0] += 1
         c = kb / RATE + rows / 16 * ROW
-        return add(G, {q: (c if q == "Y" else 0.15, LAT + c)}, lambda Q, e: Q[e].dma_start(o[1], a[1]).then_inc(T.sem[k], 16), [a], [o], key=k, cnt=16, name=name)
+        return add(G, q, c if q == "Y" else 0.15, LAT + c, lambda Q: Q[q].dma_start(o[1], a[1], **kw).then_inc(T.sem[k], 16), [a], [o], key=k, cnt=16, name=name)
 
     def send(ds, src, land, sem, kb, name):
         dsts = [T.cores[(rank - d) % NR] for d in ds]
         for x in dsts: assert topo.may_write(core, x) and topo.mask(core, x) == topo.mask(core, dsts[0])
 
-        def fn(Q, e):
+        def fn(Q):
             if len(ds) == 1:
                 rid, pid = topo.addr(dsts[0])[:2]
                 Q["G"].remote_dma(out_ap=land(ds[0])[1], in_ap=src[1], remote_sem=T.sem[sem], local_sem=T.sem.loc, pid=pid, routing_id=rid, dma_engine_mask=topo.mask(core, dsts[0]))
             else:
                 ids = [DstId(rid=topo.addr(x)[0], pnc=topo.addr(x)[1]) for x in dsts]
                 Q["G"].remote_dma_fused([RemoteDMATransfer(dst_ids=ids, dma_engine_mask=topo.mask(core, dsts[0]), remote_sem=T.sem[sem], srcs=[src[1]], dsts=[land(d)[1] for d in ds])], local_sem=T.sem.loc)
-        s = add(G, {"G": (1.0, 1.0)}, fn, [src], [], key="loc", cnt=len(topo.engines(core, dsts[0])), name=name)
-        G["ops"][s]["link"] = kb * len(ds) / LINK[0]
-        i = add(G, {"N" + sem: (0.0, FAR + kb * len(ds) / LINK[0])}, None, [], [land(d) for d in ds], key=sem, cnt=sum(len(topo.engines(T.cores[(rank + d) % NR], core)) for d in ds), name="arrive")
+        s = add(G, "G", 1.0, 1.0, fn, [src], [], key="loc", cnt=len(topo.engines(core, dsts[0])), name=name)
+        G["ops"][s]["link"] = kb * len(ds) / LINK
+        i = add(G, "N" + sem, 0.0, FAR + kb * len(ds) / LINK, None, [], [land(d) for d in ds], key=sem, cnt=sum(len(topo.engines(T.cores[(rank + d) % NR], core)) for d in ds), name="arrive")
         G["ops"][i]["deps"][s] = True
         return s
 
-    def X(n): return R("CG", _, 0, slice(128 * TMP.index(n), 128 * TMP.index(n) + 128)) if n in TMP else R("CB", _, CBN.index(n)) if n in CBN else R("CH", _, CHN.index(n)) if n in CHN else R("CX", _, CXN.index(n))
     def sl(a, b=None, c=None): return slice(a, b, c)
 
+    def X(n, w=128):
+        if n in TMP: return R("ST", _, TMP.index(n) // 2, sl(128 * (TMP.index(n) % 2), 128 * (TMP.index(n) % 2) + w))
+        for buf, names in (("CB", CBN), ("CW", CWN), ("CH", CHN), ("CX", CXN)):
+            if n in names: return R(buf, _, names.index(n))
+
     half = list(enumerate((LO, UP)))
-    for x, pp in half: dma(R("CI", pp), R("ctl"), 98, "ld ctl", "YS"[x])
-    for x, pp in half: dma(R("XR", pp), R("sha", sl(x, 128, 16)), 49, "ld xr", "S")
+    col192 = lambda n, x: R(n, _, sl(192 * x, 192 * x + 192))
+    dma(R("CI"), R("ctl"), 98, "ld ctl", "Y", 128)
+    fill(R("SA"), 0.0)
     iota(R("pi"), [[1, 1]], 0, 1)
     cpv(R("ti", _, sl(0, 1)), R("pi"))
     for o, k, op in ((1, 4, OP.arith_shift_right), (2, 15, OP.bitwise_and), (3, 63, OP.bitwise_and)): ts(R("ti", _, sl(o, o + 1)), R("pi"), k, op)
     cpv(R("tf"), R("ti"))
     F = lambda k: R("tf", _, sl(k, k + 1))
     Wq = lambda k: R("wq", _, sl(k, k + 1))
-    ts(Wq(12), F(0), 64.0, OP.is_lt, 1 / 128, OP.mult)
-    ts(Wq(13), Wq(12), -65.0, OP.mult, 1 / 128, OP.add); ts(Wq(14), Wq(12), 85.5 * 128, OP.mult, -1.5, OP.add)
+    ts(R("C16"), R("CI"), -float(MID), OP.add, name="c16")
+    s2 = send(D_OF[:1], R("C16"), lambda d: R("L%d" % d), "ar0_0", 49, "send0")
+    send(D_OF[1:3], R("C16"), lambda d: R("L%d" % d), "ar0_1", 49, "send0b")
     ts(R("CHi"), R("CI"), 1 / 64, OP.mult, 168.0, OP.add, "dig")
-    ts(R("CA"), R("CI"), Wq(12), OP.mult, name="dig")
-    flex(R("PR"), R("CHi"), "dig", bias=Wq(14), scale=Wq(13), only="S")
-    tt(R("HL0"), R("CA"), R("PR"), OP.add, "dig")
-    s2 = send(D_OF[:1], R("HL0"), lambda d: R("L%d" % d), "ar0_0", 98, "send0")
-    send(D_OF[1:3], R("HL0"), lambda d: R("L%d" % d), "ar0_1", 98, "send0b")
-    tt(R("PR"), R("XR"), R("HL0"), OP.add, "PR")
+    ts(R("CF"), R("CI"), -float(MID), OP.add, name="dig")
+    flex(col192("CA", 0), R("CF"), "dig", bias=96.0, scale=1 / 128)
+    flex(col192("PR", 0), R("CHi"), "dig", bias=0.0, scale=-0.5)
+    flex(col192("H16", 1), R("CHi"), "dig", bias=-1.5, scale=1 / 128)
+    tt(col192("H16", 0), col192("CA", 0), col192("PR", 0), OP.add, "PR")
     dma(R("XX", _, sl(0, V_)), R("sha"), 786, "ld sha", "Y", 128)
-    for c in range(2):
-        cs = sl(MID * c, MID * c + MID)
-        for e in range(2): flex(R("P", _, sl(MID * c + 768 * e, MID * c + 768 * e + 768)), R("XX", _, sl(MID * c + 768 * e, MID * c + 768 * e + 768)), "P0", only="SV"[e])
-        flex(R("XX", _, sl(V_ + MID * c, V_ + MID * c + MID)), R("XX", _, cs), "negX", bias=0.0, scale=-1.0, only="V")
-    for x, pp in half: dma(R("P", sl(x, 128, 16)), R("PR", pp), 98, "ld rows")
+    for c in range(2): flex(R("XX", _, sl(V_ + MID * c, V_ + MID * c + MID)), R("XX", _, sl(MID * c, MID * c + MID)), "negX", bias=0.0, scale=-1.0, only="V")
     for h in ORD:
         cs = sl(MID * h, MID * h + MID)
         dma(R("OI", _, cs), R("hol", _, cs), 786, "ld hol%d" % h, "Y", 128)
         cpv(R("LA", _, h), R("OI", _, sl(MID * h, MID * h + MID, 12)), "LA")
-        for c in range(2): cpv(R("O", _, sl(MID * h + 768 * c, MID * h + 768 * c + 768)), R("OI", _, sl(MID * h + 768 * c, MID * h + 768 * c + 768)), "O32")
-    fill(R("O", _, sl(V_, V_ + 32)), 0.0)
+        for c in range(MID * h, MID * h + MID, 384): flex(R("O", _, sl(c, c + 384)), R("OI", _, sl(c, c + 384)), "O32", only="S")
+    fill(R("O", _, sl(V_, V_ + 48)), 0.0)
     for d in (1, 2, 3):
-        if d == D_OF[0]: fill(R("WC%d" % d), 0.0)
-        else: G["ops"][iota(R("WC%d" % d), [[0, V_]], 0, name="zero")]["deps"][s2] = False
-        for x, pp in half: dma(R("WC%d" % d, sl(x, 128, 16)), R("L%d" % d, pp), 49, "ld flat" if d == D_OF[0] else "flat")
-    for n, pat, base in (("ci", [[1, 128]], 0), ("cg", [[1, 8], [0, 16]], 0), ("cq", [[0, 8], [1, 16]], 0), ("c64", [[0, 2], [1, 64]], 0), ("cd", [[8, 2], [16, 4], [0, 16]], 0)): iota(X(n), pat, base)
-    late = [iota(X(n), pat, base) for n, pat, base in (("K1", [[0, 8], [-1, 16]], 15), ("ONE", [[0, 128]], 1), ("KH", [[0, 128]], MID + int(BIG)), ("KL", [[0, 128]], MID - int(BIG)),
-                                                        ("c32", [[0, 4], [1, 32]], 0), ("cw0", [[2, 4], [0, 32]], 0), ("cw1", [[2, 4], [0, 32]], 1))]
-    late.append(iota(R("c8p"), [[1, 2], [2, 4]], 0))
-    late += [iota(R("pk"), [[-1, 8]], 0, 1), iota(R("c8"), [[1, 4], [4, 2]], 0), iota(R("VC"), [[1, 4], [MID, 2]], -MID, 12), iota(R("VR"), [[1, 4], [12, 256]], 0), iota(R("SB"), [[0, 288]], 0), iota(R("VB"), [[-1, 4], [-MID, 2], [-192, 8]], 0)]
+        if d == D_OF[0]:
+            for c in range(3): flex(R("WC%d" % d, _, sl(1024 * c, 1024 * c + 1024)), R("SA", _, _, sl(0, 256)), "fillW", only="S")
+        else:
+            for c in range(4): G["ops"][iota(R("WC%d" % d, _, sl(768 * c, 768 * c + 768)), [[0, 768]], 0, name="zero")]["deps"][s2] = False
+        flex(R("F%d" % d), R("L%d" % d), "wide1" if d == D_OF[0] else "wide")
+        dma(R("WC%d" % d, sl(2, 128, 16)), R("F%d" % d), 98, "flat1" if d == D_OF[0] else "flat", "S" if d == D_OF[0] else "Y", 128)
+    for n, pat, base in (("ci", [[1, 128]], 0), ("cg", [[1, 8], [0, 16]], 0), ("cq", [[0, 8], [1, 16]], 0)): iota(X(n), pat, base)
+    late = [iota(X(n), pat, base, name="late") for n, pat, base in (("ONE", [[0, 128]], 1), ("KH", [[0, 128]], MID + int(1.5 * BIG)), ("KL", [[0, 128]], MID - int(1.5 * BIG)))]
+    late += [iota(R("SB"), [[0, 288]], 0, name="late"), iota(R("MT"), [[0, 192]], MID, name="late"), iota(R("VB"), [[-1, 4], [-MID, 2], [-192, 8]], 0, name="late")]
+    late += [iota(X(n), pat, base, name="next") for n, pat, base in (("K1", [[0, 8], [-1, 16]], 15), ("cw0", [[2, 4], [0, 32]], 0), ("cw1", [[2, 4], [0, 32]], 1))]
+    late += [iota(X("x0", 256), [[0, 4], [-16, 2], [1, 32]], 0, name="next"), iota(X("x2", 256), [[32, 4], [0, 2], [1, 32]], 0, name="next")]
+    late += [iota(R("pk", _, sl(0, 4)), [[2, 4]], -15, name="next"), iota(R("VC"), [[1, 4], [MID, 2]], -MID, 12, name="next"), iota(R("E1"), [[0, 4], [-16, 2], [0, 34]], int(TOP) - V_ - 1, name="next")]
     for i in late: G["ops"][i]["deps"][s2] = False
-    fill(R("SA"), 0.0); fill(R("Zt"), 0.0)
-    c8 = R("CG", _, 0, sl(0, 8))
+    fill(R("Zt"), 1.0)
+    if any(OPT["WV"]):
+        G["ops"][iota(R("N16"), [[0, 1024]], 1, name="zero")]["deps"][s2] = False
+        fill(R("N16", _, sl(0, None, 16)), 0.0, "zero")
+    c8 = X("ci", 8)
     ts(X("Ib"), X("ci"), F(0), OP.is_equal)
-    for n, s in (("I128", 128), ("I8192", 8192), ("IB", BIG), ("ImB", -BIG), ("Im3072", -V_), ("Id128", 1 / 128), ("Imh2", -0.5), ("Ih", 1), ("Imh", -1), ("Im128", -128), ("Im8192", -8192), ("Ih128", 1 / 128), ("I32h", 32), ("Im16h", -16)):
+    for n, s in (("I128", 128), ("I8192", 8192), ("IB", BIG), ("ImB", -BIG), ("IB2", BIG / 2), ("ImB2", -BIG / 2), ("Imb", -1), ("Im3072", -V_), ("Id128", 1 / 128), ("Imh2", -0.5), ("Ih", 1), ("Imh", -1),
+                 ("Im128", -128), ("Im8192", -8192), ("Ih128", 1 / 128), ("I32h", 32), ("Im16h", -16), ("I16h", 16)):
         flex(X(n), X("Ib"), bias=0.0, scale=float(s))
-    ts(X("BOb"), X("cg"), F(1), OP.is_equal)
-    for n, s in (("BOh", 1.0), ("BOm", -1.0)): flex(X(n), X("BOb"), bias=0.0, scale=s)
+    pick = lambda j, a, z: R("MN", _, j // 8, sl(130 * (j % 8) + a, 130 * (j % 8) + z))
+    iota(X("x6", 144), [[16, 9], [1000, 16]], -16)
+    for j in range(16): ts(pick(j, 0, 129), R("ST", _, 7, sl(15, 144)), float(j), OP.add, F(0), OP.is_equal, "pick")
+    for c in range(8):
+        n = "p%s%d" % ("ACBD"[c // 2], c % 2); cs = sl(384 * c, 384 * c + 384)
+        b = lambda a, z: R(n, _, sl(a // 64, z // 64)) if n[1] == "D" else R(n, _, sl(a, z))
+        digits = [(b(192 * e, 192 * e + 192), pick(2 * c + e, 1 - x, 129 - x), col192("H16", x), False, c >= 4 and e + x == 2) for e in range(2) for x in range(2)]
+        if c < 4: mms([(b(0, 384), R("SA", _, 0, sl(0, 128)), R("H16"), True, False)] + digits[:3], "P0d"); mms(digits[3:], "P0d")
+        mm(b(0, 384), X("Ib"), R("XX", _, cs), c >= 4, c < 4, "P0p")
+        if c >= 4: mms(digits, "P0d")
+        flex(R("P", _, cs), b(0, 384), "P0", only="SV"[c % 2])
+    BOb = R("CW", _, 0, sl(0, 128))
+    for e in range(2): ts(R("CW", _, 0, sl(128 * e, 128 * e + 128)), X("cg"), F(1), OP.is_equal)
+    for n, s in (("BOh", 1.0), ("BOm", -1.0)): flex(X(n), BOb, bias=0.0, scale=s)
     ts(X("QB"), X("cq"), F(2), OP.is_equal, BIG, OP.mult)
-    ts(Wq(10), F(2), float(V_ + 16), OP.add); ts(Wq(11), F(2), 16.0, OP.add)
-    for e in range(2):
-        ts(X("TR%d" % e), X("c32"), (F(2), Wq(11))[e], OP.is_ge, BIG, OP.mult)
-        ts(X("ME%d" % e), X("cw%d" % e), F(1), OP.is_equal, -1.0, OP.mult)
-        ts(R("N32", _, sl(128 * e, 128 * e + 128)), X("c32"), 0.0, OP.not_equal)
-    ts(R("S1p"), R("c8p"), F(1), OP.is_equal)
+    ts(X("QN"), X("cq"), F(2), OP.not_equal, BIG, OP.mult)
+    for e in range(2): ts(X("ME%d" % e), X("cw%d" % e), F(1), OP.is_equal, -1.0, OP.mult)
+    x0, x2, x4 = X("x0", 256), X("x2", 256), X("x4", 256)
+    ts(X("WA"), x2, F(0), OP.is_equal, BIG / 2, OP.mult)
+    ts(x4, x0, 0.0, OP.is_ge, -2.0, OP.mult); ts(x2, x0, 16.0, OP.is_ge, 2.0, OP.mult); tt(x4, x4, x2, OP.add)
+    tt(X("WQ"), X("WA"), x4, OP.mult)
+    ts(x2, x0, F(2), OP.is_ge, 2.0, OP.mult); tt(x4, x4, x2, OP.add); ts(R("TR", _, _, sl(2, 34)), x4, BIG / 2, OP.mult, BIG / 2 - 30 * MID, OP.add)
+    fill(R("TR", _, _, sl(0, 2)), (TOP - 16 * MID) / 4096)
+    ts(R("E1"), R("E1"), F(2), OP.subtract); fill(R("E1", _, sl(0, None, 34)), 8192.0)
+    ts(R("S1n"), c8, F(1), OP.is_equal, -1 / 4096, OP.mult)
+    ts(R("VC"), R("VC"), 0.5, OP.mult)
     ts(X("NF"), X("cq"), 0.0, OP.not_equal)
     ts(X("NFa"), X("cq"), 0.0, OP.is_equal, -2.0 ** 30, OP.mult)
-    ts(Wq(0), F(2), 0.0, OP.is_equal); ts(Wq(1), F(2), 1.0, OP.is_equal)
-    ts(Wq(2), Wq(1), 64.0, OP.mult, Wq(0), OP.add); ts(Wq(2), Wq(2), 128.0, OP.mult)
+    ts(Wq(0), F(2), 0.0, OP.is_equal); ts(Wq(1), F(2), 1.0, OP.is_equal); ts(Wq(2), F(2), 2.0, OP.is_equal)
     ts(Wq(3), Wq(1), -1 / 64, OP.mult, Wq(0), OP.add); ts(Wq(3), Wq(3), 96.0, OP.mult)
     ts(Wq(4), F(0), 64.0, OP.is_lt, 4095.0, OP.mult); ts(Wq(4), Wq(4), 1.0, OP.add)
-    ts(Wq(5), F(2), float(V_), OP.add)
+    ts(Wq(10), F(0), 1.0, OP.is_equal); ts(Wq(11), F(0), 0.0, OP.is_equal)
     for n in ("S1h", "S1b", "U8"): ts(R(n), c8, F(1), OP.is_equal)
     ts(R("Rc"), c8, F(1), OP.is_equal, Wq(2), OP.mult)
     for j, w in ((0, Wq(0)), (1, Wq(1)), (2, 1.0)): ts(R("Rd", _, j), c8, F(1), OP.is_equal, w, OP.mult)
-    ts(R("R16"), R("c8"), F(1), OP.is_equal, 16.0, OP.mult)
-    ts(X("A1"), X("c64"), F(3), OP.is_equal, Wq(4), OP.mult)
-    for k in range(8):
-        ts(R("WD", _, k), X("cd"), R("pk", _, sl(k, k + 1)), OP.is_equal, 4096.0, OP.mult)
-        tt(R("WD", _, k), X("A1"), R("WD", _, k), OP.subtract)
-    flex(R("VRh"), R("VR"), bias=-float(MID))
-    cpv(R("CA", LO), R("CI", LO))
-    dma(R("YC", sl(0, 8)), R("CA", LO), 98, "yc0")
+    y = lambda k: R("ST", _, sl(8 + 2 * k, 10 + 2 * k))
+    iota(y(0), [[0, 8], [-1, 64]], 0, 1); iota(y(1), [[1, 8], [0, 64]], 1); iota(y(2), [[1, 8], [0, 64]], -15)
+    select(y(1), y(1), [[-1, 8], [0, 4], [-1, 16]], 14)
+    select(y(2), y(2), [[1, 8], [0, 4], [1, 16]], -15)
+    tt(y(2), y(0), y(2), OP.is_equal)
+    ts(y(0), y(0), F(0), OP.subtract, F(3), OP.add)
+    tt(y(1), y(0), y(1), OP.is_equal)
+    ts(R("WD"), y(1), Wq(4), OP.mult); ts(y(3), y(2), -4096.0, OP.mult); tt(R("WD"), R("WD"), y(3), OP.add)
+    pk = R("pk", _, sl(0, 4)); pw = R("pk", _, sl(4, 8))
+    ts(Wq(7), F(0), 64.0, OP.is_ge); ts(pk, pk, Wq(7), OP.add)
+    ts(pw, pk, F(2), OP.add, 0.0, OP.is_ge); tt(pk, pk, pw, OP.mult)
+    ts(Wq(9), R("pk", _, sl(3, 4)), -8.0, OP.is_equal, -99.0, OP.mult); ts(R("pk", _, sl(3, 4)), R("pk", _, sl(3, 4)), Wq(9), OP.add)
+    ts(pk, pk, F(3), OP.add)
+    for i in range(4): ts(R("R16", _, i), X("ci", 64), R("pk", _, sl(i, i + 1)), OP.is_equal, 16.0, OP.mult)
+    ts(X("KK"), X("cq"), 16.0 * MID, OP.mult, Wq(10), OP.mult); ts(X("cw2"), X("K1"), Wq(11), OP.mult); tt(X("KK"), X("KK"), X("cw2"), OP.add)
+    dma(R("WC0", sl(2, 128, 16)), R("CF"), 98, "flat", "Y", 128)
+    y0 = dma(R("yc"), R("MT"), 98, "yc0", "Y", 128)
 
     def firms(t):
-        for c in range(7, -1, -1):
-            if 2 * (c % 4) >= STS[c // 4]: iota(R("VT", _, t % 2, sl(512 * c, 512 * c + 512)), [[12, 32], [0, 16]], t + 384 * c, name="VT")
+        iota(R("VR", _, t), [[12, 256]], t, name="VR")
+        flex(R("VRh", _, t), R("VR", _, t), "VRh", bias=-float(MID), only="S")
+        for h in ORD:
+            at = 0
+            for n, q in CUT["ST", h]:
+                if q == "V":
+                    for c in range(at, at + n, 32): iota(R("VT", _, t % 2, sl(2048 * h + 16 * c, 2048 * h + 16 * c + 512)), [[12, 32], [0, 16]], t + MID * h + 12 * c, name="VT")
+                at += n
 
     def front(t, h):
-        B = lambda n, *ix: R(SAME_AS.get(n, n), _, h, *ix)
-        bank = lambda n: (lambda *ix: R("p%s%d" % (n, h), _, *ix))
-        A, Bk, C, D = bank("A"), bank("B"), bank("C"), bank("D")
+        B = lambda n, *ix: R(n, _, sl(2048 * h + ix[0].start, 2048 * h + (ix[0].stop or 2048), ix[0].step)) if n == "CG" else R(SAME_AS.get(n, n), _, h, *ix)
+        def bank(n, h=h):
+            def at(p=sl(0, 4), c=sl(0, None), pp=_):
+                a, z = (p, p + 1) if isinstance(p, int) else (p.start or 0, p.stop or 4)
+                return R("p%s%d" % (n, h), pp, sl(128 * a + c.start, 128 * a + c.stop if c.stop else 128 * z, c.step))
+            return at
+        A, Bk, C, D4 = bank("A"), bank("B"), bank("C"), lambda *ix: R("pD%d" % h, _, *ix)
+        D = lambda p, *ix: D4(sl(2 * p, 2 * p + 2), *ix)
         col = lambda b, s, k: b(s, sl(k, None, 16))
-        rows = lambda n, k, m=16: B(n, sl(k, None, m))
+        rows = lambda n, k, m=16: R(n, _, sl(8 * h, 8 * h + 8), sl(k, None, m)) if n == "ST" else B(n, sl(k, None, m))
         O, P, XX, WC = "O", "P", "XX", "WC%d" % D_OF[t]
         hs = sl(MID * h + t, MID * h + MID, 12); ls = sl(128 * h, 128 * h + 128)
-        n = 128 // NPG
-        pcs = [(sl(16 * c, 16 * (c + n)), sl(c, c + n)) for c in range(0, 128, n)]
         Xw, Ow = R(XX, _, sl(0, V_)), R(O)
+
+        def pieces(n):
+            at = 0
+            for m, q in CUT[n, h]:
+                yield sl(16 * at, 16 * (at + m)), sl(at, at + m), q
+                at += m
+
+        def sums(b, p, n, w, name, m=16): mms([(col(b, p, k), rows(n, k), w, True, True) for k in sorted(range(16), key=lambda k: k % m)], name)
+
+        def stakes(b, p):
+            for a, c, q in pieces("ST"):
+                if q == "V": tt(B("SV", a), ind(Ow if t else R("OI"), B("LA", c)), R("VT", _, t % 2, sl(2048 * h + a.start, 2048 * h + a.stop)), OP.is_equal, "ST")
+                else:
+                    for u in range(c.start // 16, c.stop // 16): act(R("ST", _, 8 * h + u), ind(Ow, B("LA", sl(16 * u, 16 * u + 16))), IDENT, bias=R("VB", _, sl(16 * t + 8 * h + u, 16 * t + 8 * h + u + 1)), name="OB")
+                    for j in range(16):
+                        x = R("ST", _, sl(8 * h + c.start // 16, 8 * h + c.stop // 16), sl(16 * j, 16 * j + 16))
+                        ts(x, x, 12.0 * j, OP.is_equal, name="SQ")
+            sums(b, p, "ST" if q == "S" else "SV", R("S1b"), "SL")
+            relu(B("nst"), b(p), 1.0, -1.0, "nst")
         if t: cpv(B("LA"), R(O, _, hs), "LA")
-        on = lambda x, j: "V" if (x, h, j) in ONV else "S"
-        for j, (a, b) in enumerate(pcs): flex(B("XK", a), ind(R(P), B("LA", b)), "XK", only=on("XK", j))
-        for k in range(16): mm(col(A, sl(0, 3), k), rows("XK", k), R("Rd"), name="dec")
+        for a, b, q in pieces("XK"): flex(B("XK", a), ind(R(P), B("LA", b)), "XK", only=q)
+        sums(A, sl(0, 3), "XK", R("Rd"), "dec")
         flex(B("KS", sl(0, 2)), A(sl(0, 2)), "Y2")
-        flex(B("R3"), A(sl(0, 3)), "R3", bias=float(MID))
+        if OPT["R3"]:
+            flex(B("R3", sl(0, 2)), A(sl(0, 2)), "R3", bias=float(MID))
+            flex(B("R3", 2), A(2), "RS", bias=float(MID))
+        else: flex(B("R3"), A(sl(0, 3)), "R3", bias=float(MID))
         grp(C(0), [(B("KS", 0), X("I128")), (B("KS", 1), X("I8192")), (B("R3", 0), X("Im128")), (B("R3", 1), X("Im8192"))], "uT")
         ts(B("LC"), C(0), MID * 8321.0, OP.add, name="LC")
-        for j, (a, b) in enumerate(pcs): flex(B("CG", a), ind(R(WC), B("LC", b)), "CG", only=on("CG", j))
-        flex(B("aN"), R(O, _, hs), "aN", bias=-float(MID))
-        for j in range(4): mm(Bk(_, sl(j, None, 4)), X("Ib"), R(XX, _, hs), name="XV")
+        if t and h == ORD[0]:
+            w = bank("C", ORD[1])
+            for e in ORD: mm(w(2 + e), R("LD", _, LAND.index((t - 1, D_OF[t])), sl(128 * e, 128 * e + 128)), X("Ih"), name="WCp")
+            flex(R(WC, _, sl(t - 1, V_, 12)), w(sl(2, 4)), "WCu")
+        for a, b, q in pieces("CG"): flex(B("CG", a), ind(R(WC), B("LC", b)), "CG", only=q)
+        if t: flex(B("aN"), R(O, _, hs), "aN", bias=-float(MID))
+        else: ts(B("aN"), R("OI", _, hs), -float(MID), OP.add, name="aN")
+        mms([(Bk(_, sl(j, None, 4)), X("Ib"), R(XX, _, hs), True, True) for j in range(4)], "XV")
         for k in range(4): tt(rows("MN", k, 4), rows("XK", k, 4), Bk(), OP.min, "MN")
-        for k in sorted(range(16), key=lambda k: k % 4): mm(col(D, 1, k), rows("MN", k), R("S1h"), name="mL")
+        sums(D, 1, "MN", R("S1h"), "mL", 4)
         flex(B("S2", _, 1), D(1), "mS", bias=float(MID))
-        for k in range(16): mm(col(C, 1, k), rows("CG", k), R("Rc"), name="cL")
+        if OPT["SL"][h] == "E": stakes(D, 2)
+        sums(C, 1, "CG", R("Rc"), "cL")
         flex(B("S2", _, 0), C(1), "cS")
-        for a, pp in half: mm(R("pA%d" % h, pp, 0), B("S2", a, 0), X("Ih"), name="TK")
-        for a in range(2): mm(A(1 + a), B("S2", a), X("Ih"), name="TK")
-        flex(B("KS"), A(sl(0, 3)), "KS")
+        if OPT["KS"]:
+            mms([(A(1 + a), B("S2", a), X("Ih"), True, True) for a in range(2)], "TK")
+            flex(B("KS", sl(1, 3)), A(sl(1, 3)), "KS")
+            mms([(A(0, pp=pp), B("S2", a, 0), X("Ih"), True, True) for a, pp in half], "TC")
+            flex(B("KS", 0), A(0), "cK")
+        else:
+            mms([(A(1 + a), B("S2", a), X("Ih"), True, True) for a in range(2)] + [(A(0, pp=pp), B("S2", a, 0), X("Ih"), True, True) for a, pp in half], "TK")
+            flex(B("KS"), A(sl(0, 3)), "KS")
+        if OPT["SL"][h] == "A": stakes(A, 3)
         cK = B("KS", 0)
-        key = D(0)
-        mm(key, X("Ib"), X("K1"), True, False, "K1")
-        for i in range(4):
-            b = (Bk, C)[i % 2]
-            for e in range(2): mm(b(sl(2 * e, 2 * e + 2)), R("WD", _, 2 * i + e), B("KS", sl(1, 3)), name="D")
+        key = C(0)
+        grp(key, [(X("ONE"), X("KK")), (X("I16h"), B("S2", _, 1))], "K1", True, False)
+        for i in range(2):
+            b = (Bk, lambda *ix: D4(sl(2 * ix[0].start, 2 * ix[0].stop)) if ix else D4())[i]
+            mms([(b(sl(2 * e, 2 * e + 2)), R("WD", _, 2 * i + e), B("KS", sl(1, 3)), True, True) for e in range(2)], "D")
             ts(B("WL", sl(2 * i, 2 * i + 2)), b(), float(MID), OP.max, MID + 4096.0, OP.min, "clip")
-            for e in range(2):
-                for a in range(2): mm(D(0, sl(64 * a + 2 * i + e, 64 * a + 64, 8)), B("WL", 2 * i + e, a), R("R16"), False, i + e + a == 5, "pool")
+            mms([(C(0, sl(64 * a, 64 * a + 64)), B("WL", 2 * i + e, a), R("R16", _, 2 * i + e), False, i + e + a == 3) for e in range(2) for a in range(2)], "pool")
         flex(B("hi"), key, "hi", bias=2.0 ** 23 - 32767)
-        tt(key, key, B("hi"), OP.subtract, "hi-")
-        scan(B("F"), X("NFa"), key, OP.add, 0.0, "F")
-        scan(B("TT", sl(None, None, -1)), X("NFa"), B("F", sl(None, None, -1)), OP.add, 0.0, "T")
+        if OPT["HIP"]: mm(key, X("Imb"), B("hi"), False, True, "hi-")
+        else: tt(key, key, B("hi"), OP.subtract, "hi-")
+        scan(B("F"), X("NFa"), key, OP.add, "F")
+        scan(B("TT", sl(None, None, -1)), X("NFa"), B("F", sl(None, None, -1)), OP.add, "T")
         tt(B("oh"), B("TT"), key, OP.is_equal, "oh")
         mm(A(0), B("oh"), X("Ib"), name="ohT")
         tt(B("wN"), cK, A(0), OP.mult, "wN")
@@ -500,88 +857,90 @@ def build(core, T, topo, rank):
         tt(B("mine"), cK, A(1), OP.is_equal, "mine")
         grp(A(2), [(X("Ih"), B("aN")), (X("Im3072"), B("mine"))], "LMp")
         ts(B("LM"), A(2), float(MID + V_), OP.add, name="LM")
-        for j, (a, b) in enumerate(pcs): flex(B("CG", a), ind(R(XX), B("LM", b)), "XM", only=on("XM", j))
-        act(B("BD"), Bk(0), RELU, bias=MID + 1 - BIG, name="BD")
+        for a, b, q in pieces("XM"): flex(B("CG", a), ind(R(XX), B("LM", b)), "XM", only=q)
+        relu(B("BD"), Bk(0), MID + 1 - BIG, 1.0, "BD")
         mm(Bk(1, sl(0, 8)), B("BD"), R("U8"), name="LBp")
         ts(B("LB"), Bk(1, sl(0, 8)), -1.0, OP.add, name="LB")
         flex(B("XB"), ind(Xw, B("LB")), "XB")
-        mm(C(0, sl(0, 8)), B("wN"), R("S1h"), name="b8")
-        flex(B("B8"), C(0, sl(0, 8)), "bm")
-        flex(B("BV"), C(0, sl(0, 8)), "bm", bias=R("VC", _, sl(2 * t + h, 2 * t + h + 1)), scale=-1.0)
-        for j in range(4): mm(Bk(_, sl(j, None, 4)), X("Ib"), B("XB"), name="XBp")
+        mm(C(1, sl(0, 8)), B("wN"), R("S1h"), name="b8")
+        vc = R("VC", _, sl(2 * t + h, 2 * t + h + 1))
+        flex(B("B8"), C(1, sl(0, 8)), "bm", bias=vc, scale=0.5)
+        flex(B("BV"), C(1, sl(0, 8)), "bm", bias=vc, scale=-0.5)
+        mms([(Bk(_, sl(j, None, 4)), X("Ib"), B("XB"), True, True) for j in range(4)], "XBp")
         for k in range(4): tt(rows("MN", k, 4), rows("XK", k, 4), Bk(), OP.max, "MX")
-        ns = STS[h]
-        for u in range(ns): act(B("ST", u), ind(Ow, B("LA", sl(16 * u, 16 * u + 16))), IDENT, bias=R("VB", _, sl(16 * t + 8 * h + u, 16 * t + 8 * h + u + 1)), name="OB")
-        for q in range(16 if ns else 0): ts(B("ST", sl(0, ns), sl(16 * q, 16 * q + 16)), B("ST", sl(0, ns), sl(16 * q, 16 * q + 16)), 12.0 * q, OP.is_equal, name="SQ")
-        for u in range(ns, 8): tt(B("ST", u), ind(Ow, B("LA", sl(16 * u, 16 * u + 16))), R("VT", _, t % 2, sl(2048 * h + 256 * u, 2048 * h + 256 * u + 256)), OP.is_equal, "ST")
-        for k in range(16): mm(col(C, 1, k), B("ST", _, sl(k, None, 16)), R("S1b"), name="SL")
-        act(B("nst"), C(1), RELU, bias=1.0, scale=-1.0, name="nst")
-        for k in sorted(range(16), key=lambda k: k % 4): mm(col(C, 2, k), rows("MN", k), R("S1h"), name="FL")
-        flex(B("FR"), C(2), "FR", bias=float(MID))
+        if OPT["SL"][h] == "D": stakes(D, 1)
+        sums(D, 2, "MN", R("S1h"), "FL", 4)
+        flex(B("FR"), D(2), "FR", bias=float(MID))
         grp(key, [(X("Ib"), X("K1")), (X("Im16h"), B("R3", 2)), (B("mine"), X("ImB")), (X("ImB"), B("nst")), (X("I32h"), B("FR"))], "K2")
-        for c in range(NPW):
-            for k in range(16): mm(A(3, sl(128 // NPW * c, 128 // NPW * (c + 1))), X("Ib"), B("CG", sl(2048 // NPW * c + k, 2048 // NPW * (c + 1), 16)), k == 0, k == 15, "WS")
-        act(B("wp"), A(3), SIGN, bias=-0.5, name="wp")
-        mm(A(0), B("wp"), X("BOb"), name="WN")
-        ts(B("nw"), A(0), R("Zt"), OP.is_le, name="nw")
-        tt(B("t8"), rows("nw", 0), B("BV"), OP.mult, "t8")
-        tt(rows("SA", 0), B("t8"), B("B8"), OP.add, "n8")
+        scan(B("F"), X("NF"), key, OP.mult, "F2")
+        scan(B("TT", sl(None, None, -1)), X("NF"), B("F", sl(None, None, -1)), OP.mult, "T2")
+        tt(B("oh2"), B("TT"), key, OP.is_equal, "oh2")
+        grp(Bk(3), [(X("Imh"), B("aN")), (B("oh2"), X("IB"))], "pzp")
+        ts(B("pz"), Bk(3), -BIG, OP.add, -float(MID), OP.max, "pz")
+        grp(Bk(3), [(X("Ib"), X("QB")), (B("pz"), X("BOm"))], "ZQp")
+        ts(B("ZQ"), Bk(3), V_ - 17.0 * MID - BIG, OP.add, -float(MID), OP.max, "ZQ")
+        run = lambda e: D4(sl(e, 8, 2), sl(2, 34))
+        mm(D4(_, sl(0, 34)), X("Ib"), R("TR"), True, False, "TRp")
+        mms([(run(e), X("BOm"), B("pz"), False, False) for e in range(2)], "DSp")
+        mms([(run(e), B("ZQ"), X("ME%d" % e), False, False) for e in range(2)] + [(D4(_, 1), B("ZQ"), R("S1n"), False, False)], "DSq")
+        mms([(Bk(1, sl(0, 8)), B("ZQ"), R("S1h"), True, True), (Bk(0), B("oh2"), X("Ib"), True, True)], "ZLp")
+        ts(B("ZL"), Bk(1, sl(0, 8)), 16.0 * MID, OP.add, name="ZL")
+        tt(B("pc"), cK, Bk(0), OP.mult, "pc")
+        grp(Bk(2), [(X("Imh"), R("VRh", _, t, ls)), (X("BOh"), B("pc"))], "csv")
+        flex(B("OC"), ind(Ow, B("ZL")), "OC")
+        tt(B("OE"), ind(Ow, B("ZL")), R("VR", _, t, ls), OP.is_equal, "OE")
+        tt(B("OE"), B("OE"), Bk(2), OP.mult, "NN")
+        if OPT["WV"][h]:
+            for a, b, q in pieces("XM"): scan(B("SV", a), R("N16", _, sl(0, a.stop - a.start)), B("CG", a), OP.mult, "WV", OP.add)
+            act(B("wp"), rows("SV", 15), SIGN, bias=-0.5, name="wp")
+        else:
+            mms([(A(3), X("Ih"), rows("CG", k), k == 0, k == 15) for k in range(16)], "WS")
+            act(B("wp"), A(3), SIGN, bias=-0.5, name="wp")
+        mms([(A(sl(0, 2)), B("wp"), X("BO2"), True, False), (A(1), X("Ib"), X("QN"), False, True)], "WN")
+        act(B("nw"), A(sl(0, 2)), SIGN, bias=R("Zt"), scale=-1.0, name="nw")
+        nw, nq = B("nw", sl(0, 128)), B("nw", sl(128, 256))
+        grp(D4(_, sl(2, 34)), [(nw, X("WA")), (nq, X("WQ"))], "DSw", False)
+        act(B("E0"), D4(_, sl(0, 34)), ABS, scale=4096.0, name="DS")
+        scan(B("E2"), B("E0"), R("E1"), OP.min, "DM")
+        ts(B("FZ"), B("E2", sl(33, None, 34)), -1.0, OP.mult, TOP, OP.add, "FZ")
+        SA = lambda at, step=None: R("SA", _, t, sl(128 * h + at, 128 * h + at + 128, step))
+        tt(B("t8"), B("nw", sl(0, 128, 16)), B("BV"), OP.mult, "t8")
+        tt(SA(2, 16), B("t8"), B("B8"), OP.add, "n8")
+        own = R("WC0", _, hs)
         if t < RO - 1:
-            flex(B("SB", sl(1, 129, 16)), rows("SA", 0), "H8", bias=192.0, scale=1 / 64)
-            grp(C(0), [(B("SA"), X("Ih128")), (B("SB", sl(0, 128)), X("Id128")), (B("SB", sl(1, 129)), X("Imh2"))], "DG")
-            PL = R("PL", _, t, ls)
-            flex(PL, C(0), "PL", bias=Wq(3))
             ds = D_OF[t + 1:]
-            send(ds[:1], PL, lambda d: R("LD", _, LAND.index((t, d)), ls), "ar%d_%d" % (t + 1, 2 * h), 32, "send")
+            send(ds[:1], SA(0), lambda d: R("LD", _, LAND.index((t, d)), ls), "ar%d_%d" % (t + 1, 2 * h), 32, "send")
+            flex(B("SB", sl(1, 129, 16)), SA(2, 16), "H8", bias=192.0, scale=1 / 64)
+            grp(A(3), [(X("Ib"), R(XX, _, hs)), (SA(2), X("Ih128")), (B("SB", sl(0, 128)), X("Id128")), (B("SB", sl(1, 129)), X("Imh2"))], "Pp")
+            later.append((None, lambda: flex(R(P, _, hs), A(3), "Pu", bias=Wq(3))))
+            mm(C(2), SA(0), X("Ih"), name="DG")
+            flex(R("PL", _, t, ls), C(2), "PL")
             if h == ORD[1]:
                 land = lambda d: R("LD", _, LAND.index((t, d)))
                 if ds[1:]: send(ds[1:], R("PL", _, t), land, "ar%d_1" % (t + 1), 64, "sendb")
-                later.extend((d, land(d)) for d in ds)
-            grp(C(1), [(X("Ib"), R(XX, _, hs)), (X("Ib"), PL)], "Pp")
-            later.append((None, lambda: flex(R(P, _, hs), C(1), "Pu")))
-        y = R("pC%d" % h, sl(0, 8), 2)
-        mm(y, rows("SA", 0), X("Ih"), name="YCp")
-        flex(R("YC", sl(0, 8), hs), y, "YC", bias=float(MID))
+                later.extend((d, land(d)) for d in ds[1:])
+                later.append((0, R("PL", _, t)))
+        else:
+            mm(A(2), SA(0), X("Ih"), name="DG")
+            flex(own, A(2), "YC")
         if t < RO - 1 and h == ORD[1]:
             z = C(3, sl(0, 8))
-            grp(z, [(X("ONE"), R("nw", _, e, sl(0, None, 16))) for e in ORD], "ZC")
-            add(G, {"S": (0.1, 0.1)}, lambda Q, e: Q["S"].activation(T.zr[:, 0:8], z[1], COPY, accum_out=T.zr[:, 8:9]), [z], [R("zr")], name="zr")
+            grp(z, [(X("ONE"), R("nw", _, e, sl(0, 128, 16))) for e in ORD], "ZC")
+            add(G, "S", 0.1, 0.1, lambda Q: [Q["S"].activation(T.zr[:, 0:8], z[1], COPY, bias=256.0, accum_out=T.zr[:, 8:9])], [z], [R("zr")], name="zr")
             cpv(R("zi", _, sl(0, 1)), R("zr", _, sl(8, 9)), "Z")
-            ts(R("zi", _, sl(1, 2)), R("zi", _, sl(0, 1)), 1, OP.bitwise_and, name="Z")
-            ts(R("Zt"), R("zi", _, sl(1, 2)), 2.0, OP.mult, name="Z")
-        scan(B("F"), X("NF"), key, OP.mult, 0.0, "F2")
-        scan(B("TT", sl(None, None, -1)), X("NF"), B("F", sl(None, None, -1)), OP.mult, 0.0, "T2")
-        tt(B("oh2"), B("TT"), key, OP.is_equal, "oh2")
-        grp(A(1), [(X("Imh"), B("aN")), (B("nw"), X("ImB")), (B("oh2"), X("IB"))], "pzp")
-        mm(Bk(0), B("oh2"), X("Ib"), name="ohT2")
-        ts(B("pz"), A(1), -BIG, OP.add, -float(MID), OP.max, "pz")
-        grp(A(2), [(X("Ib"), X("QB")), (B("pz"), X("BOm"))], "ZQp")
-        tt(B("pc"), cK, Bk(0), OP.mult, "pc")
-        ts(B("ZQ"), A(2), V_ - 17.0 * MID - BIG, OP.add, -float(MID), OP.max, "ZQ")
-        z8 = Bk(1, sl(16, 24))
-        mm(z8, B("ZQ"), R("S1p"), name="ZLp")
-        for e in range(2): grp(D(1 + e), [(X("Ib"), X("TR%d" % e)), (X("BOm"), B("pz")), (B("ZQ"), X("ME%d" % e))], "DSp")
-        mm(Bk(1, sl(0, 8)), B("ZQ"), R("S1h"), name="ZLp")
-        ts(B("ZL"), Bk(1, sl(0, 8)), 16.0 * MID, OP.add, name="ZL")
-        grp(A(3), [(X("Imh"), R("VRh", _, t, ls)), (X("BOh"), B("pc"))], "csv")
-        flex(B("OC"), ind(Ow, B("ZL")), "OC")
-        ts(B("MN", sl(0, 256)), D(sl(1, 3)), 32.0 * MID - V_, OP.is_equal, 8192.0, OP.mult, "DS")
-        scan(B("MN", sl(256, 512)), R("N32"), B("MN", sl(0, 256)), OP.mult, 0.0, "DM")
-        tt(B("x8"), B("MN", sl(256 + 31, 512, 32)), z8, OP.add, "x8")
-        for e in range(2): ts(B("FZ", sl(e, 8, 2)), B("x8", sl(4 * e, 4 * e + 4)), 16.0 * MID, OP.add, Wq((5, 10)[e]), OP.min, "FZ")
-        tt(B("OE"), ind(Ow, B("ZL")), R("VR", _, t, ls), OP.is_equal, "OE")
-        tt(B("OE"), B("OE"), A(3), OP.mult, "NN")
-        for o, kn, a, b in ((1, "KH", "ImB", "IB"), (2, "KL", "IB", "ImB")): grp(D(o), [(X("Ib"), X(kn)), (X("BOh"), B("wN")), (B("nw"), X(b)), (B("oh2"), X(a))], "HL")
+            ts(R("zi", _, sl(1, 2)), R("zi", _, sl(0, 1)), 2, OP.bitwise_and, name="Z")
+            ts(R("Zt"), R("zi", _, sl(1, 2)), 1.0, OP.add, name="Z")
+        for o, kn, a, b in ((h, "KH", "ImB", "IB2"), (2 + h, "KL", "IB", "ImB2")): grp(R("pD%d" % ORD[0], _, sl(2 * o, 2 * o + 2)), [(X("Ib"), X(kn)), (X("BOh"), B("wN")), (nw, X(b)), (B("oh2"), X(a))], "HL")
 
     def sell(t, h):
         B = lambda n, *ix: R(n, _, h, *ix)
         for u in range(3, -1, -1): tt(ind(R("O"), B("FZ", sl(2 * u, 2 * u + 2))), B("OC", sl(32 * u, 32 * u + 32)), B("OE", sl(32 * u, 32 * u + 32)), OP.add, "scatter")
 
     def own(t, h):
-        hs = sl(MID * h + t, MID * h + MID, 12)
-        tt(R("F", _, h), R("O", _, hs), R("pD%d" % h, _, 1), OP.min, "XO")
-        tt(R("O", _, hs), R("F", _, h), R("pD%d" % h, _, 2), OP.max, "O")
-        if t == RO - 1: dma(R("yo", _, sl(MID * h, MID * h + MID)), R("O", _, sl(MID * h, MID * h + MID)), 786, "st yo", "Y", 128)
+        if h == ORD[0]: return
+        tt(R("F"), R("O", _, sl(t, V_, 12)), R("pD%d" % ORD[0], _, sl(0, 4)), OP.min, "XO")
+        tt(R("O", _, sl(t, V_, 12)), R("F"), R("pD%d" % ORD[0], _, sl(4, 8)), OP.max, "O")
+        if t == RO - 1: dma(R("yo"), R("O", _, sl(0, V_)), 1572, "st yo", "Y", 128)
 
     for t in range(RO):
         G["t"] = t; later = []
@@ -591,10 +950,10 @@ def build(core, T, topo, rank):
                 G["h"] = h; step(t, h)
             for d, x in later:
                 if d is None: x()
-                else: (gcopy if "WCu" not in ASG or d != D_OF[t + 1] else flex)(R("WC%d" % d, _, sl(t, V_, 12)), x, "WCu")
+                else: gcopy(R("WC%d" % d, _, sl(t, V_, 12)), x, "WCg")
             later.clear()
         G["h"] = None
-    dma(R("yc"), R("YC", sl(0, 8)), 98, "st yc", "S", 16)
+    G["ops"][dma(R("yc"), R("WC0", sl(2, 128, 16)), 200, "st yc", "G", 48, accum_op=OP.add, max_dma_last_dim=4096)]["deps"][y0] = True
     return G
 
 
@@ -606,12 +965,13 @@ def rank_program(g, core, T, topo):
     if rank is None:
         return
     G = build(core, T, topo, rank)
-    if "o" not in ORDER: ORDER["o"] = schedule(G)
-    order, eng, fin, st = ORDER["o"]
+    if "o" not in ORDER: ORDER["o"] = schedule(G)[0]; ORDER["e"] = [o["eng"] for o in G["ops"]]
     Q = {"V": g.vector, "S": g.scalar, "P": g.tensor, "G": g, "Y": g.sync}
-    ops = G["ops"]; apart = [False]
+    ops = G["ops"]; eng = ORDER["e"]
+    for o, e in zip(ops, eng):
+        if o["eng"] != e: o["fn"] = o["alt"][2]
     count = {}; known = {e: {} for e in Q}; done = [None] * len(ops); clock = [None] * len(ops)
-    for i in order:
+    for i in ORDER["o"]:
         o = ops[i]; e = eng[i]
         if e not in Q:
             done[i] = (o["key"], o["cnt"]); clock[i] = {}; count[o["key"]] = o["cnt"]
@@ -630,14 +990,11 @@ def rank_program(g, core, T, topo):
             for j in o["deps"]:
                 if done[j][0] == k and done[j][1] <= c:
                     for kk, vv in clock[j].items(): kn[kk] = max(kn.get(kk, 0), vv)
-        if e == "G" and o["key"] is None:
-            if (o["name"] == "up" or apart[0]) and kn.get("cG", 0) < count.get("cG", 0):
-                g.wait_ge(T.sem.cG, count["cG"]); kn["cG"] = count["cG"]
-            apart[0] = o["name"] == "up"
-        ins = o["fn"](Q, e)
+        ins = o["fn"](Q)
         k = o["key"] or "c" + e
         count[k] = count.get(k, 0) + o["cnt"]
-        if o["key"] is None: ins.then_inc(T.sem[k], 1)
+        if o["key"] is None:
+            for x in ins: x.then_inc(T.sem[k], 1)
         done[i] = (k, count[k])
         c = dict(kn); c[k] = max(c.get(k, 0), count[k])
         clock[i] = c

@@ -1,3 +1,4 @@
+import math
 import numpy as np
 from concourse.bass import DstId, RemoteDMATransfer
 from concourse.mybir import dt, AluOpType, AxisListType, ActivationFunctionType
@@ -5,17 +6,17 @@ from concourse.mybir import dt, AluOpType, AxisListType, ActivationFunctionType
 V_, RO, NR = 3072, 4, 4
 MID = 1536
 BIG = 65536.0
-TOP = V_ + 128.0
 OP = AluOpType
 AF = ActivationFunctionType
 COPY, IDENT, RELU, SIGN, ABS = AF.Copy, AF.Identity, AF.Relu, AF.Sign, AF.Abs
 D_OF = [1 + t % 3 for t in range(RO)]
 ORD = (1, 0)
 LO, UP = slice(0, 64), slice(64, 128)
-CBN = ["Ib", "IB", "ImB", "IB2", "ImB2", "Imb", "Im3072", "Id128", "Imh2", "QB", "QN", "K1", "KK", "ONE", "KH", "KL"]
-CWN = ["BO2", "WA", "WQ"]
-TMP = ["ci", "cg", "cq", "cd", "c64", "cw0", "cw1", "cw2", "x0", "x1", "x2", "x3", "x4", "x5", "x6"]
-CHN = ["ME0", "ME1", "I128", "I8192", "Ih", "I01", "Imh", "Im128", "Im8192", "Ih128", "I32h", "Im16h", "I16h", "BOh", "BOm"]
+OPT = {"KS": 1, "R3": 0, "WV": [1, 0], "HIP": 0, "SL": "DD", "MG": 4, "O2": 1}
+RL, VTW, PV, HQ = 8, 0, 4, 2
+CBN = ["Ib", "IB", "ImB", "IB2", "ImB2", "Imb", "Im3072", "Id128", "Imh2", "QB", "K1", "KK", "ONE", "KH", "KL", "BOb", "TL"]
+TMP = ["ci", "cg", "cq", "cd", "c32", "cw0", "cw1", "cw2", "x0", "x1", "x2", "x3", "x4", "x5", "x6"]
+CHN = ["ME0", "ME1", "I128", "I8192", "Ih", "Imh", "Ih128", "I32h", "I16h", "BOh", "BOm", "BO4"]
 CXN = ["NF", "NFa"]
 LAND = [(t, d) for t in range(RO - 1) for d in D_OF[t + 1:]]
 
@@ -26,18 +27,18 @@ def _decl():
 
     def sb(names, shape, dtype):
         for n in names.split(): s[n] = ("sbuf", shape, dtype)
-    sb("OI", [128, V_], i); sb("O", [128, V_ + 48], f); sb("P WC0 WC1 WC2 WC3", [128, V_], f); sb("XX", [128, 2 * V_], b)
+    sb("OI", [128, V_ + 8], i); sb("O", [128, V_ + 48], f); sb("O2", [128, V_ + 8], f); sb("P WC0 WC1 WC2 WC3", [128, V_], f); sb("XX", [128, 2 * V_], b)
     sb("CI", [128, 192], i); sb("CF F1 F2 F3 MT", [128, 192], f); sb("CA PR", [128, 192], f); sb("H16", [128, 384], hf); sb("CHi", [128, 192], b); sb("C16 L1 L2 L3", [128, 192], hf)
     sb("LD", [128, len(LAND), 256], hf); sb("PL", [128, RO - 1, 256], hf)
-    sb("VT", [128, 2, 4096], f); sb("VR", [128, 4, 256], f); sb("VRh", [128, 4, 256], hf); sb("VC", [128, 8], f)
-    sb("XK MN", [128, 2, 2048], hf); sb("CG", [128, 4096], hf); sb("ST", [128, 16, 256], b); sb("SV", [128, 2, 2048], b); sb("N16", [128, 1024], b); sb("VB", [128, 64], f); sb("WL", [128, 2, 4, 2, 128], hf)
+    sb("VT", [128, 2, 2048 + VTW], f); sb("SO", [128, 128 // RL, 16 * RL if not VTW else 1], b); sb("VR", [128, RO, 256], f); sb("VRh", [128, RO + 1, 256], b); sb("VC", [128, 8], f)
+    sb("XK MN", [128, 2, 2048], hf); sb("CG", [128, 4096], hf); sb("ST", [128, 16, 256], b); sb("SV", [128, 2, 2048], b); sb("N16", [128, 1024], b); sb("VB", [128, RO, 128 // RL], f); sb("WL", [128, 2, 4, 2, 128], hf)
     sb("LA LC LM", [128, 2, 128], u); sb("LB ZL FZ", [128, 2, 8], u)
     sb("aN uS wN pz ZQ", [128, 2, 128], hf); sb("SA", [128, RO, 272], hf); sb("R3 KS", [128, 2, 3, 128], hf); sb("S2", [128, 2, 2, 2, 64], hf)
-    sb("hi oh mine nst XB oh2", [128, 2, 128], b); sb("nw", [128, 2, 256], b); sb("SB", [128, 2, 144], b)
-    sb("F TT OC OE", [128, 2, 128], f); sb("BV B8 t8", [128, 2, 8], f); sb("E0 E2", [128, 2, 272], f); sb("E1", [128, 272], f); sb("TR", [128, 8, 34], b)
-    sb("CB", [128, len(CBN), 128], b); sb("CW", [128, len(CWN), 256], b); sb("CH", [128, len(CHN), 128], hf); sb("CX", [128, len(CXN), 128], f)
-    sb("WD", [128, 4, 128], hf); sb("R16", [128, 4, 64], hf); sb("Rd", [128, 3, 8], hf); sb("S1h S1n Rc", [128, 8], hf); sb("S1b", [128, 8], b); sb("U8 pk", [128, 8], f)
-    sb("pi", [128, 1], i); sb("ti", [128, 4], i); sb("tf", [128, 4], f); sb("wq", [128, 16], f); sb("zr", [128, 9], f); sb("zi", [128, 2], i); sb("Zt", [128, 1], f)
+    sb("hi oh mine nst XB oh2 nw", [128, 2, 128], b); sb("BK", [128, 2, 2, 128], b); sb("SB", [128, 2, 144], b)
+    sb("F OC OE", [128, 2, 128], f); sb("BV B8 t8", [128, 2, 8], f); sb("TR", [128, 256], b); sb("RW", [128, 2, 8], b)
+    sb("CB", [128, len(CBN), 128], b); sb("CH", [128, len(CHN), 128], hf); sb("CX", [128, len(CXN), 128], f)
+    sb("WD", [128, 8, 4, 16], hf); sb("R16", [128, 4, 64], hf); sb("Rd", [128, 3, 8], hf); sb("S1h Rc", [128, 8], hf); sb("S1b", [128, 8], b); sb("U8 pk", [128, 8], f)
+    sb("pi", [128, 1], i); sb("ti", [128, 6], i); sb("tf", [128, 6], f); sb("wq", [128, 24], f); sb("zr", [128, 9], f); sb("zi", [128, 2], i); sb("Zt", [128, 1], f)
     for h in range(2):
         for n in "ABC": s["p%s%d" % (n, h)] = ("psum", [128, 512], f)
         s["pD%d" % h] = ("psum", [128, 8, 64], f)
@@ -46,41 +47,37 @@ def _decl():
 
 SCRATCH = _decl()
 SEMAPHORES = ["cV", "cS", "cP", "cG", "loc"] + ["d%d" % k for k in range(30)] + ["ar%d_%d" % (t, j) for t in range(RO) for j in range(3)]
-CYC, WAKE, SAME, GCY, SCY, PF, PO = 0.83e-3, 0.125, 0.07, 1.56, 3.5, 0.6, 0.02
-RATE, LAT, FAR, ROW, LINK = 230.0, 2.2, 4.5, 0.1, 25.0
-CUT = {("XK", 1): [(64, "S"), (64, "V")], ("XK", 0): [(64, "S"), (64, "S")], ("CG", 1): [(48, "S"), (48, "S"), (32, "S")], ("CG", 0): [(48, "S"), (48, "S"), (32, "V")],
-       ("XM", 1): [(64, "S"), (64, "S")], ("XM", 0): [(48, "S"), (48, "S"), (32, "S")], ("ST", 1): [(64, "V"), (64, "V")], ("ST", 0): [(32, "V")] * 4}
+CYC, GCY, SCY, PF, PO = 0.83e-3, 1.56, 3.5, 0.6, 0.02
+RATE, LAT, FAR, ROW, LINK = 240.0, 1.2, 2.5, 0.05, 25.0
+SLOW = [1.25, 1.0]
+CUT = {("XK", 1): [(64, "S"), (64, "V")], ("XK", 0): [(64, "S"), (64, "S")], ("XK", 0, 0): [(64, "S"), (32, "S"), (32, "V")], ("CG", 1): [(48, "S"), (48, "V"), (32, "S")], ("CG", 0): [(48, "S"), (48, "V"), (32, "S")],
+       ("XM", 1): [(64, "S"), (64, "S")], ("XM", 0): [(48, "S"), (48, "S"), (32, "S")], ("ST", 1): [(64, "V"), (64, "V")], ("ST", 0): [(32, "V")] * 4 if VTW else [(128, "S")]}
 INDIRECT = "XK CG XM ST OB XB OC OE scatter".split()
-OPT = {"KS": 1, "R3": 0, "WV": [1, 0], "HIP": 0, "SL": "DD", "MG": 4}
-CASES = [(1.0, 1.0, 1.0, 0.125, 0.07, 0.0, 0.65), (1.6, 1.35, 1.35, 0.17, 0.09, 1.0, 0.25)]
-SEED = [7]
-APART = [0.0]
-LOADS = {"ld ctl": -9, "ld sha": -7, "ld hol1": -6, "ld hol0": -4, "ld flat": 12}
-START = 11.0
+CASES = [(1.0, 1.0, 1.0, 0.125, 0.07, 0.0, 0.65), (1.6, 1.35, 1.35, 0.17, 0.09, 3.0, 0.25)]
+SEED = [6, 1, 1, 1, 1]
+LOADS = {"ld ctl": -9, "ld sha": -7, "ld hol1": -6, "ld hol0": -4, "ld hol2": -3.9}
+START = 9.7
 SAME_AS = {"XO": "F", "BD": "F", "FR": "uS", "wp": "hi", "pc": "uS"}
-ASG = {n: "S" for n in "R3 RS cK Y2 aN mS cS KS hi XB bm FR PL Pu OC YC WCu H8 slot dig BD nst DS".split() + [""]}
-FIXED = ["", "wide1"]
-PLAN = [(0, 0.3, "LA"), (0.3, 3.1, "XK"), (3.2, 4.1, "dec"), (4.2, 5.8, "Y2 R3 uT LC"), (5.8, 8.6, "CG"), (8.7, 9.6, "cL"), (9.7, 11, "cS TK KS"), (11, 13, "D"), (11.3, 13.5, "clip"),
-        (11.8, 13.8, "pool"), (13.8, 16.6, "hi hi- F T oh ohT wN bR mine LMp LM"), (15.5, 16.7, "bL BD LBp LB XB XBp"), (16.7, 19.4, "XM"), (17.2, 19.1, "MX"), (17.7, 19.9, "FL"),
-        (18.2, 20.3, "WS"), (19.9, 21.3, "FR K2 F2 T2 oh2"), (20.3, 21.1, "wp WN nw"), (21.4, 23.6, "pzp pz ZQp ZQ DSp DSq DSw DS DM FZ"), (22.0, 23.4, "ZLp ZL pc csv OC OE NN"),
-        (23.6, 26, "scatter"), (21.2, 24, "t8 n8 H8 DG PL send"), (24, 27, "Pp Pu"), (6.5, 8.5, "MN"), (7.5, 9.2, "mL"), (9.3, 9.6, "mS"), (3, 9, "ST"), (11, 15, "OB"), (15.5, 17.5, "SQ"), (17.5, 19, "SL"), (19.2, 19.5, "nst"),
-        (27.5, 30, "XO O"), (24, 26, "HL"), (26, 28, "YC ZC zr Z"), (3.2, 3.4, "aN"), (-1, 0, "XV"), (16, 17, "b8 bm"), (10.5, 11, "K1"), (36, 37, "sendb")]
-PER = [28.0, 3.0]
-STEPS = [("LA", .1, .2, .25, .4), ("XK", .3, .5, 1.7, 5.2), ("dec", 1.9, 2.8, 5.3, 6.2), ("Y2 R3", 3.1, 3.8, 6.2, 6.9), ("uT LC", 3.9, 4.6, 7.0, 7.7), ("WCp", 3, 5.0, 0, 0), ("WCu", 5.2, 5.5, 0, 0),
-         ("CG", 5.5, 8.3, 9.0, 12.5), ("cL", 8.9, 9.8, 12.5, 13.4), ("cS TK KS", 9.9, 11.2, 13.4, 14.7), ("K1 D", 11.0, 11.6, 14.6, 15.2), ("clip", 11.5, 12.5, 15.1, 16.1), ("pool", 12, 12.9, 15.6, 16.5),
-         ("hi hi- F T oh ohT wN", 12.9, 14.8, 16.5, 18.4), ("bL BD LBp LB XB XBp", 14.8, 16.8, 18.4, 20.4), ("bR mine LMp LM", 14.9, 16.2, 18.5, 19.8), ("XM", 16.7, 19.5, 20.3, 23.1),
-         ("MX", 16.9, 19.5, 20.4, 22.3), ("FL", 17.5, 19.8, 21, 22.6), ("WS", 19.8, 21.2, 23.2, 24.5), ("WV", 18.5, 21, 22, 24.5), ("FR", 19.8, 20, 22.6, 22.8), ("K2", 18, 22, 21, 24.5),
-         ("F2 T2 oh2 pzp pz ZQp ZQ", 20.5, 23, 23.2, 25.1), ("TRp", 20.1, 20.2, 22.9, 23), ("DSp DSq", 22.5, 23.5, 24.6, 25.6), ("wp WN nw", 21.3, 22.3, 24.5, 25.4),
-         ("DSw DS DM FZ", 23.5, 25, 25.5, 26.7), ("ZLp ZL pc csv OC OE NN", 23.1, 25, 25.2, 26.7), ("scatter", 25.2, 26.6, 26.8, 28), ("t8 n8 send", 22.4, 23, 25.4, 25.8),
-         ("H8 Pp", 24, 25, 26, 27), ("Pu", 0, 0, 27, 27.8), ("DG PL", 27, 28, 27.5, 28.5), ("MN", 2.5, 4.4, 7.5, 9.4), ("mL mS", 3.5, 8, 9, 12), ("ST", 4.6, 7.4, 9.4, 15),
-         ("SL nst", 13, 16, 16.5, 19), ("XO O", 29.8, 30.1, 30.1, 30.4), ("HL", 26.5, 27.5, 27.5, 28.2), ("ZC zr Z", 0, 0, 30, 36), ("aN", 8.5, 8.6, 12, 12.1), ("XV", 1, 1.3, 4, 4.3),
-         ("b8 bm", 17, 19, 21, 23), ("sendb", 0, 0, 29, 30), ("WCg", 0, 0, 40, 44), ("OB", 3, 9, 9, 15), ("SQ", 10, 12, 15, 17)]
-PERIOD = 28.3
-TRIES = [8500, 6000, 500, 2500, 5000]
-MOVES = [2.0, 0.4, 1.5, 0.7, 0.25, 0.06, 0.4]
+ASG = {n: "S" for n in "R3 RS cK Y2 aN mS cS KS hi XB bm FR PL Pu OC YC WCu H8 dig BD nst".split() + [""]}
+FIXED = ["wide1"]
+STEPS = [("LA aN", 0, .3, .1, .2), ("XK", .3, .5, 1.8, 4.6), ("XV", .2, .3, -1, -1), ("dec", 3.0, 3.9, 4.7, 5.5), ("Y2 R3", 4.6, 5.1, 5.7, 6.3), ("uT LC", 5.5, 6.4, 6.5, 8.7), ("WCp", 3.9, 5.1, 0, 0), ("WCu", 5.2, 5.2, 0, 0),
+         ("CG", 6.4, 7.9, 8.4, 11.2), ("MN", 2.0, 7.0, 5.0, 9.3), ("mL", 2.8, 8.4, 6.1, 11.3), ("mS", 8.2, 8.2, 12.1, 12.1), ("cL", 8.3, 9.1, 11.2, 12.0), ("cS TK KS K1", 9.4, 10.6, 12.2, 13.2), ("D", 10.5, 11.4, 13.2, 13.8),
+         ("TC cK", 10.8, 12.2, 13.9, 17.1), ("clip", 11.2, 12.1, 13.7, 14.9), ("pool", 12.0, 12.4, 14.3, 15.5), ("hi hi- F T oh ohT wN", 12.6, 14.4, 15.2, 17.3), ("bR mine LMp LM", 14.5, 16.1, 17.3, 19.5),
+         ("bL BD LBp LB XB XBp", 14.6, 16.4, 17.4, 19.6), ("b8 bm", 14.7, 16.0, 18.5, 22.0), ("XM", 16.0, 19.7, 19.3, 22.7), ("MX", 17.2, 19.8, 19.7, 22.9), ("ST", 3.2, 16.4, 9, 15), ("OB", 0, 0, 9.6, 14.7), ("SQ", 0, 0, 14.9, 17.1),
+         ("SL", 12.6, 18.0, 17.1, 19.3), ("nst", 17.4, 17.4, 20.5, 20.5), ("FL", 18.3, 20.4, 21.2, 23.4), ("FR", 20.4, 20.4, 23.2, 23.2), ("K2", 20.4, 21.1, 22.3, 24.7), ("F2 T2 oh2 pzp pz ZQp ZQ", 21.1, 23.3, 23.8, 25.9),
+         ("TRp", 23.1, 23.1, 25.0, 25.0), ("DSp DSq", 23.6, 24.0, 25.7, 26.2), ("ZLp ZL OC", 23.3, 24.2, 26.1, 27.3), ("pc csv", 23.6, 24.3, 26.6, 27.2), ("OE NN", 24.7, 25.4, 27.0, 27.6), ("WS", 19.5, 22.8, 22.8, 24), ("WV", 18, 21, 21.8, 23.9),
+         ("wp WN nw", 22.7, 24.1, 24.1, 25.4), ("BK FZp FZ", 24.2, 25.7, 26.3, 27.6), ("t8 n8 send", 23.9, 25.0, 25.3, 26.6), ("H8 Pp", 24.7, 26.0, 26.6, 27.7), ("DG PL", 25.9, 26.3, 26.2, 26.7), ("Pu", 0, 0, 26.2, 29.0),
+         ("scatter", 25.4, 27.2, 27.5, 28.6), ("HL", 27.9, 28.6, 28.6, 29.9), ("ZC zr Z", 0, 0, 27.5, 28.6), ("XO O O2", 0, 0, 30.4, 32.0), ("sendb", 0, 0, 30.3, 30.3), ("WCg WCo", 0, 0, 38, 42)]
+PERIOD = 28.7
+TRIES = [45000, 8000, 30000, 20000, 20000]
+HEATS = [[0.04, 0.003, 0.06, 0.0], [0.05, 0.004, 0.03, 0.3]]
+MIX = [0.15, 0.05, 0.6, 0.7, 0.0]
+MARK = {}
 NOTE = []
-EARLY = {"P0d": -1.5, "pick": -4, "flat1": -1, "wide1": -1, "late": None, "next": 3, "c16": -3, "send0": -3, "dig": -2, "PR": -2, "rows": -2, "P0p": -1, "P0": -1, "LA": -1, "send0b": 20, "O32": 36, "negX": 2, "zero": None, "wide": None, "flat": None, "yc0": None, "fillW": -6}
-MARK = [0.4, "LC KS hi wN LM XB FR nw ZQ FZ PL".split()]
+EARLY = {"pick": -3.5, "c16": -3, "send0": -3, "dig": -2.9, "PR": -2.8, "P0p": 1, "P0d": 1, "P0": 1, "fillW": 2, "wide1": 3, "flat1": 3, "send0b": 15, "zero": 25, "wide": 30, "flat": 31, "yc0": 32}
+FIRST = {("XK", 1, 0): (10.0, "S"), ("XK", 1, 1): (10.0, "V"), ("XK", 0, 0): (11.8, "S"), ("XK", 0, 1): (13.5, "S"), ("XK", 0, 2): (13.5, "V"), ("CG", 1, 0): (14.3, "S"), ("CG", 1, 1): (14.3, "V"), ("CG", 1, 2): (15.3, "S")}
+SOON = ["", "next", "late", "fill", "negX"]
+WAIT = {}
 _ = slice(None)
 SIZE = {"float32": 4, "int32": 4}
 
@@ -141,426 +138,265 @@ def add(G, e, use, end, fn, r=(), w=(), key=None, cnt=1, name="", alt=None):
         if x[0] is None: continue
         if x[6]: G["br"].setdefault(x[0], []).append(n)
         else: G["rd"].setdefault(x[0], []).append((x[2], x[3], n))
-    G["ops"].append({"eng": e, "use": use, "end": end, "fn": fn, "deps": deps, "key": key, "cnt": cnt, "name": name, "t": G.get("t"), "h": G.get("h"), "alt": alt})
+    c = (G.get("t"), name, G.get("h")); k = G["seen"].get(c, 0); G["seen"][c] = k + 1
+    G["ops"].append({"eng": e, "use": use, "end": end, "fn": fn, "deps": deps, "key": key, "cnt": cnt, "name": name, "t": c[0], "h": c[2], "k": k, "alt": alt})
     return n
 
 
-def place(busy, t, d):
-    lo, hi = 0, len(busy)
-    while lo < hi:
-        m = (lo + hi) // 2
-        if busy[m][1] <= t: lo = m + 1
-        else: hi = m
-    while lo < len(busy) and busy[lo][0] < t + d - 1e-9:
-        t = max(t, busy[lo][1]); lo += 1
-    return t, lo
-
-
-def schedule(G):
-    ops = G["ops"]; n = len(ops)
-    succ = [[] for i in range(n)]
-    for i, o in enumerate(ops):
-        for j in o["deps"]: succ[j].append(i)
-    pred = [list(o["deps"]) for o in ops]
-    eng = [o["eng"] for o in ops]; use = [o["use"] for o in ops]; end = [o["end"] for o in ops]
-    lag = lambda j, i: end[j] + WAKE if eng[j] != eng[i] else end[j] + SAME if ops[i]["deps"][j] or ops[j]["key"] else use[j]
-    fore = [[(j, lag(j, i)) for j in pred[i]] for i in range(n)]
-    aft = [[(j, use[j] + lag(i, j) - use[i]) for j in succ[i]] for i in range(n)]
-    first = [(i, LOADS[o["name"]]) for i, o in enumerate(ops) if o["name"] in LOADS]
-    link = {i: o["link"] for i, o in enumerate(ops) if "link" in o}
-
-    def sweep(key, before, least):
-        at = [0.0] * n; busy = {e: [] for e in eng}; wire = []
-        for i in sorted(range(n), key=lambda i: key[i]):
-            t = least[i]
-            for j, d in before[i]:
-                if at[j] + d > t: t = at[j] + d
-            b = busy[eng[i]]
-            if i in link:
-                while True:
-                    t, k = place(wire, place(b, t, use[i])[0], link[i])
-                    if place(b, t, use[i])[0] == t: break
-                wire.insert(k, (t, t + link[i]))
-            if not b or b[-1][1] <= t: b.append((t, t + use[i]))
-            else:
-                t, k = place(b, t, use[i]); b.insert(k, (t, t + use[i]))
-            at[i] = t
-        return at
-    none = [0.0] * n; tail = [end[i] - use[i] for i in range(n)]
-
-    def both(prio, sweeps):
-        best = None
-        for it in range(sweeps):
-            for i, k in first: prio[i] = k
-            for i in range(n - 1, -1, -1):
-                k = prio[i] - 1e-4
-                for j in pred[i]:
-                    if prio[j] > k: prio[j] = k
-            at = sweep(prio, fore, none)
-            fin = max([at[i] + end[i] for i in range(n)])
-            if best is None or fin < best[0]: best = (fin, at)
-            if it + 1 < sweeps:
-                key = [-(at[i] + use[i]) for i in range(n)]
-                for i in range(n):
-                    k = key[i] - 1e-4
-                    for j in succ[i]:
-                        if key[j] > k: key[j] = k
-                back = sweep(key, aft, tail)
-                prio = [fin - (back[i] + use[i]) for i in range(n)]
-        return best
-    when = {}
-    for a, z, names in PLAN:
-        for k, x in enumerate(names.split()): when[x] = (a + (z - a) * k / len(names.split()), (z - a) / len(names.split()))
-    seen, total, key = {}, {}, [None] * n
-    for o in ops: total[o["t"], o["name"], o["h"]] = total.get((o["t"], o["name"], o["h"]), 0) + 1
-    kinds = {}
-    for i, o in enumerate(ops):
-        c = (o["t"], o["name"], o["h"]); k = seen.get(c, 0); seen[c] = k + 1
-        kinds.setdefault((o["name"], o["h"]), []).append(i)
-        if total[c] > 1 and o["t"] is not None: kinds.setdefault((o["name"], o["h"], k), []).append(i)
-        if o["t"] is not None and o["h"] is not None and o["name"] in when:
-            key[i] = START + o["t"] * PER[0] + ORD.index(o["h"]) * PER[2] + PER[1] * (when[o["name"]][0] + when[o["name"]][1] * k / total[c])
-    for i in range(n - 1, -1, -1):
-        if key[i] is None: key[i] = min([key[s] for s in succ[i]] or [1e3]) - end[i]
-    kinds = list(kinds.values()); x = [SEED[0]]
-
-    def rnd():
-        x[0] = (x[0] * 1103515245 + 12345) % 2 ** 31
-        return x[0] / 2 ** 31
-
-    cases = []
-    for gather, rest, pe, wake, same, far in CASES:
-        u = [(x - 0.06) * gather + 0.06 if o["name"] in INDIRECT else x * rest if e in "VSG" else x * pe if e == "P" else x for x, e, o in zip(use, eng, ops)]
-        z = [a + y - x + (far if e[0] == "N" else 0.0) for a, x, y, e in zip(u, use, end, eng)]
-        cases.append((u, z, [[(j, z[j] + (wake if eng[j] != eng[i] else same)) for j in pred[i] if eng[j] != eng[i] or ops[i]["deps"][j] or ops[j]["key"]] for i in range(n)]))
-
-    def times(b):
-        order = sorted(range(n), key=lambda i: (b[1][i], i)); out = [b[0]]
-        for u, z, before in cases:
-            at = [0.0] * n; free = {e: 0.0 for e in eng}; last = 0.0
-            for i in order:
-                t = free[eng[i]]
-                for j, d in before[i]:
-                    if at[j] + d > t: t = at[j] + d
-                at[i] = t; free[eng[i]] = t + u[i]
-                if t + z[i] > last: last = t + z[i]
-            out.append(last)
-        return out
-
-    def score(b):
-        s = times(b)
-        return s[0] * 0.5 + 0.5 * sum(a * 150.0 / w for a, w in zip(s[1:], (135.0, 200.0))) / len(cases) if cases else s[0]
-
-    def mend(best, tries):
-        cur = best; low = now = score(best)
-        for it in range(tries):
-            key = list(cur[1])
-            for k in range(1 + int(rnd() * TRIES[1])):
-                d = (rnd() - 0.5) * TRIES[2]
-                for i in kinds[int(rnd() * len(kinds))]: key[i] += d
-            new = both(key, 1 + (rnd() < 0.3))
-            if new[0] > cur[0] + 2.0: continue
-            s = score(new)
-            if s <= now + TRIES[3] * (1 - it / tries) * rnd(): cur = new; now = s
-            if now < low: best = cur; low = now
-        return best, low
-    starts = [mend(both([k + (d if o["h"] == ORD[1] and o["t"] is not None else 0.0) for k, o in zip(key, ops)], 2), TRIES[0] // (2 * len(APART))) for d in APART]
-    best = mend(min(starts, key=lambda b: b[1])[0], TRIES[0] // 2)[0]
-    return sorted(range(n), key=lambda i: (best[1][i], i)), best[1], times(best)
-
-
-def schedule(G):
-    ops = G["ops"]; n = len(ops)
-    pred = [list(o["deps"]) for o in ops]
-    succ = [[] for i in range(n)]
-    for i in range(n):
-        for j in pred[i]: succ[j].append(i)
-    names = sorted({o["eng"] for o in ops}); eng = [names.index(o["eng"]) for o in ops]
-    link = [o.get("link", 0.0) for o in ops]
-    when = {}
-    for a, z, xs in PLAN:
-        for k, x in enumerate(xs.split()): when[x] = (a + (z - a) * k / len(xs.split()), (z - a) / len(xs.split()))
-    seen, total, key, kinds, kind = {}, {}, [None] * n, {}, [None] * n
-    for o in ops: total[o["t"], o["name"], o["h"]] = total.get((o["t"], o["name"], o["h"]), 0) + 1
-    for i, o in enumerate(ops):
-        c = (o["t"], o["name"], o["h"]); k = seen.get(c, 0); seen[c] = k + 1
-        kind[i] = kinds.setdefault((o["name"], o["h"], k) if o["t"] is not None else i, []); kind[i].append(i)
-        if o["name"] in LOADS: key[i] = LOADS[o["name"]]
-        elif o["t"] is not None and o["h"] is not None and o["name"] in when:
-            key[i] = START + o["t"] * PER[0] + ORD.index(o["h"]) * PER[2] + PER[1] * (when[o["name"]][0] + when[o["name"]][1] * k / total[c])
-    for i in range(n - 1, -1, -1):
-        if key[i] is None: key[i] = min([key[s] for s in succ[i]] or [1e3]) - ops[i]["end"]
-    x = [SEED[0]]
-
-    def rnd():
-        x[0] = (x[0] * 1103515245 + 12345) % 2 ** 31
-        return x[0] / 2 ** 31
-
-    cases = []
-    for gather, rest, pe, wake, same, far, weight in CASES:
-        u = [(o["use"] - 0.06) * gather + 0.06 if o["name"] in INDIRECT else o["use"] * (rest if o["eng"] in "VSG" else pe if o["eng"] == "P" else 1.0) for o in ops]
-        z = [a + o["end"] - o["use"] + (far if o["eng"][0] == "N" else 0.0) for a, o in zip(u, ops)]
-        cases.append((u, z, [[(j, z[j] + (wake if eng[j] != eng[i] else same)) for j in pred[i] if eng[j] != eng[i] or ops[i]["deps"][j] or ops[j]["key"]] for i in range(n)], weight))
-
-    def run(order, case):
-        u, z, before, weight = case
-        at = [0.0] * n; why = [-1] * n; free = [0.0] * len(names); who = [-1] * len(names); wire = 0.0; last = 0.0; end = 0
-        for i in order:
-            e = eng[i]; t = free[e]; w = -2 - who[e]
-            for j, d in before[i]:
-                d += at[j]
-                if d > t: t = d; w = j
-            if link[i]:
-                if wire > t: t = wire
-                wire = t + link[i]
-            at[i] = t; why[i] = w; free[e] = t + u[i]; who[e] = i
-            if t + z[i] > last: last = t + z[i]; end = i
-        return last, at, why, end
-
-    def settle(key, back):
-        if back:
-            for i in range(n - 1, -1, -1):
-                k = key[i] - 1e-5
-                for j in pred[i]:
-                    if key[j] > k: key[j] = k
-        else:
-            for i in range(n):
-                k = key[i] + 1e-5
-                for j in succ[i]:
-                    if key[j] < k: key[j] = k
-        order = sorted(range(n), key=lambda i: key[i])
-        rs = [run(order, c) for c in cases]
-        return sum(r[0] * c[3] for r, c in zip(rs, cases)), order, rs
-    cur = best = settle(key, True)
-    for it in range(TRIES[0]):
-        now, order, rs = cur
-        key = [0.0] * n
-        for p, i in enumerate(order): key[i] = rs[0][1][i] + p * 1e-7
-        last, at, why, i = rs[int(rnd() * len(rs))]
-        held = []
-        while i >= 0:
-            w = why[i]
-            if w < -1:
-                w = -2 - w; held.append((w, i))
-            i = w
-        r = rnd()
-        if held and r < 0.8:
-            j, i = held[int(rnd() * len(held))]
-            d = key[i] - key[j] + 1e-4 + (rnd() * TRIES[2] if rnd() < 0.3 else 0.0); back = rnd() < 0.5
-            m, d = (i, -d) if back else (j, d)
-        else:
-            m = int(rnd() * n); d = (rnd() - 0.5) * 2 * TRIES[2]; back = d < 0
-        for k in kind[m] if rnd() < TRIES[1] else [m]:
-            if ops[k]["name"] not in LOADS: key[k] += d
-        new = settle(key, back)
-        if new[0] <= now + TRIES[3] * (1 - it / TRIES[0]) * rnd(): cur = new
-        if cur[0] < best[0]: best = cur
-    return best[1], best[2][0][1], [r[0] for r in best[2]]
+def swap(o):
+    o["alt"], o["eng"], o["use"], o["fn"] = (o["eng"], o["use"], o["fn"]), *o["alt"]; o["end"] = o["use"]
 
 
 def plan(ops):
-    when, total, key = {}, {}, [None] * len(ops)
+    when, total = {}, {}
     for xs, *at in STEPS:
         xs = xs.split()
         for h, a, z in zip(ORD, at[0::2], at[1::2]):
             for k, x in enumerate(xs): when[x, h] = (a + (z - a) * k / len(xs), (z - a) / len(xs))
-    for o in ops: total[o["t"], o["name"], o["h"]] = total.get((o["t"], o["name"], o["h"]), 0) + 1
-    for i, o in enumerate(ops):
-        c = when.get((o["name"], o["h"]))
-        if o["t"] is not None and c: key[i] = START + o["t"] * PERIOD + c[0] + c[1] * o["k"] / total[o["t"], o["name"], o["h"]]
-    return key
+    for o in ops: total[o["name"], o["h"]] = total.get((o["name"], o["h"]), 0) + 1
+    return [when[c][0] + when[c][1] * o["k"] / total[c] if c in when else None for o in ops for c in [(o["name"], o["h"])]]
 
 
-def mend(ops, key, tries, alike, heat=1.0):
-    n = len(ops)
-    pred = [list(o["deps"]) for o in ops]; succ = [[] for o in ops]
-    for i in range(n):
-        for j in pred[i]: succ[j].append(i)
-    names = sorted({o["eng"] for o in ops} | {"V", "S"}); eng = [0] * n
-    link = [o.get("link", 0.0) for o in ops]
-    kinds = {}; kind = [kinds.setdefault((o["name"], o["h"], o["k"]) if o["t"] is not None else i, []) for i, o in enumerate(ops)]
+def tune(ops, order, tries, goal, seed, ring=False):
+    n = len(ops); (g0, r0, p0, w0, s0, f0, a0), (g1, r1, p1, w1, s1, f1, a1) = CASES; HEAT = HEATS[ring]
+    names = sorted({o["eng"] for o in ops} | {"V", "S"}); m = len(names)
+    eng = [0] * n; u0 = [0.0] * n; u1 = [0.0] * n; z0 = [0.0] * n; z1 = [0.0] * n; before = [None] * n; now = [None] * n; nxt = [None] * n
+    link = [o.get("link", 0.0) for o in ops]; least = [o.get("least", 0.0) for o in ops]; lap = [o.get("lap", 0) for o in ops]
+    rare = [a or b for a, b in zip(link, least)]; both = [i for i, o in enumerate(ops) if o["alt"]]; vec = names.index("V")
+    far = [i for i in range(n) if link[i]]; pos = [0] * n
+    succ = [[] for o in ops]
     for i, o in enumerate(ops):
-        kind[i].append(i)
-        if o["name"] in LOADS: key[i] = LOADS[o["name"]]
-    for i in range(n - 1, -1, -1):
-        if key[i] is None: key[i] = min([key[s] for s in succ[i]] or [1e3]) - ops[i]["end"]
-    x = [SEED[0]]
+        for j, raw, s in o["pre"]: succ[j].append((i, s))
+    x = [seed]
 
     def rnd():
-        x[0] = (x[0] * 1103515245 + 12345) % 2 ** 31
-        return x[0] / 2 ** 31
-    cases = [([0.0] * n, [0.0] * n, [None] * n, c[6]) for c in CASES]
-    use, end = cases[0][:2]
-    fore = [None] * n; aft = [None] * n
+        x[0] = (x[0] * 1103515245 + 12345) % 2147483648
+        return x[0] / 2147483648
 
     def price(i):
-        o = ops[i]; eng[i] = names.index(o["eng"])
-        for (gather, rest, pe, wake, same, far, weight), c in zip(CASES, cases):
-            c[0][i] = (o["use"] - 0.06) * gather + 0.06 if o["name"] in INDIRECT else o["use"] * (rest if o["eng"] in "VSG" else pe if o["eng"] == "P" else 1.0)
-            c[1][i] = c[0][i] + o["end"] - o["use"] + (far if o["eng"][0] == "N" else 0.0)
+        o = ops[i]; e = o["eng"]; eng[i] = names.index(e)
+        for u, z, g, r, p, f in ((u0, z0, g0, r0, p0, f0), (u1, z1, g1, r1, p1, f1)):
+            u[i] = (o["use"] - 0.06) * g + 0.06 if o["name"] in INDIRECT else o["use"] * (r if e in "VSG" else p if e == "P" else 1.0)
+            z[i] = u[i] + o["end"] - o["use"] + (f if e[0] == "N" else 0.0)
+        if o["cnt"] == 16 and o["key"]: u1[i] *= SLOW[0]; z1[i] = z1[i] * SLOW[0] + SLOW[1]
 
     def tie(i):
-        for (gather, rest, pe, wake, same, far, weight), c in zip(CASES, cases):
-            c[2][i] = [(j, c[1][j] + (wake if eng[j] != eng[i] else same)) for j in pred[i] if eng[j] != eng[i] or ops[i]["deps"][j] or ops[j]["key"]]
-        d = dict(cases[0][2][i]); fore[i] = [(j, d.get(j, use[j])) for j in pred[i]]
+        b = []; c = []
+        for j, raw, s in ops[i]["pre"]:
+            d = s + lap[i] - lap[j]
+            if d == 0: c.append(j)
+            if d > 1: continue
+            if eng[j] != eng[i]: b.append((j + n * d, z0[j] + w0, z1[j] + w1))
+            elif raw or ops[j]["key"]: b.append((j + n * d, z0[j] + s0, z1[j] + s1))
+        before[i] = b; now[i] = c
+        nxt[i] = [j for j, s in succ[i] if s + lap[j] - lap[i] == 0]
 
-    def untie(i): aft[i] = [(j, use[j] + dict(fore[j])[i] - use[i]) for j in succ[i]]
+    def flip(i):
+        swap(ops[i]); price(i); tie(i)
+        for j, s in succ[i]: tie(j)
 
-    def flip(ks):
-        for i in ks:
-            o = ops[i]; a = o["alt"]; o["alt"] = (o["eng"], o["use"], o["fn"]); o["eng"], o["use"], o["fn"] = a; o["end"] = o["use"]; price(i)
-        for i in ks:
-            for j in [i] + succ[i]: tie(j)
-        for i in ks:
-            for j in [i] + pred[i]: untie(j)
-    for f in (price, tie, untie):
+    def turn(i, d):
+        lap[i] += d; tie(i)
+        for j in [j for j, s in succ[i]] + [p[0] for p in ops[i]["pre"]]: tie(j)
+    for f in (price, tie):
         for i in range(n): f(i)
-    none = [o.get("least", 0.0) for o in ops]; tail = [end[i] - use[i] for i in range(n)]
-    loads = [i for i, o in enumerate(ops) if o["name"] in LOADS]
 
-    def sweep(key, before, least):
-        at = [0.0] * n; A = [[] for e in names]; Z = [[] for e in names]
-        for i in np.argsort(key, kind="stable").tolist():
-            t = least[i]
-            for j, d in before[i]:
-                d += at[j]
-                if d > t: t = d
-            a = A[eng[i]]; z = Z[eng[i]]; u = use[i]; k = m = len(z)
-            while k and z[k - 1] > t: k -= 1
-            while k < m and a[k] < t + u - 1e-9:
-                if z[k] > t: t = z[k]
-                k += 1
-            a.insert(k, t); z.insert(k, t + u); at[i] = t
-        return at
+    def run(order, old, p=0, was=None):
+        A, B = (was[0][:], was[1][:]) if p else ([0.0] * n + old[0], [0.0] * n + old[1])
+        F = list(old[2]); H = list(old[3]); wa = wb = -99.0
+        if p:
+            for i in {eng[i]: i for i in order[:p]}.values(): F[eng[i]] = A[i] + u0[i]; H[eng[i]] = B[i] + u1[i]
+            for i in far:
+                if pos[i] < p: wa = max(wa, A[i] + link[i]); wb = max(wb, B[i] + link[i])
+        for i in order[p:]:
+            e = eng[i]; a = F[e]; b = H[e]
+            for j, c, d in before[i]:
+                c += A[j]
+                if c > a: a = c
+                d += B[j]
+                if d > b: b = d
+            if rare[i]:
+                a = max(a, least[i]); b = max(b, least[i])
+                if link[i]: a = max(a, wa); b = max(b, wb); wa = a + link[i]; wb = b + link[i]
+            A[i] = a; B[i] = b; F[e] = a + u0[i]; H[e] = b + u1[i]
+        return A, B, F, H
 
-    def run(order, case):
-        u, z, before, weight = case
-        at = [0.0] * n; why = [-1] * n; free = [0.0] * len(names); who = [-1] * len(names); wire = 0.0; last = 0.0; end = 0
-        for i in order:
-            e = eng[i]; t = free[e]; w = -2 - who[e]
-            if none[i] > t: t = none[i]; w = -1
-            for j, d in before[i]:
-                d += at[j]
-                if d > t: t = d; w = j
-            if link[i]:
-                if wire > t: t = wire
-                wire = t + link[i]
-            at[i] = t; why[i] = w; free[e] = t + u[i]; who[e] = i
-            if t + z[i] > last: last = t + z[i]; end = i
-        return last, at, why, end
+    def worth(r):
+        A, B = r[:2]
+        if ring: ta = A[goal] - A[n + goal]; tb = B[goal] - B[n + goal]
+        else: ta = max([A[i] + z0[i] for i in goal]); tb = max([B[i] + z1[i] for i in goal])
+        return a0 * ta + a1 * tb + HEAT[2] * sum(A[:n]) / n + sum([A[i] * w for i, w in marks]) + HEAT[3] * sum([u0[i] for i in both if eng[i] == vec]), ta, tb
 
-    def up(key):
-        for i in range(n - 1, -1, -1):
-            k = key[i] - 1e-5
-            for j in pred[i]:
-                if key[j] > k: key[j] = k
+    def carry(r):
+        a = r[0][goal]; b = r[1][goal]
+        return [t - a for t in r[0][:n]], [t - b for t in r[1][:n]], [max(t - a, -9.0) for t in r[2]], [max(t - b, -9.0) for t in r[3]]
 
-    def shift(key, i, d):
-        key[i] += d; todo = [i]
-        while todo:
-            i = todo.pop()
-            for j in pred[i] if d < 0 else succ[i]:
-                if key[j] >= key[i] if d < 0 else key[j] <= key[i]: key[j] = key[i] + (-1e-5 if d < 0 else 1e-5); todo.append(j)
-
-    def settle(key, both=False):
-        at = sweep(key, fore, none)
-        if both:
-            key = [at[i] + use[i] for i in range(n)]
-            up(key); b = sweep([-k for k in key], aft, tail)
-            key = [-(b[i] + use[i]) for i in range(n)]
-            for i in loads: key[i] = at[i] - 1e3
-            up(key); at = sweep(key, fore, none)
-        order = np.argsort(at, kind="stable").tolist()
-        rs = [run(order, c) for c in cases]
-        return sum(r[0] * c[3] for r, c in zip(rs, cases)) + sum(rs[0][1][i] for i in marks) * MARK[0] / len(marks), order, rs
-    marks = [i for i, o in enumerate(ops) if o["name"] in MARK[1]]
-    up(key)
-    cur = best = min([settle(list(key), j) for j in (0, 1)], key=lambda b: b[0]); queues = [o["eng"] for o in ops]
-    far, slack, moves, aimed, both, swap = MOVES[:6]
-    for it in range(tries):
-        now, order, rs = cur
-        key = list(rs[0][1])
-        last, at, why, i = rs[int(rnd() * len(rs))]
-        held = []
-        while i >= 0:
-            w = why[i]
-            if w < -1: w = -2 - w; held.append((w, i))
-            i = w
-        early = rnd() < 0.5
-        for rep in range(1 + int(rnd() * moves)):
-            if held and rnd() < aimed:
-                j, i = held[int(rnd() * len(held))]
-                d = key[i] - key[j] + 1e-4 + (rnd() * far if rnd() < 0.5 else 0.0)
-                m, d = (i, -d) if early else (j, d)
-            else: m = int(rnd() * n); d = rnd() * far * (-1 if early else 1)
-            span = rnd() * 8.0 if rnd() < MOVES[6] else 0.0
-            for k in kind[m] if rnd() < alike else [m]:
-                todo = [k]; seen = {k}; last = key[k] + span
-                while todo:
-                    i = todo.pop()
-                    for j in succ[i]:
-                        if j not in seen and key[j] < last and ops[j]["h"] == ops[k]["h"]: seen.add(j); todo.append(j)
-                for i in sorted(seen, reverse=not early):
-                    if ops[i]["name"] not in LOADS: shift(key, i, d)
-        ks = []
-        if rnd() < swap:
-            c = [kind[y] for p in held for y in p if ops[y]["alt"]]
-            if c:
-                ks = c[int(rnd() * len(c))]; ks = [k for k in ks if ops[k]["alt"] and ops[k]["eng"] == ops[ks[-1]]["eng"]]
-                flip(ks)
-        new = settle(key, rnd() < both)
-        if new[0] <= now + heat * slack * (1 - it / tries) * rnd(): cur = new
-        else: flip(ks)
-        if cur[0] < best[0]: best = cur; queues = [o["eng"] for o in ops]
-    flip([i for i in range(n) if ops[i]["eng"] != queues[i]])
-    return best[1], best[2][0][1], [r[0] for r in best[2]]
+    def path(order, r, c):
+        A = r[c]; u = (u0, u1)[c]; z = (z0, z1)[c]; last = [-1] * m; prev = [-1] * n; held = []
+        for i in order: prev[i] = last[eng[i]]; last[eng[i]] = i
+        i = goal if ring else max(goal, key=lambda i: A[i] + z[i])
+        while i < n:
+            j = prev[i]
+            if j >= 0 and A[j] + u[j] >= A[i] - 1e-9: held.append((j, i)); i = j; continue
+            i = max([b[0] for b in before[i] if A[b[0]] + b[1 + c] >= A[i] - 1e-9] or [n])
+        return held
+    marks = [(i, MARK[kind(o)]) for i, o in enumerate(ops) if ring and kind(o) in MARK]
+    old = ([-99.0] * n, [-99.0] * n, [0.0] * m, [0.0] * m)
+    r = run(order, old)
+    for k in range(3 * ring): old = carry(r); r = run(order, old)
+    cur = worth(r); best = None; fresh = True
+    fixed = [o["name"] in LOADS or o.get("still") for o in ops]
+    for it in range(tries + 1):
+        if fresh:
+            A = r[0]; order = sorted(order, key=lambda i: A[i])
+            for p, i in enumerate(order): pos[i] = p
+            paths = [path(order, r, c) for c in (0, 1)]; fresh = False
+            if best is None or cur[0] < best[0][0]: best = (cur, order, list(lap), [o["eng"] for o in ops], r[0][:n])
+        if it == tries: break
+        held = paths[rnd() < 0.35]; q = rnd(); undo = None; new = order; a = 0
+        if q < MIX[0]:
+            c = [i for i in ([i for p in held for i in p] if rnd() < 0.7 else order) if ops[i]["alt"] and not fixed[i]]
+            if not c: continue
+            i = c[int(rnd() * len(c))]; flip(i); undo = (flip, i); a = pos[i]
+            if rnd() < MIX[3]:
+                a = max([pos[k] + 1 for k in now[i]] + [0]); b = min([pos[k] for k in nxt[i]] + [n]); new = order[:]
+                del new[pos[i]]; new.insert(a + int(rnd() * (b - a)), i)
+        elif ring and q < MIX[0] + MIX[1]:
+            i = int(rnd() * n); d = 1 if rnd() < 0.5 else -1
+            if i == goal or (nxt if d > 0 else now)[i] or abs(lap[i] + d) > 1: continue
+            turn(i, d); undo = (turn, i, -d); new = [k for k in order if k != i]
+            if d > 0: new.insert(min([new.index(k) for k in nxt[i]] + [int(rnd() * 30)]), i)
+            else: new.insert(max([new.index(k) + 1 for k in now[i]] + [n - 1 - int(rnd() * 30)]), i)
+        else:
+            early = rnd() < 0.5
+            if held and q < sum(MIX[:3]):
+                j, i = held[int(rnd() * len(held))]; a, b = pos[j], pos[i]
+                d = int(rnd() * 25) if rnd() < 0.4 else 0
+            else: a = b = int(rnd() * n); d = 1 + int(rnd() * rnd() * 60)
+            a, b = (max(0, a - d), b) if early else (a, min(n - 1, b + d))
+            seg = order[a:b + 1]; s = {seg[-1 if early else 0]}
+            for k in reversed(seg) if early else seg:
+                if k in s: s.update((now if early else nxt)[k])
+            if any(fixed[k] for k in seg if k in s): continue
+            new = order[:a] + [k for k in seg if (k in s) == early] + [k for k in seg if (k in s) != early] + order[b + 1:]
+        bar = cur[0] - (HEAT[1] + HEAT[0] * (1 - it / tries) ** 2) * math.log(1 - rnd() * 0.999)
+        t = run(new, old, a, r); w = worth(t)
+        if ring and w[0] <= bar: t = run(new, carry(t)); w = worth(t)
+        if w[0] <= bar:
+            r = t; cur = w; order = new; fresh = True
+            if ring: old = carry(t); r = run(order, old); cur = worth(r)
+        elif undo: undo[0](*undo[1:])
+    for o, d, e in zip(ops, best[2], best[3]):
+        o["lap"] = d
+        if o["eng"] != e: swap(o)
+    return best[1], best[4], best[0]
 
 
-def middle(ops, ts):
-    need = {i for i, o in enumerate(ops) if ts[0] and o["t"] == ts[0] or o["t"] == ts[1] and o["name"] in ("scatter", "Pu", "send")}
-    for i in range(len(ops) - 1, -1, -1):
-        if i in need: need.update(j for j in ops[i]["deps"] if ops[j]["t"] in ts)
-    at = {i: k for k, i in enumerate(sorted(need))}
-    return [dict(ops[i], i=i, deps={at[j]: r for j, r in ops[i]["deps"].items() if j in at}) for i in sorted(need)]
+def kind(o): return o["name"], o["h"], o["k"]
+
+
+def lay(ops, key):
+    n = len(ops); succ = [[] for o in ops]
+    for i, o in enumerate(ops):
+        for j, raw, s in o["pre"]:
+            if s + o.get("lap", 0) == ops[j].get("lap", 0): succ[j].append(i)
+    left = [len(s) for s in succ]; back = [i for i in range(n) if not left[i]]
+    for i in back:
+        key[i] = min([key[s] - (1e-5 if key[i] is not None else ops[i]["end"]) for s in succ[i]] + [1e3 if key[i] is None else key[i]])
+        for j, raw, s in ops[i]["pre"]:
+            if i in succ[j]:
+                left[j] -= succ[j].count(i); succ[j] = succ[j] + []
+                if left[j] == 0: back.append(j); left[j] = -1
+    return sorted(range(n), key=lambda i: key[i])
+
+
+def pack(ops):
+    wake, same = CASES[0][3:5]; at = []; busy = {}
+    for o in ops:
+        t = max([o["least"]] + [at[j] + (p["end"] + (wake if p["eng"] != o["eng"] else same) if p["eng"] != o["eng"] or raw or p["key"] else p["use"]) for j, raw, s in o["pre"] for p in [ops[j]]])
+        b = busy.setdefault(o["eng"], []); k = len(b)
+        while k and b[k - 1][1] > t: k -= 1
+        while k < len(b) and b[k][0] < t + o["use"] - 1e-9:
+            t = max(t, b[k][1]); k += 1
+        b.insert(k, (t, t + o["use"])); at.append(t)
+    return sorted(range(len(ops)), key=lambda i: at[i])
+
+
+def ring_of(ops):
+    base = {}
+    for t in (2, 1):
+        for i, o in enumerate(ops):
+            if o["t"] == t: base.setdefault(kind(o), i)
+    at = {c: k for k, c in enumerate(base)}; ring = []
+    for i in base.values():
+        o = ops[i]; pre = {}
+        for j, raw in o["deps"].items():
+            if ops[j]["t"] is not None and kind(ops[j]) in at:
+                c = (at[kind(ops[j])], o["t"] - ops[j]["t"]); pre[c] = pre.get(c, False) or raw
+        ring.append(dict(o, pre=[(j, raw, s) for (j, s), raw in pre.items()]))
+    key = plan(ring)
+    for i, o in enumerate(ring):
+        if key[i] and key[i] > PERIOD: o["lap"] = 1; key[i] -= PERIOD
+    for k in range(3):
+        for i, o in enumerate(ring):
+            for j, raw, s in o["pre"]:
+                if s + o.get("lap", 0) < ring[j].get("lap", 0): o["lap"] = 1; key[i] = None
+    key = [PERIOD if k is None and o.get("lap") else k for k, o in zip(key, ring)]
+    return ring, lay(ring, key), max(i for i, o in enumerate(ring) if o["name"] == "scatter")
+
+
+def part(ops, keep, at):
+    k = {i: p for p, i in enumerate(keep)}
+    return [dict(ops[i], pre=[(k[j], r, 0) for j, r in ops[i]["deps"].items() if j in k], least=max([at[j] + ops[j]["end"] + CASES[0][3] for j in ops[i]["deps"] if j not in k] + [WAIT.get(ops[i]["name"], 0.0)])) for i in keep]
 
 
 def schedule(G):
-    ops = G["ops"]; seen = {}
-    for o in ops:
-        c = (o["t"], o["name"], o["h"]); o["k"] = seen.get(c, 0); seen[c] = o["k"] + 1
-    mid = middle(ops, (1, 2))
-    order, at, times = mend(mid, plan(mid), TRIES[0], 1.0)
-    order, at, times = mend(mid, list(at), TRIES[3], 1.0, 0.4)
-    ends = [max(a + o["end"] for a, o in zip(at, mid) if o["t"] == t and o["name"] == "scatter") for t in (1, 2)]; per = ends[1] - ends[0]
-    like = {}
-    for a, o in zip(at, mid): like[o["name"], o["h"], o["k"]] = (a - ends[0] + (2 - o["t"]) * per, o["eng"])
-    key = plan(ops)
+    ops = G["ops"]; n = len(ops)
+    if not NOTE:
+        ring, order, goal = ring_of(ops)
+        order, at, (w, per, slow) = tune(ring, order, TRIES[0], goal, SEED[0], True)
+        NOTE.append((per, slow, ring, at, order))
+    per, slow, ring, at, order = NOTE[0]
+    first = min(a + o["lap"] * per for a, o in zip(at, ring) if o["name"] == "LA")
+    like = {kind(o): (a + o["lap"] * per - first, o["eng"]) for a, o in zip(at, ring)}
+    key = [None] * n
     for i, o in enumerate(ops):
-        c = like.get((o["name"], o["h"], o["k"]))
-        if o["t"] is None: key[i] = EARLY.get(o["name"], i * 1e-3)
-        if c and o["t"] is not None:
-            key[i] = START + o["t"] * per + c[0]
-            if o["t"] == 0 and o["name"] == "XK": c = (c[0], "SV"[o["k"] % 2]); key[i] = START + (5.3 if o["h"] == ORD[1] else 1.3)
-            if c[1] != o["eng"] and o["alt"]: o["alt"], o["eng"], o["use"], o["fn"] = (o["eng"], o["use"], o["fn"]), *o["alt"]; o["end"] = o["use"]
-            if o["t"] == 0 and o["name"] == "XK": o["alt"] = None
-    NOTE.append((per, mid, at, ends, order))
-    head = middle(ops, (None, 0))
-    order, at, times = mend(head, [key[o["i"]] for o in head], TRIES[1], 0.0)
-    late = max(a + o["end"] for a, o in zip(at, head) if o["name"] == "scatter") - per - START
-    key = [k and k + late for k in key]
-    for a, o in zip(at, head):
-        key[o["i"]] = a
-        if o["t"] is not None or o["alt"]: ops[o["i"]].update({x: o[x] for x in ("alt", "eng", "use", "end", "fn")})
-    order, at, times = mend(ops, key, TRIES[2], 0.3)
-    keep = [i for i, o in enumerate(ops) if o["t"] == RO - 1 or at[i] > START + late + (RO - 1) * per - 3.0]; at_ = {i: k for k, i in enumerate(keep)}
-    tail = [dict(ops[i], i=i, deps={at_[j]: r for j, r in ops[i]["deps"].items() if j in at_}, least=max([at[j] + ops[j]["end"] + WAKE for j in ops[i]["deps"] if j not in at_] + [START + late + (RO - 1) * per - 3.0])) for i in keep]
-    for a, o in zip(mend(tail, [at[i] for i in keep], TRIES[4], 0.0, 0.5)[1], tail):
-        at[o["i"]] = a; ops[o["i"]].update({x: o[x] for x in ("alt", "eng", "use", "end", "fn")})
-    return mend(ops, list(at), 0, 0.0)
+        c = like.get(kind(o))
+        if o["t"] is None: key[i] = LOADS.get(o["name"], EARLY.get(o["name"]))
+        elif c or kind(o) in FIRST:
+            key[i] = START + o["t"] * per + (c or [0])[0]
+            if o["t"] == 0 and kind(o) in FIRST: key[i], c = FIRST[kind(o)][0], FIRST[kind(o)]
+            if o["t"] == 0 and o["eng"] == "G": key[i] = max(key[i], START - 3)
+            if c[1] != o["eng"] and o["alt"]: swap(o)
+            if o["t"] == 0 and kind(o) in FIRST: o["alt"] = None
+
+    def mend(keep, at, goal, tries, seed=0, gaps=False):
+        sub = part(ops, keep, at); inside = set(keep)
+        free = {ops[i]["eng"]: at[i] + ops[i]["use"] for i in sorted(at, key=lambda i: at[i]) if i not in inside and at[i] <= at[keep[0]]} if at else {}
+        for o in sub: o["least"] = max(o["least"], at[keep[0]] if at else 0.0, free.get(o["eng"], 0.0))
+        order, got, w = tune(sub, pack(sub) if gaps else list(range(len(keep))), tries, [p for p, i in enumerate(keep) if goal(ops[i])], seed)
+        for i, o in zip(keep, sub):
+            if o["eng"] != ops[i]["eng"]: swap(ops[i])
+        return [keep[p] for p in order], dict(zip(keep, got)), w
+    lay(part(ops, range(n), None), key)
+    key = [min(k, 5 + k / 100) if o["t"] is None and o["name"] in SOON else k for k, o in zip(key, ops)]
+    order = lay(part(ops, range(n), None), key)
+    cut = max(p for p, i in enumerate(order) if ops[i]["t"] == 0 and ops[i]["name"] == "scatter") + 1
+    pre = max(p for p, i in enumerate(order) if ops[i]["t"] == 0 and kind(ops[i])[:2] == ("CG", ORD[0])) + 1
+    order[:pre] = mend(order[:pre], None, lambda o: o["name"] == "CG", TRIES[1], SEED[1], True)[0]
+    order[:cut] = mend(order[:cut], None, lambda o: o["name"] in ("scatter", "send"), TRIES[2], SEED[2], True)[0]
+    order, at, w = mend(order, None, lambda o: True, 0)
+    a = min(p for p, i in enumerate(order) if ops[i]["t"] == 0 and ops[i]["name"] == "CG"); z = max(p for p, i in enumerate(order) if ops[i]["t"] == 1 and ops[i]["name"] == "XM") + 1
+    for i in order[a:z]: ops[i]["still"] = ops[i]["t"] == 1 and ops[i]["eng"] != "G"
+    order[a:z] = mend(order[a:z], at, lambda o: o["t"] == 1 and o["name"] == "XM", TRIES[3], SEED[3])[0]
+    order, at, w = mend(order, None, lambda o: True, 0)
+    cut = min(p for p, i in enumerate(order) if ops[i]["t"] == RO - 1 and ops[i]["name"] == "LA")
+    order[cut:] = mend(order[cut:], at, lambda o: o["key"], TRIES[4], SEED[4])[0]
+    return mend(order, None, lambda o: True, 0)
 
 
 def build(core, T, topo, rank):
-    G = {"ops": [], "wr": {}, "rd": {}, "bw": {}, "br": {}}
+    G = {"ops": [], "wr": {}, "rd": {}, "bw": {}, "br": {}, "seen": {}}
     nd = [0]
     R = lambda n, *ix: ref(T, n, *ix)
 
@@ -624,10 +460,6 @@ def build(core, T, topo, rank):
         c = 0.17 + 2 * o[4] * CYC
         return add(G, "G", c, c, lambda Q: [Q["G"].affine_select(o[1], a[1], [[0, o[4]]], OP.is_ge, 0.0, 0, 0)], [a], [o], name=name)
 
-    def select(o, a, pat, base):
-        c = 0.17 + 2 * o[4] * CYC
-        return add(G, "G", c, c, lambda Q: [Q["G"].affine_select(o[1], a[1], pat, OP.is_ge, 0.0, base, 0)], [a], [o])
-
     def dma(o, a, kb, name, q="Y", rows=64, **kw):
         k = "d%d" % nd[0]; nd[0] += 1
         c = kb / RATE + rows / 16 * ROW
@@ -654,7 +486,7 @@ def build(core, T, topo, rank):
 
     def X(n, w=128):
         if n in TMP: return R("ST", _, TMP.index(n) // 2, sl(128 * (TMP.index(n) % 2), 128 * (TMP.index(n) % 2) + w))
-        for buf, names in (("CB", CBN), ("CW", CWN), ("CH", CHN), ("CX", CXN)):
+        for buf, names in (("CB", CBN), ("CH", CHN), ("CX", CXN)):
             if n in names: return R(buf, _, names.index(n))
 
     half = list(enumerate((LO, UP)))
@@ -664,6 +496,7 @@ def build(core, T, topo, rank):
     iota(R("pi"), [[1, 1]], 0, 1)
     cpv(R("ti", _, sl(0, 1)), R("pi"))
     for o, k, op in ((1, 4, OP.arith_shift_right), (2, 15, OP.bitwise_and), (3, 63, OP.bitwise_and)): ts(R("ti", _, sl(o, o + 1)), R("pi"), k, op)
+    for o, k in ((4, 6), (5, 3)): ts(R("ti", _, sl(o, o + 1)), R("pi"), 4, OP.arith_shift_right, k, OP.bitwise_and)
     cpv(R("tf"), R("ti"))
     F = lambda k: R("tf", _, sl(k, k + 1))
     Wq = lambda k: R("wq", _, sl(k, k + 1))
@@ -677,13 +510,16 @@ def build(core, T, topo, rank):
     flex(col192("H16", 1), R("CHi"), "dig", bias=-1.5, scale=1 / 128)
     tt(col192("H16", 0), col192("CA", 0), col192("PR", 0), OP.add, "PR")
     dma(R("XX", _, sl(0, V_)), R("sha"), 786, "ld sha", "Y", 128)
-    for c in range(2): flex(R("XX", _, sl(V_ + MID * c, V_ + MID * c + MID)), R("XX", _, sl(MID * c, MID * c + MID)), "negX", bias=0.0, scale=-1.0, only="V")
+    for c in range(0, V_, 768): flex(R("XX", _, sl(V_ + c, V_ + c + 768)), R("XX", _, sl(c, c + 768)), "negX", bias=0.0, scale=-1.0, only="S" if c < MID else "V")
     for h in ORD:
         cs = sl(MID * h, MID * h + MID)
-        dma(R("OI", _, cs), R("hol", _, cs), 786, "ld hol%d" % h, "Y", 128)
-        cpv(R("LA", _, h), R("OI", _, sl(MID * h, MID * h + MID, 12)), "LA")
+        m = 1 if h == ORD[0] else HQ
+        for c in range(m):
+            a = MID * h + MID // m * c; cs = sl(a, a + MID // m)
+            dma(R("OI", _, cs), R("hol", _, cs), 786 / m, "ld hol%d" % (h + 2 * c), "Y", 128)
+            cpv(R("LA", _, h, sl(128 // m * c, 128 // m * (c + 1))), R("OI", _, sl(a, a + MID // m, 12)), "LA")
         for c in range(MID * h, MID * h + MID, 384): flex(R("O", _, sl(c, c + 384)), R("OI", _, sl(c, c + 384)), "O32", only="S")
-    fill(R("O", _, sl(V_, V_ + 48)), 0.0)
+    fill(R("O", _, sl(V_, V_ + 48)), 0.0); fill(R("O2", _, sl(V_, V_ + 8)), 0.0); fill(R("OI", _, sl(V_, V_ + 8)), 0)
     for d in (1, 2, 3):
         if d == D_OF[0]:
             for c in range(3): flex(R("WC%d" % d, _, sl(1024 * c, 1024 * c + 1024)), R("SA", _, _, sl(0, 256)), "fillW", only="S")
@@ -692,11 +528,11 @@ def build(core, T, topo, rank):
         flex(R("F%d" % d), R("L%d" % d), "wide1" if d == D_OF[0] else "wide")
         dma(R("WC%d" % d, sl(2, 128, 16)), R("F%d" % d), 98, "flat1" if d == D_OF[0] else "flat", "S" if d == D_OF[0] else "Y", 128)
     for n, pat, base in (("ci", [[1, 128]], 0), ("cg", [[1, 8], [0, 16]], 0), ("cq", [[0, 8], [1, 16]], 0)): iota(X(n), pat, base)
-    late = [iota(X(n), pat, base, name="late") for n, pat, base in (("ONE", [[0, 128]], 1), ("KH", [[0, 128]], MID + int(1.5 * BIG)), ("KL", [[0, 128]], MID - int(1.5 * BIG)))]
-    late += [iota(R("SB"), [[0, 288]], 0, name="late"), iota(R("MT"), [[0, 192]], MID, name="late"), iota(R("VB"), [[-1, 4], [-MID, 2], [-192, 8]], 0, name="late")]
+    late = [iota(X(n), pat, base, name="late") for n, pat, base in (("ONE", [[0, 128]], 1), ("KH", [[0, 128]], MID + int(1.5 * BIG)), ("KL", [[0, 128]], MID - int(1.5 * BIG)), ("c32", [[0, 4], [1, 32]], 0))]
+    late += [iota(R("SB"), [[0, 288]], 0, name="late"), iota(R("MT"), [[0, 192]], MID, name="late"), iota(R("VB"), [[-1, RO], [-12 * RL, 128 // RL]], 0, name="next")]
     late += [iota(X(n), pat, base, name="next") for n, pat, base in (("K1", [[0, 8], [-1, 16]], 15), ("cw0", [[2, 4], [0, 32]], 0), ("cw1", [[2, 4], [0, 32]], 1))]
-    late += [iota(X("x0", 256), [[0, 4], [-16, 2], [1, 32]], 0, name="next"), iota(X("x2", 256), [[32, 4], [0, 2], [1, 32]], 0, name="next")]
-    late += [iota(R("pk", _, sl(0, 4)), [[2, 4]], -15, name="next"), iota(R("VC"), [[1, 4], [MID, 2]], -MID, 12, name="next"), iota(R("E1"), [[0, 4], [-16, 2], [0, 34]], int(TOP) - V_ - 1, name="next")]
+    late += [iota(X("x0", 256), [[-32, 2], [0, 8], [-2, 16]], 1, name="next")]
+    late += [iota(R("pk", _, sl(0, 4)), [[2, 4]], -15, name="next"), iota(R("VC"), [[1, 4], [MID, 2]], -MID, 12, name="next")]
     for i in late: G["ops"][i]["deps"][s2] = False
     fill(R("Zt"), 1.0)
     if any(OPT["WV"]):
@@ -705,7 +541,7 @@ def build(core, T, topo, rank):
     c8 = X("ci", 8)
     ts(X("Ib"), X("ci"), F(0), OP.is_equal)
     for n, s in (("I128", 128), ("I8192", 8192), ("IB", BIG), ("ImB", -BIG), ("IB2", BIG / 2), ("ImB2", -BIG / 2), ("Imb", -1), ("Im3072", -V_), ("Id128", 1 / 128), ("Imh2", -0.5), ("Ih", 1), ("Imh", -1),
-                 ("Im128", -128), ("Im8192", -8192), ("Ih128", 1 / 128), ("I32h", 32), ("Im16h", -16), ("I16h", 16)):
+                 ("Ih128", 1 / 128), ("I32h", 32), ("I16h", 16)):
         flex(X(n), X("Ib"), bias=0.0, scale=float(s))
     pick = lambda j, a, z: R("MN", _, j // 8, sl(130 * (j % 8) + a, 130 * (j % 8) + z))
     iota(X("x6", 144), [[16, 9], [1000, 16]], -16)
@@ -713,61 +549,58 @@ def build(core, T, topo, rank):
     for c in range(8):
         n = "p%s%d" % ("ACBD"[c // 2], c % 2); cs = sl(384 * c, 384 * c + 384)
         b = lambda a, z: R(n, _, sl(a // 64, z // 64)) if n[1] == "D" else R(n, _, sl(a, z))
-        digits = [(b(192 * e, 192 * e + 192), pick(2 * c + e, 1 - x, 129 - x), col192("H16", x), False, c >= 4 and e + x == 2) for e in range(2) for x in range(2)]
-        if c < 4: mms([(b(0, 384), R("SA", _, 0, sl(0, 128)), R("H16"), True, False)] + digits[:3], "P0d"); mms(digits[3:], "P0d")
-        mm(b(0, 384), X("Ib"), R("XX", _, cs), c >= 4, c < 4, "P0p")
-        if c >= 4: mms(digits, "P0d")
-        flex(R("P", _, cs), b(0, 384), "P0", only="SV"[c % 2])
-    BOb = R("CW", _, 0, sl(0, 128))
-    for e in range(2): ts(R("CW", _, 0, sl(128 * e, 128 * e + 128)), X("cg"), F(1), OP.is_equal)
-    for n, s in (("BOh", 1.0), ("BOm", -1.0)): flex(X(n), BOb, bias=0.0, scale=s)
+        digits = [(b(192 * e, 192 * e + 192), pick(2 * c + e, 1 - x, 129 - x), col192("H16", x), c < PV and x == 0, x == 1 and (c < PV or e == 1)) for e in range(2) for x in range(2)]
+        if c >= PV: mm(b(0, 384), X("Ib"), R("XX", _, cs), True, False, "P0p")
+        mms(digits, "P0d")
+        if c < PV: tt(R("P", _, cs), R("XX", _, cs), b(0, 384), OP.add, "P0")
+        else: flex(R("P", _, cs), b(0, 384), "P0", only="S")
+    ts(X("BOb"), X("cg"), F(1), OP.is_equal)
+    for n, s in (("BOh", 1.0), ("BOm", -1.0), ("BO4", 4.0)): flex(X(n), X("BOb"), bias=0.0, scale=s)
     ts(X("QB"), X("cq"), F(2), OP.is_equal, BIG, OP.mult)
-    ts(X("QN"), X("cq"), F(2), OP.not_equal, BIG, OP.mult)
-    for e in range(2): ts(X("ME%d" % e), X("cw%d" % e), F(1), OP.is_equal, -1.0, OP.mult)
-    x0, x2, x4 = X("x0", 256), X("x2", 256), X("x4", 256)
-    ts(X("WA"), x2, F(0), OP.is_equal, BIG / 2, OP.mult)
-    ts(x4, x0, 0.0, OP.is_ge, -2.0, OP.mult); ts(x2, x0, 16.0, OP.is_ge, 2.0, OP.mult); tt(x4, x4, x2, OP.add)
-    tt(X("WQ"), X("WA"), x4, OP.mult)
-    ts(x2, x0, F(2), OP.is_ge, 2.0, OP.mult); tt(x4, x4, x2, OP.add); ts(R("TR", _, _, sl(2, 34)), x4, BIG / 2, OP.mult, BIG / 2 - 30 * MID, OP.add)
-    fill(R("TR", _, _, sl(0, 2)), (TOP - 16 * MID) / 4096)
-    ts(R("E1"), R("E1"), F(2), OP.subtract); fill(R("E1", _, sl(0, None, 34)), 8192.0)
-    ts(R("S1n"), c8, F(1), OP.is_equal, -1 / 4096, OP.mult)
+    for e in range(2): ts(X("ME%d" % e), X("cw%d" % e), F(1), OP.is_equal, 4.0, OP.mult)
+    x0, low = X("x0", 256), 4.0 * (32 * MID - V_)
+    ts(Wq(12), F(0), 32.0, OP.is_equal); ts(X("TL"), X("c32"), F(0), OP.is_equal, Wq(12), OP.max)
+    ts(Wq(13), Wq(12), low + 1, OP.mult, -1.0, OP.add); ts(Wq(14), Wq(12), low - 2, OP.mult, 2.0, OP.add); ts(Wq(19), F(0), 2.0, OP.mult)
+    ts(x0, x0, Wq(19), OP.add, Wq(13), OP.max); ts(R("TR"), x0, Wq(14), OP.min)
+    ts(Wq(15), F(4), 1.0, OP.add)
+    for e, w in enumerate((F(4), Wq(15))): ts(R("RW", _, e), c8, w, OP.is_equal, BIG, OP.mult)
+    for e in range(2): ts(Wq(5 + e), F(2), V_ + 1.0 + 16 * e, OP.add)
     ts(R("VC"), R("VC"), 0.5, OP.mult)
-    ts(X("NF"), X("cq"), 0.0, OP.not_equal)
-    ts(X("NFa"), X("cq"), 0.0, OP.is_equal, -2.0 ** 30, OP.mult)
-    ts(Wq(0), F(2), 0.0, OP.is_equal); ts(Wq(1), F(2), 1.0, OP.is_equal); ts(Wq(2), F(2), 2.0, OP.is_equal)
+    act(X("NF"), X("cq"), SIGN); flex(X("NFa"), X("NF"), bias=-2.0 ** 30, scale=2.0 ** 30)
+    ts(R("wq", _, sl(0, 3)), X("ci", 3), F(2), OP.is_equal)
     ts(Wq(3), Wq(1), -1 / 64, OP.mult, Wq(0), OP.add); ts(Wq(3), Wq(3), 96.0, OP.mult)
     ts(Wq(4), F(0), 64.0, OP.is_lt, 4095.0, OP.mult); ts(Wq(4), Wq(4), 1.0, OP.add)
-    ts(Wq(10), F(0), 1.0, OP.is_equal); ts(Wq(11), F(0), 0.0, OP.is_equal)
+    ts(R("wq", _, sl(10, 12)), X("ci", 2), F(0), OP.is_equal)
     for n in ("S1h", "S1b", "U8"): ts(R(n), c8, F(1), OP.is_equal)
     ts(R("Rc"), c8, F(1), OP.is_equal, Wq(2), OP.mult)
     for j, w in ((0, Wq(0)), (1, Wq(1)), (2, 1.0)): ts(R("Rd", _, j), c8, F(1), OP.is_equal, w, OP.mult)
-    y = lambda k: R("ST", _, sl(8 + 2 * k, 10 + 2 * k))
-    iota(y(0), [[0, 8], [-1, 64]], 0, 1); iota(y(1), [[1, 8], [0, 64]], 1); iota(y(2), [[1, 8], [0, 64]], -15)
-    select(y(1), y(1), [[-1, 8], [0, 4], [-1, 16]], 14)
-    select(y(2), y(2), [[1, 8], [0, 4], [1, 16]], -15)
-    tt(y(2), y(0), y(2), OP.is_equal)
-    ts(y(0), y(0), F(0), OP.subtract, F(3), OP.add)
-    tt(y(1), y(0), y(1), OP.is_equal)
-    ts(R("WD"), y(1), Wq(4), OP.mult); ts(y(3), y(2), -4096.0, OP.mult); tt(R("WD"), R("WD"), y(3), OP.add)
+    y = lambda k: R("ST", _, 8 + k, sl(0, 128))
+    iota(y(0), [[1, 8], [1, 16]], 1, name="next")
+    ts(Wq(16), F(0), 64.0, OP.is_lt, -4096.0, OP.mult); ts(Wq(17), Wq(16), -1.0, OP.mult, Wq(4), OP.add); ts(Wq(18), F(2), 16.0, OP.add)
+    ts(y(1), y(0), F(2), OP.is_equal, Wq(4), OP.mult); ts(y(2), y(0), Wq(18), OP.is_equal, Wq(16), OP.mult); tt(y(1), y(1), y(2), OP.add)
+    ts(y(2), y(0), 16.0, OP.is_ge, Wq(17), OP.mult); ts(y(2), y(2), Wq(16), OP.add); ts(y(3), X("cq"), F(2), OP.is_equal); tt(y(2), y(2), y(3), OP.mult); tt(y(1), y(1), y(2), OP.add)
+    ts(R("wq", _, sl(20, 24)), X("ci", 4), F(5), OP.is_equal)
+    for g in range(4): ts(R("WD", _, _, g), y(1), Wq(20 + g), OP.mult)
     pk = R("pk", _, sl(0, 4)); pw = R("pk", _, sl(4, 8))
     ts(Wq(7), F(0), 64.0, OP.is_ge); ts(pk, pk, Wq(7), OP.add)
     ts(pw, pk, F(2), OP.add, 0.0, OP.is_ge); tt(pk, pk, pw, OP.mult)
     ts(Wq(9), R("pk", _, sl(3, 4)), -8.0, OP.is_equal, -99.0, OP.mult); ts(R("pk", _, sl(3, 4)), R("pk", _, sl(3, 4)), Wq(9), OP.add)
     ts(pk, pk, F(3), OP.add)
     for i in range(4): ts(R("R16", _, i), X("ci", 64), R("pk", _, sl(i, i + 1)), OP.is_equal, 16.0, OP.mult)
-    ts(X("KK"), X("cq"), 16.0 * MID, OP.mult, Wq(10), OP.mult); ts(X("cw2"), X("K1"), Wq(11), OP.mult); tt(X("KK"), X("KK"), X("cw2"), OP.add)
+    ts(Wq(11), Wq(11), 16.0 * MID, OP.mult, Wq(10), OP.subtract); ts(Wq(10), Wq(10), 15.0, OP.mult)
+    ts(X("KK"), X("cq"), Wq(11), OP.mult, Wq(10), OP.add)
     dma(R("WC0", sl(2, 128, 16)), R("CF"), 98, "flat", "Y", 128)
     y0 = dma(R("yc"), R("MT"), 98, "yc0", "Y", 128)
 
     def firms(t):
         iota(R("VR", _, t), [[12, 256]], t, name="VR")
-        flex(R("VRh", _, t), R("VR", _, t), "VRh", bias=-float(MID), only="S")
+        if t == 0: iota(R("VRh", _, RO), [[192, 16], [0, 16]], -MID, name="VR")
+        iota(R("VRh", _, t), [[0, 16], [12, 16]], t, name="VRh")
         for h in ORD:
             at = 0
             for n, q in CUT["ST", h]:
                 if q == "V":
-                    for c in range(at, at + n, 32): iota(R("VT", _, t % 2, sl(2048 * h + 16 * c, 2048 * h + 16 * c + 512)), [[12, 32], [0, 16]], t + MID * h + 12 * c, name="VT")
+                    for c in range(at, at + n, 32): iota(R("VT", _, t % 2, sl(VTW * h + 16 * c, VTW * h + 16 * c + 512)), [[12, 32], [0, 16]], t + MID * h + 12 * c, name="VT")
                 at += n
 
     def front(t, h):
@@ -780,14 +613,14 @@ def build(core, T, topo, rank):
         A, Bk, C, D4 = bank("A"), bank("B"), bank("C"), lambda *ix: R("pD%d" % h, _, *ix)
         D = lambda p, *ix: D4(sl(2 * p, 2 * p + 2), *ix)
         col = lambda b, s, k: b(s, sl(k, None, 16))
-        rows = lambda n, k, m=16: R(n, _, sl(8 * h, 8 * h + 8), sl(k, None, m)) if n == "ST" else B(n, sl(k, None, m))
+        rows = lambda n, k, m=16: R(n, _, _, sl(k, None, m)) if n == "SO" else B(n, sl(k, None, m))
         O, P, XX, WC = "O", "P", "XX", "WC%d" % D_OF[t]
         hs = sl(MID * h + t, MID * h + MID, 12); ls = sl(128 * h, 128 * h + 128)
         Xw, Ow = R(XX, _, sl(0, V_)), R(O)
 
         def pieces(n):
             at = 0
-            for m, q in CUT[n, h]:
+            for m, q in CUT.get((n, h, t), CUT[n, h]):
                 yield sl(16 * at, 16 * (at + m)), sl(at, at + m), q
                 at += m
 
@@ -795,23 +628,20 @@ def build(core, T, topo, rank):
 
         def stakes(b, p):
             for a, c, q in pieces("ST"):
-                if q == "V": tt(B("SV", a), ind(Ow if t else R("OI"), B("LA", c)), R("VT", _, t % 2, sl(2048 * h + a.start, 2048 * h + a.stop)), OP.is_equal, "ST")
+                if q == "V": tt(B("SV", a), ind(Ow if t else R("OI"), B("LA", c)), R("VT", _, t % 2, sl(VTW * h + a.start, VTW * h + a.stop)), OP.is_equal, "ST")
                 else:
-                    for u in range(c.start // 16, c.stop // 16): act(R("ST", _, 8 * h + u), ind(Ow, B("LA", sl(16 * u, 16 * u + 16))), IDENT, bias=R("VB", _, sl(16 * t + 8 * h + u, 16 * t + 8 * h + u + 1)), name="OB")
-                    for j in range(16):
-                        x = R("ST", _, sl(8 * h + c.start // 16, 8 * h + c.stop // 16), sl(16 * j, 16 * j + 16))
+                    for u in range(128 // RL): act(R("SO", _, u), ind(Ow if t else R("OI"), B("LA", sl(RL * u, RL * u + RL))), IDENT, bias=R("VB", _, t, sl(u, u + 1)), name="OB")
+                    for j in range(RL):
+                        x = R("SO", _, _, sl(16 * j, 16 * j + 16))
                         ts(x, x, 12.0 * j, OP.is_equal, name="SQ")
-            sums(b, p, "ST" if q == "S" else "SV", R("S1b"), "SL")
+            sums(b, p, "SO" if q == "S" else "SV", R("S1b"), "SL")
             relu(B("nst"), b(p), 1.0, -1.0, "nst")
         if t: cpv(B("LA"), R(O, _, hs), "LA")
         for a, b, q in pieces("XK"): flex(B("XK", a), ind(R(P), B("LA", b)), "XK", only=q)
         sums(A, sl(0, 3), "XK", R("Rd"), "dec")
         flex(B("KS", sl(0, 2)), A(sl(0, 2)), "Y2")
-        if OPT["R3"]:
-            flex(B("R3", sl(0, 2)), A(sl(0, 2)), "R3", bias=float(MID))
-            flex(B("R3", 2), A(2), "RS", bias=float(MID))
-        else: flex(B("R3"), A(sl(0, 3)), "R3", bias=float(MID))
-        grp(C(0), [(B("KS", 0), X("I128")), (B("KS", 1), X("I8192")), (B("R3", 0), X("Im128")), (B("R3", 1), X("Im8192"))], "uT")
+        flex(B("R3"), A(sl(0, 3)), "R3", bias=-float(MID), scale=-1.0)
+        grp(C(0), [(B("KS", 0), X("I128")), (B("KS", 1), X("I8192")), (B("R3", 0), X("I128")), (B("R3", 1), X("I8192"))], "uT")
         ts(B("LC"), C(0), MID * 8321.0, OP.add, name="LC")
         if t and h == ORD[0]:
             w = bank("C", ORD[1])
@@ -841,15 +671,16 @@ def build(core, T, topo, rank):
         grp(key, [(X("ONE"), X("KK")), (X("I16h"), B("S2", _, 1))], "K1", True, False)
         for i in range(2):
             b = (Bk, lambda *ix: D4(sl(2 * ix[0].start, 2 * ix[0].stop)) if ix else D4())[i]
-            mms([(b(sl(2 * e, 2 * e + 2)), R("WD", _, 2 * i + e), B("KS", sl(1, 3)), True, True) for e in range(2)], "D")
+            mms([(b(sl(2 * e, 2 * e + 2)), R("WD", _, sl(4 * i + 2 * e, 4 * i + 2 * e + 2)), B("KS", sl(1, 3)), True, True) for e in range(2)], "D")
             ts(B("WL", sl(2 * i, 2 * i + 2)), b(), float(MID), OP.max, MID + 4096.0, OP.min, "clip")
             mms([(C(0, sl(64 * a, 64 * a + 64)), B("WL", 2 * i + e, a), R("R16", _, 2 * i + e), False, i + e + a == 3) for e in range(2) for a in range(2)], "pool")
         flex(B("hi"), key, "hi", bias=2.0 ** 23 - 32767)
         if OPT["HIP"]: mm(key, X("Imb"), B("hi"), False, True, "hi-")
         else: tt(key, key, B("hi"), OP.subtract, "hi-")
         scan(B("F"), X("NFa"), key, OP.add, "F")
-        scan(B("TT", sl(None, None, -1)), X("NFa"), B("F", sl(None, None, -1)), OP.add, "T")
-        tt(B("oh"), B("TT"), key, OP.is_equal, "oh")
+        back = lambda p: R("pC%d" % h, _, sl(128 * p + 127, 128 * p - 1 if p else None, -1))
+        scan(back(2), X("NFa"), back(0), OP.add, "T")
+        tt(B("oh"), B("F"), C(2), OP.is_equal, "oh")
         mm(A(0), B("oh"), X("Ib"), name="ohT")
         tt(B("wN"), cK, A(0), OP.mult, "wN")
         mm(A(1), X("BOh"), B("wN"), name="bR")
@@ -871,24 +702,24 @@ def build(core, T, topo, rank):
         if OPT["SL"][h] == "D": stakes(D, 1)
         sums(D, 2, "MN", R("S1h"), "FL", 4)
         flex(B("FR"), D(2), "FR", bias=float(MID))
-        grp(key, [(X("Ib"), X("K1")), (X("Im16h"), B("R3", 2)), (B("mine"), X("ImB")), (X("ImB"), B("nst")), (X("I32h"), B("FR"))], "K2")
+        grp(key, [(X("Ib"), X("K1")), (X("I16h"), B("R3", 2)), (B("mine"), X("ImB")), (X("ImB"), B("nst")), (X("I32h"), B("FR"))], "K2")
         scan(B("F"), X("NF"), key, OP.mult, "F2")
-        scan(B("TT", sl(None, None, -1)), X("NF"), B("F", sl(None, None, -1)), OP.mult, "T2")
-        tt(B("oh2"), B("TT"), key, OP.is_equal, "oh2")
+        scan(back(2), X("NFa"), back(0), OP.add, "T2")
+        tt(B("oh2"), B("F"), C(2), OP.is_equal, "oh2")
         grp(Bk(3), [(X("Imh"), B("aN")), (B("oh2"), X("IB"))], "pzp")
         ts(B("pz"), Bk(3), -BIG, OP.add, -float(MID), OP.max, "pz")
         grp(Bk(3), [(X("Ib"), X("QB")), (B("pz"), X("BOm"))], "ZQp")
         ts(B("ZQ"), Bk(3), V_ - 17.0 * MID - BIG, OP.add, -float(MID), OP.max, "ZQ")
-        run = lambda e: D4(sl(e, 8, 2), sl(2, 34))
-        mm(D4(_, sl(0, 34)), X("Ib"), R("TR"), True, False, "TRp")
-        mms([(run(e), X("BOm"), B("pz"), False, False) for e in range(2)], "DSp")
-        mms([(run(e), B("ZQ"), X("ME%d" % e), False, False) for e in range(2)] + [(D4(_, 1), B("ZQ"), R("S1n"), False, False)], "DSq")
+        mm(D4(sl(0, 4)), X("TL"), R("TR"), True, False, "TRp")
+        mms([(D(e), B("pz"), X("BO4"), False, False) for e in range(2)], "DSp")
+        mms([(D(e), X("ME%d" % e), B("ZQ"), False, e == 1) for e in range(2)], "DSq")
         mms([(Bk(1, sl(0, 8)), B("ZQ"), R("S1h"), True, True), (Bk(0), B("oh2"), X("Ib"), True, True)], "ZLp")
         ts(B("ZL"), Bk(1, sl(0, 8)), 16.0 * MID, OP.add, name="ZL")
         tt(B("pc"), cK, Bk(0), OP.mult, "pc")
-        grp(Bk(2), [(X("Imh"), R("VRh", _, t, ls)), (X("BOh"), B("pc"))], "csv")
-        flex(B("OC"), ind(Ow, B("ZL")), "OC")
-        tt(B("OE"), ind(Ow, B("ZL")), R("VR", _, t, ls), OP.is_equal, "OE")
+        grp(Bk(2), [(X("Imb"), R("VRh", _, RO, ls)), (X("Imb"), R("VRh", _, t, ls)), (X("BOh"), B("pc"))], "csv")
+        was = R("OI") if t == 0 else Ow if h == ORD[0] or not OPT["O2"] else R("O2")
+        flex(B("OC"), ind(was, B("ZL")), "OC")
+        tt(B("OE"), ind(was, B("ZL")), R("VR", _, t, ls), OP.is_equal, "OE")
         tt(B("OE"), B("OE"), Bk(2), OP.mult, "NN")
         if OPT["WV"][h]:
             for a, b, q in pieces("XM"): scan(B("SV", a), R("N16", _, sl(0, a.stop - a.start)), B("CG", a), OP.mult, "WV", OP.add)
@@ -896,13 +727,12 @@ def build(core, T, topo, rank):
         else:
             mms([(A(3), X("Ih"), rows("CG", k), k == 0, k == 15) for k in range(16)], "WS")
             act(B("wp"), A(3), SIGN, bias=-0.5, name="wp")
-        mms([(A(sl(0, 2)), B("wp"), X("BO2"), True, False), (A(1), X("Ib"), X("QN"), False, True)], "WN")
-        act(B("nw"), A(sl(0, 2)), SIGN, bias=R("Zt"), scale=-1.0, name="nw")
-        nw, nq = B("nw", sl(0, 128)), B("nw", sl(128, 256))
-        grp(D4(_, sl(2, 34)), [(nw, X("WA")), (nq, X("WQ"))], "DSw", False)
-        act(B("E0"), D4(_, sl(0, 34)), ABS, scale=4096.0, name="DS")
-        scan(B("E2"), B("E0"), R("E1"), OP.min, "DM")
-        ts(B("FZ"), B("E2", sl(33, None, 34)), -1.0, OP.mult, TOP, OP.add, "FZ")
+        mm(A(0), B("wp"), X("BOb"), name="WN")
+        nw = B("nw")
+        act(nw, A(0), SIGN, bias=R("Zt"), scale=-1.0, name="nw")
+        for e in range(2): tt(B("BK", e), nw, D(e), OP.is_equal, "BK")
+        grp(D4(4, sl(0, 8)), [(B("ZQ"), R("S1h"))] + [(B("BK", e), R("RW", _, e)) for e in range(2)], "FZp")
+        for e in range(2): ts(B("FZ", sl(e, 8, 2)), D4(4, sl(e, 8, 2)), 16.0 * MID, OP.add, Wq(5 + e), OP.min, "FZ")
         SA = lambda at, step=None: R("SA", _, t, sl(128 * h + at, 128 * h + at + 128, step))
         tt(B("t8"), B("nw", sl(0, 128, 16)), B("BV"), OP.mult, "t8")
         tt(SA(2, 16), B("t8"), B("B8"), OP.add, "n8")
@@ -941,6 +771,7 @@ def build(core, T, topo, rank):
         tt(R("F"), R("O", _, sl(t, V_, 12)), R("pD%d" % ORD[0], _, sl(0, 4)), OP.min, "XO")
         tt(R("O", _, sl(t, V_, 12)), R("F"), R("pD%d" % ORD[0], _, sl(4, 8)), OP.max, "O")
         if t == RO - 1: dma(R("yo"), R("O", _, sl(0, V_)), 1572, "st yo", "Y", 128)
+        elif OPT["O2"]: dma(R("O2", _, sl(0, V_)), R("O", _, sl(0, V_)), 1572, "O2", "Y", 128)
 
     for t in range(RO):
         G["t"] = t; later = []
@@ -950,10 +781,11 @@ def build(core, T, topo, rank):
                 G["h"] = h; step(t, h)
             for d, x in later:
                 if d is None: x()
-                else: gcopy(R("WC%d" % d, _, sl(t, V_, 12)), x, "WCg")
+                else: gcopy(R("WC%d" % d, _, sl(t, V_, 12)), x, "WCg" if d else "WCo")
             later.clear()
         G["h"] = None
-    G["ops"][dma(R("yc"), R("WC0", sl(2, 128, 16)), 200, "st yc", "G", 48, accum_op=OP.add, max_dma_last_dim=4096)]["deps"][y0] = True
+    last = G["ops"][dma(R("yc"), R("WC0", sl(2, 128, 16)), 200, "st yc", "G", 48, accum_op=OP.add, max_dma_last_dim=4096)]
+    last["deps"][y0] = True; last["end"] += 1572 / RATE
     return G
 
 

import math
import numpy as np
from concourse.bass import DstId, RemoteDMATransfer
from concourse.mybir import dt, AluOpType, AxisListType, ActivationFunctionType

V_, RO, NR = 3072, 4, 4
MID = 1536
BIG = 65536.0
OP = AluOpType
AF = ActivationFunctionType
COPY, IDENT, RELU, SIGN, ABS = AF.Copy, AF.Identity, AF.Relu, AF.Sign, AF.Abs
D_OF = [1 + t % 3 for t in range(RO)]
ORD = (1, 0)
LO, UP = slice(0, 64), slice(64, 128)
OPT = {"KS": 1, "R3": 0, "WV": [1, 0], "HIP": 0, "SL": "DD", "MG": 4, "O2": 1}
RL, VTW, PV, HQ = 8, 0, 4, 2
CBN = ["Ib", "IB", "ImB", "IB2", "ImB2", "Imb", "Im3072", "Id128", "Imh2", "QB", "K1", "KK", "ONE", "KH", "KL", "BOb", "TL"]
TMP = ["ci", "cg", "cq", "cd", "c32", "cw0", "cw1", "cw2", "x0", "x1", "x2", "x3", "x4", "x5", "x6"]
CHN = ["ME0", "ME1", "I128", "I8192", "Ih", "Imh", "Ih128", "I32h", "I16h", "BOh", "BOm", "BO4"]
CXN = ["NF", "NFa"]
LAND = [(t, d) for t in range(RO - 1) for d in D_OF[t + 1:]]


def _decl():
    s = {}
    f, b, i, u, hf = "float32", "bfloat16", "int32", "uint16", "float16"

    def sb(names, shape, dtype):
        for n in names.split(): s[n] = ("sbuf", shape, dtype)
    sb("OI", [128, V_ + 8], i); sb("O", [128, V_ + 48], f); sb("O2", [128, V_ + 8], f); sb("P WC0 WC1 WC2 WC3", [128, V_], f); sb("XX", [128, 2 * V_], b)
    sb("CI", [128, 192], i); sb("CF F1 F2 F3 MT", [128, 192], f); sb("CA PR", [128, 192], f); sb("H16", [128, 384], hf); sb("CHi", [128, 192], b); sb("C16 L1 L2 L3", [128, 192], hf)
    sb("LD", [128, len(LAND), 256], hf); sb("PL", [128, RO - 1, 256], hf)
    sb("VT", [128, 2, 2048 + VTW], f); sb("SO", [128, 128 // RL, 16 * RL if not VTW else 1], b); sb("VR", [128, RO, 256], f); sb("VRh", [128, RO + 1, 256], b); sb("VC", [128, 8], f)
    sb("XK MN", [128, 2, 2048], hf); sb("CG", [128, 4096], hf); sb("ST", [128, 16, 256], b); sb("SV", [128, 2, 2048], b); sb("N16", [128, 1024], b); sb("VB", [128, RO, 128 // RL], f); sb("WL", [128, 2, 4, 2, 128], hf)
    sb("LA LC LM", [128, 2, 128], u); sb("LB ZL FZ", [128, 2, 8], u)
    sb("aN uS wN pz ZQ", [128, 2, 128], hf); sb("SA", [128, RO, 272], hf); sb("R3 KS", [128, 2, 3, 128], hf); sb("S2", [128, 2, 2, 2, 64], hf)
    sb("hi oh mine nst XB oh2 nw", [128, 2, 128], b); sb("BK", [128, 2, 2, 128], b); sb("SB", [128, 2, 144], b)
    sb("F OC OE", [128, 2, 128], f); sb("BV B8 t8", [128, 2, 8], f); sb("TR", [128, 256], b); sb("RW", [128, 2, 8], b)
    sb("CB", [128, len(CBN), 128], b); sb("CH", [128, len(CHN), 128], hf); sb("CX", [128, len(CXN), 128], f)
    sb("WD", [128, 8, 4, 16], hf); sb("R16", [128, 4, 64], hf); sb("Rd", [128, 3, 8], hf); sb("S1h Rc", [128, 8], hf); sb("S1b", [128, 8], b); sb("U8 pk", [128, 8], f)
    sb("pi", [128, 1], i); sb("ti", [128, 6], i); sb("tf", [128, 6], f); sb("wq", [128, 24], f); sb("zr", [128, 9], f); sb("zi", [128, 2], i); sb("Zt", [128, 1], f)
    for h in range(2):
        for n in "ABC": s["p%s%d" % (n, h)] = ("psum", [128, 512], f)
        s["pD%d" % h] = ("psum", [128, 8, 64], f)
    return s


SCRATCH = _decl()
SEMAPHORES = ["cV", "cS", "cP", "cG", "loc"] + ["d%d" % k for k in range(30)] + ["ar%d_%d" % (t, j) for t in range(RO) for j in range(3)]
CYC, GCY, SCY, PF, PO = 0.83e-3, 1.56, 3.5, 0.6, 0.02
RATE, LAT, FAR, ROW, LINK = 240.0, 1.2, 2.5, 0.05, 25.0
SLOW = [1.25, 1.0]
CUT = {("XK", 1): [(64, "S"), (64, "V")], ("XK", 0): [(64, "S"), (64, "S")], ("XK", 0, 0): [(64, "S"), (32, "S"), (32, "V")], ("CG", 1): [(48, "S"), (48, "V"), (32, "S")], ("CG", 0): [(48, "S"), (48, "V"), (32, "S")],
       ("XM", 1): [(64, "S"), (64, "S")], ("XM", 0): [(48, "S"), (48, "S"), (32, "S")], ("ST", 1): [(64, "V"), (64, "V")], ("ST", 0): [(32, "V")] * 4 if VTW else [(128, "S")]}
INDIRECT = "XK CG XM ST OB XB OC OE scatter".split()
CASES = [(1.0, 1.0, 1.0, 0.125, 0.07, 0.0, 0.65), (1.6, 1.35, 1.35, 0.17, 0.09, 3.0, 0.25)]
SEED = [6, 1, 1, 1, 1]
LOADS = {"ld ctl": -9, "ld sha": -7, "ld hol1": -6, "ld hol0": -4, "ld hol2": -3.9}
START = 9.7
SAME_AS = {"XO": "F", "BD": "F", "FR": "uS", "wp": "hi", "pc": "uS"}
ASG = {n: "S" for n in "R3 RS cK Y2 aN mS cS KS hi XB bm FR PL Pu OC YC WCu H8 dig BD nst".split() + [""]}
FIXED = ["wide1"]
STEPS = [("LA aN", 0, .3, .1, .2), ("XK", .3, .5, 1.8, 4.6), ("XV", .2, .3, -1, -1), ("dec", 3.0, 3.9, 4.7, 5.5), ("Y2 R3", 4.6, 5.1, 5.7, 6.3), ("uT LC", 5.5, 6.4, 6.5, 8.7), ("WCp", 3.9, 5.1, 0, 0), ("WCu", 5.2, 5.2, 0, 0),
         ("CG", 6.4, 7.9, 8.4, 11.2), ("MN", 2.0, 7.0, 5.0, 9.3), ("mL", 2.8, 8.4, 6.1, 11.3), ("mS", 8.2, 8.2, 12.1, 12.1), ("cL", 8.3, 9.1, 11.2, 12.0), ("cS TK KS K1", 9.4, 10.6, 12.2, 13.2), ("D", 10.5, 11.4, 13.2, 13.8),
         ("TC cK", 10.8, 12.2, 13.9, 17.1), ("clip", 11.2, 12.1, 13.7, 14.9), ("pool", 12.0, 12.4, 14.3, 15.5), ("hi hi- F T oh ohT wN", 12.6, 14.4, 15.2, 17.3), ("bR mine LMp LM", 14.5, 16.1, 17.3, 19.5),
         ("bL BD LBp LB XB XBp", 14.6, 16.4, 17.4, 19.6), ("b8 bm", 14.7, 16.0, 18.5, 22.0), ("XM", 16.0, 19.7, 19.3, 22.7), ("MX", 17.2, 19.8, 19.7, 22.9), ("ST", 3.2, 16.4, 9, 15), ("OB", 0, 0, 9.6, 14.7), ("SQ", 0, 0, 14.9, 17.1),
         ("SL", 12.6, 18.0, 17.1, 19.3), ("nst", 17.4, 17.4, 20.5, 20.5), ("FL", 18.3, 20.4, 21.2, 23.4), ("FR", 20.4, 20.4, 23.2, 23.2), ("K2", 20.4, 21.1, 22.3, 24.7), ("F2 T2 oh2 pzp pz ZQp ZQ", 21.1, 23.3, 23.8, 25.9),
         ("TRp", 23.1, 23.1, 25.0, 25.0), ("DSp DSq", 23.6, 24.0, 25.7, 26.2), ("ZLp ZL OC", 23.3, 24.2, 26.1, 27.3), ("pc csv", 23.6, 24.3, 26.6, 27.2), ("OE NN", 24.7, 25.4, 27.0, 27.6), ("WS", 19.5, 22.8, 22.8, 24), ("WV", 18, 21, 21.8, 23.9),
         ("wp WN nw", 22.7, 24.1, 24.1, 25.4), ("BK FZp FZ", 24.2, 25.7, 26.3, 27.6), ("t8 n8 send", 23.9, 25.0, 25.3, 26.6), ("H8 Pp", 24.7, 26.0, 26.6, 27.7), ("DG PL", 25.9, 26.3, 26.2, 26.7), ("Pu", 0, 0, 26.2, 29.0),
         ("scatter", 25.4, 27.2, 27.5, 28.6), ("HL", 27.9, 28.6, 28.6, 29.9), ("ZC zr Z", 0, 0, 27.5, 28.6), ("XO O O2", 0, 0, 30.4, 32.0), ("sendb", 0, 0, 30.3, 30.3), ("WCg WCo", 0, 0, 38, 42)]
PERIOD = 28.7
TRIES = [45000, 8000, 30000, 20000, 20000]
HEATS = [[0.04, 0.003, 0.06, 0.0], [0.05, 0.004, 0.03, 0.3]]
MIX = [0.15, 0.05, 0.6, 0.7, 0.0]
MARK = {}
NOTE = []
EARLY = {"pick": -3.5, "c16": -3, "send0": -3, "dig": -2.9, "PR": -2.8, "P0p": 1, "P0d": 1, "P0": 1, "fillW": 2, "wide1": 3, "flat1": 3, "send0b": 15, "zero": 25, "wide": 30, "flat": 31, "yc0": 32}
FIRST = {("XK", 1, 0): (10.0, "S"), ("XK", 1, 1): (10.0, "V"), ("XK", 0, 0): (11.8, "S"), ("XK", 0, 1): (13.5, "S"), ("XK", 0, 2): (13.5, "V"), ("CG", 1, 0): (14.3, "S"), ("CG", 1, 1): (14.3, "V"), ("CG", 1, 2): (15.3, "S")}
SOON = ["", "next", "late", "fill", "negX"]
WAIT = {}
_ = slice(None)
SIZE = {"float32": 4, "int32": 4}


def bits(ix):
    m = np.zeros(int(ix.max()) + 1, np.uint8); m[ix.reshape(-1)] = 1
    return int.from_bytes(np.packbits(m, bitorder="little").tobytes(), "little")


MASKS = {}


def ref(T, name, *ix):
    ix = ix or (_,)
    if name not in SCRATCH: return (None, T[name][ix], 0, 0, 0, 4, False, None)
    key = (name, repr(ix))
    where, shape, dtype = SCRATCH[name]
    if key not in MASKS:
        fr = np.arange(int(np.prod(shape[1:]))).reshape(shape[1:])[ix[1:]]
        MASKS[key] = (bits(np.arange(128)[ix[0]]), bits(np.asarray(fr)), int(np.asarray(fr).size))
    return (name, T[name][ix]) + MASKS[key] + (SIZE.get(dtype, 2), where == "psum", None)


def ind(win, off): return (win[0], win[1].indirect(off[1]), win[2], win[3], 16 * off[4], win[5], False, off)
def ap(x): return x[1] if isinstance(x, tuple) else x


def add(G, e, use, end, fn, r=(), w=(), key=None, cnt=1, name="", alt=None):
    n = len(G["ops"]); deps = {}
    r = [x for x in r if isinstance(x, tuple)]
    r += [x[7] for x in list(r) + list(w) if x[7] is not None]

    def dep(j, raw):
        if j != n: deps[j] = deps.get(j, False) or raw
    for x in r:
        if x[0] is None: continue
        if x[6]:
            if x[0] in G["bw"]: dep(G["bw"][x[0]], True)
            for j in G["br"].get(x[0], []):
                if G["ops"][j]["eng"] != e or alt or G["ops"][j]["alt"]: dep(j, False)
            continue
        for (a, b, j) in G["wr"].get(x[0], []):
            if a & x[2] and b & x[3]: dep(j, True)
    for x in w:
        if x[0] is None: continue
        if x[6]:
            if x[0] in G["bw"]: dep(G["bw"][x[0]], False)
            for j in G["br"].get(x[0], []): dep(j, False)
            G["bw"][x[0]] = n; G["br"][x[0]] = []
            continue
        for (a, b, j) in G["wr"].get(x[0], []):
            if a & x[2] and b & x[3]: dep(j, True)
        for (a, b, j) in G["rd"].get(x[0], []):
            if a & x[2] and b & x[3]: dep(j, True)
        for k in ("wr", "rd"): G[k][x[0]] = [y for y in G[k].get(x[0], []) if y[0] & ~x[2] or y[1] & ~x[3]]
        G["wr"][x[0]].append((x[2], x[3], n))
    for x in r:
        if x[0] is None: continue
        if x[6]: G["br"].setdefault(x[0], []).append(n)
        else: G["rd"].setdefault(x[0], []).append((x[2], x[3], n))
    c = (G.get("t"), name, G.get("h")); k = G["seen"].get(c, 0); G["seen"][c] = k + 1
    G["ops"].append({"eng": e, "use": use, "end": end, "fn": fn, "deps": deps, "key": key, "cnt": cnt, "name": name, "t": c[0], "h": c[2], "k": k, "alt": alt})
    return n


def swap(o):
    o["alt"], o["eng"], o["use"], o["fn"] = (o["eng"], o["use"], o["fn"]), *o["alt"]; o["end"] = o["use"]


def plan(ops):
    when, total = {}, {}
    for xs, *at in STEPS:
        xs = xs.split()
        for h, a, z in zip(ORD, at[0::2], at[1::2]):
            for k, x in enumerate(xs): when[x, h] = (a + (z - a) * k / len(xs), (z - a) / len(xs))
    for o in ops: total[o["name"], o["h"]] = total.get((o["name"], o["h"]), 0) + 1
    return [when[c][0] + when[c][1] * o["k"] / total[c] if c in when else None for o in ops for c in [(o["name"], o["h"])]]


def tune(ops, order, tries, goal, seed, ring=False):
    n = len(ops); (g0, r0, p0, w0, s0, f0, a0), (g1, r1, p1, w1, s1, f1, a1) = CASES; HEAT = HEATS[ring]
    names = sorted({o["eng"] for o in ops} | {"V", "S"}); m = len(names)
    eng = [0] * n; u0 = [0.0] * n; u1 = [0.0] * n; z0 = [0.0] * n; z1 = [0.0] * n; before = [None] * n; now = [None] * n; nxt = [None] * n
    link = [o.get("link", 0.0) for o in ops]; least = [o.get("least", 0.0) for o in ops]; lap = [o.get("lap", 0) for o in ops]
    rare = [a or b for a, b in zip(link, least)]; both = [i for i, o in enumerate(ops) if o["alt"]]; vec = names.index("V")
    far = [i for i in range(n) if link[i]]; pos = [0] * n
    succ = [[] for o in ops]
    for i, o in enumerate(ops):
        for j, raw, s in o["pre"]: succ[j].append((i, s))
    x = [seed]

    def rnd():
        x[0] = (x[0] * 1103515245 + 12345) % 2147483648
        return x[0] / 2147483648

    def price(i):
        o = ops[i]; e = o["eng"]; eng[i] = names.index(e)
        for u, z, g, r, p, f in ((u0, z0, g0, r0, p0, f0), (u1, z1, g1, r1, p1, f1)):
            u[i] = (o["use"] - 0.06) * g + 0.06 if o["name"] in INDIRECT else o["use"] * (r if e in "VSG" else p if e == "P" else 1.0)
            z[i] = u[i] + o["end"] - o["use"] + (f if e[0] == "N" else 0.0)
        if o["cnt"] == 16 and o["key"]: u1[i] *= SLOW[0]; z1[i] = z1[i] * SLOW[0] + SLOW[1]

    def tie(i):
        b = []; c = []
        for j, raw, s in ops[i]["pre"]:
            d = s + lap[i] - lap[j]
            if d == 0: c.append(j)
            if d > 1: continue
            if eng[j] != eng[i]: b.append((j + n * d, z0[j] + w0, z1[j] + w1))
            elif raw or ops[j]["key"]: b.append((j + n * d, z0[j] + s0, z1[j] + s1))
        before[i] = b; now[i] = c
        nxt[i] = [j for j, s in succ[i] if s + lap[j] - lap[i] == 0]

    def flip(i):
        swap(ops[i]); price(i); tie(i)
        for j, s in succ[i]: tie(j)

    def turn(i, d):
        lap[i] += d; tie(i)
        for j in [j for j, s in succ[i]] + [p[0] for p in ops[i]["pre"]]: tie(j)
    for f in (price, tie):
        for i in range(n): f(i)

    def run(order, old, p=0, was=None):
        A, B = (was[0][:], was[1][:]) if p else ([0.0] * n + old[0], [0.0] * n + old[1])
        F = list(old[2]); H = list(old[3]); wa = wb = -99.0
        if p:
            for i in {eng[i]: i for i in order[:p]}.values(): F[eng[i]] = A[i] + u0[i]; H[eng[i]] = B[i] + u1[i]
            for i in far:
                if pos[i] < p: wa = max(wa, A[i] + link[i]); wb = max(wb, B[i] + link[i])
        for i in order[p:]:
            e = eng[i]; a = F[e]; b = H[e]
            for j, c, d in before[i]:
                c += A[j]
                if c > a: a = c
                d += B[j]
                if d > b: b = d
            if rare[i]:
                a = max(a, least[i]); b = max(b, least[i])
                if link[i]: a = max(a, wa); b = max(b, wb); wa = a + link[i]; wb = b + link[i]
            A[i] = a; B[i] = b; F[e] = a + u0[i]; H[e] = b + u1[i]
        return A, B, F, H

    def worth(r):
        A, B = r[:2]
        if ring: ta = A[goal] - A[n + goal]; tb = B[goal] - B[n + goal]
        else: ta = max([A[i] + z0[i] for i in goal]); tb = max([B[i] + z1[i] for i in goal])
        return a0 * ta + a1 * tb + HEAT[2] * sum(A[:n]) / n + sum([A[i] * w for i, w in marks]) + HEAT[3] * sum([u0[i] for i in both if eng[i] == vec]), ta, tb

    def carry(r):
        a = r[0][goal]; b = r[1][goal]
        return [t - a for t in r[0][:n]], [t - b for t in r[1][:n]], [max(t - a, -9.0) for t in r[2]], [max(t - b, -9.0) for t in r[3]]

    def path(order, r, c):
        A = r[c]; u = (u0, u1)[c]; z = (z0, z1)[c]; last = [-1] * m; prev = [-1] * n; held = []
        for i in order: prev[i] = last[eng[i]]; last[eng[i]] = i
        i = goal if ring else max(goal, key=lambda i: A[i] + z[i])
        while i < n:
            j = prev[i]
            if j >= 0 and A[j] + u[j] >= A[i] - 1e-9: held.append((j, i)); i = j; continue
            i = max([b[0] for b in before[i] if A[b[0]] + b[1 + c] >= A[i] - 1e-9] or [n])
        return held
    marks = [(i, MARK[kind(o)]) for i, o in enumerate(ops) if ring and kind(o) in MARK]
    old = ([-99.0] * n, [-99.0] * n, [0.0] * m, [0.0] * m)
    r = run(order, old)
    for k in range(3 * ring): old = carry(r); r = run(order, old)
    cur = worth(r); best = None; fresh = True
    fixed = [o["name"] in LOADS or o.get("still") for o in ops]
    for it in range(tries + 1):
        if fresh:
            A = r[0]; order = sorted(order, key=lambda i: A[i])
            for p, i in enumerate(order): pos[i] = p
            paths = [path(order, r, c) for c in (0, 1)]; fresh = False
            if best is None or cur[0] < best[0][0]: best = (cur, order, list(lap), [o["eng"] for o in ops], r[0][:n])
        if it == tries: break
        held = paths[rnd() < 0.35]; q = rnd(); undo = None; new = order; a = 0
        if q < MIX[0]:
            c = [i for i in ([i for p in held for i in p] if rnd() < 0.7 else order) if ops[i]["alt"] and not fixed[i]]
            if not c: continue
            i = c[int(rnd() * len(c))]; flip(i); undo = (flip, i); a = pos[i]
            if rnd() < MIX[3]:
                a = max([pos[k] + 1 for k in now[i]] + [0]); b = min([pos[k] for k in nxt[i]] + [n]); new = order[:]
                del new[pos[i]]; new.insert(a + int(rnd() * (b - a)), i)
        elif ring and q < MIX[0] + MIX[1]:
            i = int(rnd() * n); d = 1 if rnd() < 0.5 else -1
            if i == goal or (nxt if d > 0 else now)[i] or abs(lap[i] + d) > 1: continue
            turn(i, d); undo = (turn, i, -d); new = [k for k in order if k != i]
            if d > 0: new.insert(min([new.index(k) for k in nxt[i]] + [int(rnd() * 30)]), i)
            else: new.insert(max([new.index(k) + 1 for k in now[i]] + [n - 1 - int(rnd() * 30)]), i)
        else:
            early = rnd() < 0.5
            if held and q < sum(MIX[:3]):
                j, i = held[int(rnd() * len(held))]; a, b = pos[j], pos[i]
                d = int(rnd() * 25) if rnd() < 0.4 else 0
            else: a = b = int(rnd() * n); d = 1 + int(rnd() * rnd() * 60)
            a, b = (max(0, a - d), b) if early else (a, min(n - 1, b + d))
            seg = order[a:b + 1]; s = {seg[-1 if early else 0]}
            for k in reversed(seg) if early else seg:
                if k in s: s.update((now if early else nxt)[k])
            if any(fixed[k] for k in seg if k in s): continue
            new = order[:a] + [k for k in seg if (k in s) == early] + [k for k in seg if (k in s) != early] + order[b + 1:]
        bar = cur[0] - (HEAT[1] + HEAT[0] * (1 - it / tries) ** 2) * math.log(1 - rnd() * 0.999)
        t = run(new, old, a, r); w = worth(t)
        if ring and w[0] <= bar: t = run(new, carry(t)); w = worth(t)
        if w[0] <= bar:
            r = t; cur = w; order = new; fresh = True
            if ring: old = carry(t); r = run(order, old); cur = worth(r)
        elif undo: undo[0](*undo[1:])
    for o, d, e in zip(ops, best[2], best[3]):
        o["lap"] = d
        if o["eng"] != e: swap(o)
    return best[1], best[4], best[0]


def kind(o): return o["name"], o["h"], o["k"]


def lay(ops, key):
    n = len(ops); succ = [[] for o in ops]
    for i, o in enumerate(ops):
        for j, raw, s in o["pre"]:
            if s + o.get("lap", 0) == ops[j].get("lap", 0): succ[j].append(i)
    left = [len(s) for s in succ]; back = [i for i in range(n) if not left[i]]
    for i in back:
        key[i] = min([key[s] - (1e-5 if key[i] is not None else ops[i]["end"]) for s in succ[i]] + [1e3 if key[i] is None else key[i]])
        for j, raw, s in ops[i]["pre"]:
            if i in succ[j]:
                left[j] -= succ[j].count(i); succ[j] = succ[j] + []
                if left[j] == 0: back.append(j); left[j] = -1
    return sorted(range(n), key=lambda i: key[i])


def pack(ops):
    wake, same = CASES[0][3:5]; at = []; busy = {}
    for o in ops:
        t = max([o["least"]] + [at[j] + (p["end"] + (wake if p["eng"] != o["eng"] else same) if p["eng"] != o["eng"] or raw or p["key"] else p["use"]) for j, raw, s in o["pre"] for p in [ops[j]]])
        b = busy.setdefault(o["eng"], []); k = len(b)
        while k and b[k - 1][1] > t: k -= 1
        while k < len(b) and b[k][0] < t + o["use"] - 1e-9:
            t = max(t, b[k][1]); k += 1
        b.insert(k, (t, t + o["use"])); at.append(t)
    return sorted(range(len(ops)), key=lambda i: at[i])


def ring_of(ops):
    base = {}
    for t in (2, 1):
        for i, o in enumerate(ops):
            if o["t"] == t: base.setdefault(kind(o), i)
    at = {c: k for k, c in enumerate(base)}; ring = []
    for i in base.values():
        o = ops[i]; pre = {}
        for j, raw in o["deps"].items():
            if ops[j]["t"] is not None and kind(ops[j]) in at:
                c = (at[kind(ops[j])], o["t"] - ops[j]["t"]); pre[c] = pre.get(c, False) or raw
        ring.append(dict(o, pre=[(j, raw, s) for (j, s), raw in pre.items()]))
    key = plan(ring)
    for i, o in enumerate(ring):
        if key[i] and key[i] > PERIOD: o["lap"] = 1; key[i] -= PERIOD
    for k in range(3):
        for i, o in enumerate(ring):
            for j, raw, s in o["pre"]:
                if s + o.get("lap", 0) < ring[j].get("lap", 0): o["lap"] = 1; key[i] = None
    key = [PERIOD if k is None and o.get("lap") else k for k, o in zip(key, ring)]
    return ring, lay(ring, key), max(i for i, o in enumerate(ring) if o["name"] == "scatter")


def part(ops, keep, at):
    k = {i: p for p, i in enumerate(keep)}
    return [dict(ops[i], pre=[(k[j], r, 0) for j, r in ops[i]["deps"].items() if j in k], least=max([at[j] + ops[j]["end"] + CASES[0][3] for j in ops[i]["deps"] if j not in k] + [WAIT.get(ops[i]["name"], 0.0)])) for i in keep]


def schedule(G):
    ops = G["ops"]; n = len(ops)
    if not NOTE:
        ring, order, goal = ring_of(ops)
        order, at, (w, per, slow) = tune(ring, order, TRIES[0], goal, SEED[0], True)
        NOTE.append((per, slow, ring, at, order))
    per, slow, ring, at, order = NOTE[0]
    first = min(a + o["lap"] * per for a, o in zip(at, ring) if o["name"] == "LA")
    like = {kind(o): (a + o["lap"] * per - first, o["eng"]) for a, o in zip(at, ring)}
    key = [None] * n
    for i, o in enumerate(ops):
        c = like.get(kind(o))
        if o["t"] is None: key[i] = LOADS.get(o["name"], EARLY.get(o["name"]))
        elif c or kind(o) in FIRST:
            key[i] = START + o["t"] * per + (c or [0])[0]
            if o["t"] == 0 and kind(o) in FIRST: key[i], c = FIRST[kind(o)][0], FIRST[kind(o)]
            if o["t"] == 0 and o["eng"] == "G": key[i] = max(key[i], START - 3)
            if c[1] != o["eng"] and o["alt"]: swap(o)
            if o["t"] == 0 and kind(o) in FIRST: o["alt"] = None

    def mend(keep, at, goal, tries, seed=0, gaps=False):
        sub = part(ops, keep, at); inside = set(keep)
        free = {ops[i]["eng"]: at[i] + ops[i]["use"] for i in sorted(at, key=lambda i: at[i]) if i not in inside and at[i] <= at[keep[0]]} if at else {}
        for o in sub: o["least"] = max(o["least"], at[keep[0]] if at else 0.0, free.get(o["eng"], 0.0))
        order, got, w = tune(sub, pack(sub) if gaps else list(range(len(keep))), tries, [p for p, i in enumerate(keep) if goal(ops[i])], seed)
        for i, o in zip(keep, sub):
            if o["eng"] != ops[i]["eng"]: swap(ops[i])
        return [keep[p] for p in order], dict(zip(keep, got)), w
    lay(part(ops, range(n), None), key)
    key = [min(k, 5 + k / 100) if o["t"] is None and o["name"] in SOON else k for k, o in zip(key, ops)]
    order = lay(part(ops, range(n), None), key)
    cut = max(p for p, i in enumerate(order) if ops[i]["t"] == 0 and ops[i]["name"] == "scatter") + 1
    pre = max(p for p, i in enumerate(order) if ops[i]["t"] == 0 and kind(ops[i])[:2] == ("CG", ORD[0])) + 1
    order[:pre] = mend(order[:pre], None, lambda o: o["name"] == "CG", TRIES[1], SEED[1], True)[0]
    order[:cut] = mend(order[:cut], None, lambda o: o["name"] in ("scatter", "send"), TRIES[2], SEED[2], True)[0]
    order, at, w = mend(order, None, lambda o: True, 0)
    a = min(p for p, i in enumerate(order) if ops[i]["t"] == 0 and ops[i]["name"] == "CG"); z = max(p for p, i in enumerate(order) if ops[i]["t"] == 1 and ops[i]["name"] == "XM") + 1
    for i in order[a:z]: ops[i]["still"] = ops[i]["t"] == 1 and ops[i]["eng"] != "G"
    order[a:z] = mend(order[a:z], at, lambda o: o["t"] == 1 and o["name"] == "XM", TRIES[3], SEED[3])[0]
    order, at, w = mend(order, None, lambda o: True, 0)
    cut = min(p for p, i in enumerate(order) if ops[i]["t"] == RO - 1 and ops[i]["name"] == "LA")
    order[cut:] = mend(order[cut:], at, lambda o: o["key"], TRIES[4], SEED[4])[0]
    return mend(order, None, lambda o: True, 0)


def build(core, T, topo, rank):
    G = {"ops": [], "wr": {}, "rd": {}, "bw": {}, "br": {}, "seen": {}}
    nd = [0]
    R = lambda n, *ix: ref(T, n, *ix)

    def cost(e, o, ins, two=False):
        fix = 0.05 if e == "V" else 0.065
        ts_ = [x for x in [o] + ins if isinstance(x, tuple) and x[4] > 1]
        n = max([1] + [x[4] for x in ts_])
        if o[7] is not None: return fix + max(n, 56) * SCY * CYC
        if any(x[7] is not None for x in ts_): return fix + n * GCY * CYC
        if e == "S": return fix + n * CYC
        if two: return fix + n * CYC * (1.0 if any(x[6] for x in ts_) else 2.0)
        return fix + n * CYC * (0.5 if all(x[5] == 2 for x in ts_) else 1.0)

    def vop(fn, o, ins, name, two=False):
        c = cost("V", o, ins, two)
        return add(G, "V", c, c, lambda Q: [fn(Q["V"])], ins, [o], name=name)

    def tt(o, a, b, op, name=""): return vop(lambda v: v.tensor_tensor(o[1], a[1], b[1], op), o, [a, b], name, True)

    def ts(o, a, s1, op0, s2=None, op1=None, name=""):
        if op1 is None: return vop(lambda v: v.tensor_scalar(o[1], a[1], ap(s1), None, op0), o, [a, s1], name)
        return vop(lambda v: v.tensor_scalar(o[1], a[1], ap(s1), ap(s2), op0, op1), o, [a, s1, s2], name)

    def cpv(o, a, name=""): return vop(lambda v: v.tensor_copy(o[1], a[1]), o, [a], name)
    def scan(o, d0, a, op0, name, op1=OP.max): return vop(lambda v: v.tensor_tensor_scan(o[1], d0[1], a[1], 0.0, op0, op1), o, [d0, a], name)
    def fill(o, v, name="fill"): return vop(lambda q: q.memset(o[1], v), o, [], name)

    def act(o, a, func, bias=0.0, scale=1.0, name=""):
        c = cost("S", o, [a])
        return add(G, "S", c, c, lambda Q: [Q["S"].activation(o[1], a[1], func, bias=ap(bias), scale=ap(scale))], [a, bias, scale], [o], name=name)

    def flex(o, a, name="", bias=None, scale=1.0, only=None):
        fs = lambda Q: Q["S"].activation(o[1], a[1], IDENT if isinstance(bias, tuple) else COPY, bias=ap(bias or 0.0), scale=scale)
        fv = lambda Q: Q["V"].tensor_copy(o[1], a[1]) if bias is None else Q["V"].tensor_scalar(o[1], a[1], scale, ap(bias), OP.mult, OP.add)
        return either(o, [a, bias], fv, fs, name, only)

    def either(o, ins, fv, fs, name, only=None):
        ways = {e: (e, cost(e, o, ins), lambda Q, f=f: [f(Q)]) for e, f in (("V", fv), ("S", fs))}
        e = only or ASG.get(name, "V")
        return add(G, e, ways[e][1], ways[e][1], ways[e][2], ins, [o], name=name, alt=ways["VS".replace(e, "")] if name not in FIXED else None)

    def relu(o, a, bias, scale, name):
        fv = (lambda Q: Q["V"].tensor_scalar(o[1], a[1], bias, 0.0, OP.add, OP.max)) if scale == 1.0 else (lambda Q: Q["V"].tensor_scalar(o[1], a[1], 0.5, None, OP.is_lt))
        return either(o, [a], fv, lambda Q: Q["S"].activation(o[1], a[1], RELU, bias=bias, scale=scale), name)

    def mms(calls, name):
        for k in range(0, len(calls), OPT["MG"]):
            cs = calls[k:k + OPT["MG"]]
            c = sum(max(min(64, l[4]), rh[4]) * CYC * PF * (4.0 if l[5] == 4 else 1.0) + PO for o, l, rh, a, z in cs)
            add(G, "P", c, c, lambda Q, cs=cs: [Q["P"].matmul(o[1], l[1], rh[1], a, z) for o, l, rh, a, z in cs], [x for y in cs for x in y[1:3]], [y[0] for y in cs], cnt=len(cs), name=name)

    def mm(o, l, rh, start=True, stop=True, name=""): mms([(o, l, rh, start, stop)], name)
    def grp(o, terms, name, start=True, stop=True): mms([(o, x[0], x[1], start and j == 0, stop and j == len(terms) - 1) for j, x in enumerate(terms)], name)

    def iota(o, pat, base, cm=0, name=""):
        c = 0.14 + 2 * o[4] * CYC
        flag = {} if o[0] == "pi" else {"allow_small_or_imprecise_dtypes": True}
        return add(G, "G", c, c, lambda Q: [Q["G"].iota(o[1], pat, base, cm, **flag)], [], [o], name=name)

    def gcopy(o, a, name):
        c = 0.17 + 2 * o[4] * CYC
        return add(G, "G", c, c, lambda Q: [Q["G"].affine_select(o[1], a[1], [[0, o[4]]], OP.is_ge, 0.0, 0, 0)], [a], [o], name=name)

    def dma(o, a, kb, name, q="Y", rows=64, **kw):
        k = "d%d" % nd[0]; nd[0] += 1
        c = kb / RATE + rows / 16 * ROW
        return add(G, q, c if q == "Y" else 0.15, LAT + c, lambda Q: Q[q].dma_start(o[1], a[1], **kw).then_inc(T.sem[k], 16), [a], [o], key=k, cnt=16, name=name)

    def send(ds, src, land, sem, kb, name):
        dsts = [T.cores[(rank - d) % NR] for d in ds]
        for x in dsts: assert topo.may_write(core, x) and topo.mask(core, x) == topo.mask(core, dsts[0])

        def fn(Q):
            if len(ds) == 1:
                rid, pid = topo.addr(dsts[0])[:2]
                Q["G"].remote_dma(out_ap=land(ds[0])[1], in_ap=src[1], remote_sem=T.sem[sem], local_sem=T.sem.loc, pid=pid, routing_id=rid, dma_engine_mask=topo.mask(core, dsts[0]))
            else:
                ids = [DstId(rid=topo.addr(x)[0], pnc=topo.addr(x)[1]) for x in dsts]
                Q["G"].remote_dma_fused([RemoteDMATransfer(dst_ids=ids, dma_engine_mask=topo.mask(core, dsts[0]), remote_sem=T.sem[sem], srcs=[src[1]], dsts=[land(d)[1] for d in ds])], local_sem=T.sem.loc)
        s = add(G, "G", 1.0, 1.0, fn, [src], [], key="loc", cnt=len(topo.engines(core, dsts[0])), name=name)
        G["ops"][s]["link"] = kb * len(ds) / LINK
        i = add(G, "N" + sem, 0.0, FAR + kb * len(ds) / LINK, None, [], [land(d) for d in ds], key=sem, cnt=sum(len(topo.engines(T.cores[(rank + d) % NR], core)) for d in ds), name="arrive")
        G["ops"][i]["deps"][s] = True
        return s

    def sl(a, b=None, c=None): return slice(a, b, c)

    def X(n, w=128):
        if n in TMP: return R("ST", _, TMP.index(n) // 2, sl(128 * (TMP.index(n) % 2), 128 * (TMP.index(n) % 2) + w))
        for buf, names in (("CB", CBN), ("CH", CHN), ("CX", CXN)):
            if n in names: return R(buf, _, names.index(n))

    half = list(enumerate((LO, UP)))
    col192 = lambda n, x: R(n, _, sl(192 * x, 192 * x + 192))
    dma(R("CI"), R("ctl"), 98, "ld ctl", "Y", 128)
    fill(R("SA"), 0.0)
    iota(R("pi"), [[1, 1]], 0, 1)
    cpv(R("ti", _, sl(0, 1)), R("pi"))
    for o, k, op in ((1, 4, OP.arith_shift_right), (2, 15, OP.bitwise_and), (3, 63, OP.bitwise_and)): ts(R("ti", _, sl(o, o + 1)), R("pi"), k, op)
    for o, k in ((4, 6), (5, 3)): ts(R("ti", _, sl(o, o + 1)), R("pi"), 4, OP.arith_shift_right, k, OP.bitwise_and)
    cpv(R("tf"), R("ti"))
    F = lambda k: R("tf", _, sl(k, k + 1))
    Wq = lambda k: R("wq", _, sl(k, k + 1))
    ts(R("C16"), R("CI"), -float(MID), OP.add, name="c16")
    s2 = send(D_OF[:1], R("C16"), lambda d: R("L%d" % d), "ar0_0", 49, "send0")
    send(D_OF[1:3], R("C16"), lambda d: R("L%d" % d), "ar0_1", 49, "send0b")
    ts(R("CHi"), R("CI"), 1 / 64, OP.mult, 168.0, OP.add, "dig")
    ts(R("CF"), R("CI"), -float(MID), OP.add, name="dig")
    flex(col192("CA", 0), R("CF"), "dig", bias=96.0, scale=1 / 128)
    flex(col192("PR", 0), R("CHi"), "dig", bias=0.0, scale=-0.5)
    flex(col192("H16", 1), R("CHi"), "dig", bias=-1.5, scale=1 / 128)
    tt(col192("H16", 0), col192("CA", 0), col192("PR", 0), OP.add, "PR")
    dma(R("XX", _, sl(0, V_)), R("sha"), 786, "ld sha", "Y", 128)
    for c in range(0, V_, 768): flex(R("XX", _, sl(V_ + c, V_ + c + 768)), R("XX", _, sl(c, c + 768)), "negX", bias=0.0, scale=-1.0, only="S" if c < MID else "V")
    for h in ORD:
        cs = sl(MID * h, MID * h + MID)
        m = 1 if h == ORD[0] else HQ
        for c in range(m):
            a = MID * h + MID // m * c; cs = sl(a, a + MID // m)
            dma(R("OI", _, cs), R("hol", _, cs), 786 / m, "ld hol%d" % (h + 2 * c), "Y", 128)
            cpv(R("LA", _, h, sl(128 // m * c, 128 // m * (c + 1))), R("OI", _, sl(a, a + MID // m, 12)), "LA")
        for c in range(MID * h, MID * h + MID, 384): flex(R("O", _, sl(c, c + 384)), R("OI", _, sl(c, c + 384)), "O32", only="S")
    fill(R("O", _, sl(V_, V_ + 48)), 0.0); fill(R("O2", _, sl(V_, V_ + 8)), 0.0); fill(R("OI", _, sl(V_, V_ + 8)), 0)
    for d in (1, 2, 3):
        if d == D_OF[0]:
            for c in range(3): flex(R("WC%d" % d, _, sl(1024 * c, 1024 * c + 1024)), R("SA", _, _, sl(0, 256)), "fillW", only="S")
        else:
            for c in range(4): G["ops"][iota(R("WC%d" % d, _, sl(768 * c, 768 * c + 768)), [[0, 768]], 0, name="zero")]["deps"][s2] = False
        flex(R("F%d" % d), R("L%d" % d), "wide1" if d == D_OF[0] else "wide")
        dma(R("WC%d" % d, sl(2, 128, 16)), R("F%d" % d), 98, "flat1" if d == D_OF[0] else "flat", "S" if d == D_OF[0] else "Y", 128)
    for n, pat, base in (("ci", [[1, 128]], 0), ("cg", [[1, 8], [0, 16]], 0), ("cq", [[0, 8], [1, 16]], 0)): iota(X(n), pat, base)
    late = [iota(X(n), pat, base, name="late") for n, pat, base in (("ONE", [[0, 128]], 1), ("KH", [[0, 128]], MID + int(1.5 * BIG)), ("KL", [[0, 128]], MID - int(1.5 * BIG)), ("c32", [[0, 4], [1, 32]], 0))]
    late += [iota(R("SB"), [[0, 288]], 0, name="late"), iota(R("MT"), [[0, 192]], MID, name="late"), iota(R("VB"), [[-1, RO], [-12 * RL, 128 // RL]], 0, name="next")]
    late += [iota(X(n), pat, base, name="next") for n, pat, base in (("K1", [[0, 8], [-1, 16]], 15), ("cw0", [[2, 4], [0, 32]], 0), ("cw1", [[2, 4], [0, 32]], 1))]
    late += [iota(X("x0", 256), [[-32, 2], [0, 8], [-2, 16]], 1, name="next")]
    late += [iota(R("pk", _, sl(0, 4)), [[2, 4]], -15, name="next"), iota(R("VC"), [[1, 4], [MID, 2]], -MID, 12, name="next")]
    for i in late: G["ops"][i]["deps"][s2] = False
    fill(R("Zt"), 1.0)
    if any(OPT["WV"]):
        G["ops"][iota(R("N16"), [[0, 1024]], 1, name="zero")]["deps"][s2] = False
        fill(R("N16", _, sl(0, None, 16)), 0.0, "zero")
    c8 = X("ci", 8)
    ts(X("Ib"), X("ci"), F(0), OP.is_equal)
    for n, s in (("I128", 128), ("I8192", 8192), ("IB", BIG), ("ImB", -BIG), ("IB2", BIG / 2), ("ImB2", -BIG / 2), ("Imb", -1), ("Im3072", -V_), ("Id128", 1 / 128), ("Imh2", -0.5), ("Ih", 1), ("Imh", -1),
                 ("Ih128", 1 / 128), ("I32h", 32), ("I16h", 16)):
        flex(X(n), X("Ib"), bias=0.0, scale=float(s))
    pick = lambda j, a, z: R("MN", _, j // 8, sl(130 * (j % 8) + a, 130 * (j % 8) + z))
    iota(X("x6", 144), [[16, 9], [1000, 16]], -16)
    for j in range(16): ts(pick(j, 0, 129), R("ST", _, 7, sl(15, 144)), float(j), OP.add, F(0), OP.is_equal, "pick")
    for c in range(8):
        n = "p%s%d" % ("ACBD"[c // 2], c % 2); cs = sl(384 * c, 384 * c + 384)
        b = lambda a, z: R(n, _, sl(a // 64, z // 64)) if n[1] == "D" else R(n, _, sl(a, z))
        digits = [(b(192 * e, 192 * e + 192), pick(2 * c + e, 1 - x, 129 - x), col192("H16", x), c < PV and x == 0, x == 1 and (c < PV or e == 1)) for e in range(2) for x in range(2)]
        if c >= PV: mm(b(0, 384), X("Ib"), R("XX", _, cs), True, False, "P0p")
        mms(digits, "P0d")
        if c < PV: tt(R("P", _, cs), R("XX", _, cs), b(0, 384), OP.add, "P0")
        else: flex(R("P", _, cs), b(0, 384), "P0", only="S")
    ts(X("BOb"), X("cg"), F(1), OP.is_equal)
    for n, s in (("BOh", 1.0), ("BOm", -1.0), ("BO4", 4.0)): flex(X(n), X("BOb"), bias=0.0, scale=s)
    ts(X("QB"), X("cq"), F(2), OP.is_equal, BIG, OP.mult)
    for e in range(2): ts(X("ME%d" % e), X("cw%d" % e), F(1), OP.is_equal, 4.0, OP.mult)
    x0, low = X("x0", 256), 4.0 * (32 * MID - V_)
    ts(Wq(12), F(0), 32.0, OP.is_equal); ts(X("TL"), X("c32"), F(0), OP.is_equal, Wq(12), OP.max)
    ts(Wq(13), Wq(12), low + 1, OP.mult, -1.0, OP.add); ts(Wq(14), Wq(12), low - 2, OP.mult, 2.0, OP.add); ts(Wq(19), F(0), 2.0, OP.mult)
    ts(x0, x0, Wq(19), OP.add, Wq(13), OP.max); ts(R("TR"), x0, Wq(14), OP.min)
    ts(Wq(15), F(4), 1.0, OP.add)
    for e, w in enumerate((F(4), Wq(15))): ts(R("RW", _, e), c8, w, OP.is_equal, BIG, OP.mult)
    for e in range(2): ts(Wq(5 + e), F(2), V_ + 1.0 + 16 * e, OP.add)
    ts(R("VC"), R("VC"), 0.5, OP.mult)
    act(X("NF"), X("cq"), SIGN); flex(X("NFa"), X("NF"), bias=-2.0 ** 30, scale=2.0 ** 30)
    ts(R("wq", _, sl(0, 3)), X("ci", 3), F(2), OP.is_equal)
    ts(Wq(3), Wq(1), -1 / 64, OP.mult, Wq(0), OP.add); ts(Wq(3), Wq(3), 96.0, OP.mult)
    ts(Wq(4), F(0), 64.0, OP.is_lt, 4095.0, OP.mult); ts(Wq(4), Wq(4), 1.0, OP.add)
    ts(R("wq", _, sl(10, 12)), X("ci", 2), F(0), OP.is_equal)
    for n in ("S1h", "S1b", "U8"): ts(R(n), c8, F(1), OP.is_equal)
    ts(R("Rc"), c8, F(1), OP.is_equal, Wq(2), OP.mult)
    for j, w in ((0, Wq(0)), (1, Wq(1)), (2, 1.0)): ts(R("Rd", _, j), c8, F(1), OP.is_equal, w, OP.mult)
    y = lambda k: R("ST", _, 8 + k, sl(0, 128))
    iota(y(0), [[1, 8], [1, 16]], 1, name="next")
    ts(Wq(16), F(0), 64.0, OP.is_lt, -4096.0, OP.mult); ts(Wq(17), Wq(16), -1.0, OP.mult, Wq(4), OP.add); ts(Wq(18), F(2), 16.0, OP.add)
    ts(y(1), y(0), F(2), OP.is_equal, Wq(4), OP.mult); ts(y(2), y(0), Wq(18), OP.is_equal, Wq(16), OP.mult); tt(y(1), y(1), y(2), OP.add)
    ts(y(2), y(0), 16.0, OP.is_ge, Wq(17), OP.mult); ts(y(2), y(2), Wq(16), OP.add); ts(y(3), X("cq"), F(2), OP.is_equal); tt(y(2), y(2), y(3), OP.mult); tt(y(1), y(1), y(2), OP.add)
    ts(R("wq", _, sl(20, 24)), X("ci", 4), F(5), OP.is_equal)
    for g in range(4): ts(R("WD", _, _, g), y(1), Wq(20 + g), OP.mult)
    pk = R("pk", _, sl(0, 4)); pw = R("pk", _, sl(4, 8))
    ts(Wq(7), F(0), 64.0, OP.is_ge); ts(pk, pk, Wq(7), OP.add)
    ts(pw, pk, F(2), OP.add, 0.0, OP.is_ge); tt(pk, pk, pw, OP.mult)
    ts(Wq(9), R("pk", _, sl(3, 4)), -8.0, OP.is_equal, -99.0, OP.mult); ts(R("pk", _, sl(3, 4)), R("pk", _, sl(3, 4)), Wq(9), OP.add)
    ts(pk, pk, F(3), OP.add)
    for i in range(4): ts(R("R16", _, i), X("ci", 64), R("pk", _, sl(i, i + 1)), OP.is_equal, 16.0, OP.mult)
    ts(Wq(11), Wq(11), 16.0 * MID, OP.mult, Wq(10), OP.subtract); ts(Wq(10), Wq(10), 15.0, OP.mult)
    ts(X("KK"), X("cq"), Wq(11), OP.mult, Wq(10), OP.add)
    dma(R("WC0", sl(2, 128, 16)), R("CF"), 98, "flat", "Y", 128)
    y0 = dma(R("yc"), R("MT"), 98, "yc0", "Y", 128)

    def firms(t):
        iota(R("VR", _, t), [[12, 256]], t, name="VR")
        if t == 0: iota(R("VRh", _, RO), [[192, 16], [0, 16]], -MID, name="VR")
        iota(R("VRh", _, t), [[0, 16], [12, 16]], t, name="VRh")
        for h in ORD:
            at = 0
            for n, q in CUT["ST", h]:
                if q == "V":
                    for c in range(at, at + n, 32): iota(R("VT", _, t % 2, sl(VTW * h + 16 * c, VTW * h + 16 * c + 512)), [[12, 32], [0, 16]], t + MID * h + 12 * c, name="VT")
                at += n

    def front(t, h):
        B = lambda n, *ix: R(n, _, sl(2048 * h + ix[0].start, 2048 * h + (ix[0].stop or 2048), ix[0].step)) if n == "CG" else R(SAME_AS.get(n, n), _, h, *ix)
        def bank(n, h=h):
            def at(p=sl(0, 4), c=sl(0, None), pp=_):
                a, z = (p, p + 1) if isinstance(p, int) else (p.start or 0, p.stop or 4)
                return R("p%s%d" % (n, h), pp, sl(128 * a + c.start, 128 * a + c.stop if c.stop else 128 * z, c.step))
            return at
        A, Bk, C, D4 = bank("A"), bank("B"), bank("C"), lambda *ix: R("pD%d" % h, _, *ix)
        D = lambda p, *ix: D4(sl(2 * p, 2 * p + 2), *ix)
        col = lambda b, s, k: b(s, sl(k, None, 16))
        rows = lambda n, k, m=16: R(n, _, _, sl(k, None, m)) if n == "SO" else B(n, sl(k, None, m))
        O, P, XX, WC = "O", "P", "XX", "WC%d" % D_OF[t]
        hs = sl(MID * h + t, MID * h + MID, 12); ls = sl(128 * h, 128 * h + 128)
        Xw, Ow = R(XX, _, sl(0, V_)), R(O)

        def pieces(n):
            at = 0
            for m, q in CUT.get((n, h, t), CUT[n, h]):
                yield sl(16 * at, 16 * (at + m)), sl(at, at + m), q
                at += m

        def sums(b, p, n, w, name, m=16): mms([(col(b, p, k), rows(n, k), w, True, True) for k in sorted(range(16), key=lambda k: k % m)], name)

        def stakes(b, p):
            for a, c, q in pieces("ST"):
                if q == "V": tt(B("SV", a), ind(Ow if t else R("OI"), B("LA", c)), R("VT", _, t % 2, sl(VTW * h + a.start, VTW * h + a.stop)), OP.is_equal, "ST")
                else:
                    for u in range(128 // RL): act(R("SO", _, u), ind(Ow if t else R("OI"), B("LA", sl(RL * u, RL * u + RL))), IDENT, bias=R("VB", _, t, sl(u, u + 1)), name="OB")
                    for j in range(RL):
                        x = R("SO", _, _, sl(16 * j, 16 * j + 16))
                        ts(x, x, 12.0 * j, OP.is_equal, name="SQ")
            sums(b, p, "SO" if q == "S" else "SV", R("S1b"), "SL")
            relu(B("nst"), b(p), 1.0, -1.0, "nst")
        if t: cpv(B("LA"), R(O, _, hs), "LA")
        for a, b, q in pieces("XK"): flex(B("XK", a), ind(R(P), B("LA", b)), "XK", only=q)
        sums(A, sl(0, 3), "XK", R("Rd"), "dec")
        flex(B("KS", sl(0, 2)), A(sl(0, 2)), "Y2")
        flex(B("R3"), A(sl(0, 3)), "R3", bias=-float(MID), scale=-1.0)
        grp(C(0), [(B("KS", 0), X("I128")), (B("KS", 1), X("I8192")), (B("R3", 0), X("I128")), (B("R3", 1), X("I8192"))], "uT")
        ts(B("LC"), C(0), MID * 8321.0, OP.add, name="LC")
        if t and h == ORD[0]:
            w = bank("C", ORD[1])
            for e in ORD: mm(w(2 + e), R("LD", _, LAND.index((t - 1, D_OF[t])), sl(128 * e, 128 * e + 128)), X("Ih"), name="WCp")
            flex(R(WC, _, sl(t - 1, V_, 12)), w(sl(2, 4)), "WCu")
        for a, b, q in pieces("CG"): flex(B("CG", a), ind(R(WC), B("LC", b)), "CG", only=q)
        if t: flex(B("aN"), R(O, _, hs), "aN", bias=-float(MID))
        else: ts(B("aN"), R("OI", _, hs), -float(MID), OP.add, name="aN")
        mms([(Bk(_, sl(j, None, 4)), X("Ib"), R(XX, _, hs), True, True) for j in range(4)], "XV")
        for k in range(4): tt(rows("MN", k, 4), rows("XK", k, 4), Bk(), OP.min, "MN")
        sums(D, 1, "MN", R("S1h"), "mL", 4)
        flex(B("S2", _, 1), D(1), "mS", bias=float(MID))
        if OPT["SL"][h] == "E": stakes(D, 2)
        sums(C, 1, "CG", R("Rc"), "cL")
        flex(B("S2", _, 0), C(1), "cS")
        if OPT["KS"]:
            mms([(A(1 + a), B("S2", a), X("Ih"), True, True) for a in range(2)], "TK")
            flex(B("KS", sl(1, 3)), A(sl(1, 3)), "KS")
            mms([(A(0, pp=pp), B("S2", a, 0), X("Ih"), True, True) for a, pp in half], "TC")
            flex(B("KS", 0), A(0), "cK")
        else:
            mms([(A(1 + a), B("S2", a), X("Ih"), True, True) for a in range(2)] + [(A(0, pp=pp), B("S2", a, 0), X("Ih"), True, True) for a, pp in half], "TK")
            flex(B("KS"), A(sl(0, 3)), "KS")
        if OPT["SL"][h] == "A": stakes(A, 3)
        cK = B("KS", 0)
        key = C(0)
        grp(key, [(X("ONE"), X("KK")), (X("I16h"), B("S2", _, 1))], "K1", True, False)
        for i in range(2):
            b = (Bk, lambda *ix: D4(sl(2 * ix[0].start, 2 * ix[0].stop)) if ix else D4())[i]
            mms([(b(sl(2 * e, 2 * e + 2)), R("WD", _, sl(4 * i + 2 * e, 4 * i + 2 * e + 2)), B("KS", sl(1, 3)), True, True) for e in range(2)], "D")
            ts(B("WL", sl(2 * i, 2 * i + 2)), b(), float(MID), OP.max, MID + 4096.0, OP.min, "clip")
            mms([(C(0, sl(64 * a, 64 * a + 64)), B("WL", 2 * i + e, a), R("R16", _, 2 * i + e), False, i + e + a == 3) for e in range(2) for a in range(2)], "pool")
        flex(B("hi"), key, "hi", bias=2.0 ** 23 - 32767)
        if OPT["HIP"]: mm(key, X("Imb"), B("hi"), False, True, "hi-")
        else: tt(key, key, B("hi"), OP.subtract, "hi-")
        scan(B("F"), X("NFa"), key, OP.add, "F")
        back = lambda p: R("pC%d" % h, _, sl(128 * p + 127, 128 * p - 1 if p else None, -1))
        scan(back(2), X("NFa"), back(0), OP.add, "T")
        tt(B("oh"), B("F"), C(2), OP.is_equal, "oh")
        mm(A(0), B("oh"), X("Ib"), name="ohT")
        tt(B("wN"), cK, A(0), OP.mult, "wN")
        mm(A(1), X("BOh"), B("wN"), name="bR")
        grp(Bk(0), [(X("Ib"), X("QB")), (B("wN"), X("BOh"))], "bL")
        tt(B("mine"), cK, A(1), OP.is_equal, "mine")
        grp(A(2), [(X("Ih"), B("aN")), (X("Im3072"), B("mine"))], "LMp")
        ts(B("LM"), A(2), float(MID + V_), OP.add, name="LM")
        for a, b, q in pieces("XM"): flex(B("CG", a), ind(R(XX), B("LM", b)), "XM", only=q)
        relu(B("BD"), Bk(0), MID + 1 - BIG, 1.0, "BD")
        mm(Bk(1, sl(0, 8)), B("BD"), R("U8"), name="LBp")
        ts(B("LB"), Bk(1, sl(0, 8)), -1.0, OP.add, name="LB")
        flex(B("XB"), ind(Xw, B("LB")), "XB")
        mm(C(1, sl(0, 8)), B("wN"), R("S1h"), name="b8")
        vc = R("VC", _, sl(2 * t + h, 2 * t + h + 1))
        flex(B("B8"), C(1, sl(0, 8)), "bm", bias=vc, scale=0.5)
        flex(B("BV"), C(1, sl(0, 8)), "bm", bias=vc, scale=-0.5)
        mms([(Bk(_, sl(j, None, 4)), X("Ib"), B("XB"), True, True) for j in range(4)], "XBp")
        for k in range(4): tt(rows("MN", k, 4), rows("XK", k, 4), Bk(), OP.max, "MX")
        if OPT["SL"][h] == "D": stakes(D, 1)
        sums(D, 2, "MN", R("S1h"), "FL", 4)
        flex(B("FR"), D(2), "FR", bias=float(MID))
        grp(key, [(X("Ib"), X("K1")), (X("I16h"), B("R3", 2)), (B("mine"), X("ImB")), (X("ImB"), B("nst")), (X("I32h"), B("FR"))], "K2")
        scan(B("F"), X("NF"), key, OP.mult, "F2")
        scan(back(2), X("NFa"), back(0), OP.add, "T2")
        tt(B("oh2"), B("F"), C(2), OP.is_equal, "oh2")
        grp(Bk(3), [(X("Imh"), B("aN")), (B("oh2"), X("IB"))], "pzp")
        ts(B("pz"), Bk(3), -BIG, OP.add, -float(MID), OP.max, "pz")
        grp(Bk(3), [(X("Ib"), X("QB")), (B("pz"), X("BOm"))], "ZQp")
        ts(B("ZQ"), Bk(3), V_ - 17.0 * MID - BIG, OP.add, -float(MID), OP.max, "ZQ")
        mm(D4(sl(0, 4)), X("TL"), R("TR"), True, False, "TRp")
        mms([(D(e), B("pz"), X("BO4"), False, False) for e in range(2)], "DSp")
        mms([(D(e), X("ME%d" % e), B("ZQ"), False, e == 1) for e in range(2)], "DSq")
        mms([(Bk(1, sl(0, 8)), B("ZQ"), R("S1h"), True, True), (Bk(0), B("oh2"), X("Ib"), True, True)], "ZLp")
        ts(B("ZL"), Bk(1, sl(0, 8)), 16.0 * MID, OP.add, name="ZL")
        tt(B("pc"), cK, Bk(0), OP.mult, "pc")
        grp(Bk(2), [(X("Imb"), R("VRh", _, RO, ls)), (X("Imb"), R("VRh", _, t, ls)), (X("BOh"), B("pc"))], "csv")
        was = R("OI") if t == 0 else Ow if h == ORD[0] or not OPT["O2"] else R("O2")
        flex(B("OC"), ind(was, B("ZL")), "OC")
        tt(B("OE"), ind(was, B("ZL")), R("VR", _, t, ls), OP.is_equal, "OE")
        tt(B("OE"), B("OE"), Bk(2), OP.mult, "NN")
        if OPT["WV"][h]:
            for a, b, q in pieces("XM"): scan(B("SV", a), R("N16", _, sl(0, a.stop - a.start)), B("CG", a), OP.mult, "WV", OP.add)
            act(B("wp"), rows("SV", 15), SIGN, bias=-0.5, name="wp")
        else:
            mms([(A(3), X("Ih"), rows("CG", k), k == 0, k == 15) for k in range(16)], "WS")
            act(B("wp"), A(3), SIGN, bias=-0.5, name="wp")
        mm(A(0), B("wp"), X("BOb"), name="WN")
        nw = B("nw")
        act(nw, A(0), SIGN, bias=R("Zt"), scale=-1.0, name="nw")
        for e in range(2): tt(B("BK", e), nw, D(e), OP.is_equal, "BK")
        grp(D4(4, sl(0, 8)), [(B("ZQ"), R("S1h"))] + [(B("BK", e), R("RW", _, e)) for e in range(2)], "FZp")
        for e in range(2): ts(B("FZ", sl(e, 8, 2)), D4(4, sl(e, 8, 2)), 16.0 * MID, OP.add, Wq(5 + e), OP.min, "FZ")
        SA = lambda at, step=None: R("SA", _, t, sl(128 * h + at, 128 * h + at + 128, step))
        tt(B("t8"), B("nw", sl(0, 128, 16)), B("BV"), OP.mult, "t8")
        tt(SA(2, 16), B("t8"), B("B8"), OP.add, "n8")
        own = R("WC0", _, hs)
        if t < RO - 1:
            ds = D_OF[t + 1:]
            send(ds[:1], SA(0), lambda d: R("LD", _, LAND.index((t, d)), ls), "ar%d_%d" % (t + 1, 2 * h), 32, "send")
            flex(B("SB", sl(1, 129, 16)), SA(2, 16), "H8", bias=192.0, scale=1 / 64)
            grp(A(3), [(X("Ib"), R(XX, _, hs)), (SA(2), X("Ih128")), (B("SB", sl(0, 128)), X("Id128")), (B("SB", sl(1, 129)), X("Imh2"))], "Pp")
            later.append((None, lambda: flex(R(P, _, hs), A(3), "Pu", bias=Wq(3))))
            mm(C(2), SA(0), X("Ih"), name="DG")
            flex(R("PL", _, t, ls), C(2), "PL")
            if h == ORD[1]:
                land = lambda d: R("LD", _, LAND.index((t, d)))
                if ds[1:]: send(ds[1:], R("PL", _, t), land, "ar%d_1" % (t + 1), 64, "sendb")
                later.extend((d, land(d)) for d in ds[1:])
                later.append((0, R("PL", _, t)))
        else:
            mm(A(2), SA(0), X("Ih"), name="DG")
            flex(own, A(2), "YC")
        if t < RO - 1 and h == ORD[1]:
            z = C(3, sl(0, 8))
            grp(z, [(X("ONE"), R("nw", _, e, sl(0, 128, 16))) for e in ORD], "ZC")
            add(G, "S", 0.1, 0.1, lambda Q: [Q["S"].activation(T.zr[:, 0:8], z[1], COPY, bias=256.0, accum_out=T.zr[:, 8:9])], [z], [R("zr")], name="zr")
            cpv(R("zi", _, sl(0, 1)), R("zr", _, sl(8, 9)), "Z")
            ts(R("zi", _, sl(1, 2)), R("zi", _, sl(0, 1)), 2, OP.bitwise_and, name="Z")
            ts(R("Zt"), R("zi", _, sl(1, 2)), 1.0, OP.add, name="Z")
        for o, kn, a, b in ((h, "KH", "ImB", "IB2"), (2 + h, "KL", "IB", "ImB2")): grp(R("pD%d" % ORD[0], _, sl(2 * o, 2 * o + 2)), [(X("Ib"), X(kn)), (X("BOh"), B("wN")), (nw, X(b)), (B("oh2"), X(a))], "HL")

    def sell(t, h):
        B = lambda n, *ix: R(n, _, h, *ix)
        for u in range(3, -1, -1): tt(ind(R("O"), B("FZ", sl(2 * u, 2 * u + 2))), B("OC", sl(32 * u, 32 * u + 32)), B("OE", sl(32 * u, 32 * u + 32)), OP.add, "scatter")

    def own(t, h):
        if h == ORD[0]: return
        tt(R("F"), R("O", _, sl(t, V_, 12)), R("pD%d" % ORD[0], _, sl(0, 4)), OP.min, "XO")
        tt(R("O", _, sl(t, V_, 12)), R("F"), R("pD%d" % ORD[0], _, sl(4, 8)), OP.max, "O")
        if t == RO - 1: dma(R("yo"), R("O", _, sl(0, V_)), 1572, "st yo", "Y", 128)
        elif OPT["O2"]: dma(R("O2", _, sl(0, V_)), R("O", _, sl(0, V_)), 1572, "O2", "Y", 128)

    for t in range(RO):
        G["t"] = t; later = []
        firms(t)
        for step in (front, sell, own):
            for h in ORD:
                G["h"] = h; step(t, h)
            for d, x in later:
                if d is None: x()
                else: gcopy(R("WC%d" % d, _, sl(t, V_, 12)), x, "WCg" if d else "WCo")
            later.clear()
        G["h"] = None
    last = G["ops"][dma(R("yc"), R("WC0", sl(2, 128, 16)), 200, "st yc", "G", 48, accum_op=OP.add, max_dma_last_dim=4096)]
    last["deps"][y0] = True; last["end"] += 1572 / RATE
    return G


ORDER = {}


def rank_program(g, core, T, topo):
    rank = T.rank_of(core)
    if rank is None:
        return
    G = build(core, T, topo, rank)
    if "o" not in ORDER: ORDER["o"] = schedule(G)[0]; ORDER["e"] = [o["eng"] for o in G["ops"]]
    Q = {"V": g.vector, "S": g.scalar, "P": g.tensor, "G": g, "Y": g.sync}
    ops = G["ops"]; eng = ORDER["e"]
    for o, e in zip(ops, eng):
        if o["eng"] != e: o["fn"] = o["alt"][2]
    count = {}; known = {e: {} for e in Q}; done = [None] * len(ops); clock = [None] * len(ops)
    for i in ORDER["o"]:
        o = ops[i]; e = eng[i]
        if e not in Q:
            done[i] = (o["key"], o["cnt"]); clock[i] = {}; count[o["key"]] = o["cnt"]
            continue
        kn = known[e]
        need = {}
        for j, raw in o["deps"].items():
            if eng[j] == e and not raw and ops[j]["key"] is None: continue
            if ops[j]["key"] == "loc": continue
            k, c = done[j]
            if kn.get(k, 0) < c: need[k] = max(need.get(k, 0), c)
        for k, c in sorted(need.items()):
            if kn.get(k, 0) >= c: continue
            Q[e].wait_ge(T.sem[k], c)
            kn[k] = max(kn.get(k, 0), c)
            for j in o["deps"]:
                if done[j][0] == k and done[j][1] <= c:
                    for kk, vv in clock[j].items(): kn[kk] = max(kn.get(kk, 0), vv)
        ins = o["fn"](Q)
        k = o["key"] or "c" + e
        count[k] = count.get(k, 0) + o["cnt"]
        if o["key"] is None:
            for x in ins: x.then_inc(T.sem[k], 1)
        done[i] = (k, count[k])
        c = dict(kn); c[k] = max(c.get(k, 0), count[k])
        clock[i] = c
    for k in sorted(count): g.wait_ge(T.sem[k], count[k])
